import numpy as np, ml_dtypes
CORES = [9,25,41,57]
N = 4
BF = ml_dtypes.bfloat16
C, L, B, S, P, VOTE = 1024, 256, 4, 6, 8, 64
R = B * L
M = N * R
def parts(rng):
    z = rng.integers(0, 256, (N, 8, 16, C)) + rng.integers(-64, 65, (N, 8, 1, C))
    return {"cd": rng.integers(0, 16, (N, 8, 16, C)), "zt": np.clip(z, 0, 255), "kid": rng.integers(0, C, (N, 8, C)), "ky": rng.integers(0, C, (N, 8, C)),
            "e0": rng.integers(0, M, (N, 8, 16, L)), "c0": rng.integers(0, C, (N, 8, L)), "x0": rng.integers(0, 256, (N, 8, 16, R)),
            "ce0": rng.integers(0, M, (N, 8, 16, R)), "cc0": rng.integers(0, C, (N, 8, R))}
def pack(d):
    o = {}
    for k in ("cd", "zt", "kid", "ky", "e0", "c0", "x0", "ce0", "cc0"):
        v = np.ascontiguousarray(d[k].reshape(N, -1, d[k].shape[-1]))
        o[k] = v.astype(np.float32).astype(BF) if k in ("zt", "x0") else v.astype(np.int32)
    return o
def setup_inputs(rng):
    return pack(parts(rng))
def uneven(rng, n, shape, coin):
    v = np.minimum(np.exp2(rng.random(shape) * np.log2(n + 1.0)).astype(np.int64) - 1, n - 1)
    return np.where(rng.random(coin) < 0.5, v, n - 1 - v)
def setup_inputs_spread(rng):
    return pack({"cd": uneven(rng, 16, (N, 8, 16, C), (N, 8, 1, C)), "zt": uneven(rng, 256, (N, 8, 16, C), (N, 8, 1, C)),
                 "kid": uneven(rng, C, (N, 8, C), (N, 8, C)), "ky": uneven(rng, C, (N, 8, C), (N, 8, C)),
                 "e0": uneven(rng, M, (N, 8, 16, L), (N, 8, 1, L)), "c0": uneven(rng, C, (N, 8, L), (N, 8, L)),
                 "x0": uneven(rng, 256, (N, 8, 16, R), (N, 8, 1, R)), "ce0": uneven(rng, M, (N, 8, 16, R), (N, 8, 1, R)), "cc0": uneven(rng, C, (N, 8, R), (N, 8, R))})
def mix(rng, hi, *shape):
    v = np.where(rng.random(shape) < 0.5, 0, hi)
    return np.where(rng.random(shape) < 0.72, v, rng.integers(0, hi + 1, shape))
def setup_inputs_ends(rng):
    d = {"cd": mix(rng, 15, N, 8, 16, C), "zt": mix(rng, 255, N, 8, 16, C), "kid": mix(rng, C - 1, N, 8, C), "ky": mix(rng, C - 1, N, 8, C),
         "e0": mix(rng, M - 1, N, 8, 16, L), "c0": mix(rng, C - 1, N, 8, L), "x0": mix(rng, 255, N, 8, 16, R), "ce0": mix(rng, M - 1, N, 8, 16, R), "cc0": mix(rng, C - 1, N, 8, R)}
    rec = rng.random((N, 8, 1, R)); d["x0"] = np.where(rec < 0.15, 0, np.where(rec < 0.3, 255, d["x0"]))
    d["e0"][:, :, 0] = np.where(rng.random((N, 8, L)) < 0.8, rng.integers(0, M, (N, 8, L)), d["e0"][:, :, 0])
    d["ce0"][:, :, 0] = np.where(rng.random((N, 8, R)) < 0.8, rng.integers(0, M, (N, 8, R)), d["ce0"][:, :, 0])
    d["cd"][:, :, 0] = np.where(rng.random((N, 8, C)) < 0.7, 0, d["cd"][:, :, 0])
    d["x0"][0, :, :, 0] = 0; d["x0"][N - 1, :, :, R - 1] = 255
    cd, zt, c0 = d["cd"], d["zt"], d["c0"]
    cd[:, :, :8, C - 1] = 0; cd[:, :, 8:, C - 1] = 15
    cd[:, :, :, 0] = 0; cd[:, :, 15, 0] = 15
    cd[:, :, :, C - 2] = 0
    zt[..., 0] = np.where(rng.random((N, 8, 16)) < 0.5, 255, 0); zt[..., C - 2] = 255
    for q in range(N):
        v = np.full(128, 255); v[rng.permutation(128)[:VOTE - q % 2]] = 0; zt[q, :, :, C - 1] = v.reshape(8, 16)
    c0[..., 0] = C - 1; c0[..., L - 1] = C - 1; c0[..., 1] = 0; c0[..., L - 2] = 0; c0[..., 2] = C - 2; c0[..., L - 3] = C - 2
    for i in (0, 1, 2, L - 3, L - 2, L - 1): d["e0"][:, :, 0, i] = 0; d["e0"][:, :, 15, i] = M - 1
    return pack(d)
def setup_inputs_corners(rng):
    d = parts(rng); own = lambda n, top, *lead: 16 * rng.integers(0, top // 16, lead + (n,)) + np.arange(n) % 16
    d["kid"] = own(C, C, N, 8); d["ky"] = own(C, C, N, 8); d["e0"] = own(L, M, N, 8, 16); d["c0"] = own(L, C, N, 8); d["ce0"] = own(R, M, N, 8, 16); d["cc0"] = own(R, C, N, 8)
    d["x0"] = 2 * rng.integers(0, 128, (N, 8, 16, R)); d["e0"][:, :, 0, 0] = 0; d["e0"][:, :, 15, L - 1] = M - 1; d["c0"][..., 0] = 0; d["c0"][..., L - 1] = C - 1
    want = (0, 1, 2, 3, VOTE - 16, VOTE - 2, VOTE - 1, VOTE - 1, VOTE, VOTE, VOTE + 1, VOTE + 16, 112, 126, 127, 128)
    need = np.zeros((N, 8, 16), np.int64)
    for q in range(N):
        for k in range(16): need[q, :, k] = np.bincount(rng.permutation(128)[:want[(k + 5 * q) % 16]] // 16, minlength=8)
    place = np.argsort(np.argsort(rng.random((N, 8, 16, C)), axis=2), axis=2)
    d["zt"] = np.where(place < need[:, :, np.arange(C) % 16][:, :, None, :], 0, 255)
    return pack(d)
def setup_inputs_crowd(rng):
    d = parts(rng); mode = rng.permutation(8); s = np.arange(R)
    one = rng.choice(np.array([0, M - 1, M // 2, R - 1]), 8); lane = int(rng.integers(0, L))
    for q in range(N):
        for g in range(8):
            m = mode[g]
            if m < 2:
                ke, kc = d["e0"][q, g, :, lane].copy(), d["c0"][q, g, lane]
                d["e0"][q, g] = one[g]; d["c0"][q, g] = (0, C - 1)[q % 2]
                if m == 1: d["e0"][q, g, :, lane] = ke; d["c0"][q, g, lane] = (kc + (kc == 0)) % (C - 1)
            elif m == 2: d["e0"][q, g] = np.where(rng.random((16, L)) < 0.5, 0, M - 1)
            elif m == 3: d["e0"][q, g] = q * R + np.arange(L); d["ce0"][q, g] = q * R + s
            elif m == 4: d["cd"][q, g] = 0
            elif m == 5: d["cd"][q, g] = 15
            elif m == 6: d["ce0"][q, g] = (q * R + s + 1) % M; d["cd"][q, g] = np.arange(16)[:, None]
            else:
                for k in ("c0", "kid", "ky", "cc0"): d[k][q, g] = rng.choice(np.array([0, C - 1, C // 2]), d[k][q, g].shape)
    return pack(d)
def setup_inputs_full(rng):
    d = parts(rng); K = 16 // N; kind = rng.permutation(np.arange(N) % 4)[:, None, None]; o = int(rng.integers(0, N))
    cd = np.argsort(rng.random((N, 8, 16, C)), axis=2); u = (np.arange(N) + int(rng.integers(0, N))).reshape(N, 1, 1, 1)
    cd = (cd + (u - cd[:, :, :1]) % N) % 16
    s = np.argsort(rng.random((N, 8, B, N, R)), axis=4)[..., :K * L].reshape(N, 8, B, N, K, L)
    s = s + R * ((np.arange(8)[:, None] + np.arange(N)[None, :]) % N).reshape(1, 8, 1, N, 1, 1)
    c0 = 2 * np.argsort(rng.random((N, 8, C // 2)), axis=2)[..., :L] + np.where(kind < 2, rng.integers(0, 2, (N, 8, L)), kind - 2)
    kid = np.argsort(rng.random((N, 8, C)), axis=2); kk = kind[..., None]
    e0 = o * R + rng.integers(0, R, (N, 8, 16, L))
    t0 = o * R + L * rng.integers(0, B, (N, 8, 1)) + np.argsort(rng.random((N, 8, L)), axis=2)
    np.put_along_axis(e0, np.take_along_axis(cd[:, :, 0], c0, 2)[:, :, None, :], t0[:, :, None, :], 2)
    d["cd"] = cd; d["ce0"] = s.transpose(0, 1, 4, 3, 2, 5).reshape(N, 8, 16, R); d["c0"] = c0; d["e0"] = e0
    d["kid"] = np.where(kind < 2, kid, kid | 1); d["ky"] = d["ky"] & -2; d["cc0"] = d["cc0"] & -2; d["x0"] = d["x0"] & -2
    z = np.where(kk == 0, 0, np.where(kk == 1, 255, 255 * (np.arange(C) % 2)))
    d["zt"] = np.array(np.broadcast_to(z, (N, 8, 16, C)))
    return pack(d)
def check_inputs(d):
    bad = []
    for k, hi in (("cd", 15), ("zt", 255), ("kid", C - 1), ("ky", C - 1), ("e0", M - 1), ("c0", C - 1), ("x0", 255), ("ce0", M - 1), ("cc0", C - 1)):
        v = np.asarray(d[k]).astype(np.float64)
        if not (np.min(v) >= 0 and np.max(v) <= hi): bad.append("range of " + k)
        elif np.any(v != np.floor(v)): bad.append("whole numbers of " + k)
    return bad
def reference(cd, zt, kid, ky, e0, c0, x0, ce0, cc0):
    row = cd.astype(np.int64).reshape(N, 8, 16, C); z = zt.astype(np.float32).astype(np.int64).reshape(N, 8, 16, C)
    kd = kid.astype(np.int64); kc = ky.astype(np.int64); e = e0.astype(np.int64).reshape(N, 8, 16, L); c = c0.astype(np.int64)
    hx = np.array(x0.astype(np.float32).astype(np.int64).reshape(N, 8, 16, R).transpose(1, 2, 0, 3)).reshape(8, 16, M)
    he = np.array(ce0.astype(np.int64).reshape(N, 8, 16, R).transpose(1, 2, 0, 3)).reshape(8, 16, M)
    hc = np.array(cc0.astype(np.int64).transpose(1, 0, 2)).reshape(8, M)
    out = []
    for t in range(S):
        nm = np.take_along_axis(e, np.take_along_axis(row, c[:, :, None, :], 3), 2)
        w = []
        for q in range(N):
            v = np.take_along_axis(hx, nm[q].reshape(8, 1, 16 * L), 2).reshape(8, 16, 16 // P, P, L)
            w.append(np.add.reduce(np.maximum.reduce(v, axis=2), axis=2) & 255)
        w = np.stack(w)
        yes = (w >= np.take_along_axis(z, c[:, :, None, :], 3)).astype(np.int64)
        binds = np.add.reduce(yes.reshape(N, 128, L), axis=1) >= VOTE
        place = np.arange(N)[:, None] * R + L * (t % B) + np.arange(L)[None, :]
        first = np.broadcast_to(place[:, None, None, :], (N, 8, 1, L))
        eb = np.concatenate([first, e[:, :, :15]], axis=2)
        ea = np.stack([np.take_along_axis(he, nm[q][:, 0:1, :], 2) for q in range(N)])
        ca = np.stack([np.take_along_axis(hc, nm[q][:, 0, :], 1) for q in range(N)])
        en = np.where(binds[:, None, None, :], eb, ea); cn = np.where(binds[:, None, :], np.take_along_axis(kd, c, 2), ca)
        if t < S - 1:
            kq = np.take_along_axis(kc, c, 2)
            for q in range(N):
                lo = q * R + L * (t % B)
                hx[:, :, lo:lo + L] = w[q]; he[:, :, lo:lo + L] = e[q]; hc[:, lo:lo + L] = kq[q]
        e = en; c = cn; out.append(w.reshape(N, 128, L))
    return {"ye": e.reshape(N, 128, L).astype(np.float32), "yc": c.astype(np.float32), "yx": np.concatenate(out, axis=2).astype(np.float32).astype(BF)}

@@ -1,0 +1,753 @@
+from concourse.bass import DstId, RemoteDMATransfer
+from concourse.mybir import AluOpType, AxisListType, ActivationFunctionType
+
+N, S = 4, 6
+F32, BF, F16, I32, U16 = "float32", "bfloat16", "float16", "int32", "uint16"
+W1, W2 = 896, 512
+SHARE = ((("act", 40), ("dve", 24)),) * 4
+
+
+def _sb(cols, dtype):
+    return ("sbuf", [128, cols], dtype)
+
+
+SCRATCH = {
+    "LX": _sb(1024, BF), "LCE": _sb(1024, I32), "LCD": _sb(1024, I32), "LE": _sb(256, I32), "CT": _sb(832, I32),
+    "SG": _sb(1024, BF), "CF": _sb(832, F16), "FP": _sb(832, F16), "FF": _sb(832, F16),
+    "M1": _sb(4 * W1, F16), "L1": _sb(4 * W1, F16), "M2": _sb(4 * W2, BF), "L2": _sb(4 * W2, BF),
+    "H": _sb(4096, F32), "CD": _sb(1024, BF), "ZT": _sb(1024, BF), "KK": _sb(1024, BF),
+    "V": _sb(4096, F32), "GA": _sb(2048, F32), "GB": _sb(2048, BF),
+    "EL": _sb(256, U16), "E16": _sb(256, F16), "QL": _sb(16, U16), "RG": _sb(256, BF), "KG": _sb(256, BF),
+    "LL": _sb(256, U16), "FB": _sb(256, BF), "WS": _sb(1536, BF), "MK": _sb(256, BF), "YS": _sb(256, BF),
+    "PV": _sb(320, BF), "BL": _sb(16, U16), "X32": _sb(256, I32), "N32": _sb(256, I32), "C32": _sb(256, I32),
+    "CB": _sb(256, BF), "EB16": _sb(256, F16), "EA16": _sb(256, F16),
+    "MF": _sb(512, F16), "LF": _sb(512, F16), "MG": _sb(512, F16), "LG": _sb(512, F16), "MH": _sb(512, BF), "LH": _sb(512, BF),
+    "EA2": _sb(320, F32), "OM": _sb(320, F32), "OUT": _sb(320, F32), "BB": _sb(64, F32),
+    "XF": _sb(160, F32), "XL": _sb(516, F32), "PI": _sb(1, I32), "PJ": _sb(8, I32), "PC": _sb(32, F32), "TA": _sb(8, F32),
+    "TB": _sb(8, F32), "V1": _sb(128, BF), "V2": _sb(128, BF), "V3": _sb(128, BF), "V5": _sb(224, BF), "VA": _sb(512, BF),
+    "VWv": _sb(160, F32), "VY": _sb(516, BF), "VV": _sb(128, BF), "SV": _sb(128, BF), "CLv": _sb(128, BF),
+    "IB": _sb(128, BF), "IS": _sb(128, BF), "I128": _sb(128, BF), "I8": _sb(128, BF), "I1K": _sb(128, BF), "IH": _sb(128, F16),
+    "NH": _sb(128, F16), "PA": _sb(532, F16), "PA1": _sb(512, F16), "PA2": _sb(512, F16), "PB": _sb(532, F16),
+    "RE": _sb(512, F16), "RW": _sb(512, BF), "RK": _sb(512, BF), "RA": _sb(512, F16), "RB": _sb(512, F16), "ZW": _sb(896, F16),
+    "SH": _sb(128, F16), "KID": _sb(128, BF), "SAB": _sb(512, BF), "CL": _sb(128, BF), "C8": _sb(8, BF), "IT": _sb(128, BF),
+    "BC": _sb(8, F32), "BC2": _sb(2, F32), "VW": _sb(160, BF), "QW": _sb(144, BF), "YH": _sb(516, F16), "YB": _sb(516, BF),
+    "YC": _sb(516, BF), "YK": _sb(516, BF), "YV": _sb(516, BF), "CS": _sb(128, BF), "ZR": _sb(512, BF), "K64": _sb(512, BF),
+    "SF": _sb(1, F32),
+    "DW": ("dram", [4, 128, 320], BF), "DL": ("dram", [4, 128, 320], BF),
+}
+for _b in range(8):
+    SCRATCH["P%d" % _b] = ("psum", [128, 512], F32)
+NDMA = 56
+SEMAPHORES = (["pe", "act", "dve", "pool", "sent"] + ["d%d" % i for i in range(NDMA)]
+              + ["a%d_%d" % (j, k) for j in (0, 1, 2) for k in (1, 2, 3)] + ["v%d" % i for i in range(10)]
+              + ["ay", "af", "ag", "ah"])
+
+R0, R1, S0, S1, BL2, BEB, BVW, BVS = range(8)
+CYC, GAT, PEC, HOP, LAT, RATE = 1.0e-3, 1.45e-3, 0.5e-3, 0.09, 2.7, 80.0
+CASES = ((1.0, 1.0, 1.0, 0.0), (0.75, 0.9, 0.9, 0.7), (1.2, 1.1, 1.2, -0.6))
+ROUNDS, HEAT, SEED, PLAN = 12000, 0.15, 1, {}
+PERIOD = 11.5
+AIM = {("V", 0, "act"): 0.0, ("V", 0, "dve"): 0.0, ("V", 1, "dve"): 0.4, ("V", 1, "act"): 1.0, ("GA", 0, "act"): 1.2,
+       ("GA", 1, "act"): 2.0, ("GB", 0, "dve"): 2.0, ("GB", 1, "dve"): 3.9, ("FB", 0, "act"): 5.1, ("WS", 0, "dve"): 5.4,
+       ("YS", 0, "dve"): 5.6, ("PV", 0, "act"): 6.4, ("PV", 0, "pool"): 6.5, ("PV", 0, "link"): 7.0, ("MK", 0, "dve"): 8.8,
+       ("H", 0, "act"): 8.5, ("BL", 0, "dve"): 10.2, ("X32", 0, "dve"): 10.4, ("C32", 0, "dve"): 10.9, ("CB", 0, "dve"): 11.0,
+       ("N32", 0, "dve"): 10.6, ("EL", 0, "dve"): 10.8, ("QL", 0, "dve"): 11.9, ("E16", 0, "dve"): 13.0,
+       ("RG", 0, "act"): 0.9, ("LL", 0, "dve"): 1.3, ("KG", 0, "act"): 2.9,
+       ("BL", 1, "dve"): 14.3, ("X32", 1, "dve"): 14.4, ("N32", 1, "dve"): 14.6, ("EL", 1, "dve"): 14.8, ("C32", 1, "dve"): 15.0,
+       ("CB", 1, "dve"): 15.1, ("QL", 1, "dve"): 16.2, ("E16", 1, "dve"): 17.5, ("V", 2, "act"): 3.7, ("V", 2, "dve"): 4.8,
+       ("V", 3, "dve"): 5.0, ("V", 3, "act"): 6.6, ("RG", 1, "act"): 5.0, ("LL", 1, "dve"): 5.7, ("GA", 2, "act"): 5.8,
+       ("GA", 3, "act"): 7.0, ("KG", 1, "act"): 7.9, ("GB", 2, "dve"): 6.7, ("GB", 3, "dve"): 7.9, ("FB", 1, "act"): 9.1,
+       ("WS", 1, "dve"): 9.4, ("MK", 1, "dve"): 9.6, ("YS", 1, "dve"): 9.7, ("PV", 1, "act"): 10.5, ("PV", 1, "pool"): 10.6,
+       ("PV", 1, "link"): 11.0, ("H", 1, "act"): 10.2, ("H", 1, "dve"): 10.5, ("EB", 0, "act"): 8.4, ("EB", 1, "act"): 12.9}
+
+
+def build_ops(g, T, topo, core, me):
+    A, ACT = AluOpType, ActivationFunctionType
+    ops = []
+    role = [None, 0, 0]
+
+    def op(eng, fn, rd, wr, dur, lat=0.0, kind="c", **kw):
+        kw["role"] = ("once", len(ops)) if role[0] is None else (role[0], role[1])
+        kw["step"] = role[2]
+        role[1] += 1
+        ops.append(dict(eng=eng, fn=fn, rd=list(rd), wr=list(wr), dur=dur, lat=lat, kind=kind, **kw))
+        return len(ops) - 1
+
+    def dv(fn, rd, wr, n):
+        return op("dve", fn, rd, wr, 0.03 + max(64, n) * CYC)
+
+    def ts(out, in0, s1, s2, o0, o1, rd, wr, n):
+        if o1 is None:
+            return dv(lambda: g.vector.tensor_scalar(out, in0, s1, None, o0), rd, wr, n)
+        return dv(lambda: g.vector.tensor_scalar(out, in0, s1, s2, o0, o1), rd, wr, n)
+
+    def cp(out, in_, rd, wr, n):
+        return dv(lambda: g.vector.tensor_copy(out, in_), rd, wr, n)
+
+    def tt(out, a, b, o, rd, wr, n):
+        return dv(lambda: g.vector.tensor_tensor(out, a, b, o), rd, wr, n)
+
+    def ms(ap, v, wr, n):
+        return dv(lambda: g.vector.memset(ap, v), [], wr, n)
+
+    def ac(out, in_, rd, wr, n, bias=None, func=None):
+        f = ACT.Identity if func is None else func
+        if bias is None:
+            return op("act", lambda: g.scalar.activation(out, in_, ACT.Copy), rd, wr, 0.06 + n * CYC)
+        return op("act", lambda: g.scalar.activation(out, in_, f, bias=bias), rd, wr, 0.06 + n * CYC)
+
+    def gat(eng, fn, rd, wr, n):
+        return op(eng, fn, rd, wr, 0.06 + n * GAT, cls=0)
+
+    def mm(lst, rd, wr):
+        def fn():
+            last = None
+            for o, l, r, n, st, sp in lst:
+                last = g.tensor.matmul(o, l, r, st, sp)
+            return last
+        return op("pe", fn, rd, wr, 0.05 + sum(max(64, x[3]) for x in lst) * PEC)
+
+    def group(items):
+        return [(o, l, r, n, i == 0, i == len(items) - 1) for i, (o, l, r, n) in enumerate(items)]
+
+    def more(items, stop=False):
+        return [(o, l, r, n, False, stop and i == len(items) - 1) for i, (o, l, r, n) in enumerate(items)]
+
+    def zero(bank, n):
+        return (P(bank)[:, 0:n], T.ZR[0:1, 0:128], T.ZR[0:1, 0:n], n, True, False)
+
+    def io(out, pat, base, cm, wr, n, flag=True):
+        if flag:
+            return op("pool", lambda: g.iota(out, pat, base, cm, allow_small_or_imprecise_dtypes=True), [], wr, 0.13 + 2 * n * CYC)
+        return op("pool", lambda: g.iota(out, pat, base, cm), [], wr, 0.13 + 2 * n * CYC)
+
+    def dma(q, out, in_, rd, wr, kb):
+        e = g.sync if q == "sp" else g.scalar
+        return op(q, lambda: e.dma_start(out, in_), rd, wr, 0.1, lat=2.0 + kb / 200.0, kind="dma")
+
+    def P(b):
+        return T["P%d" % b]
+
+    def B(b):
+        return ("B", b)
+
+    def peer(k):
+        return (me + k) % N
+
+    def dst_id(r):
+        rid, pid, _ = topo.addr(T.cores[r])
+        return DstId(rid=rid, pnc=pid)
+
+    lanes_out = topo.engines(core, T.cores[peer(1)])
+    full = sum(1 << e for e in lanes_out)
+    ne = len(lanes_out)
+    per = ne // 4
+
+    def send(out, in_, r, sem, rd, kb):
+        rid, pid, _ = topo.addr(T.cores[r])
+        return op("pool", lambda: g.remote_dma(out, in_, T.sem[sem], T.sem.sent, pid, rid, full), rd, [], 0.5,
+                  kind="send", inc=ne, kb=kb)
+
+    def recv(after, sem, cnt, wr):
+        return op("link", None, [], wr, 0.01 + ops[after]["kb"] / RATE, lat=LAT, kind="recv", after=after, sem=sem, cnt=cnt)
+
+    def fan(src, dst, sem, rd, kb):
+        trs = [RemoteDMATransfer(dst_ids=[dst_id(peer(k))], dma_engine_mask=sum(1 << e for e in lanes_out[per * (k - 1):per * k]),
+                                 remote_sem=T.sem[sem], src=src(peer(k)), dst=dst) for k in (1, 2, 3)]
+        sd = op("pool", lambda: g.remote_dma_fused(trs, local_sem=T.sem.sent), rd, [], 0.5, kind="send", inc=3 * per, kb=kb)
+        recv(sd, sem, 3 * per, [sem])
+
+    order = [peer(1), peer(2), peer(3), me]
+    dma("sp", T.CT[0:32, 0:256], T.cc0[:], [], ["CT0"], 32)
+    dma("act", T.CT[0:32, 256:320], T.c0[:], [], ["CT1"], 8)
+    for d in order:
+        rows = slice(32 * d, 32 * d + 32)
+        dma("sp", T.LCE[:, 256 * d:256 * d + 256], T.ce0[rows, :], [], [("LCE", d)], 128)
+        dma("act", T.LX[:, 256 * d:256 * d + 256], T.x0[rows, :], [], [("LX", d)], 64)
+        dma("sp", T.LCD[:, 256 * d:256 * d + 256], T.cd[rows, :], [], [("LCD", d)], 128)
+        dma("act", T.LE[:, 64 * d:64 * d + 64], T.e0[rows, :], [], [("LE", d)], 32)
+    dma("sp", T.CT[0:32, 320:576], T.ky[:], [], ["CT2"], 32)
+    dma("sp", T.CT[0:32, 576:832], T.kid[:], [], ["CT3"], 32)
+    for d in order:
+        dma("sp", T.M2[:, W2 * d:W2 * d + 256], T.zt[32 * d:32 * d + 32, :], [], [("M2z", d)], 64)
+
+    io(T.V2[:], [[0, 4], [-1, 32]], 0, 1, ["V2"], 128)
+    io(T.VA[:], [[-4, 8], [-32, 16], [-1, 4]], 0, 1, ["VA"], 512)
+    io(T.V1[:], [[-1, 128]], 0, 1, ["V1"], 128)
+    io(T.V3[:], [[0, 4], [-4, 32]], 0, 1, ["V3"], 128)
+    io(T.V5[:], [[4, 224]], -384, -1, ["V5"], 224)
+    io(T.PI[:], [[0, 1]], 0, 1, ["PI"], 1, flag=False)
+    io(T.XF[:], [[1, 160]], 0, 0, ["XF"], 160)
+    io(T.CLv[:], [[0, 4], [32, 32]], 0, 0, ["CLv"], 128)
+    io(T.VWv[:], [[32, 5], [0, 2], [1000, 16]], 0, 0, ["VWv"], 160)
+    io(T.VY[:], [[-1, 516]], 3, 4, ["VY"], 516)
+    io(T.VV[:], [[0, 32], [-1, 4]], -64, 1, ["VV"], 128)
+    io(T.XL[:], [[1, 516]], 0, 0, ["XL"], 516)
+    for b in range(4):
+        ms(T.SF[32 * b:32 * b + 32, :], 0.25 ** (b + 1), [("SF", b)], 1)
+    SFt = [("SF", b) for b in range(4)]
+    ms(T.ZR[:], 0.0, ["ZR"], 256)
+    ms(T.K64[:], 64.0, ["K64"], 256)
+    ms(T.CS[:], 49152.0 * 65536.0, ["CS"], 64)
+    ms(T.PA[:, 0:20], 0.0, ["PAp"], 10)
+    ms(T.PB[:, 0:20], 0.0, ["PBp"], 10)
+    for r in range(4):
+        ts(T.RE[:, 128 * r:128 * r + 128], T.V2[:], 32.0 * r, None, A.is_equal, None, ["V2"], [("RE", r)], 64)
+    ts(T.PA1[:], T.VA[:], -32.0, None, A.is_equal, None, ["VA"], ["PA1"], 256)
+    ts(T.PA2[:], T.VA[:], 0.0, -4.0, A.is_equal, A.mult, ["VA"], ["PA2"], 256)
+    ts(T.PB[:, 20:532], T.VA[:], 0.0, None, A.is_equal, None, ["VA"], ["PB"], 256)
+    tt(T.PA[:, 20:532], T.PA1[:], T.PA2[:], A.add, ["PA1", "PA2"], ["PA"], 1024)
+    for name, sc in (("I8", 8.0), ("I1K", 1024.0), ("IB", 1.0), ("IS", 2.0 ** -16), ("I128", 1.0 / 128), ("IH", 1.0), ("NH", -1.0)):
+        ts(T[name][:], T.V1[:], 0.0, sc, A.is_equal, A.mult, ["V1"], [name], 64)
+    for u in range(4):
+        ts(T.RA[:, 128 * u:128 * u + 128], T.V3[:], float(u), 8192.0, A.is_equal, A.mult, ["V3"], [("RA", u)], 64)
+        ts(T.RB[:, 128 * u:128 * u + 128], T.V3[:], float(u), None, A.is_equal, None, ["V3"], [("RB", u)], 64)
+        ts(T.ZW[:, 224 * u:224 * u + 224], T.V5[:], float(-u), None, A.is_equal, None, ["V5"], [("ZW", u)], 112)
+    for j, (s1, s2, o0, o1) in enumerate(((15, None, A.bitwise_and, None), (112, None, A.bitwise_and, None),
+                                          (5, None, A.arith_shift_right, None), (3, 1, A.arith_shift_right, A.bitwise_and),
+                                          (4, 1, A.arith_shift_right, A.bitwise_and))):
+        ts(T.PJ[:, j:j + 1], T.PI[:], s1, s2, o0, o1, ["PI"], [("PJ", j)], 1)
+    cp(T.PC[:, 0:5], T.PJ[:, 0:5], [("PJ", j) for j in range(5)], ["PC"], 5)
+
+    def col(j):
+        return T.PC[:, j:j + 1]
+
+    cF, cG, cR, cU, cH = range(5)
+    (LO8, HI8, N15, K5, K10, KIDC, F0, F128, BT, BASE, F8, U16C, G16, R32, TV, PW, PWK, P4, P4K, TY0, TY) = range(5, 26)
+
+    def cs(j, src, s1, s2, o0, o1, rd=()):
+        ts(col(j), col(src), s1, s2, o0, o1, ["PC"] + [("c", x) for x in rd], [("c", j)], 1)
+
+    cs(LO8, cF, 8.0, None, A.is_lt, None)
+    cs(HI8, cF, 8.0, None, A.is_ge, None)
+    cs(N15, cF, 15.0, None, A.is_lt, None)
+    cs(K5, cF, 5.0, 8192.0, A.is_lt, A.mult)
+    cs(K10, cF, 10.0, 8192.0, A.is_lt, A.mult)
+    cs(KIDC, K10, col(K5), None, A.subtract, None, (K10, K5))
+    cs(F0, cF, 0.0, None, A.is_equal, None)
+    cs(F128, cF, 0.0, 128.0, A.is_equal, A.mult)
+    cs(BT, cR, 1024.0, -2048.0, A.mult, A.add)
+    cs(BASE, BT, col(F0), 2048.0, A.mult, A.add, (BT, F0))
+    cs(F8, cF, 8.0, None, A.mult, None)
+    cs(U16C, cU, 16.0, None, A.mult, None)
+    cs(G16, cG, 16.0, None, A.add, None)
+    cs(R32, cR, 32.0, 32.0, A.mult, A.add)
+    cs(TV, cR, 128.0, 67.0, A.mult, A.add)
+    cs(TY0, cH, 4.0, 8.0 * me + 3.0, A.mult, A.add)
+    cs(TY, cR, 128.0, col(TY0), A.mult, A.add, (TY0,))
+    for i, (x0, pw, ind, p4) in enumerate(((0, PW, K5, P4), (5, PWK, KIDC, P4K))):
+        ts(T.TA[:, 4 * i:4 * i + 4], T.XF[:, x0:x0 + 4], col(cF), 3.0, A.is_lt, A.mult, ["XF", "PC"], [("TA", i)], 4)
+        ts(T.TB[:, 4 * i:4 * i + 4], T.TA[:, 4 * i:4 * i + 4], 1.0, None, A.add, None, [("TA", i)], [("TB", i)], 4)
+        dv(lambda i=i, pw=pw: g.vector.tensor_reduce(col(pw), T.TB[:, 4 * i:4 * i + 4], AxisListType.X, A.mult),
+           [("TB", i)], [("c", pw)], 4)
+        cs(p4, pw, col(ind), 1.0 / 8192, A.mult, A.mult, (pw, ind))
+    ts(T.QW[:], T.XF[:, 0:144], col(G16), col(P4), A.is_equal, A.mult, ["XF", ("c", G16), ("c", P4)], ["QW"], 144)
+    for i, (v, m) in enumerate(((0.0, LO8), (-8.0, LO8), (8.0, HI8), (0.0, HI8))):
+        ts(T.SAB[:, 128 * i:128 * i + 128], T.V1[:], v, col(m), A.is_equal, A.mult, ["V1", ("c", m)], [("SAB", i)], 64)
+    ts(T.CL[:], T.CLv[:], col(U16C), None, A.add, None, ["CLv", ("c", U16C)], ["CL"], 64)
+    ts(T.SH[:], T.V1[:], -1.0, col(N15), A.is_equal, A.mult, ["V1", ("c", N15)], ["SH"], 64)
+    ts(T.KID[:], T.V1[:], 5.0, col(KIDC), A.is_equal, A.mult, ["V1", ("c", KIDC)], ["KID"], 64)
+    ts(T.IT[:], T.XF[:, 0:128], col(F0), None, A.mult, None, ["XF", ("c", F0)], ["IT"], 128)
+    ts(T.BC[:], T.XF[:, 0:8], col(F128), col(BASE), A.mult, A.add, ["XF", ("c", F128), ("c", BASE)], ["BC"], 8)
+    ts(T.BC2[:], T.BC[:, 2:4], -2048.0, None, A.add, None, ["BC"], ["BC2"], 2)
+    ts(T.C8[:], T.XF[:, 0:8], 128.0, col(F8), A.mult, A.add, ["XF", ("c", F8)], ["C8"], 8)
+    ts(T.VW[:], T.VWv[:], col(R32), None, A.is_equal, None, ["VWv", ("c", R32)], ["VW"], 160)
+    for r in range(4):
+        ts(T.RW[:, 128 * r:128 * r + 128], T.V2[:], 32.0 * r, 65536.0, A.is_equal, A.mult, ["V2"], [("RW", r)], 64)
+        ts(T.RK[:, 128 * r:128 * r + 128], T.V2[:], 32.0 * r, col(K5), A.is_equal, A.mult, ["V2", ("c", K5)], [("RK", r)], 64)
+    ts(T.YH[:], T.VY[:], 0.0, None, A.is_equal, None, ["VY"], ["YH"], 258)
+    ts(T.YB[:], T.VY[:], 0.0, None, A.is_equal, None, ["VY"], ["YB"], 258)
+    ts(T.YV[:], T.XL[:], col(TV), None, A.is_equal, None, ["XL", ("c", TV)], ["YV"], 516)
+    ts(T.SV[:], T.VV[:], 0.0, None, A.is_equal, None, ["VV"], ["SV"], 64)
+    ts(T.YC[:], T.XL[:], col(TY), col(P4), A.is_equal, A.mult, ["XL", ("c", TY), ("c", P4)], ["YC"], 516)
+    ts(T.YK[:], T.XL[:], col(TY), col(P4K), A.is_equal, A.mult, ["XL", ("c", TY), ("c", P4K)], ["YK"], 516)
+
+    for i, (a, b, bank, tk) in enumerate(((0, 320, BL2, ["CT0", "CT1"]), (320, 832, BEB, ["CT2", "CT3"]))):
+        n = b - a
+        cp(T.CF[0:32, a:b], T.CT[0:32, a:b], tk, [("CF", i)], n)
+        mm(group([(P(bank)[:, 0:n], T.RE[0:32, 0:128], T.CF[0:32, a:b], n)]), [("CF", i), ("RE", 0)], [B(bank)])
+        ts(T.FP[:, a:b], P(bank)[:, 0:n], T.SF[:, 0:1], 1536.0 - 127.5 / 256, A.mult, A.add, SFt, [B(bank), ("FP", i)], n)
+        ts(T.FF[:, a:b], T.FP[:, a:b], -1536.0, None, A.add, None, [("FP", i)], [("FF", i)], n // 2)
+
+    def pieces(out, d, a, n, pad):
+        c0 = pad + 128 * d
+        return [(out, T.PA[:, c0:c0 + 128], T.FF[:, a:a + n], n), (out, T.PB[0:32, c0:c0 + 128], T.CF[0:32, a:a + n], n)]
+
+    PAt = ["PA", "PB", "PAp", "PBp"]
+    s0, s1, s2 = {}, {}, {}
+    for i, d in enumerate(order):
+        c = slice(256 * d, 256 * d + 256)
+        m = W1 * d
+        bank = (S0, S1)[i % 2]
+        ac(T.SG[:, c], T.LX[:, c], [("LX", d)], [("SG", d)], 256, bias=-127.5, func=ACT.Sign)
+        o = P(bank)[:, 0:256]
+        mm(group([(o, T.I8[:], T.LX[:, c], 256), (o, T.I1K[:], T.SG[:, c], 256)] + pieces(o, d, 0, 256, 20))
+           + group(pieces(P(bank)[:, 256:320], d, 256, 64, 20)),
+           [("LX", d), ("SG", d), "I8", "I1K", ("FF", 0), ("CF", 0)] + PAt, [B(bank)])
+        ts(T.M1[:, m + 256:m + 512], T.LCE[:, c], -2048.0, None, A.add, None, [("LCE", d)], [("M1", d, 1)], 256)
+        cp(T.M1[:, m:m + 256], T.LCD[:, c], [("LCD", d)], [("M1", d, 2)], 256)
+        ts(T.M1[:, m + 768:m + 832], T.LE[:, 64 * d:64 * d + 64], -2048.0, None, A.add, None, [("LE", d)], [("M1", d, 3)], 64)
+        ts(T.M1[:, m + 512:m + 768], o, -1023.0, None, A.add, None, [], [B(bank), ("M1", d, 0)], 256)
+        ts(T.M1[:, m + 832:m + 896], P(bank)[:, 256:320], 8192.0, None, A.mult, None, [], [B(bank), ("M1", d, 4)], 64)
+        if d != me:
+            s0[i + 1] = send(T.L1[:, W1 * me:W1 * me + 512], T.M1[:, m:m + 512], d, "a0_%d" % (i + 1),
+                             [("M1", d, x) for x in (1, 2)], 128)
+            s1[i + 1] = send(T.L1[:, W1 * me + 512:W1 * me + W1], T.M1[:, m + 512:m + W1], d, "a1_%d" % (i + 1),
+                             [("M1", d, x) for x in (0, 3, 4)], 96)
+    for i, d in enumerate(order):
+        o = P(BVS)[:, 0:256]
+        mm(group(pieces(o, d, 320, 256, 20) + pieces(o, d, 576, 256, 0)), [("FF", 1), ("CF", 1)] + PAt, [B(BVS)])
+        ac(T.M2[:, W2 * d + 256:W2 * d + 512], o, [], [B(BVS), ("M2k", d)], 256)
+        if d != me:
+            s2[i + 1] = send(T.L2[:, W2 * me:W2 * me + W2], T.M2[:, W2 * d:W2 * d + W2], d, "a2_%d" % (i + 1),
+                             [("M2z", d), ("M2k", d)], 128)
+
+    mm([zero(BL2, 512), zero(BEB, 512), zero(BVW, 256)], ["ZR"], [B(BL2), B(BEB), B(BVW)])
+    for k in range(4):
+        s = (me - k) % N
+        if k:
+            recv(s0[k], "a0_%d" % k, ne, [("L0", s)])
+            recv(s1[k], "a1_%d" % k, ne, [("L1", s)])
+        src, tk = (T.M1, [("M1", me, x) for x in range(5)]) if k == 0 else (T.L1, [("L0", s), ("L1", s)])
+        tc = [("M1", me, 2)] if k == 0 else [("L0", s)]
+        m = W1 * s
+        for hb in range(2):
+            bank = (R0, R1, S0, S1)[(2 * k + hb) % 4]
+            lst = []
+            for u in (2 * hb, 2 * hb + 1):
+                o = P(bank)[:, 256 * (u % 2):256 * (u % 2) + 256]
+                lst += group([(o, T.RA[:, 128 * u:128 * u + 128], src[:, m + 512:m + 768], 256),
+                              (o, T.RB[:, 128 * u:128 * u + 128], src[:, m + 256:m + 512], 256)])
+            mm(lst, tk + [("RA", u) for u in range(4)] + [("RB", u) for u in range(4)], [B(bank)])
+            o = T.H[:, 1024 * s + 512 * hb:1024 * s + 512 * hb + 512]
+            wr = [B(bank)] + [("H", s, x) for x in range(4 * hb, 4 * hb + 4)]
+            if hb == 0:
+                ac(o, P(bank)[:], [], wr, 512, bias=-6144.0)
+            else:
+                ts(o, P(bank)[:], -6144.0, None, A.add, None, [], wr, 512)
+        Z = [T.ZW[:, 224 * u + 96 - 32 * s:224 * u + 224 - 32 * s] for u in range(4)]
+        Zt = [("ZW", u) for u in range(4)]
+        lst = []
+        for u in range(4):
+            o = P(BVW)[:, 64 * u:64 * u + 64]
+            lst += [(o, Z[u], src[:, m + 768:m + 832], 64), (o, Z[u], src[:, m + 832:m + 896], 64)]
+        mm(more(lst, k == 3), tk + Zt, [B(BVW)])
+        for hb, bank in enumerate((BL2, BEB)):
+            mm(more([(P(bank)[:, 256 * (u % 2):256 * (u % 2) + 256], Z[u], src[:, m:m + 256], 256)
+                     for u in (2 * hb, 2 * hb + 1)], k == 3), tc + Zt, [B(bank)])
+    for hb, bank in enumerate((BL2, BEB)):
+        ac(T.CD[:, 512 * hb:512 * hb + 512], P(bank)[:], [], [B(bank), ("CD", hb)], 512)
+    for k in range(4):
+        s = (me - k) % N
+        if k:
+            recv(s2[k], "a2_%d" % k, ne, [("L2", s)])
+        src, tz, tk = (T.M2, [("M2z", me)], [("M2k", me)]) if k == 0 else (T.L2, [("L2", s)], [("L2", s)])
+        dma("sp", T.ZT[32 * s:32 * s + 32, :], src[:, W2 * s:W2 * s + 256], tz, [("ZT", s)], 64)
+        dma("sp", T.KK[32 * s:32 * s + 32, :], src[:, W2 * s + 256:W2 * s + 512], tk, [("KK", s)], 64)
+    Ht = [("H", s, x) for s in range(4) for x in range(8)]
+    CDt, ZTt, KKt = [("CD", 0), ("CD", 1)], [("ZT", s) for s in range(4)], [("KK", s) for s in range(4)]
+
+    def pieces_of(X):
+        c = slice(128 * X, 128 * X + 128)
+        ts(T.N32[:, c], T.X32[:, c], 4095, None, A.bitwise_and, None, [("X32", X)], [("N32", X)], 128)
+        ts(T.C32[:, c], T.X32[:, c], 13, 3, A.arith_shift_right, A.bitwise_and, [("X32", X)], [("C32", X)], 128)
+        cp(T.CB[:, c], T.C32[:, c], [("C32", X)], [("CB", X)], 128)
+
+    def unpack(X):
+        c = slice(128 * X, 128 * X + 128)
+        pieces_of(X)
+        cp(T.EL[:, c], T.N32[:, c], [("N32", X)], [("EL", X)], 128)
+        ts(T.E16[:, c], T.EL[:, c], -2048.0, None, A.add, None, [("EL", X)], [("E16", X)], 64)
+        o = P(BVS)[:, 16:24]
+        mm(group([(o, T.QW[:, 16 - s:144 - s], T.CB[:, 128 * X + s:128 * X + 128:16], 8) for s in range(16)]),
+           ["QW", ("CB", X)], [B(BVS)])
+        cp(T.QL[:, 8 * X:8 * X + 8], o, [], [B(BVS), ("QL", X)], 8)
+
+    ts(T.X32[:], P(BVW)[:, 0:256], 2048.0, None, A.add, None, [], [B(BVW), ("X32", 0), ("X32", 1)], 256)
+    unpack(0)
+    unpack(1)
+
+    def front(t, X):
+        c = slice(128 * X, 128 * X + 128)
+        q = T.QL[:, 8 * X:8 * X + 8]
+        gat("act", lambda: g.scalar.activation(T.RG[:, c], T.CD[:, 0:1024].indirect(q), ACT.Copy), CDt + [("QL", X)], [("RG", X)], 128)
+        o = P(BL2)
+        lst = [(o[:, 0:128], T.IB[:], T.CL[:], 128)]
+        for i in range(4):
+            lst.append((o[:, 64 * (i // 2):64 * (i // 2) + 64], T.SAB[:, 128 * i:128 * i + 128],
+                        T.RG[:, 128 * X + i % 2:128 * X + 128:2], 64))
+        mm(group(lst), ["IB", "CL", ("RG", X)] + [("SAB", i) for i in range(4)], [B(BL2)])
+        cp(T.LL[:, c], o[:, 0:128], [], [B(BL2), ("LL", X)], 128)
+        gat("act", lambda: g.scalar.activation(T.KG[:, c], T.KK[:, 0:1024].indirect(q), ACT.Copy), KKt + [("QL", X)], [("KG", X)], 128)
+        bank = S0
+        mm([(P(bank)[:, 0:128], T.IS[:], T.CS[:], 128, True, False)], ["IS", "CS"], [B(bank)])
+        for j in (2 * X, 2 * X + 1):
+            v0, e0 = 1024 * j, 64 * j
+            Vt, lo = [("LL", X)], 0
+            for i, (e, wd) in enumerate(SHARE[j]):
+                out, src = T.V[:, v0 + 16 * lo:v0 + 16 * (lo + wd)], T.H[:, 0:4096].indirect(T.EL[:, e0 + lo:e0 + lo + wd])
+                if e == "act":
+                    gat(e, lambda out=out, src=src: g.scalar.activation(out, src, ACT.Copy), Ht + [("EL", X)], [("V", j, i)], 16 * wd)
+                else:
+                    gat(e, lambda out=out, src=src: g.vector.tensor_copy(out, src), Ht + [("EL", X)], [("V", j, i)], 16 * wd)
+                Vt.append(("V", j, i))
+                lo += wd
+            la, ga = 128 * X + 32 * (j % 2), slice(512 * j, 512 * j + 512)
+            gat("act", lambda v0=v0, la=la, ga=ga: g.scalar.activation(
+                T.GA[:, ga], T.V[:, v0:v0 + 1024].indirect(T.LL[:, la:la + 32]), ACT.Copy), Vt, [("GA", j)], 512)
+            gat("dve", lambda v0=v0, la=la, ga=ga: g.vector.tensor_tensor(
+                T.GB[:, ga], T.V[:, v0:v0 + 1024].indirect(T.LL[:, la + 64:la + 96]), T.GA[:, ga], A.max),
+                Vt + [("GA", j)], [("GB", j)], 512)
+            o = P(bank)[:, 64 * (j % 2):64 * (j % 2) + 64]
+            mm(more([(o, T.IS[:], T.GB[:, 512 * j + k:512 * j + 512:8], 64) for k in range(8)], j % 2 == 1),
+               ["IS", ("GB", j)], [B(bank)])
+        w = T.WS[:, 256 * t + 128 * X:256 * t + 128 * X + 128]
+        ac(T.FB[:, c], P(bank)[:, 0:128], [], [B(bank), ("FB", X)], 128, bias=-127.5)
+        tt(w, P(bank)[:, 0:128], T.FB[:, c], A.subtract, [("FB", X)], [B(bank), ("WS", t, X)], 128)
+        gat("dve", lambda: g.vector.tensor_tensor(T.YS[:, c], T.ZT[:, 0:1024].indirect(q), w, A.is_le),
+            ZTt + [("QL", X), ("WS", t, X)], [("YS", X)], 128)
+        return c, w
+
+    def votes(t, X):
+        i = 2 * t + X
+        o = P(BVW)[:, 0:8]
+        mm(group([(o, T.VW[:, 32 - s:160 - s], T.YS[:, 128 * X + s:128 * X + 128:16], 8) for s in range(16)]),
+           ["VW", ("YS", X)], [B(BVW)])
+        mine = T.PV[:, 32 * i + 8 * me:32 * i + 8 * me + 8]
+        ac(mine, o, [], [B(BVW), ("PV", i, me)], 8)
+        tr = RemoteDMATransfer(dst_ids=[dst_id(peer(k)) for k in (1, 2, 3)], dma_engine_mask=full, remote_sem=T.sem["v%d" % i],
+                               srcs=[mine], dsts=[mine, mine, mine])
+        sd = op("pool", lambda: g.remote_dma_fused([tr], local_sem=T.sem.sent), [("PV", i, me)], [], 0.5, kind="send", inc=ne, kb=12)
+        recv(sd, "v%d" % i, 3 * ne, [("PV", i, peer(k)) for k in (1, 2, 3)])
+
+    def update(t, X, c, w):
+        ts(T.MK[:, c], w, 128.0, -256.0, A.is_lt, A.mult, [("WS", t, X)], [("MK", X)], 64)
+        for hb, (bank, rs) in enumerate(((R0, (0, 1, 2, 3)),) if X == 0 else ((R1, (0, 1)), (S1, (2, 3)))):
+            early, late, wd = [], [], 128 * len(rs)
+            for i, r in enumerate(rs):
+                o, m = P(bank)[:, 128 * i:128 * i + 128], slice(128 * r, 128 * r + 128)
+                early += [(o, T.RE[:, m], T.E16[:, c], 128), (o, T.RK[:, m], T.KG[:, c], 128)]
+                late += [(o, T.RW[:, m], w, 128), (o, T.RW[:, m], T.MK[:, c], 128)]
+            early = [(P(bank)[:, 0:wd], T.K64[0:1, 0:128], T.K64[0:1, 0:wd], wd, True, False)] + more(early)
+            late = more(late, True)
+            for x in range(0, len(late), 4):
+                mm(early[:5] if x == 0 else early[x + 1:x + 5],
+                   ["K64", ("E16", X), ("KG", X)] + [(n, r) for n in ("RE", "RK") for r in range(4)], [B(bank)])
+            for x in range(0, len(late), 4):
+                mm(late[x:x + 4], [("WS", t, X), ("MK", X)] + [("RW", r) for r in range(4)], [B(bank)])
+            for i, r in enumerate(rs):
+                h0 = 1024 * r + 256 * (t % 4) + 128 * X
+                o, i_ = T.H[:, h0:h0 + 128], P(bank)[:, 128 * i:128 * i + 128]
+                wr = [B(bank), ("H", r, 2 * (t % 4) + X)]
+                if hb == 1:
+                    ts(o, i_, -2048.0, None, A.add, None, [], wr, 128)
+                else:
+                    ac(o, i_, [], wr, 128, bias=-2048.0)
+
+    def bound(t, X, c):
+        o = P(BEB)[:, 0:128]
+        mm(group([(o, T.IB[:], T.IT[:], 128), (o, T.SH[:], T.E16[:, c], 128), (o, T.KID[:], T.KG[:, c], 128)]),
+           ["IB", "IT", "SH", "KID", ("E16", X), ("KG", X)], [B(BEB)])
+        b = 2 * (t % 4) + X
+        ac(T.GA[:, 1024 * X + 1:1024 * X + 1024:8], o, ["BC"], [B(BEB), ("GA", 2 * X), ("GA", 2 * X + 1), ("EB", X)], 128,
+           bias=T.BC[:, b:b + 1])
+
+    def choose(t, X, c):
+        i = 2 * t + X
+        o = P(BVS)[:, 0:8]
+        mm(group([(o, T.IB[:], T.C8[:], 8)] + [(o, T.I128[:], T.PV[:, 32 * i + 8 * r:32 * i + 8 * r + 8], 8) for r in range(4)]),
+           ["IB", "C8", "I128"] + [("PV", i, r) for r in range(4)], [B(BVS)])
+        bl = T.BL[:, 8 * X:8 * X + 8]
+        ts(bl, o, 1.0 / 512, None, A.add, None, [], [B(BVS), ("BL", X)], 8)
+        gat("dve", lambda: g.vector.tensor_copy(T.X32[:, c], T.GA[:, 1024 * X:1024 * X + 1024].indirect(bl)),
+            [("GA", 2 * X), ("GA", 2 * X + 1), ("BL", X)], [("X32", X)], 128)
+        unpack(X)
+
+    for t in range(S - 1):
+        cw = []
+        role[2] = t
+        for X in range(2):
+            role[0], role[1] = X, 0
+            cw.append(front(t, X))
+            votes(t, X)
+            bound(t, X, cw[X][0])
+        role[0], role[1] = 2, 0
+        update(t, 0, *cw[0])
+        choose(t, 0, cw[0][0])
+        update(t, 1, *cw[1])
+        choose(t, 1, cw[1][0])
+
+    role[0], role[2] = None, S - 1
+    Wt = [("WS", t, X) for t in range(S - 1) for X in range(2)]
+    dma("sp", T.DW[:], T.WS[:, 0:1280], Wt, ["DW"], 320)
+    dma("sp", T.yx[32 * me:32 * me + 32, 0:1280], T.WS[32 * me:32 * me + 32, 0:1280], Wt, [], 80)
+    fan(lambda r: T.DW[r], T.DL[me], "ay", ["DW"], 240)
+    for k in (1, 2, 3):
+        s = peer(k)
+        dma("sp", T.yx[32 * s:32 * s + 32, 0:1280], T.DL[s], ["ay"], [], 80)
+
+    t = S - 1
+    mm([zero(BVW, 512)], ["ZR"], [B(BVW)])
+    mm([zero(R0, 512), zero(R1, 512)], ["ZR"], [B(R0), B(R1)])
+
+    def spread(bank, x, M, D, X, d0=0):
+        return [(P(bank)[:, 128 * r + x:128 * r + x + 64], M[:, 128 * r + 3 - u:128 * r + 131 - u],
+                 D[:, d0 + 64 * u:d0 + 64 * u + 64], 64) for r in range(4) for u in (2 * X, 2 * X + 1)]
+
+    for X in range(2):
+        role[0], role[1] = X, 0
+        c, w = front(t, X)
+        role[0] = None
+        o = P(BEB)[:, 0:128]
+        mm(group([(o, T.IB[:], T.IT[:], 128), (o, T.SH[:], T.E16[:, c], 128)]), ["IB", "IT", "SH", ("E16", X)], [B(BEB)])
+        ts(T.EB16[:, c], o, T.BC2[:, X:X + 1], None, A.add, None, ["BC2"], [B(BEB), ("EB16", X)], 128)
+        mm(more(spread(BVW, 0, T.YH, T.EB16, X) + spread(BVW, 64, T.YK, T.KG, X), X == 1),
+           ["YH", "YK", ("EB16", X), ("KG", X)], [B(BVW)])
+        cp(T.X32[:, c], T.GA[:, 1024 * X:1024 * X + 1024:8], [("GA", 2 * X), ("GA", 2 * X + 1)], [("X32", X)], 128)
+        pieces_of(X)
+        ts(T.EA16[:, c], T.N32[:, c], -2048.0, None, A.add, None, [("N32", X)], [("EA16", X)], 128)
+        mm(more(spread(R0, 0, T.YH, T.EA16, X)), ["YH", ("EA16", X)], [B(R0)])
+        mm(more(spread(R0, 64, T.YC, T.CB, X), X == 1), ["YC", ("CB", X)], [B(R0)])
+        mm(more(spread(R1, 0, T.YB, T.WS, X, 1280)), ["YB", ("WS", t, X)], [B(R1)])
+        mm(more(spread(R1, 64, T.YV, T.YS, X), X == 1), ["YV", ("YS", X)], [B(R1)])
+    mine = slice(128 * me, 128 * me + 128)
+    cp(T.MF[:], P(BVW)[:], [], [B(BVW), "MF"], 512)
+    fan(lambda r: T.MF[:, 128 * r:128 * r + 128], T.LF[:, mine], "af", ["MF"], 96)
+    cp(T.MG[:], P(R0)[:], [], [B(R0), "MG"], 512)
+    fan(lambda r: T.MG[:, 128 * r:128 * r + 128], T.LG[:, mine], "ag", ["MG"], 96)
+    ac(T.MH[:], P(R1)[:], [], [B(R1), "MH"], 512)
+    fan(lambda r: T.MH[:, 128 * r:128 * r + 128], T.LH[:, mine], "ah", ["MH"], 96)
+    Ft, Gt, Wt = ["af", "MF"], ["ag", "MG"], ["ah", "MH"]
+
+    def got(M, L, s, a):
+        return (M if s == me else L)[:, 128 * s + a:128 * s + a + 64]
+
+    for s in range(4):
+        ts(T.EA2[:, 64 * s:64 * s + 64], got(T.MF, T.LF, s, 0), 2048.0, None, A.add, None, Ft, [("EA2", s)], 64)
+    o = P(BEB)[:, 0:64]
+    mm(group([(o, T.IH[:], got(T.MF, T.LF, s, 64), 64) for s in range(4)]), ["IH"] + Ft, [B(BEB)])
+    ac(T.EA2[:, 256:320], o, [], [B(BEB), ("EA2", 4)], 64)
+    lst = []
+    for s in range(4):
+        o = P(BL2)[:, 64 * s:64 * s + 64]
+        lst += group([(o, T.NH[:], got(T.MF, T.LF, s, 0), 64), (o, T.IH[:], got(T.MG, T.LG, s, 0), 64)])
+    o = P(BL2)[:, 256:320]
+    lst += group([(o, M, got(a, b, s, 64), 64) for s in range(4) for M, a, b in ((T.NH[:], T.MF, T.LF), (T.IH[:], T.MG, T.LG))])
+    mm(lst, ["IH", "NH"] + Ft + Gt, [B(BL2)])
+    o = P(BVS)[:, 0:64]
+    mm(group([(o, T.SV[:], got(T.MH, T.LH, s, 64), 64) for s in range(4)]), ["SV"] + Wt, [B(BVS)])
+    ts(T.BB[:], o, 64.0, None, A.is_lt, None, [], [B(BVS), "BB"], 64)
+    for s in range(4):
+        dma(("act", "sp")[s % 2], T.yx[32 * s:32 * s + 32, 1280:1536], got(T.MH, T.LH, s, 0), Wt, [], 16)
+    for s in range(5):
+        c = slice(64 * s, 64 * s + 64)
+        tt(T.OM[:, c], P(BL2)[:, c], T.BB[:], A.mult, ["BB"], [B(BL2), ("OM", s)], 64)
+        tt(T.OUT[:, c], T.OM[:, c], T.EA2[:, c], A.add, [("OM", s), ("EA2", s)], [("OUT", s)], 128)
+        if s < 4:
+            dma(("sp", "act")[s % 2], T.ye[32 * s:32 * s + 32, :], T.OUT[:, c], [("OUT", s)], [], 32)
+        else:
+            dma("sp", T.yc[:], T.OUT[0:32, c], [("OUT", s)], [], 8)
+    return ops
+
+
+def arrange(ops):
+    lastw, readers = {}, {}
+    n = len(ops)
+    for i, o in enumerate(ops):
+        raw, other = set(), set()
+        for k in o["rd"]:
+            if k in lastw:
+                raw.add(lastw[k])
+        for k in o["wr"]:
+            if k in lastw:
+                other.add(lastw[k])
+            other.update(readers.get(k, ()))
+        for k in o["rd"]:
+            readers.setdefault(k, []).append(i)
+        for k in o["wr"]:
+            lastw[k] = i
+            readers[k] = []
+        o["raw"], o["dep"] = raw, (raw | other) - {i}
+        if o["kind"] == "recv":
+            o["dep"] = o["dep"] | {o["after"]}
+    if "t0" not in PLAN:
+        PLAN["end"], PLAN["t0"] = search(ops)
+    for i in range(n):
+        ops[i]["t0"] = PLAN["t0"][i]
+    return sorted(range(n), key=lambda i: (ops[i]["t0"], i)), PLAN["end"]
+
+
+def search(ops):
+    n = len(ops)
+
+    def gap(i, d):
+        p = ops[d]
+        if p["eng"] == ops[i]["eng"] and p["kind"] == "c" and ops[i]["kind"] == "c" and d not in ops[i]["raw"]:
+            return p["dur"] + 0.001
+        return p["dur"] + p["lat"] + HOP
+
+    pre = [[(d, gap(i, d)) for d in sorted(ops[i]["dep"])] for i in range(n)]
+    dur = [o["dur"] for o in ops]
+    eng = [o["eng"] for o in ops]
+    prio = [o["dur"] + o["lat"] for o in ops]
+    for i in range(n - 1, -1, -1):
+        for d, x in pre[i]:
+            prio[d] = max(prio[d], prio[i] + x)
+    cases = []
+    for cs in CASES:
+        du = [o["dur"] * (cs[o.get("cls", 2 if o["eng"] == "pe" else 1)] if o["kind"] == "c" else 1.0) for o in ops]
+        cases.append((du, [[(d, x - dur[d] + du[d] + (cs[3] if ops[d]["kind"] == "recv" else 0.0)) for d, x in pre[i]]
+                           for i in range(n)]))
+
+    def place(key):
+        for i in range(n - 1, -1, -1):
+            for d, _ in pre[i]:
+                if key[d] > key[i]:
+                    key[d] = key[i]
+        busy, t0 = {}, [0.0] * n
+        for i in sorted(range(n), key=lambda j: (key[j], j)):
+            s = max([t0[d] + x for d, x in pre[i]], default=0.0)
+            row = busy.setdefault(eng[i], [])
+            k = len(row)
+            while k > 0 and row[k - 1][1] > s:
+                k -= 1
+            while k < len(row) and row[k][0] < s + dur[i] - 1e-9:
+                s = max(s, row[k][1])
+                k += 1
+            row.insert(k, (s, s + dur[i]))
+            t0[i] = s
+        seq = sorted(range(n), key=lambda j: (t0[j], j))
+        total = 0.0
+        for du, pr in cases:
+            free, t1, last = {}, [0.0] * n, 0.0
+            for i in seq:
+                s = free.get(eng[i], 0.0)
+                for d, x in pr[i]:
+                    if t1[d] + x > s:
+                        s = t1[d] + x
+                t1[i] = s
+                free[eng[i]] = s + du[i]
+                last = max(last, s + du[i] + ops[i]["lat"])
+            total += last
+        return total / len(cases), t0
+
+    state = [SEED]
+
+    def rnd():
+        state[0] = (state[0] * 6364136223846793005 + 1442695040888963407) % 2 ** 64
+        return (state[0] >> 11) / 2.0 ** 53
+
+    names = sorted(set(o["role"] for o in ops), key=str)
+    place_of = {x: i for i, x in enumerate(names)}
+    rid = [place_of[o["role"]] for o in ops]
+    pools = ([i for i, x in enumerate(names) if x[0] != "once"], [i for i, x in enumerate(names) if x[0] == "once"])
+    top = max(prio)
+    base = [top - p for p in prio]
+    first = min(base[i] for i in range(n) if ops[i]["wr"] and ops[i]["wr"][-1][0] == "V" and ops[i]["role"][0] != "once")
+    for i, o in enumerate(ops):
+        if o["role"][0] != "once":
+            k = o["wr"][-1] if o["wr"] else o["rd"][0]
+            k = (k[0], k[1] % 2 if k[0] == "PV" else k[2] % 2 if k[0] == "H" else k[2] if k[0] == "WS" else k[1], o["eng"])
+            base[i] = first + PERIOD * o["step"] + AIM.get(k, 99.0)
+        elif o["step"]:
+            base[i] += first + PERIOD * S - top + 8.0
+
+    def queue_links(t0):
+        prev, last = {}, {}
+        for i in sorted(range(n), key=lambda j: (t0[j], j)):
+            prev[i] = last.get(eng[i])
+            last[eng[i]] = i
+        i, out = max(range(n), key=lambda j: t0[j] + dur[j] + ops[j]["lat"]), []
+        while True:
+            s, d = max([(t0[d] + x, d) for d, x in pre[i]], default=(0.0, None))
+            if prev[i] is not None and t0[i] > s + 1e-6:
+                out.append((prev[i], i))
+                i = prev[i]
+            elif d is None:
+                return out
+            else:
+                i = d
+
+    end, t0 = place(base)
+    links = queue_links(t0)
+    best, off = (end, t0), [0.0] * len(names)
+    for it in range(ROUNDS):
+        if it % 400 == 399:
+            base, off = list(t0), [0.0] * len(names)
+        o2 = list(off)
+        if links and rnd() < 0.6:
+            a, b = links[int(rnd() * len(links))]
+            x = t0[b] - t0[a] + 0.05 + rnd() * rnd() * 2.0
+            if rnd() < 0.5:
+                o2[rid[b]] -= x
+            else:
+                o2[rid[a]] += x
+        else:
+            pool = pools[0] if rnd() < 0.7 else pools[1]
+            amp = (0.6, 2.0, 6.0)[int(rnd() * 3)]
+            for _ in range(1 + int(rnd() * 3)):
+                o2[pool[int(rnd() * len(pool))]] += amp * (rnd() + rnd() - 1.0)
+        e2, t2 = place([base[i] + o2[rid[i]] for i in range(n)])
+        if e2 <= end + 2.0 * HEAT * (1.0 - it / ROUNDS) * rnd():
+            end, off, t0 = e2, o2, t2
+            links = queue_links(t0)
+            if e2 < best[0]:
+                best = (e2, t2)
+    return best
+
+
+def emit(g, T, ops, seq):
+    queue = {"pe": g.tensor, "act": g.scalar, "dve": g.vector, "pool": g, "sp": g.sync}
+    count, known, total, waited = {}, {e: {} for e in queue}, {}, {}
+    ndma, sent = 0, 0
+    for i in seq:
+        o = ops[i]
+        if o["kind"] == "recv":
+            o["mark"], o["clock"] = (o["sem"], o["cnt"]), {}
+            total[o["sem"]] = o["cnt"]
+            continue
+        e, kn = o["eng"], known[o["eng"]]
+        need = {}
+        for d in o["dep"]:
+            p = ops[d]
+            if p["kind"] == "c" and o["kind"] == "c" and p["eng"] == e and d not in o["raw"]:
+                continue
+            s, n = p["mark"]
+            if need.get(s, (0, None))[0] < n:
+                need[s] = (n, p)
+        for s, (n, p) in sorted(need.items(), key=lambda x: -x[1][1]["t0"]):
+            if kn.get(s, 0) >= n:
+                continue
+            queue[e].wait_ge(T.sem[s], n)
+            waited[s] = max(waited.get(s, 0), n)
+            kn[s] = n
+            for s2, n2 in p["clock"].items():
+                kn[s2] = max(kn.get(s2, 0), n2)
+        ins = o["fn"]()
+        o["clock"] = dict(kn)
+        if o["kind"] == "c":
+            count[e] = count.get(e, 0) + 1
+            ins.then_inc(T.sem[e], 1)
+            o["mark"] = (e, count[e])
+            total[e] = count[e]
+        elif o["kind"] == "dma":
+            s = "d%d" % ndma
+            ndma += 1
+            ins.then_inc(T.sem[s], 16)
+            o["mark"] = (s, 16)
+            total[s] = 16
+        else:
+            sent += o["inc"]
+    total["sent"] = sent
+    for s, n in total.items():
+        if waited.get(s, 0) < n:
+            g.wait_ge(T.sem[s], n)
+
+
+def rank_program(g, core, T, topo):
+    me = T.rank_of(core)
+    if me is None:
+        return
+    ops = build_ops(g, T, topo, core, me)
+    seq, _ = arrange(ops)
+    emit(g, T, ops, seq)

@@ -3,8 +3,14 @@ from concourse.mybir import AluOpType, AxisListType, ActivationFunctionType
 
 N, S = 4, 6
 F32, BF, F16, I32, U16 = "float32", "bfloat16", "float16", "int32", "uint16"
-W1, W2 = 896, 512
-SHARE = ((("act", 40), ("dve", 24)),) * 4
+REP = 2
+HB = 17408.0
+ENV = "u16"
+EARLY = False
+AF16 = True
+OWN = (0, 2, 3)
+VOWN = (0, 1)
+KT = [(1, m) for m in range(5)] + [(0, m) for m in (0, 1, 2)] + [(2, m) for m in range(5)] + [(0, m) for m in (3, 4, 6)]
 
 
 def _sb(cols, dtype):
@@ -12,53 +18,72 @@ def _sb(cols, dtype):
 
 
 SCRATCH = {
-    "LX": _sb(1024, BF), "LCE": _sb(1024, I32), "LCD": _sb(1024, I32), "LE": _sb(256, I32), "CT": _sb(832, I32),
-    "SG": _sb(1024, BF), "CF": _sb(832, F16), "FP": _sb(832, F16), "FF": _sb(832, F16),
-    "M1": _sb(4 * W1, F16), "L1": _sb(4 * W1, F16), "M2": _sb(4 * W2, BF), "L2": _sb(4 * W2, BF),
-    "H": _sb(4096, F32), "CD": _sb(1024, BF), "ZT": _sb(1024, BF), "KK": _sb(1024, BF),
-    "V": _sb(4096, F32), "GA": _sb(2048, F32), "GB": _sb(2048, BF),
-    "EL": _sb(256, U16), "E16": _sb(256, F16), "QL": _sb(16, U16), "RG": _sb(256, BF), "KG": _sb(256, BF),
-    "LL": _sb(256, U16), "FB": _sb(256, BF), "WS": _sb(1536, BF), "MK": _sb(256, BF), "YS": _sb(256, BF),
-    "PV": _sb(320, BF), "BL": _sb(16, U16), "X32": _sb(256, I32), "N32": _sb(256, I32), "C32": _sb(256, I32),
-    "CB": _sb(256, BF), "EB16": _sb(256, F16), "EA16": _sb(256, F16),
-    "MF": _sb(512, F16), "LF": _sb(512, F16), "MG": _sb(512, F16), "LG": _sb(512, F16), "MH": _sb(512, BF), "LH": _sb(512, BF),
-    "EA2": _sb(320, F32), "OM": _sb(320, F32), "OUT": _sb(320, F32), "BB": _sb(64, F32),
-    "XF": _sb(160, F32), "XL": _sb(516, F32), "PI": _sb(1, I32), "PJ": _sb(8, I32), "PC": _sb(32, F32), "TA": _sb(8, F32),
-    "TB": _sb(8, F32), "V1": _sb(128, BF), "V2": _sb(128, BF), "V3": _sb(128, BF), "V5": _sb(224, BF), "VA": _sb(512, BF),
-    "VWv": _sb(160, F32), "VY": _sb(516, BF), "VV": _sb(128, BF), "SV": _sb(128, BF), "CLv": _sb(128, BF),
-    "IB": _sb(128, BF), "IS": _sb(128, BF), "I128": _sb(128, BF), "I8": _sb(128, BF), "I1K": _sb(128, BF), "IH": _sb(128, F16),
-    "NH": _sb(128, F16), "PA": _sb(532, F16), "PA1": _sb(512, F16), "PA2": _sb(512, F16), "PB": _sb(532, F16),
-    "RE": _sb(512, F16), "RW": _sb(512, BF), "RK": _sb(512, BF), "RA": _sb(512, F16), "RB": _sb(512, F16), "ZW": _sb(896, F16),
-    "SH": _sb(128, F16), "KID": _sb(128, BF), "SAB": _sb(512, BF), "CL": _sb(128, BF), "C8": _sb(8, BF), "IT": _sb(128, BF),
-    "BC": _sb(8, F32), "BC2": _sb(2, F32), "VW": _sb(160, BF), "QW": _sb(144, BF), "YH": _sb(516, F16), "YB": _sb(516, BF),
-    "YC": _sb(516, BF), "YK": _sb(516, BF), "YV": _sb(516, BF), "CS": _sb(128, BF), "ZR": _sb(512, BF), "K64": _sb(512, BF),
+    "HV": _sb(9216, BF), "HE": _sb(9472, F32), "W5": _sb(256, BF),
+    "LCD": _sb(1024, I32), "LCE": _sb(1024, I32), "LE": _sb(256, I32), "CT": _sb(1024, I32), "C0": _sb(256, I32),
+    "U": _sb(1024, BF), "U2": _sb(1024, BF), "CF": _sb(1024, F16), "C16": _sb(256, F16), "FF": _sb(1024, BF),
+    "N16": _sb(1280, F16), "MU": _sb(1024, U16), "LU": _sb(4096, U16),
+    "TB0": _sb(2048, BF), "TB1": _sb(2048, BF), "TB2": _sb(2048, BF), "ZT": _sb(2048, BF), "IDX": _sb(2048, F32),
+    "ER": _sb(256 * REP, F32), "G0": _sb(256, BF), "G1": _sb(256, BF), "HK": _sb(512, BF), "GZ": _sb(256, BF),
+    "E16": _sb(256, F16), "WR": _sb(256, F16), "F1": _sb(1280, BF), "F2": _sb(1280, BF), "VR": _sb(32, BF),
+    "Q0L": _sb(16, U16), "U0": _sb(512, BF), "GF": _sb(768, BF), "BX": _sb(8, BF), "DG": _sb(128, BF), "M16": _sb(16, BF), "O16": _sb(16, BF),
+    "Y": _sb(4096, F16), "TL": _sb(256, U16), "T16": _sb(128, F16), "T0L": _sb(16, U16),
+    "HI": _sb(32, F32), "LO": _sb(32, F16 if AF16 else F32), "Z1": _sb(32, F32), "Z2": _sb(32, F32), "Z16": _sb(32, U16),
+    "GA": _sb(2048, BF), "GB": _sb(2048, BF), "FB": _sb(256, BF), "YS": _sb(512, BF),
+    "OE": _sb(256, F32), "OUT": _sb(256, F32), "YC": _sb(256, F32),
+    "PI": _sb(1, I32), "PJ": _sb(8, I32), "PC": _sb(48, F32), "XF": _sb(176, BF), "V1": _sb(128, BF), "JP": _sb(128, BF),
+    "BG": _sb(128, BF), "VA": _sb(384, BF), "V2": _sb(128, BF), "VQ": _sb(144, BF), "TA": _sb(8, F32), "SEL": _sb(8, F32),
+    "Q": _sb(384, BF), "PEN": _sb(896, BF), "SW": _sb(144, F16), "CWL": _sb(144, BF), "QW": _sb(144, F16), "VW": _sb(144, BF),
+    "Q0": _sb(144, F16), "AW": _sb(3 * 144, BF), "CR": _sb(3 * 144, BF), "PA": _sb(384, BF), "PA0": _sb(384, BF),
+    "PA1": _sb(384, BF), "PB": _sb(384, F16), "RE": _sb(128, F16), "IB": _sb(128, BF), "ID": _sb(640, BF), "IH": _sb(128, F16),
+    "IS": _sb(128, F16), "SH": _sb(128, F16), "KY": _sb(128, BF), "IT": _sb(128, BF), "BC": _sb(8, F32), "CK": _sb(256, BF),
     "SF": _sb(1, F32),
-    "DW": ("dram", [4, 128, 320], BF), "DL": ("dram", [4, 128, 320], BF),
 }
 for _b in range(8):
     SCRATCH["P%d" % _b] = ("psum", [128, 512], F32)
-NDMA = 56
+NDMA = 40
 SEMAPHORES = (["pe", "act", "dve", "pool", "sent"] + ["d%d" % i for i in range(NDMA)]
-              + ["a%d_%d" % (j, k) for j in (0, 1, 2) for k in (1, 2, 3)] + ["v%d" % i for i in range(10)]
-              + ["ay", "af", "ag", "ah"])
+              + ["%s%d" % (x, i) for x in ("w", "e", "h") for i in range(10)] + ["%s%d" % (x, i) for x in ("u", "hu", "v", "hv") for i in range(4)])
 
-R0, R1, S0, S1, BL2, BEB, BVW, BVS = range(8)
-CYC, GAT, PEC, HOP, LAT, RATE = 1.0e-3, 1.45e-3, 0.5e-3, 0.09, 2.7, 80.0
-CASES = ((1.0, 1.0, 1.0, 0.0), (0.75, 0.9, 0.9, 0.7), (1.2, 1.1, 1.2, -0.6))
-ROUNDS, HEAT, SEED, PLAN = 12000, 0.15, 1, {}
-PERIOD = 11.5
-AIM = {("V", 0, "act"): 0.0, ("V", 0, "dve"): 0.0, ("V", 1, "dve"): 0.4, ("V", 1, "act"): 1.0, ("GA", 0, "act"): 1.2,
-       ("GA", 1, "act"): 2.0, ("GB", 0, "dve"): 2.0, ("GB", 1, "dve"): 3.9, ("FB", 0, "act"): 5.1, ("WS", 0, "dve"): 5.4,
-       ("YS", 0, "dve"): 5.6, ("PV", 0, "act"): 6.4, ("PV", 0, "pool"): 6.5, ("PV", 0, "link"): 7.0, ("MK", 0, "dve"): 8.8,
-       ("H", 0, "act"): 8.5, ("BL", 0, "dve"): 10.2, ("X32", 0, "dve"): 10.4, ("C32", 0, "dve"): 10.9, ("CB", 0, "dve"): 11.0,
-       ("N32", 0, "dve"): 10.6, ("EL", 0, "dve"): 10.8, ("QL", 0, "dve"): 11.9, ("E16", 0, "dve"): 13.0,
-       ("RG", 0, "act"): 0.9, ("LL", 0, "dve"): 1.3, ("KG", 0, "act"): 2.9,
-       ("BL", 1, "dve"): 14.3, ("X32", 1, "dve"): 14.4, ("N32", 1, "dve"): 14.6, ("EL", 1, "dve"): 14.8, ("C32", 1, "dve"): 15.0,
-       ("CB", 1, "dve"): 15.1, ("QL", 1, "dve"): 16.2, ("E16", 1, "dve"): 17.5, ("V", 2, "act"): 3.7, ("V", 2, "dve"): 4.8,
-       ("V", 3, "dve"): 5.0, ("V", 3, "act"): 6.6, ("RG", 1, "act"): 5.0, ("LL", 1, "dve"): 5.7, ("GA", 2, "act"): 5.8,
-       ("GA", 3, "act"): 7.0, ("KG", 1, "act"): 7.9, ("GB", 2, "dve"): 6.7, ("GB", 3, "dve"): 7.9, ("FB", 1, "act"): 9.1,
-       ("WS", 1, "dve"): 9.4, ("MK", 1, "dve"): 9.6, ("YS", 1, "dve"): 9.7, ("PV", 1, "act"): 10.5, ("PV", 1, "pool"): 10.6,
-       ("PV", 1, "link"): 11.0, ("H", 1, "act"): 10.2, ("H", 1, "dve"): 10.5, ("EB", 0, "act"): 8.4, ("EB", 1, "act"): 12.9}
+CYC, GAT, PEC, HOP, LAT, RATE, LOCAL = 1.0e-3, 1.45e-3, 0.5e-3, 0.09, 2.7, 80.0, 250.0
+CASES = ((1.0, 1.0, 1.0, 0.0), (0.75, 0.9, 0.9, 0.7), (1.2, 1.1, 1.2, -0.3))
+ROUNDS, HEAT, SEED, PLAN = 10000, 0.1, 1, {}
+PERIOD, FIRST = 10.8, 15.5
+START = {"x01": 0.0, "codes": 0.1, "x23": 0.2, "ce0": 0.3, "ce1": 0.4, "cd": 0.5, "e": 0.6, "z": 6.0, "send": 0.0, "iota": 0.0,
+         "idx": 12.0, "early": 0.1, "cols": 2.7, "mats": 6.3, "late": 12.0, "q0": 6.0, "cf": 3.0, "env0": 4.5, "env1": 5.6,
+         "fast": 8.0, "e16": 8.2, "u": 13.3, "tb": 16.0, "conv": 17.0, "g0": 17.0}
+
+
+def _mins(a):
+    return [a + 0.6 * i + x for i in range(4) for x in [-0.5] + [0.3 * y * REP / 2 for y in range(4 // REP)] + [0.7]] + [a + 2.8]
+
+
+AIM = {("V", 0): [-1.0, 0.0, 0.9, 1.7, 0.8, 1.8, 2.5, 2.9, 3.3, 3.4, 3.5, 3.5, 3.7],
+       ("V", 1): [0.0, 2.0, 2.9, 3.4, 2.95, 3.6, 4.4, 4.7, 4.9, 5.0, 5.1, 5.2, 5.4],
+       ("C", 0): [3.9, 4.0, 4.1, 4.45, 4.5, 4.6, 4.95], ("C", 1): [5.6, 5.7, 5.8, 6.6, 6.9, 7.2, 7.5],
+       ("T", 0): [4.7, 5.0, 5.6, 7.0], ("T", 1): [7.3, 7.5, 7.9, 8.4], ("W", 0): [5.2], ("W", 1): [7.8],
+       ("W2", 0): [5.3, 5.35], ("W2", 1): [7.9, 8.0], ("T1", 0): _mins(5.9), ("T1", 1): _mins(8.9)[:-1] + [12.55],
+       ("R", 0): [-4.0], ("R", 1): [-2.0], ("O", 0): [-0.9, -0.8, -0.3, 1.6, 1.6, 1.9, 2.8],
+       ("O", 1): [2.6, 2.7, 3.5, 3.8, 3.8, 4.6], ("E", 0): [1.9, 2.8], ("E", 1): [5.0],
+       ("D", 0): [6.0], ("D", 1): [7.0]}
+
+
+def helper_of(core, topo):
+    return [c for c in topo.cores_of(core) if topo.die(c) != topo.die(core)][0]
+
+
+def dst_id(topo, c):
+    rid, pid, _ = topo.addr(c)
+    return DstId(rid=rid, pnc=pid)
+
+
+def env_at(T, t, r, X):
+    c = 4352 + 1024 * t + 256 * r + 128 * X
+    return T.HE[:, c:c + 128], ("HE", c // 128)
+
+
+def inner_engines(topo, core, far):
+    out = topo.engines(core, far)
+    return [e for e in topo.engines(core, helper_of(core, topo)) if e not in out]
 
 
 def build_ops(g, T, topo, core, me):
@@ -66,9 +91,23 @@ def build_ops(g, T, topo, core, me):
     ops = []
     role = [None, 0, 0]
 
+    now = [0.0]
+
+    def when(name):
+        now[0] = START[name]
+
+    def part(name):
+        role[0], role[1] = name, 0
+
     def op(eng, fn, rd, wr, dur, lat=0.0, kind="c", **kw):
         kw["role"] = ("once", len(ops)) if role[0] is None else (role[0], role[1])
         kw["step"] = role[2]
+        if role[0] is not None:
+            a = AIM[role[0]]
+            kw["aim"] = a[min(role[1], len(a) - 1)] + 0.001 * role[1]
+        else:
+            kw["at"] = now[0]
+            now[0] += 0.002
         role[1] += 1
         ops.append(dict(eng=eng, fn=fn, rd=list(rd), wr=list(wr), dur=dur, lat=lat, kind=kind, **kw))
         return len(ops) - 1
@@ -90,31 +129,37 @@ def build_ops(g, T, topo, core, me):
     def ms(ap, v, wr, n):
         return dv(lambda: g.vector.memset(ap, v), [], wr, n)
 
-    def ac(out, in_, rd, wr, n, bias=None, func=None):
-        f = ACT.Identity if func is None else func
-        if bias is None:
-            return op("act", lambda: g.scalar.activation(out, in_, ACT.Copy), rd, wr, 0.06 + n * CYC)
-        return op("act", lambda: g.scalar.activation(out, in_, f, bias=bias), rd, wr, 0.06 + n * CYC)
+    def ac(out, in_, rd, wr, n, bias=None, scale=None, func=None):
+        kw = {}
+        if bias is not None:
+            kw["bias"] = bias
+        if scale is not None:
+            kw["scale"] = scale
+        f = func if func is not None else (ACT.Identity if kw else ACT.Copy)
+        return op("act", lambda: g.scalar.activation(out, in_, f, **kw), rd, wr, 0.06 + n * CYC)
 
-    def gat(eng, fn, rd, wr, n):
-        return op(eng, fn, rd, wr, 0.06 + n * GAT, cls=0)
+    def ag(out, src, rd, wr, n):
+        return op("act", lambda: g.scalar.activation(out, src, ACT.Copy), rd, wr, 0.06 + n * GAT, cls=0)
 
-    def mm(lst, rd, wr):
+    def dg(out, src, in1, o, rd, wr, n):
+        return op("dve", lambda: g.vector.tensor_tensor(out, src, in1, o), rd, wr, 0.06 + n * GAT, cls=0)
+
+    def mm(lst, rd, wr, start=True, stop=True):
         def fn():
             last = None
-            for o, l, r, n, st, sp in lst:
-                last = g.tensor.matmul(o, l, r, st, sp)
+            for i, (o, l, r, n) in enumerate(lst):
+                last = g.tensor.matmul(o, l, r, start and i == 0, stop and i == len(lst) - 1)
             return last
         return op("pe", fn, rd, wr, 0.05 + sum(max(64, x[3]) for x in lst) * PEC)
 
-    def group(items):
-        return [(o, l, r, n, i == 0, i == len(items) - 1) for i, (o, l, r, n) in enumerate(items)]
-
-    def more(items, stop=False):
-        return [(o, l, r, n, False, stop and i == len(items) - 1) for i, (o, l, r, n) in enumerate(items)]
-
-    def zero(bank, n):
-        return (P(bank)[:, 0:n], T.ZR[0:1, 0:128], T.ZR[0:1, 0:n], n, True, False)
+    def mms(groups, rd, wr):
+        def fn():
+            last = None
+            for lst in groups:
+                for i, (o, l, r, n) in enumerate(lst):
+                    last = g.tensor.matmul(o, l, r, i == 0, i == len(lst) - 1)
+            return last
+        return op("pe", fn, rd, wr, 0.05 + sum(max(64, x[3]) for lst in groups for x in lst) * PEC)
 
     def io(out, pat, base, cm, wr, n, flag=True):
         if flag:
@@ -123,7 +168,8 @@ def build_ops(g, T, topo, core, me):
 
     def dma(q, out, in_, rd, wr, kb):
         e = g.sync if q == "sp" else g.scalar
-        return op(q, lambda: e.dma_start(out, in_), rd, wr, 0.1, lat=2.0 + kb / 200.0, kind="dma")
+        i = op(q, lambda: e.dma_start(out, in_), rd, wr, 0.1, kind="dma")
+        return op("ring", None, [], wr, 0.01 + kb / LOCAL, lat=1.9, kind="land", after=i)
 
     def P(b):
         return T["P%d" % b]
@@ -131,423 +177,504 @@ def build_ops(g, T, topo, core, me):
     def B(b):
         return ("B", b)
 
-    def peer(k):
-        return (me + k) % N
+    peers = [(me + k) % N for k in (1, 2, 3)]
+    out_e = topo.engines(core, T.cores[peers[0]])
+    ne = len(out_e)
+    hc = helper_of(core, topo)
+    in_e = inner_engines(topo, core, T.cores[peers[0]])
+    ids = [dst_id(topo, T.cores[r]) for r in peers]
 
-    def dst_id(r):
-        rid, pid, _ = topo.addr(T.cores[r])
-        return DstId(rid=rid, pnc=pid)
+    def mask(es):
+        return sum(1 << e for e in es)
 
-    lanes_out = topo.engines(core, T.cores[peer(1)])
-    full = sum(1 << e for e in lanes_out)
-    ne = len(lanes_out)
-    per = ne // 4
+    def recv(after, link, lat, kb, sem, cnt, wr):
+        return op(link, None, [], wr, 0.01 + kb / RATE, lat=lat, kind="recv", after=after, sem=sem, cnt=cnt)
 
-    def send(out, in_, r, sem, rd, kb):
-        rid, pid, _ = topo.addr(T.cores[r])
-        return op("pool", lambda: g.remote_dma(out, in_, T.sem[sem], T.sem.sent, pid, rid, full), rd, [], 0.5,
-                  kind="send", inc=ne, kb=kb)
+    def spread(aps, sem, rd, wr, kb, to=None):
+        per = ne // len(aps)
+        trs = [RemoteDMATransfer(dst_ids=ids, dma_engine_mask=mask(out_e[per * i:per * i + per]), remote_sem=T.sem[sem],
+                                 srcs=[a], dsts=3 * [to[i] if to else a]) for i, a in enumerate(aps)]
+        sd = op("pool", lambda: g.remote_dma_fused(trs, local_sem=T.sem.sent), rd, [], 0.5, kind="send", inc=ne)
+        recv(sd, "link", LAT, kb, sem, 3 * ne, wr)
 
-    def recv(after, sem, cnt, wr):
-        return op("link", None, [], wr, 0.01 + ops[after]["kb"] / RATE, lat=LAT, kind="recv", after=after, sem=sem, cnt=cnt)
+    last = [None]
 
-    def fan(src, dst, sem, rd, kb):
-        trs = [RemoteDMATransfer(dst_ids=[dst_id(peer(k))], dma_engine_mask=sum(1 << e for e in lanes_out[per * (k - 1):per * k]),
-                                 remote_sem=T.sem[sem], src=src(peer(k)), dst=dst) for k in (1, 2, 3)]
-        sd = op("pool", lambda: g.remote_dma_fused(trs, local_sem=T.sem.sent), rd, [], 0.5, kind="send", inc=3 * per, kb=kb)
-        recv(sd, sem, 3 * per, [sem])
+    def relay(ap, hsem, sem, rd, wr, kb):
+        rid, pid, _ = topo.addr(hc)
+        sd = op("pool", lambda: g.remote_dma(ap, ap, T.sem[hsem], T.sem.sent, pid, rid, mask(in_e)), rd, [], 0.5,
+                kind="send", inc=len(in_e))
+        i = recv(sd, "link2", 2 * LAT + 0.5 + kb / 450.0, kb, sem, 3 * ne, wr)
+        ops[i]["also"] = last[0]
+        last[0] = i
 
-    order = [peer(1), peer(2), peer(3), me]
-    dma("sp", T.CT[0:32, 0:256], T.cc0[:], [], ["CT0"], 32)
-    dma("act", T.CT[0:32, 256:320], T.c0[:], [], ["CT1"], 8)
-    for d in order:
-        rows = slice(32 * d, 32 * d + 32)
-        dma("sp", T.LCE[:, 256 * d:256 * d + 256], T.ce0[rows, :], [], [("LCE", d)], 128)
-        dma("act", T.LX[:, 256 * d:256 * d + 256], T.x0[rows, :], [], [("LX", d)], 64)
-        dma("sp", T.LCD[:, 256 * d:256 * d + 256], T.cd[rows, :], [], [("LCD", d)], 128)
-        dma("act", T.LE[:, 64 * d:64 * d + 64], T.e0[rows, :], [], [("LE", d)], 32)
-    dma("sp", T.CT[0:32, 320:576], T.ky[:], [], ["CT2"], 32)
-    dma("sp", T.CT[0:32, 576:832], T.kid[:], [], ["CT3"], 32)
-    for d in order:
-        dma("sp", T.M2[:, W2 * d:W2 * d + 256], T.zt[32 * d:32 * d + 32, :], [], [("M2z", d)], 64)
-
-    io(T.V2[:], [[0, 4], [-1, 32]], 0, 1, ["V2"], 128)
-    io(T.VA[:], [[-4, 8], [-32, 16], [-1, 4]], 0, 1, ["VA"], 512)
-    io(T.V1[:], [[-1, 128]], 0, 1, ["V1"], 128)
-    io(T.V3[:], [[0, 4], [-4, 32]], 0, 1, ["V3"], 128)
-    io(T.V5[:], [[4, 224]], -384, -1, ["V5"], 224)
-    io(T.PI[:], [[0, 1]], 0, 1, ["PI"], 1, flag=False)
-    io(T.XF[:], [[1, 160]], 0, 0, ["XF"], 160)
-    io(T.CLv[:], [[0, 4], [32, 32]], 0, 0, ["CLv"], 128)
-    io(T.VWv[:], [[32, 5], [0, 2], [1000, 16]], 0, 0, ["VWv"], 160)
-    io(T.VY[:], [[-1, 516]], 3, 4, ["VY"], 516)
-    io(T.VV[:], [[0, 32], [-1, 4]], -64, 1, ["VV"], 128)
-    io(T.XL[:], [[1, 516]], 0, 0, ["XL"], 516)
     for b in range(4):
-        ms(T.SF[32 * b:32 * b + 32, :], 0.25 ** (b + 1), [("SF", b)], 1)
+        c = 1024 * b + 256 * me
+        when("x01" if b < 2 else "x23")
+        dma("sp", T.HV[:, c:c + 256], T.x0[:, 256 * b:256 * b + 256], [], [("HV", c // 128), ("HV", c // 128 + 1)], 64)
+    when("codes")
+    for i, src in enumerate((T.cc0, T.ky, T.kid)):
+        dma("act", T.CT[8 * i:8 * i + 8, :], src[:], [], [("CT", i)], 64)
+    dma("act", T.C0[0:8, :], T.c0[:], [], ["C0"], 16)
+    for h in range(2):
+        when("ce%d" % h)
+        dma("sp", T.LCE[:, 512 * h:512 * h + 512], T.ce0[:, 512 * h:512 * h + 512], [], [("LCE", h)], 256)
+    when("cd")
+    for h in range(2):
+        dma("sp", T.LCD[:, 512 * h:512 * h + 512], T.cd[:, 512 * h:512 * h + 512], [], [("LCD", h)], 256)
+    when("e")
+    dma("sp", T.LE[:], T.e0[:], [], ["LE"], 128)
+    when("z")
+    for h in range(2):
+        dma("sp", T.ZT[:, 1024 * h:1024 * h + 1024], T.zt[:], [("LCD", 1), ("LCE", 1)], [("ZT", h)], 256)
+    when("send")
+    for bs in (VOWN[:2], VOWN[2:]):
+        if bs:
+            spread([T.HV[:, 1024 * b + 256 * me:1024 * b + 256 * me + 256] for b in bs], "v%d" % bs[0],
+                   [("HV", 8 * b + 2 * me + x) for b in bs for x in (0, 1)],
+                   [("HV", 8 * b + 2 * r + x) for b in bs for r in peers for x in (0, 1)], 192 * len(bs))
+    for b in range(4):
+        if b not in VOWN:
+            relay(T.HV[:, 1024 * b + 256 * me:1024 * b + 256 * me + 256], "hv%d" % b, "v%d" % b,
+                  [("HV", 8 * b + 2 * me + x) for x in (0, 1)], [("HV", 8 * b + 2 * r + x) for r in peers for x in (0, 1)], 192)
+
+    when("iota")
+    io(T.PI[:], [[0, 1]], 0, 1, ["PI"], 1, flag=False)
+    io(T.VA[:], [[-1, 24], [-32, 16]], 416, 1, ["VA"], 384)
+    io(T.V2[:], [[0, 4], [-1, 32]], 0, 1, ["V2"], 128)
+    io(T.V1[:], [[-1, 128]], 0, 1, ["V1"], 128)
+    io(T.XF[:], [[1, 176]], -16, 0, ["XF"], 176)
+    io(T.VQ[0:8, :], [[1, 144]], -16, -16, ["VQ"], 144)
+    io(T.JP[:], [[0, 8], [1, 16]], -8, 0, ["JP"], 128)
+    io(T.BG[:], [[16, 8], [0, 16]], 0, 0, ["BG"], 128)
+    when("early")
+
+    def X_(d, n):
+        return T.XF[:, 16 - d:16 - d + n]
+
+    for b in range(4):
+        ms(T.SF[32 * b:32 * b + 32, :], 0.125 ** (b + 1) if b < 3 else 0.0, [("SF", b)], 1)
     SFt = [("SF", b) for b in range(4)]
-    ms(T.ZR[:], 0.0, ["ZR"], 256)
-    ms(T.K64[:], 64.0, ["K64"], 256)
-    ms(T.CS[:], 49152.0 * 65536.0, ["CS"], 64)
-    ms(T.PA[:, 0:20], 0.0, ["PAp"], 10)
-    ms(T.PB[:, 0:20], 0.0, ["PBp"], 10)
-    for r in range(4):
-        ts(T.RE[:, 128 * r:128 * r + 128], T.V2[:], 32.0 * r, None, A.is_equal, None, ["V2"], [("RE", r)], 64)
-    ts(T.PA1[:], T.VA[:], -32.0, None, A.is_equal, None, ["VA"], ["PA1"], 256)
-    ts(T.PA2[:], T.VA[:], 0.0, -4.0, A.is_equal, A.mult, ["VA"], ["PA2"], 256)
-    ts(T.PB[:, 20:532], T.VA[:], 0.0, None, A.is_equal, None, ["VA"], ["PB"], 256)
-    tt(T.PA[:, 20:532], T.PA1[:], T.PA2[:], A.add, ["PA1", "PA2"], ["PA"], 1024)
-    for name, sc in (("I8", 8.0), ("I1K", 1024.0), ("IB", 1.0), ("IS", 2.0 ** -16), ("I128", 1.0 / 128), ("IH", 1.0), ("NH", -1.0)):
-        ts(T[name][:], T.V1[:], 0.0, sc, A.is_equal, A.mult, ["V1"], [name], 64)
-    for u in range(4):
-        ts(T.RA[:, 128 * u:128 * u + 128], T.V3[:], float(u), 8192.0, A.is_equal, A.mult, ["V3"], [("RA", u)], 64)
-        ts(T.RB[:, 128 * u:128 * u + 128], T.V3[:], float(u), None, A.is_equal, None, ["V3"], [("RB", u)], 64)
-        ts(T.ZW[:, 224 * u:224 * u + 224], T.V5[:], float(-u), None, A.is_equal, None, ["V5"], [("ZW", u)], 112)
-    for j, (s1, s2, o0, o1) in enumerate(((15, None, A.bitwise_and, None), (112, None, A.bitwise_and, None),
-                                          (5, None, A.arith_shift_right, None), (3, 1, A.arith_shift_right, A.bitwise_and),
-                                          (4, 1, A.arith_shift_right, A.bitwise_and))):
-        ts(T.PJ[:, j:j + 1], T.PI[:], s1, s2, o0, o1, ["PI"], [("PJ", j)], 1)
-    cp(T.PC[:, 0:5], T.PJ[:, 0:5], [("PJ", j) for j in range(5)], ["PC"], 5)
+    when("late")
+    ms(T.CK[:, 0:128], 192.0, [("CK", 0)], 64)
+    ms(T.CK[:, 128:256], 256.0, [("CK", 1)], 64)
+    CKt = [("CK", 0), ("CK", 1)]
+    ms(T.O16[:], -1.0 / 16, ["O16"], 8)
+    io(T.BX[:], [[16, 4], [2, 2]], 4 * me - 32, 0, ["BX"], 8)
+    ts(T.IH[:], T.V1[:], 0.0, None, A.is_equal, None, ["V1"], ["IH"], 64)
+    when("early")
+    ts(T.RE[0:32, :], T.V2[0:32, :], 0.0, None, A.is_equal, None, ["V2"], ["RE"], 64)
+    ts(T.PA0[0:96, :], T.VA[0:96, :], 0.0, 128.0, A.is_equal, A.mult, ["VA"], ["PA0"], 192)
+    ts(T.PA1[0:96, :], T.VA[0:96, :], 32.0, -1024.0, A.is_equal, A.mult, ["VA"], ["PA1"], 192)
+    ts(T.PB[0:32, :], T.VA[0:32, :], 32.0, 128.0, A.is_equal, A.mult, ["VA"], ["PB"], 192)
+    tt(T.PA[0:96, :], T.PA0[0:96, :], T.PA1[0:96, :], A.add, ["PA0", "PA1"], ["PA"], 768)
+    ms(T.PA[96:128, :], 0.0, ["PAc"], 192)
+    for r, v in ((12, 1024.0), (13, 896.0), (14, 896.0), (15, -128.0)):
+        ms(T.PA[96:97, r:384:16], v, ["PAc"], 24)
+    ts(T.IB[:], T.V1[:], 0.0, None, A.is_equal, None, ["V1"], ["IB"], 64)
+    ts(T.IS[:], T.V1[:], 0.0, 1.0 / 64, A.is_equal, A.mult, ["V1"], ["IS"], 64)
+    ts(T.Q0[0:8, :], T.VQ[0:8, :], 0.0, None, A.is_equal, None, ["VQ"], ["Q0"], 72)
+    SC = (-1.0, 3.0 / 64, -3.75 / 64)
+    for i, v in enumerate(SC):
+        ac(T.ID[:, 128 * i:128 * i + 128], T.IB[:], ["IB"], [("ID", i)], 128, scale=v)
 
-    def col(j):
-        return T.PC[:, j:j + 1]
+    def ID(v):
+        i = SC.index(v)
+        return T.ID[:, 128 * i:128 * i + 128]
 
-    cF, cG, cR, cU, cH = range(5)
-    (LO8, HI8, N15, K5, K10, KIDC, F0, F128, BT, BASE, F8, U16C, G16, R32, TV, PW, PWK, P4, P4K, TY0, TY) = range(5, 26)
-
-    def cs(j, src, s1, s2, o0, o1, rd=()):
-        ts(col(j), col(src), s1, s2, o0, o1, ["PC"] + [("c", x) for x in rd], [("c", j)], 1)
-
-    cs(LO8, cF, 8.0, None, A.is_lt, None)
-    cs(HI8, cF, 8.0, None, A.is_ge, None)
-    cs(N15, cF, 15.0, None, A.is_lt, None)
-    cs(K5, cF, 5.0, 8192.0, A.is_lt, A.mult)
-    cs(K10, cF, 10.0, 8192.0, A.is_lt, A.mult)
-    cs(KIDC, K10, col(K5), None, A.subtract, None, (K10, K5))
-    cs(F0, cF, 0.0, None, A.is_equal, None)
-    cs(F128, cF, 0.0, 128.0, A.is_equal, A.mult)
-    cs(BT, cR, 1024.0, -2048.0, A.mult, A.add)
-    cs(BASE, BT, col(F0), 2048.0, A.mult, A.add, (BT, F0))
-    cs(F8, cF, 8.0, None, A.mult, None)
-    cs(U16C, cU, 16.0, None, A.mult, None)
-    cs(G16, cG, 16.0, None, A.add, None)
-    cs(R32, cR, 32.0, 32.0, A.mult, A.add)
-    cs(TV, cR, 128.0, 67.0, A.mult, A.add)
-    cs(TY0, cH, 4.0, 8.0 * me + 3.0, A.mult, A.add)
-    cs(TY, cR, 128.0, col(TY0), A.mult, A.add, (TY0,))
-    for i, (x0, pw, ind, p4) in enumerate(((0, PW, K5, P4), (5, PWK, KIDC, P4K))):
-        ts(T.TA[:, 4 * i:4 * i + 4], T.XF[:, x0:x0 + 4], col(cF), 3.0, A.is_lt, A.mult, ["XF", "PC"], [("TA", i)], 4)
-        ts(T.TB[:, 4 * i:4 * i + 4], T.TA[:, 4 * i:4 * i + 4], 1.0, None, A.add, None, [("TA", i)], [("TB", i)], 4)
-        dv(lambda i=i, pw=pw: g.vector.tensor_reduce(col(pw), T.TB[:, 4 * i:4 * i + 4], AxisListType.X, A.mult),
-           [("TB", i)], [("c", pw)], 4)
-        cs(p4, pw, col(ind), 1.0 / 8192, A.mult, A.mult, (pw, ind))
-    ts(T.QW[:], T.XF[:, 0:144], col(G16), col(P4), A.is_equal, A.mult, ["XF", ("c", G16), ("c", P4)], ["QW"], 144)
-    for i, (v, m) in enumerate(((0.0, LO8), (-8.0, LO8), (8.0, HI8), (0.0, HI8))):
-        ts(T.SAB[:, 128 * i:128 * i + 128], T.V1[:], v, col(m), A.is_equal, A.mult, ["V1", ("c", m)], [("SAB", i)], 64)
-    ts(T.CL[:], T.CLv[:], col(U16C), None, A.add, None, ["CLv", ("c", U16C)], ["CL"], 64)
-    ts(T.SH[:], T.V1[:], -1.0, col(N15), A.is_equal, A.mult, ["V1", ("c", N15)], ["SH"], 64)
-    ts(T.KID[:], T.V1[:], 5.0, col(KIDC), A.is_equal, A.mult, ["V1", ("c", KIDC)], ["KID"], 64)
-    ts(T.IT[:], T.XF[:, 0:128], col(F0), None, A.mult, None, ["XF", ("c", F0)], ["IT"], 128)
-    ts(T.BC[:], T.XF[:, 0:8], col(F128), col(BASE), A.mult, A.add, ["XF", ("c", F128), ("c", BASE)], ["BC"], 8)
-    ts(T.BC2[:], T.BC[:, 2:4], -2048.0, None, A.add, None, ["BC"], ["BC2"], 2)
-    ts(T.C8[:], T.XF[:, 0:8], 128.0, col(F8), A.mult, A.add, ["XF", ("c", F8)], ["C8"], 8)
-    ts(T.VW[:], T.VWv[:], col(R32), None, A.is_equal, None, ["VWv", ("c", R32)], ["VW"], 160)
-    for r in range(4):
-        ts(T.RW[:, 128 * r:128 * r + 128], T.V2[:], 32.0 * r, 65536.0, A.is_equal, A.mult, ["V2"], [("RW", r)], 64)
-        ts(T.RK[:, 128 * r:128 * r + 128], T.V2[:], 32.0 * r, col(K5), A.is_equal, A.mult, ["V2", ("c", K5)], [("RK", r)], 64)
-    ts(T.YH[:], T.VY[:], 0.0, None, A.is_equal, None, ["VY"], ["YH"], 258)
-    ts(T.YB[:], T.VY[:], 0.0, None, A.is_equal, None, ["VY"], ["YB"], 258)
-    ts(T.YV[:], T.XL[:], col(TV), None, A.is_equal, None, ["XL", ("c", TV)], ["YV"], 516)
-    ts(T.SV[:], T.VV[:], 0.0, None, A.is_equal, None, ["VV"], ["SV"], 64)
-    ts(T.YC[:], T.XL[:], col(TY), col(P4), A.is_equal, A.mult, ["XL", ("c", TY), ("c", P4)], ["YC"], 516)
-    ts(T.YK[:], T.XL[:], col(TY), col(P4K), A.is_equal, A.mult, ["XL", ("c", TY), ("c", P4K)], ["YK"], 516)
-
-    for i, (a, b, bank, tk) in enumerate(((0, 320, BL2, ["CT0", "CT1"]), (320, 832, BEB, ["CT2", "CT3"]))):
-        n = b - a
-        cp(T.CF[0:32, a:b], T.CT[0:32, a:b], tk, [("CF", i)], n)
-        mm(group([(P(bank)[:, 0:n], T.RE[0:32, 0:128], T.CF[0:32, a:b], n)]), [("CF", i), ("RE", 0)], [B(bank)])
-        ts(T.FP[:, a:b], P(bank)[:, 0:n], T.SF[:, 0:1], 1536.0 - 127.5 / 256, A.mult, A.add, SFt, [B(bank), ("FP", i)], n)
-        ts(T.FF[:, a:b], T.FP[:, a:b], -1536.0, None, A.add, None, [("FP", i)], [("FF", i)], n // 2)
-
-    def pieces(out, d, a, n, pad):
-        c0 = pad + 128 * d
-        return [(out, T.PA[:, c0:c0 + 128], T.FF[:, a:a + n], n), (out, T.PB[0:32, c0:c0 + 128], T.CF[0:32, a:a + n], n)]
-
-    PAt = ["PA", "PB", "PAp", "PBp"]
-    s0, s1, s2 = {}, {}, {}
-    for i, d in enumerate(order):
-        c = slice(256 * d, 256 * d + 256)
-        m = W1 * d
-        bank = (S0, S1)[i % 2]
-        ac(T.SG[:, c], T.LX[:, c], [("LX", d)], [("SG", d)], 256, bias=-127.5, func=ACT.Sign)
-        o = P(bank)[:, 0:256]
-        mm(group([(o, T.I8[:], T.LX[:, c], 256), (o, T.I1K[:], T.SG[:, c], 256)] + pieces(o, d, 0, 256, 20))
-           + group(pieces(P(bank)[:, 256:320], d, 256, 64, 20)),
-           [("LX", d), ("SG", d), "I8", "I1K", ("FF", 0), ("CF", 0)] + PAt, [B(bank)])
-        ts(T.M1[:, m + 256:m + 512], T.LCE[:, c], -2048.0, None, A.add, None, [("LCE", d)], [("M1", d, 1)], 256)
-        cp(T.M1[:, m:m + 256], T.LCD[:, c], [("LCD", d)], [("M1", d, 2)], 256)
-        ts(T.M1[:, m + 768:m + 832], T.LE[:, 64 * d:64 * d + 64], -2048.0, None, A.add, None, [("LE", d)], [("M1", d, 3)], 64)
-        ts(T.M1[:, m + 512:m + 768], o, -1023.0, None, A.add, None, [], [B(bank), ("M1", d, 0)], 256)
-        ts(T.M1[:, m + 832:m + 896], P(bank)[:, 256:320], 8192.0, None, A.mult, None, [], [B(bank), ("M1", d, 4)], 64)
-        if d != me:
-            s0[i + 1] = send(T.L1[:, W1 * me:W1 * me + 512], T.M1[:, m:m + 512], d, "a0_%d" % (i + 1),
-                             [("M1", d, x) for x in (1, 2)], 128)
-            s1[i + 1] = send(T.L1[:, W1 * me + 512:W1 * me + W1], T.M1[:, m + 512:m + W1], d, "a1_%d" % (i + 1),
-                             [("M1", d, x) for x in (0, 3, 4)], 96)
-    for i, d in enumerate(order):
-        o = P(BVS)[:, 0:256]
-        mm(group(pieces(o, d, 320, 256, 20) + pieces(o, d, 576, 256, 0)), [("FF", 1), ("CF", 1)] + PAt, [B(BVS)])
-        ac(T.M2[:, W2 * d + 256:W2 * d + 512], o, [], [B(BVS), ("M2k", d)], 256)
-        if d != me:
-            s2[i + 1] = send(T.L2[:, W2 * me:W2 * me + W2], T.M2[:, W2 * d:W2 * d + W2], d, "a2_%d" % (i + 1),
-                             [("M2z", d), ("M2k", d)], 128)
-
-    mm([zero(BL2, 512), zero(BEB, 512), zero(BVW, 256)], ["ZR"], [B(BL2), B(BEB), B(BVW)])
-    for k in range(4):
-        s = (me - k) % N
-        if k:
-            recv(s0[k], "a0_%d" % k, ne, [("L0", s)])
-            recv(s1[k], "a1_%d" % k, ne, [("L1", s)])
-        src, tk = (T.M1, [("M1", me, x) for x in range(5)]) if k == 0 else (T.L1, [("L0", s), ("L1", s)])
-        tc = [("M1", me, 2)] if k == 0 else [("L0", s)]
-        m = W1 * s
-        for hb in range(2):
-            bank = (R0, R1, S0, S1)[(2 * k + hb) % 4]
-            lst = []
-            for u in (2 * hb, 2 * hb + 1):
-                o = P(bank)[:, 256 * (u % 2):256 * (u % 2) + 256]
-                lst += group([(o, T.RA[:, 128 * u:128 * u + 128], src[:, m + 512:m + 768], 256),
-                              (o, T.RB[:, 128 * u:128 * u + 128], src[:, m + 256:m + 512], 256)])
-            mm(lst, tk + [("RA", u) for u in range(4)] + [("RB", u) for u in range(4)], [B(bank)])
-            o = T.H[:, 1024 * s + 512 * hb:1024 * s + 512 * hb + 512]
-            wr = [B(bank)] + [("H", s, x) for x in range(4 * hb, 4 * hb + 4)]
-            if hb == 0:
-                ac(o, P(bank)[:], [], wr, 512, bias=-6144.0)
-            else:
-                ts(o, P(bank)[:], -6144.0, None, A.add, None, [], wr, 512)
-        Z = [T.ZW[:, 224 * u + 96 - 32 * s:224 * u + 224 - 32 * s] for u in range(4)]
-        Zt = [("ZW", u) for u in range(4)]
-        lst = []
-        for u in range(4):
-            o = P(BVW)[:, 64 * u:64 * u + 64]
-            lst += [(o, Z[u], src[:, m + 768:m + 832], 64), (o, Z[u], src[:, m + 832:m + 896], 64)]
-        mm(more(lst, k == 3), tk + Zt, [B(BVW)])
-        for hb, bank in enumerate((BL2, BEB)):
-            mm(more([(P(bank)[:, 256 * (u % 2):256 * (u % 2) + 256], Z[u], src[:, m:m + 256], 256)
-                     for u in (2 * hb, 2 * hb + 1)], k == 3), tc + Zt, [B(bank)])
-    for hb, bank in enumerate((BL2, BEB)):
-        ac(T.CD[:, 512 * hb:512 * hb + 512], P(bank)[:], [], [B(bank), ("CD", hb)], 512)
-    for k in range(4):
-        s = (me - k) % N
-        if k:
-            recv(s2[k], "a2_%d" % k, ne, [("L2", s)])
-        src, tz, tk = (T.M2, [("M2z", me)], [("M2k", me)]) if k == 0 else (T.L2, [("L2", s)], [("L2", s)])
-        dma("sp", T.ZT[32 * s:32 * s + 32, :], src[:, W2 * s:W2 * s + 256], tz, [("ZT", s)], 64)
-        dma("sp", T.KK[32 * s:32 * s + 32, :], src[:, W2 * s + 256:W2 * s + 512], tk, [("KK", s)], 64)
-    Ht = [("H", s, x) for s in range(4) for x in range(8)]
-    CDt, ZTt, KKt = [("CD", 0), ("CD", 1)], [("ZT", s) for s in range(4)], [("KK", s) for s in range(4)]
-
-    def pieces_of(X):
-        c = slice(128 * X, 128 * X + 128)
-        ts(T.N32[:, c], T.X32[:, c], 4095, None, A.bitwise_and, None, [("X32", X)], [("N32", X)], 128)
-        ts(T.C32[:, c], T.X32[:, c], 13, 3, A.arith_shift_right, A.bitwise_and, [("X32", X)], [("C32", X)], 128)
-        cp(T.CB[:, c], T.C32[:, c], [("C32", X)], [("CB", X)], 128)
-
-    def unpack(X):
-        c = slice(128 * X, 128 * X + 128)
-        pieces_of(X)
-        cp(T.EL[:, c], T.N32[:, c], [("N32", X)], [("EL", X)], 128)
-        ts(T.E16[:, c], T.EL[:, c], -2048.0, None, A.add, None, [("EL", X)], [("E16", X)], 64)
-        o = P(BVS)[:, 16:24]
-        mm(group([(o, T.QW[:, 16 - s:144 - s], T.CB[:, 128 * X + s:128 * X + 128:16], 8) for s in range(16)]),
-           ["QW", ("CB", X)], [B(BVS)])
-        cp(T.QL[:, 8 * X:8 * X + 8], o, [], [B(BVS), ("QL", X)], 8)
-
-    ts(T.X32[:], P(BVW)[:, 0:256], 2048.0, None, A.add, None, [], [B(BVW), ("X32", 0), ("X32", 1)], 256)
-    unpack(0)
-    unpack(1)
-
-    def front(t, X):
-        c = slice(128 * X, 128 * X + 128)
-        q = T.QL[:, 8 * X:8 * X + 8]
-        gat("act", lambda: g.scalar.activation(T.RG[:, c], T.CD[:, 0:1024].indirect(q), ACT.Copy), CDt + [("QL", X)], [("RG", X)], 128)
-        o = P(BL2)
-        lst = [(o[:, 0:128], T.IB[:], T.CL[:], 128)]
-        for i in range(4):
-            lst.append((o[:, 64 * (i // 2):64 * (i // 2) + 64], T.SAB[:, 128 * i:128 * i + 128],
-                        T.RG[:, 128 * X + i % 2:128 * X + 128:2], 64))
-        mm(group(lst), ["IB", "CL", ("RG", X)] + [("SAB", i) for i in range(4)], [B(BL2)])
-        cp(T.LL[:, c], o[:, 0:128], [], [B(BL2), ("LL", X)], 128)
-        gat("act", lambda: g.scalar.activation(T.KG[:, c], T.KK[:, 0:1024].indirect(q), ACT.Copy), KKt + [("QL", X)], [("KG", X)], 128)
-        bank = S0
-        mm([(P(bank)[:, 0:128], T.IS[:], T.CS[:], 128, True, False)], ["IS", "CS"], [B(bank)])
-        for j in (2 * X, 2 * X + 1):
-            v0, e0 = 1024 * j, 64 * j
-            Vt, lo = [("LL", X)], 0
-            for i, (e, wd) in enumerate(SHARE[j]):
-                out, src = T.V[:, v0 + 16 * lo:v0 + 16 * (lo + wd)], T.H[:, 0:4096].indirect(T.EL[:, e0 + lo:e0 + lo + wd])
-                if e == "act":
-                    gat(e, lambda out=out, src=src: g.scalar.activation(out, src, ACT.Copy), Ht + [("EL", X)], [("V", j, i)], 16 * wd)
-                else:
-                    gat(e, lambda out=out, src=src: g.vector.tensor_copy(out, src), Ht + [("EL", X)], [("V", j, i)], 16 * wd)
-                Vt.append(("V", j, i))
-                lo += wd
-            la, ga = 128 * X + 32 * (j % 2), slice(512 * j, 512 * j + 512)
-            gat("act", lambda v0=v0, la=la, ga=ga: g.scalar.activation(
-                T.GA[:, ga], T.V[:, v0:v0 + 1024].indirect(T.LL[:, la:la + 32]), ACT.Copy), Vt, [("GA", j)], 512)
-            gat("dve", lambda v0=v0, la=la, ga=ga: g.vector.tensor_tensor(
-                T.GB[:, ga], T.V[:, v0:v0 + 1024].indirect(T.LL[:, la + 64:la + 96]), T.GA[:, ga], A.max),
-                Vt + [("GA", j)], [("GB", j)], 512)
-            o = P(bank)[:, 64 * (j % 2):64 * (j % 2) + 64]
-            mm(more([(o, T.IS[:], T.GB[:, 512 * j + k:512 * j + 512:8], 64) for k in range(8)], j % 2 == 1),
-               ["IS", ("GB", j)], [B(bank)])
-        w = T.WS[:, 256 * t + 128 * X:256 * t + 128 * X + 128]
-        ac(T.FB[:, c], P(bank)[:, 0:128], [], [B(bank), ("FB", X)], 128, bias=-127.5)
-        tt(w, P(bank)[:, 0:128], T.FB[:, c], A.subtract, [("FB", X)], [B(bank), ("WS", t, X)], 128)
-        gat("dve", lambda: g.vector.tensor_tensor(T.YS[:, c], T.ZT[:, 0:1024].indirect(q), w, A.is_le),
-            ZTt + [("QL", X), ("WS", t, X)], [("YS", X)], 128)
-        return c, w
-
-    def votes(t, X):
-        i = 2 * t + X
-        o = P(BVW)[:, 0:8]
-        mm(group([(o, T.VW[:, 32 - s:160 - s], T.YS[:, 128 * X + s:128 * X + 128:16], 8) for s in range(16)]),
-           ["VW", ("YS", X)], [B(BVW)])
-        mine = T.PV[:, 32 * i + 8 * me:32 * i + 8 * me + 8]
-        ac(mine, o, [], [B(BVW), ("PV", i, me)], 8)
-        tr = RemoteDMATransfer(dst_ids=[dst_id(peer(k)) for k in (1, 2, 3)], dma_engine_mask=full, remote_sem=T.sem["v%d" % i],
-                               srcs=[mine], dsts=[mine, mine, mine])
-        sd = op("pool", lambda: g.remote_dma_fused([tr], local_sem=T.sem.sent), [("PV", i, me)], [], 0.5, kind="send", inc=ne, kb=12)
-        recv(sd, "v%d" % i, 3 * ne, [("PV", i, peer(k)) for k in (1, 2, 3)])
-
-    def update(t, X, c, w):
-        ts(T.MK[:, c], w, 128.0, -256.0, A.is_lt, A.mult, [("WS", t, X)], [("MK", X)], 64)
-        for hb, (bank, rs) in enumerate(((R0, (0, 1, 2, 3)),) if X == 0 else ((R1, (0, 1)), (S1, (2, 3)))):
-            early, late, wd = [], [], 128 * len(rs)
-            for i, r in enumerate(rs):
-                o, m = P(bank)[:, 128 * i:128 * i + 128], slice(128 * r, 128 * r + 128)
-                early += [(o, T.RE[:, m], T.E16[:, c], 128), (o, T.RK[:, m], T.KG[:, c], 128)]
-                late += [(o, T.RW[:, m], w, 128), (o, T.RW[:, m], T.MK[:, c], 128)]
-            early = [(P(bank)[:, 0:wd], T.K64[0:1, 0:128], T.K64[0:1, 0:wd], wd, True, False)] + more(early)
-            late = more(late, True)
-            for x in range(0, len(late), 4):
-                mm(early[:5] if x == 0 else early[x + 1:x + 5],
-                   ["K64", ("E16", X), ("KG", X)] + [(n, r) for n in ("RE", "RK") for r in range(4)], [B(bank)])
-            for x in range(0, len(late), 4):
-                mm(late[x:x + 4], [("WS", t, X), ("MK", X)] + [("RW", r) for r in range(4)], [B(bank)])
-            for i, r in enumerate(rs):
-                h0 = 1024 * r + 256 * (t % 4) + 128 * X
-                o, i_ = T.H[:, h0:h0 + 128], P(bank)[:, 128 * i:128 * i + 128]
-                wr = [B(bank), ("H", r, 2 * (t % 4) + X)]
-                if hb == 1:
-                    ts(o, i_, -2048.0, None, A.add, None, [], wr, 128)
-                else:
-                    ac(o, i_, [], wr, 128, bias=-2048.0)
-
-    def bound(t, X, c):
-        o = P(BEB)[:, 0:128]
-        mm(group([(o, T.IB[:], T.IT[:], 128), (o, T.SH[:], T.E16[:, c], 128), (o, T.KID[:], T.KG[:, c], 128)]),
-           ["IB", "IT", "SH", "KID", ("E16", X), ("KG", X)], [B(BEB)])
-        b = 2 * (t % 4) + X
-        ac(T.GA[:, 1024 * X + 1:1024 * X + 1024:8], o, ["BC"], [B(BEB), ("GA", 2 * X), ("GA", 2 * X + 1), ("EB", X)], 128,
-           bias=T.BC[:, b:b + 1])
-
-    def choose(t, X, c):
-        i = 2 * t + X
-        o = P(BVS)[:, 0:8]
-        mm(group([(o, T.IB[:], T.C8[:], 8)] + [(o, T.I128[:], T.PV[:, 32 * i + 8 * r:32 * i + 8 * r + 8], 8) for r in range(4)]),
-           ["IB", "C8", "I128"] + [("PV", i, r) for r in range(4)], [B(BVS)])
-        bl = T.BL[:, 8 * X:8 * X + 8]
-        ts(bl, o, 1.0 / 512, None, A.add, None, [], [B(BVS), ("BL", X)], 8)
-        gat("dve", lambda: g.vector.tensor_copy(T.X32[:, c], T.GA[:, 1024 * X:1024 * X + 1024].indirect(bl)),
-            [("GA", 2 * X), ("GA", 2 * X + 1), ("BL", X)], [("X32", X)], 128)
-        unpack(X)
-
-    for t in range(S - 1):
-        cw = []
-        role[2] = t
-        for X in range(2):
-            role[0], role[1] = X, 0
-            cw.append(front(t, X))
-            votes(t, X)
-            bound(t, X, cw[X][0])
-        role[0], role[1] = 2, 0
-        update(t, 0, *cw[0])
-        choose(t, 0, cw[0][0])
-        update(t, 1, *cw[1])
-        choose(t, 1, cw[1][0])
-
-    role[0], role[2] = None, S - 1
-    Wt = [("WS", t, X) for t in range(S - 1) for X in range(2)]
-    dma("sp", T.DW[:], T.WS[:, 0:1280], Wt, ["DW"], 320)
-    dma("sp", T.yx[32 * me:32 * me + 32, 0:1280], T.WS[32 * me:32 * me + 32, 0:1280], Wt, [], 80)
-    fan(lambda r: T.DW[r], T.DL[me], "ay", ["DW"], 240)
-    for k in (1, 2, 3):
-        s = peer(k)
-        dma("sp", T.yx[32 * s:32 * s + 32, 0:1280], T.DL[s], ["ay"], [], 80)
-
-    t = S - 1
-    mm([zero(BVW, 512)], ["ZR"], [B(BVW)])
-    mm([zero(R0, 512), zero(R1, 512)], ["ZR"], [B(R0), B(R1)])
-
-    def spread(bank, x, M, D, X, d0=0):
-        return [(P(bank)[:, 128 * r + x:128 * r + x + 64], M[:, 128 * r + 3 - u:128 * r + 131 - u],
-                 D[:, d0 + 64 * u:d0 + 64 * u + 64], 64) for r in range(4) for u in (2 * X, 2 * X + 1)]
-
-    for X in range(2):
-        role[0], role[1] = X, 0
-        c, w = front(t, X)
-        role[0] = None
-        o = P(BEB)[:, 0:128]
-        mm(group([(o, T.IB[:], T.IT[:], 128), (o, T.SH[:], T.E16[:, c], 128)]), ["IB", "IT", "SH", ("E16", X)], [B(BEB)])
-        ts(T.EB16[:, c], o, T.BC2[:, X:X + 1], None, A.add, None, ["BC2"], [B(BEB), ("EB16", X)], 128)
-        mm(more(spread(BVW, 0, T.YH, T.EB16, X) + spread(BVW, 64, T.YK, T.KG, X), X == 1),
-           ["YH", "YK", ("EB16", X), ("KG", X)], [B(BVW)])
-        cp(T.X32[:, c], T.GA[:, 1024 * X:1024 * X + 1024:8], [("GA", 2 * X), ("GA", 2 * X + 1)], [("X32", X)], 128)
-        pieces_of(X)
-        ts(T.EA16[:, c], T.N32[:, c], -2048.0, None, A.add, None, [("N32", X)], [("EA16", X)], 128)
-        mm(more(spread(R0, 0, T.YH, T.EA16, X)), ["YH", ("EA16", X)], [B(R0)])
-        mm(more(spread(R0, 64, T.YC, T.CB, X), X == 1), ["YC", ("CB", X)], [B(R0)])
-        mm(more(spread(R1, 0, T.YB, T.WS, X, 1280)), ["YB", ("WS", t, X)], [B(R1)])
-        mm(more(spread(R1, 64, T.YV, T.YS, X), X == 1), ["YV", ("YS", X)], [B(R1)])
-    mine = slice(128 * me, 128 * me + 128)
-    cp(T.MF[:], P(BVW)[:], [], [B(BVW), "MF"], 512)
-    fan(lambda r: T.MF[:, 128 * r:128 * r + 128], T.LF[:, mine], "af", ["MF"], 96)
-    cp(T.MG[:], P(R0)[:], [], [B(R0), "MG"], 512)
-    fan(lambda r: T.MG[:, 128 * r:128 * r + 128], T.LG[:, mine], "ag", ["MG"], 96)
-    ac(T.MH[:], P(R1)[:], [], [B(R1), "MH"], 512)
-    fan(lambda r: T.MH[:, 128 * r:128 * r + 128], T.LH[:, mine], "ah", ["MH"], 96)
-    Ft, Gt, Wt = ["af", "MF"], ["ag", "MG"], ["ah", "MH"]
-
-    def got(M, L, s, a):
-        return (M if s == me else L)[:, 128 * s + a:128 * s + a + 64]
-
-    for s in range(4):
-        ts(T.EA2[:, 64 * s:64 * s + 64], got(T.MF, T.LF, s, 0), 2048.0, None, A.add, None, Ft, [("EA2", s)], 64)
-    o = P(BEB)[:, 0:64]
-    mm(group([(o, T.IH[:], got(T.MF, T.LF, s, 64), 64) for s in range(4)]), ["IH"] + Ft, [B(BEB)])
-    ac(T.EA2[:, 256:320], o, [], [B(BEB), ("EA2", 4)], 64)
-    lst = []
-    for s in range(4):
-        o = P(BL2)[:, 64 * s:64 * s + 64]
-        lst += group([(o, T.NH[:], got(T.MF, T.LF, s, 0), 64), (o, T.IH[:], got(T.MG, T.LG, s, 0), 64)])
-    o = P(BL2)[:, 256:320]
-    lst += group([(o, M, got(a, b, s, 64), 64) for s in range(4) for M, a, b in ((T.NH[:], T.MF, T.LF), (T.IH[:], T.MG, T.LG))])
-    mm(lst, ["IH", "NH"] + Ft + Gt, [B(BL2)])
-    o = P(BVS)[:, 0:64]
-    mm(group([(o, T.SV[:], got(T.MH, T.LH, s, 64), 64) for s in range(4)]), ["SV"] + Wt, [B(BVS)])
-    ts(T.BB[:], o, 64.0, None, A.is_lt, None, [], [B(BVS), "BB"], 64)
-    for s in range(4):
-        dma(("act", "sp")[s % 2], T.yx[32 * s:32 * s + 32, 1280:1536], got(T.MH, T.LH, s, 0), Wt, [], 16)
-    for s in range(5):
-        c = slice(64 * s, 64 * s + 64)
-        tt(T.OM[:, c], P(BL2)[:, c], T.BB[:], A.mult, ["BB"], [B(BL2), ("OM", s)], 64)
-        tt(T.OUT[:, c], T.OM[:, c], T.EA2[:, c], A.add, [("OM", s), ("EA2", s)], [("OUT", s)], 128)
-        if s < 4:
-            dma(("sp", "act")[s % 2], T.ye[32 * s:32 * s + 32, :], T.OUT[:, c], [("OUT", s)], [], 32)
+    when("iota")
+    for j, (s1, s2) in enumerate(((0, 15), (0, 112), (0, 1), (1, 7), (3, 1), (0, 7))):
+        if s1:
+            ts(T.PJ[:, j:j + 1], T.PI[:], s1, s2, A.arith_shift_right, A.bitwise_and, ["PI"], [("PJ", j)], 1)
         else:
-            dma("sp", T.yc[:], T.OUT[0:32, c], [("OUT", s)], [], 8)
+            ts(T.PJ[:, j:j + 1], T.PI[:], s2, None, A.bitwise_and, None, ["PI"], [("PJ", j)], 1)
+    names = ["row", "g16", "par", "hm", "u8", "r7"]
+    cp(T.PC[:, 0:6], T.PJ[:, 0:6], [("PJ", j) for j in range(6)], [("c", x) for x in names], 6)
+
+    def col(x):
+        return T.PC[:, names.index(x):names.index(x) + 1]
+
+    def cs(x, src, s1, s2, o0, o1=None):
+        names.append(x)
+        rd = [("c", y) for y in (src, s1, s2) if isinstance(y, str)]
+        s1, s2 = (col(y) if isinstance(y, str) else y for y in (s1, s2))
+        if o0 == A.mult and o1 in (None, A.add):
+            ac(col(x), col(src), rd, [("c", x)], 1, scale=s1, bias=s2)
+        elif o0 == A.add and o1 is None:
+            ac(col(x), col(src), rd, [("c", x)], 1, bias=s1)
+        else:
+            ts(col(x), col(src), s1, s2, o0, o1, rd, [("c", x)], 1)
+
+    def eq(out, d, n, x, v, wr):
+        ts(out, X_(d, n), col(x), col(v) if isinstance(v, str) else v, A.is_equal, A.mult,
+           ["XF", ("c", x)] + ([("c", v)] if isinstance(v, str) else []), wr, n // 2)
+
+    when("cols")
+    cs("is10", "row", 10.0, None, A.is_equal)
+    cs("is11", "row", 11.0, None, A.is_equal)
+    cs("h5", "hm", 5.0, None, A.is_equal)
+    cs("gam", "is11", -64.0, None, A.mult)
+    cs("a1", "par", -128.0, 128.0, A.mult, A.add)
+    cs("al", "is10", -128.0, "a1", A.mult, A.add)
+    cs("b1", "is10", 32.0, None, A.mult)
+    cs("b2", "is11", 64.0, "b1", A.mult, A.add)
+    cs("be", "par", -64.0, "b2", A.mult, A.add)
+    for x, (a, b, c10, c11) in (("e0", (224.0, 448.0, 32.0, -26880.0)), ("e15", (672.0, 448.0, 0.0, -26624.0))):
+        cs(x + "a", "par", b - a, a, A.mult, A.add)
+        cs(x + "b", "is10", c10 - a, x + "a", A.mult, A.add)
+        cs(x, "is11", c11 - b, x + "b", A.mult, A.add)
+    cs("c23", "r7", 2.0, "g16", A.mult, A.add)
+    cs("v5", "r7", 5.0, None, A.is_lt)
+    cs("v2", "row", 5.0, None, A.is_lt)
+    cs("v3", "v5", "u8", None, A.mult)
+    cs("v1", "r7", 5.0, None, A.is_ge)
+    cs("t1", "row", 15.0, 2.0, A.is_equal, A.mult)
+    cs("t2", "u8", 6.0, "t1", A.mult, A.add)
+    cs("c1", "t2", "c23", -10.0, A.add, A.add)
+    when("mats")
+    for i, (x, v) in enumerate((("c1", "v1"), ("c23", "v2"), ("c23", "v3"))):
+        eq(T.AW[:, 144 * i:144 * i + 130], 1, 130, x, v, [("AW", i)])
+    ts(T.Q[:, 0:128], T.JP[:], col("gam"), col("al"), A.mult, A.add, ["JP", ("c", "gam"), ("c", "al")], ["Q1"], 64)
+    tt(T.Q[:, 128:256], T.Q[:, 0:128], T.JP[:], A.mult, ["Q1", "JP"], ["Q2"], 256)
+    ts(T.Q[:, 0:128], T.BG[:], col("g16"), None, A.is_equal, None, ["BG", ("c", "g16")], ["Q1"], 64)
+    ts(T.Q[:, 256:384], T.Q[:, 128:256], col("be"), None, A.add, None, ["Q2", ("c", "be")], ["Q3"], 64)
+    for j, x in ((0, "e0"), (15, "e15")):
+        ac(T.Q[:, 256 + j:384:16], X_(0, 8), ["XF", ("c", x), "Q3"], [("Q3", j)], 8, scale=0.0, bias=col(x))
+    tt(T.Q[:, 128:256], T.Q[:, 256:384], T.Q[:, 0:128], A.mult, ["Q1", "Q3", ("Q3", 0), ("Q3", 15)], ["Q2"], 256)
+    ts(T.SEL[:], X_(0, 8), col("hm"), col("h5"), A.is_equal, A.add, ["XF", ("c", "hm"), ("c", "h5")], ["SEL"], 8)
+    for m in (0, 1, 2, 3, 4, 6):
+        ac(T.PEN[:, 128 * m:128 * m + 128], T.Q[:, 128:256], ["Q2", "SEL"], [("PEN", m)], 128, scale=T.SEL[:, m:m + 1])
+    eq(T.SW[:], 16, 144, "g16", 64.0, ["SW"])
+    when("late")
+    if not EARLY:
+        cs("cq", "u8", "g16", None, A.add)
+        cs("mq", "r7", 0.0, None, A.is_equal)
+        eq(T.QW[:], 14, 144, "cq", "mq", ["QW"])
+    cs("m12", "row", 12.0, None, A.is_ge)
+    ts(T.TA[:, 0:4], X_(-12, 4), col("row"), 7.0, A.is_lt, A.mult, ["XF", ("c", "row")], ["TA0"], 4)
+    ts(T.TA[:, 4:8], T.TA[:, 0:4], 1.0, None, A.add, None, ["TA0"], ["TA1"], 4)
+    names.append("pw")
+    dv(lambda: g.vector.tensor_reduce(col("pw"), T.TA[:, 4:8], AxisListType.X, A.mult), ["TA1"], [("c", "pw")], 4)
+    cs("p8", "pw", "m12", 1.0 / 128, A.mult, A.mult)
+    eq(T.CWL[:], 16, 144, "g16", "p8", ["CWL"])
+    ac(T.KY[:], T.IB[:], ["IB", ("c", "m12")], ["KY"], 128, scale=col("m12"))
+    cs("n15", "row", 15.0, None, A.is_lt)
+    ts(T.SH[:], T.V1[:], -1.0, col("n15"), A.is_equal, A.mult, ["V1", ("c", "n15")], ["SH"], 64)
+    cs("f64", "row", 0.0, 1.0 / 64, A.is_equal, A.mult)
+    cs("is0", "f64", 64.0, None, A.mult)
+    ac(T.IT[:], X_(0, 128), ["XF", ("c", "f64")], ["IT"], 128, scale=col("f64"))
+    ac(T.BC[:], T.BX[:], ["BX", ("c", "is0")], ["BC"], 8, scale=col("is0"))
+    cs("r8", "row", -8.0, None, A.add)
+    ts(T.DG[:], T.JP[:], col("r8"), 65536.0, A.is_equal, A.mult, ["JP", ("c", "r8")], ["DG"], 64)
+    for x in range(2):
+        ac(T.M16[:, 8 * x:8 * x + 8], T.Q[:, 0:128:16], ["Q1"], [("M16", x)], 8)
+    for X in range(2):
+        ac(T.LO[:, 16 * X + 8:16 * X + 16], X_(0, 8), ["XF", ("c", "row")], [("LOc", X)], 8, scale=16.0, bias=col("row"))
+
+    CTt = [("CT", i) for i in range(3)]
+    when("q0")
+    cp(T.C16[0:8, :], T.C0[0:8, :], ["C0"], ["C16"], 256)
+    mms([[(P(6)[:, 0:16], T.Q0[0:8, 16 - s:144 - s], T.C16[0:8, s:256:16], 16) for s in range(16)]], ["Q0", "C16"], [B(6)])
+    cp(T.Q0L[:], P(6)[:, 0:16], [], [B(6), "Q0L"], 16)
+    when("fast")
+    op("dve", lambda: g.vector.tensor_scalar(T.U0[:, 0:256], T.LCD[:, 0:1024].indirect(T.Q0L[:]), -8.0, None, A.add),
+       [("LCD", 0), ("LCD", 1), "Q0L"], ["U0"], 0.06 + 256 * GAT, cls=0)
+    ac(T.U0[:, 256:512], T.U0[:, 0:256], ["U0"], ["U02"], 256, func=ACT.Square)
+    for i in (1, 0, 2):
+        bank = (3, 2, 3)[i]
+        o = P(bank)[:, 0:256]
+        mm([(o, T.AW[:, 144 * i + 1:144 * i + 129], T.U0[:, 0:256], 256), (o, T.AW[:, 144 * i:144 * i + 128], T.U0[:, 256:512], 256)],
+           [("AW", i), "U0", "U02"], [B(bank)])
+        ac(T.GF[:, 256 * i:256 * i + 256], o, [("c", "h5")], [B(bank), ("GF", i)], 256, bias=col("h5"))
+    when("cf")
+    for h in range(2):
+        c = slice(512 * h, 512 * h + 512)
+        cp(T.CF[0:24, c], T.CT[0:24, c], CTt, [("CF", h)], 512)
+        mm([(P(h)[:], T.RE[0:24, :], T.CF[0:24, c], 512)], ["RE", ("CF", h)], [B(h)])
+        ac(T.FF[:, c], P(h)[:], SFt, [B(h), ("FF", h)], 512, scale=T.SF[:, 0:1], bias=128.5 + 1.0 / 1024)
+
+    def pieces(o, tb, c):
+        return [(o, T.PA[:, 128 * tb:128 * tb + 128], T.FF[:, c], 512), (o, T.PB[0:24, 128 * tb:128 * tb + 128], T.CF[0:24, c], 512)]
+
+    SWC = 9216.0
+
+    def swap(o, src, unit, c, tk, j, ident):
+        n = c.stop - c.start
+        for F, nm, b in ((T.F2, "F2", 2048 + 49152 - 127.5), (T.F1, "F1", 2048 + 196608 - 511.5)):
+            if nm == "F2":
+                ac(F[:, c], src, [tk], [(nm, j)], n, scale=unit, bias=b)
+            else:
+                ts(F[:, c], src, unit, b, A.mult, A.add, [tk], [(nm, j)], n // 2)
+        return ([(o, ID(3.0 / 64), T.F2[:, c], n), (o, ID(-3.75 / 64), T.F1[:, c], n), (o, ident, src, n)],
+                [tk, ("F1", j), ("F2", j), ("ID", 1), ("ID", 2)])
+
+    PAt = ["PA", "PAc", "PB"]
+    for h in range(2):
+        c = slice(512 * h, 512 * h + 512)
+        when("env%d" % h)
+        ts(T.N16[:, c], T.LCE[:, c], -2048.0, None, A.add, None, [("LCE", h)], [("N16", h)], 512)
+        lst, rd = swap(P(6 + h)[:], T.N16[:, c], 1.0, c, ("N16", h), h, T.IS[:])
+        mm(pieces(P(6 + h)[:], 0, c) + lst, ["IS", ("FF", h), ("CF", h)] + rd + PAt, [B(6 + h)])
+        if ENV == "u16":
+            ts(T.MU[:, c], P(6 + h)[:], 64.0, 2048.0 + 64 * SWC, A.mult, A.add, [], [B(6 + h), ("MU", h)], 512)
+            for b in (2 * h, 2 * h + 1):
+                m = T.MU[:, 256 * b:256 * b + 256]
+                if b in OWN:
+                    spread([m], "u%d" % b, [("MU", h)], [("LU", b)], 192, [T.LU[:, 1024 * me + 256 * b:1024 * me + 256 * b + 256]])
+                else:
+                    relay(m, "hu%d" % b, "u%d" % b, [("MU", h)], [("LU", b)], 192)
+        for b in (2 * h, 2 * h + 1):
+            e = 256 + 1024 * b + 256 * me
+            tk = [("HE", e // 128), ("HE", e // 128 + 1)]
+            ac(T.HE[:, e:e + 256], P(6 + h)[:, 256 * (b % 2):256 * (b % 2) + 256], [], [B(6 + h)] + tk, 256, bias=HB + SWC)
+            if ENV == "f32":
+                far = [("HE", 2 + 8 * b + 2 * r + x) for r in peers for x in (0, 1)]
+                if b in OWN:
+                    spread([T.HE[:, e:e + 256]], "u%d" % b, tk, far, 384)
+                else:
+                    relay(T.HE[:, e:e + 256], "hu%d" % b, "u%d" % b, tk, far, 384)
+    when("idx")
+    for x in range(4):
+        i = io(T.IDX[:, 512 * x:512 * x + 512], [[1, 512]], 512 * (x % 2), 0, [("IDX", x)], 512)
+        ops[i]["also"] = max(j for j, o in enumerate(ops) if o["kind"] == "send")
+    when("e16")
+    c = slice(1024, 1280)
+    ts(T.N16[:, c], T.LE[:], -2048.0, None, A.add, None, ["LE"], [("N16", 2)], 256)
+    lst, rd = swap(P(5)[:, 0:256], T.N16[:, c], 1.0, c, ("N16", 2), 2, T.IS[:])
+    mm(lst, ["IS"] + rd, [B(5)])
+    for X in range(2):
+        for x in range(REP):
+            e = 128 * (REP * X + x)
+            ac(T.ER[:, e:e + 128], P(5)[:, 128 * X:128 * X + 128], [], [B(5), ("ER", X, x)], 128, bias=SWC)
+    ac(T.E16[:], P(5)[:, 0:256], [], [B(5), ("E16", 0), ("E16", 1)], 256, bias=SWC)
+    when("u")
+    for h in range(2):
+        c = slice(512 * h, 512 * h + 512)
+        ts(T.U[:, c], T.LCD[:, c], -8.0, None, A.add, None, [("LCD", h)], [("U", h)], 512)
+        ac(T.U2[:, c], T.U[:, c], [("U", h)], [("U2", h)], 512, func=ACT.Square)
+    TB = (T.TB0, T.TB1, T.TB2)
+    when("tb")
+    for i in (1, 0, 2):
+        for h in range(2):
+            c, bank = slice(512 * h, 512 * h + 512), 6 + h
+            o = P(bank)[:]
+            lst = [(o, T.AW[:, 144 * i + 1:144 * i + 129], T.U[:, c], 512), (o, T.AW[:, 144 * i:144 * i + 128], T.U2[:, c], 512)]
+            mm(lst + (pieces(o, i, c) if i else []), [("AW", i), ("U", h), ("U2", h), ("FF", h), ("CF", h)] + PAt, [B(bank)])
+            ac(TB[i][:, c], o, [("c", "h5")], [B(bank), ("TB", i, h)], 512, bias=col("h5"))
+        dma("sp", TB[i][:, 1024:2048], TB[i][:, 0:1024], [("TB", i, 0), ("TB", i, 1)], [("TB", i, 2), ("TB", i, 3)], 256)
+    when("conv")
+    for b in range(4 if ENV == "u16" else 0):
+        for r in peers:
+            e, l = 256 + 1024 * b + 256 * r, 1024 * r + 256 * b
+            ts(T.HE[:, e:e + 256], T.LU[:, l:l + 256], 1.0 / 64, HB - 32, A.mult, A.add, [("LU", b)],
+               [("HE", e // 128), ("HE", e // 128 + 1)], 256)
+    when("g0")
+
+    C0 = 64.0 * 67840 + 2048
+
+    def side_at(X, side):
+        return 64 * (side if X else 1 - side)
+
+    G = (T.G0, T.G1, T.HK)
+
+    def tile(i, X):
+        a = 256 * X + 128 if i == 2 else 128 * X
+        return G[i][:, a:a + 128]
+
+    def names_of(t, X):
+        part(("T", X) if t else None)
+        wide = 2048 if t else 1024
+        q, qt = (T.Z16[:, 16 * X:16 * X + 8], ("Z16", X)) if t else (T.Q0L[:, 8 * X:8 * X + 8], "Q0L")
+        for i in (1, 0, 2) if t else (1, 2):
+            ag(tile(i, X), TB[i][:, 0:wide].indirect(q), [("TB", i, h) for h in range(wide // 512)] + [qt], [("G", i, X)], 128)
+        ag(T.GZ[:, 128 * X:128 * X + 128], T.ZT[:, 0:wide].indirect(q), [("ZT", h) for h in range(wide // 1024)] + [qt],
+           [("GZ", X)], 128)
+
+        def rows(i):
+            if t:
+                return tile(i, X), ("G", i, X)
+            return T.GF[:, 256 * i + 128 * X:256 * i + 128 * X + 128], ("GF", i)
+
+        tb = P(2 + X)
+        if t:
+            part(("W", X))
+            c, o, tt_ = slice(128 * X, 128 * X + 128), tb[:, 128:256], t % 4
+            lst, rd = [(o, T.IH[:], T.E16[:, c], 128)], ["IH", ("E16", X)]
+            if tt_:
+                ts(T.WR[:, c], T.E16[:, c], 16.0 * tt_ - 32, 64.0, A.is_lt, A.mult, [("E16", X)], [("WR", X)], 64)
+                lst.append((o, T.IH[:], T.WR[:, c], 128))
+                rd.append(("WR", X))
+            part(("W2", X))
+            mm(lst, rd, [B(2 + X)])
+            for x in range(REP):
+                e = 128 * (REP * X + x)
+                ac(T.ER[:, e:e + 128], o, [], [B(2 + X), ("ER", X, x)], 128, bias=-16.0 * tt_)
+        part(("T1", X))
+        ERt = [("ER", X, x) for x in range(REP)]
+        for i in range(4):
+            ks = range(4 * i, 4 * i + 4)
+            bank = (0, 1, 4 + X, 1 - X)[i]
+            mms([[(P(bank)[:, 128 * (k % 4):128 * (k % 4) + 128], T.PEN[:, 128 * KT[k][1]:128 * KT[k][1] + 128], rows(KT[k][0])[0], 128)]
+                 for k in ks], [("PEN", KT[k][1]) for k in ks] + [rows(KT[k][0])[1] for k in ks], [B(bank)])
+            wd = 128 * REP
+            for x in range(4 // REP):
+                y0 = 2048 * X + 512 * i + wd * x
+                tt(T.Y[:, y0:y0 + wd], P(bank)[:, wd * x:wd * x + wd], T.ER[:, wd * X:wd * X + wd], A.min, ERt,
+                   [B(bank), ("Y", X, i, x)], wd)
+            lst, o = [], tb[:, side_at(X, i // 2):side_at(X, i // 2) + 64]
+            for k in ks:
+                for u in range(2):
+                    s, y0 = 8 * u + k % 8, 2048 * X + 128 * k
+                    lst.append((o, T.SW[:, 16 - s:144 - s], T.Y[:, y0 + u:y0 + 128:2], 64))
+            mm(lst, ["SW"] + [("Y", X, i, x) for x in range(4 // REP)], [B(2 + X)], i % 2 == 0, i % 2 == 1)
+        ts(T.TL[:, 128 * X:128 * X + 128], tb[:, 0:128], C0, None, A.add, None, [], [B(2 + X), ("TL", X)], 128)
+
+    def record(t, X):
+        part(("R", X))
+        o = P(7)[:, 128 * X:128 * X + 128]
+        e = T.E16[:, 128 * X:128 * X + 128]
+        mm([(o, T.IH[:], e, 128), (o, T.KY[:], tile(1, X), 128)], ["IH", "KY", ("E16", X), ("G", 1, X)], [B(7)])
+        ap, tk = env_at(T, t, me, X)
+        ac(ap, o, [], [B(7), tk], 128, bias=HB)
+        relay(ap, "h%d" % (2 * t + X), "e%d" % (2 * t + X), [tk], [env_at(T, t, r, X)[1] for r in peers], 192)
+
+    def high(X):
+        return T.HK[:, 256 * X:256 * X + 128]
+
+    def outcomes(t, X):
+        part(("O", X))
+        o, l = P(6)[:, 0:8], T.T0L[:, 8 * X:8 * X + 8]
+        if EARLY:
+            mm([(o, T.SW[:, 16 - s:144 - s], T.Y[:, 2048 * X + s:2048 * X + 128:16], 8) for s in range(16)], ["SW", ("Y", X, 0, 0)], [B(6)])
+            c0 = C0
+        else:
+            if AF16:
+                a = side_at(X, 0)
+                ac(T.T16[:, 64 * X:64 * X + 64], P(2 + X)[:, a:a + 64], [], [B(2 + X), ("T16", X)], 64, bias=C0 - 2048)
+            else:
+                ts(T.T16[:, 64 * X:64 * X + 64], T.TL[:, 64 + 64 * X:128 + 64 * X], -2048.0, None, A.add, None, [("TL", X)], [("T16", X)], 32)
+            mm([(o, T.QW[:, 14 - 2 * a:142 - 2 * a], T.T16[:, 64 * X + a:64 * X + 64:8], 8) for a in range(8)], ["QW", ("T16", X)], [B(6)])
+            c0 = 2048.0
+        ts(l, o, c0, None, A.add, None, [], [B(6), ("T0L", X)], 8)
+        ac(T.HI[:, 16 * X + 8:16 * X + 16], o, [], [B(6), ("HIl", X)], 8, bias=c0 + 128 + 128 * X)
+        e = 256 + 1024 * t
+        ag(high(X), T.HE[:, e:e + 4096].indirect(l), [("HE", e // 128 + x) for x in range(32)] + [("T0L", X)], [("HA", X)], 128)
+        mm([(P(6)[:, 16:32], T.CWL[:, 16 - s:144 - s], T.HK[:, 256 * X + s:256 * X + 256:16], 16) for s in range(16)],
+           ["CWL", ("HA", X), ("G", 2, X)], [B(6)])
+        ac(T.HI[:, 16 * X:16 * X + 8], P(6)[:, 16:24], [], [B(6), ("HIq", X)], 8, bias=1024.0 - 585 * HB / 128)
+        ac(T.LO[:, 16 * X:16 * X + 8], P(6)[:, 24:32], [], [B(6), ("LOq", X)], 8)
+
+    def bound(t, X):
+        part(("E", X))
+        o = P(7)[:, 256 + 128 * X:384 + 128 * X]
+        e = T.E16[:, 128 * X:128 * X + 128]
+        mm([(o, T.SH[:], e, 128), (o, T.IB[:], T.IT[:], 128), (o, T.IB[:], high(X), 128)],
+           ["SH", "IB", "IT", ("E16", X), ("HA", X)], [B(7)])
+        c, b = 1024 * t + 128 * (1 - X), 2 * (t % 4) + X
+        ac(T.HE[:, c:c + 128], o, ["BC"], [B(7), ("HE", c // 128)], 128, bias=T.BC[:, b:b + 1])
+
+    def values(t, X):
+        part(("V", X))
+        win, wt = T.HV[:, 1024 * t:1024 * t + 4096], [("HV", 8 * t + x) for x in range(32)]
+        sb = P(4 + X)
+        mm([(sb[:, 0:128], T.CK[0:1, 0:128], T.CK[0:1, 128:256], 128)], CKt, [B(4 + X)], True, False)
+        for h in range(2):
+            j, la, lb = 2 * X + h, 128 * X + 32 * h + side_at(X, 0), 128 * X + 32 * h + side_at(X, 1)
+            c = slice(512 * j, 512 * j + 512)
+            ag(T.GA[:, c], win.indirect(T.TL[:, la:la + 32]), wt + [("TL", X)], [("GA", j)], 512)
+            dg(T.GB[:, c], win.indirect(T.TL[:, lb:lb + 32]), T.GA[:, c], A.max, wt + [("TL", X), ("GA", j)], [("GB", j)], 512)
+            mm([(sb[:, 64 * h:64 * h + 64], T.IB[:], T.GB[:, 512 * j + p:512 * j + 512:8], 64) for p in range(8)],
+               ["IB", ("GB", j)], [B(4 + X)], False, h == 1)
+        c, o = slice(128 * X, 128 * X + 128), sb[:, 0:128]
+        ac(T.FB[:, c], o, [], [B(4 + X), ("FB", X)], 128, bias=-127.5)
+        if t < S - 1:
+            h0 = 4096 + 1024 * t + 256 * me + 128 * X
+            w, tk = T.HV[:, h0:h0 + 128], ("HV", h0 // 128)
+        else:
+            w, tk = T.W5[:, c], ("W5", X)
+        tt(w, o, T.FB[:, c], A.subtract, [("FB", X)], [B(4 + X), tk], 128)
+        if t < S - 1:
+            spread([w], "w%d" % (2 * t + X), [tk], [("HV", (h0 + 256 * (r - me)) // 128) for r in peers], 96)
+        o = sb[:, 128:256]
+        mm([(o, ID(-1.0), T.GZ[:, c], 128), (o, T.IB[:], w, 128)], [("ID", 0), "IB", tk, ("GZ", X)], [B(4 + X)])
+        ac(T.YS[:, c], o, [], [B(4 + X), ("YS", X)], 128, bias=0.5, func=ACT.Sign)
+        part(("D", X))
+        if t == S - 1:
+            dma("sp", T.yx[:, 1280 + 128 * X:1408 + 128 * X], w, [tk], [], 32)
+        elif X == 1:
+            dma("sp", T.yx[:, 256 * t:256 * t + 256], T.HV[:, h0 - 128:h0 + 128], [tk, ("HV", h0 // 128 - 1)], [], 64)
+
+    def choose(t, X):
+        part(("C", X))
+        o, c, sb = P(4 + X)[:, 256:272], slice(16 * X, 16 * X + 16), B(4 + X)
+        mm([(o, T.Q[:, 0:128], T.M16[:], 16), (o, T.YS[:, 128 * X:128 * X + 128], T.O16[:], 16)],
+           ["Q1", ("M16", 0), ("M16", 1), "O16", ("YS", X)], [sb])
+        ac(T.VR[:, c], o, [], [sb, ("VR", X)], 16, bias=-16.0, func=ACT.Relu)
+        o = P(4 + X)[:, 272:288]
+        if AF16:
+            mm([(o, T.IH[:], T.LO[:, c], 16), (o, T.DG[:], T.VR[:, c], 16)], ["DG", "IH", ("VR", X), ("LOc", X), ("LOq", X)], [sb])
+            tt(T.Z2[:, c], o, T.HI[:, c], A.min, [("HIl", X), ("HIq", X)], [sb, ("Z2", X)], 16)
+        else:
+            mm([(o, T.DG[:], T.VR[:, c], 16)], ["DG", ("VR", X)], [sb])
+            tt(T.Z1[:, c], o, T.LO[:, c], A.max, [("LOc", X), ("LOq", X)], [sb, ("Z1", X)], 16)
+            tt(T.Z2[:, c], T.Z1[:, c], T.HI[:, c], A.min, [("Z1", X), ("HIl", X), ("HIq", X)], [("Z2", X)], 32)
+        cp(T.Z16[:, c], T.Z2[:, c], [("Z2", X)], [("Z16", X)], 16)
+        src = T.HE[:, 1024 * t:1024 * t + 4352].indirect(T.Z16[:, 16 * X + 8:16 * X + 16])
+        a = 1024 * t + 128 * (1 - X)
+        src = T.HE[:, a:1024 * t + 4352].indirect(T.Z16[:, 16 * X + 8:16 * X + 16])
+        rd = [("HE", 8 * t + x) for x in range(1 - X, 34)] + [("Z16", X), ("HA", X)]
+        ha, c = high(X), slice(128 * X, 128 * X + 128)
+        dg(T.E16[:, c], src, ha, A.subtract, rd, [("E16", X)], 128)
+        if t < S - 1:
+            return
+        part(None)
+        o = P(2 + X)[:, 256:384]
+        lst, rd = swap(o, T.E16[:, c], 64.0, c, ("E16", X), 3 + X, T.IH[:])
+        mm(lst, ["IH"] + rd, [B(2 + X)])
+        ac(T.OUT[:, c], o, [], [B(2 + X), ("OUT", X)], 128, scale=64.0, bias=2048.0 + 64 * SWC)
+        dma("sp", T.ye[:, c], T.OUT[:, c], [("OUT", X)], [], 64)
+        ag(T.YC[:, c], T.IDX[:, 0:2048].indirect(T.Z16[:, 16 * X:16 * X + 8]), [("IDX", x) for x in range(4)] + [("Z16", X)],
+           [("YC", X)], 128)
+        dma("act", T.yc[:, c], T.YC[0:128:16, c], [("YC", X)], [], 4)
+
+    role[2] = -1
+    names_of(0, 0)
+    names_of(0, 1)
+    for t in range(S):
+        role[2] = t
+        for X in range(2 if t < S - 1 else 0):
+            record(t, X)
+        for X in range(2):
+            outcomes(t, X)
+            bound(t, X)
+        for X in range(2):
+            values(t, X)
+            choose(t, X)
+            if t < S - 1:
+                names_of(t + 1, X)
     return ops
+
+
+def helper_program(g, core, T, topo, r):
+    peers = [(r + k) % N for k in (1, 2, 3)]
+    es = topo.engines(core, T.cores[peers[0]])
+    full = sum(1 << e for e in es)
+    n_in = len(inner_engines(topo, T.cores[r], T.cores[peers[0]]))
+    ids = [dst_id(topo, T.cores[p]) for p in peers]
+    jobs = [("hu%d" % b, "u%d" % b, T.MU[:, 256 * b:256 * b + 256], T.LU[:, 1024 * r + 256 * b:1024 * r + 256 * b + 256])
+            for b in range(4) if b not in OWN]
+    if ENV == "f32":
+        jobs = [("hu%d" % b, "u%d" % b) + 2 * (T.HE[:, 256 + 1024 * b + 256 * r:512 + 1024 * b + 256 * r],)
+                for b in range(4) if b not in OWN]
+    jobs = [("hv%d" % b, "v%d" % b) + 2 * (T.HV[:, 1024 * b + 256 * r:1024 * b + 256 * r + 256],)
+            for b in range(4) if b not in VOWN] + jobs
+    for i in range(2 * (S - 1)):
+        ap = env_at(T, i // 2, r, i % 2)[0]
+        jobs.append(("h%d" % i, "e%d" % i, ap, ap))
+    for got, sem, src, dst in jobs:
+        g.wait_ge(T.sem[got], n_in)
+        g.remote_dma_fused([RemoteDMATransfer(dst_ids=ids, dma_engine_mask=full, remote_sem=T.sem[sem], srcs=[src],
+                                              dsts=[dst, dst, dst])], local_sem=T.sem.sent)
+    g.wait_ge(T.sem.sent, len(jobs) * len(es))
 
 
 def arrange(ops):
@@ -559,17 +686,20 @@ def arrange(ops):
             if k in lastw:
                 raw.add(lastw[k])
         for k in o["wr"]:
+            into = other if isinstance(k, tuple) and k[0] == "B" else raw
             if k in lastw:
-                other.add(lastw[k])
-            other.update(readers.get(k, ()))
+                into.add(lastw[k])
+            into.update(readers.get(k, ()))
         for k in o["rd"]:
             readers.setdefault(k, []).append(i)
         for k in o["wr"]:
             lastw[k] = i
             readers[k] = []
-        o["raw"], o["dep"] = raw, (raw | other) - {i}
-        if o["kind"] == "recv":
+        o["raw"], o["dep"] = raw - {i}, (raw | other) - {i}
+        if "after" in o:
             o["dep"] = o["dep"] | {o["after"]}
+        if o.get("also") is not None:
+            o["dep"] = o["dep"] | {o["also"]}
     if "t0" not in PLAN:
         PLAN["end"], PLAN["t0"] = search(ops)
     for i in range(n):
@@ -582,6 +712,8 @@ def search(ops):
 
     def gap(i, d):
         p = ops[d]
+        if ops[i].get("also") == d:
+            return p["dur"]
         if p["eng"] == ops[i]["eng"] and p["kind"] == "c" and ops[i]["kind"] == "c" and d not in ops[i]["raw"]:
             return p["dur"] + 0.001
         return p["dur"] + p["lat"] + HOP
@@ -643,14 +775,11 @@ def search(ops):
     pools = ([i for i, x in enumerate(names) if x[0] != "once"], [i for i, x in enumerate(names) if x[0] == "once"])
     top = max(prio)
     base = [top - p for p in prio]
-    first = min(base[i] for i in range(n) if ops[i]["wr"] and ops[i]["wr"][-1][0] == "V" and ops[i]["role"][0] != "once")
     for i, o in enumerate(ops):
-        if o["role"][0] != "once":
-            k = o["wr"][-1] if o["wr"] else o["rd"][0]
-            k = (k[0], k[1] % 2 if k[0] == "PV" else k[2] % 2 if k[0] == "H" else k[2] if k[0] == "WS" else k[1], o["eng"])
-            base[i] = first + PERIOD * o["step"] + AIM.get(k, 99.0)
-        elif o["step"]:
-            base[i] += first + PERIOD * S - top + 8.0
+        if "aim" in o:
+            base[i] = FIRST + PERIOD * o["step"] + o["aim"]
+        else:
+            base[i] = FIRST + PERIOD * S if o["step"] > 0 else o["at"]
 
     def queue_links(t0):
         prev, last = {}, {}
@@ -684,7 +813,7 @@ def search(ops):
                 o2[rid[a]] += x
         else:
             pool = pools[0] if rnd() < 0.7 else pools[1]
-            amp = (0.6, 2.0, 6.0)[int(rnd() * 3)]
+            amp = (0.3, 1.0, 3.0)[int(rnd() * 3)]
             for _ in range(1 + int(rnd() * 3)):
                 o2[pool[int(rnd() * len(pool))]] += amp * (rnd() + rnd() - 1.0)
         e2, t2 = place([base[i] + o2[rid[i]] for i in range(n)])
@@ -706,11 +835,16 @@ def emit(g, T, ops, seq):
             o["mark"], o["clock"] = (o["sem"], o["cnt"]), {}
             total[o["sem"]] = o["cnt"]
             continue
+        if o["kind"] == "land":
+            o["mark"], o["clock"] = ops[o["after"]]["mark"], ops[o["after"]]["clock"]
+            continue
         e, kn = o["eng"], known[o["eng"]]
         need = {}
         for d in o["dep"]:
             p = ops[d]
             if p["kind"] == "c" and o["kind"] == "c" and p["eng"] == e and d not in o["raw"]:
+                continue
+            if p["kind"] == "send":
                 continue
             s, n = p["mark"]
             if need.get(s, (0, None))[0] < n:
@@ -747,6 +881,9 @@ def emit(g, T, ops, seq):
 def rank_program(g, core, T, topo):
     me = T.rank_of(core)
     if me is None:
+        for r, c in enumerate(T.cores):
+            if helper_of(c, topo) == core:
+                helper_program(g, core, T, topo, r)
         return
     ops = build_ops(g, T, topo, core, me)
     seq, _ = arrange(ops)

@@ -7,7 +7,10 @@ REP = 2
 HB = 17408.0
 ENV = "u16"
 EARLY = False
-AF16 = True
+ON_SCALAR = {("TL", 0, 0), ("WR", 1), ("T0L", 0), ("T0L", 1), ("N16", 0), ("N16", 1), ("N16", 2), ("U", 0), ("U", 1), ("CF", 1),
+             ("FB", 0), ("FB", 1)} | {("ER", X, x) for X in range(2) for x in range(REP)}
+ON_VECTOR = set()
+FUSED = (0,)
 OWN = (0, 2, 3)
 VOWN = (0, 1)
 KT = [(1, m) for m in range(5)] + [(0, m) for m in (0, 1, 2)] + [(2, m) for m in range(5)] + [(0, m) for m in (3, 4, 6)]
@@ -20,23 +23,23 @@ def _sb(cols, dtype):
 SCRATCH = {
     "HV": _sb(9216, BF), "HE": _sb(9472, F32), "W5": _sb(256, BF),
     "LCD": _sb(1024, I32), "LCE": _sb(1024, I32), "LE": _sb(256, I32), "CT": _sb(1024, I32), "C0": _sb(256, I32),
-    "U": _sb(1024, BF), "U2": _sb(1024, BF), "CF": _sb(1024, F16), "C16": _sb(256, F16), "FF": _sb(1024, BF),
+    "U": _sb(1024, BF), "U2": _sb(1024, BF), "CF": _sb(1024, F16), "C16": _sb(256, F16), "FF": _sb(1024, F16),
     "N16": _sb(1280, F16), "MU": _sb(1024, U16), "LU": _sb(4096, U16),
     "TB0": _sb(2048, BF), "TB1": _sb(2048, BF), "TB2": _sb(2048, BF), "ZT": _sb(2048, BF), "IDX": _sb(2048, F32),
-    "ER": _sb(256 * REP, F32), "G0": _sb(256, BF), "G1": _sb(256, BF), "HK": _sb(512, BF), "GZ": _sb(256, BF),
+    "ER": _sb(256 * REP, F16), "SG": _sb(256, BF), "OW": _sb(512, F32), "EO": _sb(512, F16), "G0": _sb(256, BF), "G1": _sb(256, BF), "HK": _sb(512, BF), "GZ": _sb(256, BF),
     "E16": _sb(256, F16), "WR": _sb(256, F16), "F1": _sb(1280, BF), "F2": _sb(1280, BF), "VR": _sb(32, BF),
-    "Q0L": _sb(16, U16), "U0": _sb(512, BF), "GF": _sb(768, BF), "BX": _sb(8, BF), "DG": _sb(128, BF), "M16": _sb(16, BF), "O16": _sb(16, BF),
+    "IN": _sb(128, F16), "C4": _sb(128, F16), "Q4": _sb(144, F16), "Q0L": _sb(16, U16), "U0": _sb(512, BF), "GF": _sb(768, BF), "BX": _sb(8, BF), "DG": _sb(128, BF), "M16": _sb(16, BF), "O16": _sb(32, BF),
     "Y": _sb(4096, F16), "TL": _sb(256, U16), "T16": _sb(128, F16), "T0L": _sb(16, U16),
-    "HI": _sb(32, F32), "LO": _sb(32, F16 if AF16 else F32), "Z1": _sb(32, F32), "Z2": _sb(32, F32), "Z16": _sb(32, U16),
+    "HI": _sb(32, F32), "LO": _sb(32, F16), "Z1": _sb(32, F32), "Z2": _sb(32, F32), "Z16": _sb(32, U16),
     "GA": _sb(2048, BF), "GB": _sb(2048, BF), "FB": _sb(256, BF), "YS": _sb(512, BF),
     "OE": _sb(256, F32), "OUT": _sb(256, F32), "YC": _sb(256, F32),
-    "PI": _sb(1, I32), "PJ": _sb(8, I32), "PC": _sb(48, F32), "XF": _sb(176, BF), "V1": _sb(128, BF), "JP": _sb(128, BF),
+    "PI": _sb(1, I32), "PJ": _sb(8, I32), "PC": _sb(64, F32), "XF": _sb(176, BF), "V1": _sb(128, BF), "JP": _sb(128, BF),
     "BG": _sb(128, BF), "VA": _sb(384, BF), "V2": _sb(128, BF), "VQ": _sb(144, BF), "TA": _sb(8, F32), "SEL": _sb(8, F32),
     "Q": _sb(384, BF), "PEN": _sb(896, BF), "SW": _sb(144, F16), "CWL": _sb(144, BF), "QW": _sb(144, F16), "VW": _sb(144, BF),
-    "Q0": _sb(144, F16), "AW": _sb(3 * 144, BF), "CR": _sb(3 * 144, BF), "PA": _sb(384, BF), "PA0": _sb(384, BF),
-    "PA1": _sb(384, BF), "PB": _sb(384, F16), "RE": _sb(128, F16), "IB": _sb(128, BF), "ID": _sb(640, BF), "IH": _sb(128, F16),
+    "Q0": _sb(144, F16), "AW": _sb(3 * 144, BF), "PA0": _sb(384, F16),
+    "PA1": _sb(384, F16), "RE": _sb(128, F16), "IB": _sb(128, BF), "ID": _sb(640, BF), "IH": _sb(128, F16),
     "IS": _sb(128, F16), "SH": _sb(128, F16), "KY": _sb(128, BF), "IT": _sb(128, BF), "BC": _sb(8, F32), "CK": _sb(256, BF),
-    "SF": _sb(1, F32),
+    "SF": _sb(2, F32),
 }
 for _b in range(8):
     SCRATCH["P%d" % _b] = ("psum", [128, 512], F32)
@@ -45,25 +48,27 @@ SEMAPHORES = (["pe", "act", "dve", "pool", "sent"] + ["d%d" % i for i in range(N
               + ["%s%d" % (x, i) for x in ("w", "e", "h") for i in range(10)] + ["%s%d" % (x, i) for x in ("u", "hu", "v", "hv") for i in range(4)])
 
 CYC, GAT, PEC, HOP, LAT, RATE, LOCAL = 1.0e-3, 1.45e-3, 0.5e-3, 0.09, 2.7, 80.0, 250.0
-CASES = ((1.0, 1.0, 1.0, 0.0), (0.75, 0.9, 0.9, 0.7), (1.2, 1.1, 1.2, -0.3))
-ROUNDS, HEAT, SEED, PLAN = 10000, 0.1, 1, {}
-PERIOD, FIRST = 10.8, 15.5
-START = {"x01": 0.0, "codes": 0.1, "x23": 0.2, "ce0": 0.3, "ce1": 0.4, "cd": 0.5, "e": 0.6, "z": 6.0, "send": 0.0, "iota": 0.0,
-         "idx": 12.0, "early": 0.1, "cols": 2.7, "mats": 6.3, "late": 12.0, "q0": 6.0, "cf": 3.0, "env0": 4.5, "env1": 5.6,
-         "fast": 8.0, "e16": 8.2, "u": 13.3, "tb": 16.0, "conv": 17.0, "g0": 17.0}
+CASES = ((1.0, 1.0, 1.0, 0.0, 1.0), (0.75, 0.9, 0.9, 0.7, 1.4), (1.2, 1.1, 1.1, -0.3, 0.8))
+ROUNDS, HEAT, SEED, PLAN = 20000, 0.04, 1, {}
+PERIOD, FIRST = 10.4, 16.5
+START = {"x01": 0.0, "codes": 0.1, "x23": 0.2, "ce0": 0.3, "ce1": 0.4, "cd": 0.5, "e": 0.6, "z": 6.0, "send": 2.6, "iota": 0.0,
+         "iota2": 2.9, "idx": 12.0, "early": 0.1, "cols": 0.5, "mats": 4.6, "late": 9.5, "q0": 4.5, "cf": 1.0, "env0": 1.5,
+         "env1": 2.0, "fast": 5.0, "e16": 5.5, "u": 11.5, "tb": 13.5, "conv": 16.0, "g0": 15.0, "t0": 4.2}
 
 
 def _mins(a):
-    return [a + 0.6 * i + x for i in range(4) for x in [-0.5] + [0.3 * y * REP / 2 for y in range(4 // REP)] + [0.7]] + [a + 2.8]
+    return [a + 0.6 * i + x for i in range(4)
+            for x in [-1.2] + [0.3 * y * REP / 2 for y in range(4 // REP)] + [1.0] + [1.3] * (0, 2, 0, 1)[i]]
 
 
-AIM = {("V", 0): [-1.0, 0.0, 0.9, 1.7, 0.8, 1.8, 2.5, 2.9, 3.3, 3.4, 3.5, 3.5, 3.7],
-       ("V", 1): [0.0, 2.0, 2.9, 3.4, 2.95, 3.6, 4.4, 4.7, 4.9, 5.0, 5.1, 5.2, 5.4],
-       ("C", 0): [3.9, 4.0, 4.1, 4.45, 4.5, 4.6, 4.95], ("C", 1): [5.6, 5.7, 5.8, 6.6, 6.9, 7.2, 7.5],
-       ("T", 0): [4.7, 5.0, 5.6, 7.0], ("T", 1): [7.3, 7.5, 7.9, 8.4], ("W", 0): [5.2], ("W", 1): [7.8],
-       ("W2", 0): [5.3, 5.35], ("W2", 1): [7.9, 8.0], ("T1", 0): _mins(5.9), ("T1", 1): _mins(8.9)[:-1] + [12.55],
-       ("R", 0): [-4.0], ("R", 1): [-2.0], ("O", 0): [-0.9, -0.8, -0.3, 1.6, 1.6, 1.9, 2.8],
-       ("O", 1): [2.6, 2.7, 3.5, 3.8, 3.8, 4.6], ("E", 0): [1.9, 2.8], ("E", 1): [5.0],
+AIM = {("V", 0): [-0.3, 0.0, 0.9, 1.8, 0.8, 1.7, 2.6, 3.0, 3.3, 3.6, 4.2, 3.5],
+       ("V", 1): [1.0, 1.6, 2.5, 3.5, 2.4, 3.75, 4.6, 5.0, 5.25, 5.5, 6.2, 5.5],
+       ("C", 0): [3.8, 4.0, 4.2, 4.55, 4.7], ("C", 1): [5.8, 6.0, 6.2, 6.4, 6.7],
+       ("T", 0): [4.7, 5.2, 6.0], ("T", 1): [6.6, 6.9, 7.2], ("W", 0): [5.0], ("W", 1): [7.0],
+       ("W2", 0): [5.15, 5.4, 5.6], ("W2", 1): [7.2, 7.5, 7.7], ("T1", 0): _mins(5.9), ("T1", 1): _mins(8.6),
+       ("R", 0): [-2.0, -1.8, -1.6, -1.0], ("R", 1): [-1.2, -1.0, -0.8, 0.0],
+       ("O", 0): [-1.3, -0.9, -0.8, -0.7, -0.4, -0.2, 2.0, 3.4], ("O", 1): [3.6, 3.9, 4.0, 4.1, 4.4, 4.6, 4.9, 5.3],
+       ("E", 0): [1.5, 3.5], ("E", 1): [4.6, 5.9], ("L", 0): [-0.5], ("L", 1): [4.0],
        ("D", 0): [6.0], ("D", 1): [7.0]}
 
 
@@ -105,6 +110,8 @@ def build_ops(g, T, topo, core, me):
         if role[0] is not None:
             a = AIM[role[0]]
             kw["aim"] = a[min(role[1], len(a) - 1)] + 0.001 * role[1]
+            if role[2] < 0:
+                kw["role"], kw["at"] = ("once", len(ops)), START["t0"] + kw.pop("aim")
         else:
             kw["at"] = now[0]
             now[0] += 0.002
@@ -138,7 +145,14 @@ def build_ops(g, T, topo, core, me):
         f = func if func is not None else (ACT.Identity if kw else ACT.Copy)
         return op("act", lambda: g.scalar.activation(out, in_, f, **kw), rd, wr, 0.06 + n * CYC)
 
+    def lin(key, out, in_, a, b, rd, wr, n):
+        if key in ON_SCALAR:
+            return ac(out, in_, rd, wr, n, scale=a, bias=b)
+        return ts(out, in_, a, b, A.mult, A.add, rd, wr, n)
+
     def ag(out, src, rd, wr, n):
+        if wr[-1] in ON_VECTOR:
+            return op("dve", lambda: g.vector.tensor_copy(out, src), rd, wr, 0.06 + n * GAT, cls=0)
         return op("act", lambda: g.scalar.activation(out, src, ACT.Copy), rd, wr, 0.06 + n * GAT, cls=0)
 
     def dg(out, src, in1, o, rd, wr, n):
@@ -239,10 +253,11 @@ def build_ops(g, T, topo, core, me):
 
     when("iota")
     io(T.PI[:], [[0, 1]], 0, 1, ["PI"], 1, flag=False)
-    io(T.VA[:], [[-1, 24], [-32, 16]], 416, 1, ["VA"], 384)
-    io(T.V2[:], [[0, 4], [-1, 32]], 0, 1, ["V2"], 128)
+    io(T.VA[:], [[-1, 24], [-1000, 4], [-32, 4]], 2999, 1, ["VA"], 384)
+    io(T.V2[0:32, :], [[0, 4], [-1, 32]], 1, 1, ["V2"], 128)
     io(T.V1[:], [[-1, 128]], 0, 1, ["V1"], 128)
     io(T.XF[:], [[1, 176]], -16, 0, ["XF"], 176)
+    when("iota2")
     io(T.VQ[0:8, :], [[1, 144]], -16, -16, ["VQ"], 144)
     io(T.JP[:], [[0, 8], [1, 16]], -8, 0, ["JP"], 128)
     io(T.BG[:], [[16, 8], [0, 16]], 0, 0, ["BG"], 128)
@@ -252,43 +267,45 @@ def build_ops(g, T, topo, core, me):
         return T.XF[:, 16 - d:16 - d + n]
 
     for b in range(4):
-        ms(T.SF[32 * b:32 * b + 32, :], 0.125 ** (b + 1) if b < 3 else 0.0, [("SF", b)], 1)
-    SFt = [("SF", b) for b in range(4)]
+        ms(T.SF[32 * b:32 * b + 32, 0:1], 0.125 ** b, [("SF", b)], 1)
+    ms(T.SF[:, 1:2], 1535.5 + 1.0 / 1024, [("SF", 4)], 1)
+    ms(T.SF[0:32, 1:2], 0.0, [("SF", 4)], 1)
+    SFt = [("SF", b) for b in range(5)]
     when("late")
     ms(T.CK[:, 0:128], 192.0, [("CK", 0)], 64)
     ms(T.CK[:, 128:256], 256.0, [("CK", 1)], 64)
     CKt = [("CK", 0), ("CK", 1)]
-    ms(T.O16[:], -1.0 / 16, ["O16"], 8)
+    ms(T.O16[:, 0:16], -1.0 / 16, ["O16"], 8)
+    ms(T.O16[:, 16:32], -1.0 / 8, ["O16"], 8)
     io(T.BX[:], [[16, 4], [2, 2]], 4 * me - 32, 0, ["BX"], 8)
     ts(T.IH[:], T.V1[:], 0.0, None, A.is_equal, None, ["V1"], ["IH"], 64)
+    if ("WR", 0) in ON_SCALAR or ("WR", 1) in ON_SCALAR:
+        ts(T.IN[:], T.V1[:], 0.0, -32.0, A.is_equal, A.mult, ["V1"], ["IN"], 64)
     when("early")
     ts(T.RE[0:32, :], T.V2[0:32, :], 0.0, None, A.is_equal, None, ["V2"], ["RE"], 64)
-    ts(T.PA0[0:96, :], T.VA[0:96, :], 0.0, 128.0, A.is_equal, A.mult, ["VA"], ["PA0"], 192)
-    ts(T.PA1[0:96, :], T.VA[0:96, :], 32.0, -1024.0, A.is_equal, A.mult, ["VA"], ["PA1"], 192)
-    ts(T.PB[0:32, :], T.VA[0:32, :], 32.0, 128.0, A.is_equal, A.mult, ["VA"], ["PB"], 192)
-    tt(T.PA[0:96, :], T.PA0[0:96, :], T.PA1[0:96, :], A.add, ["PA0", "PA1"], ["PA"], 768)
-    ms(T.PA[96:128, :], 0.0, ["PAc"], 192)
+    ts(T.PA0[:], T.VA[:], 0.0, 128.0, A.is_equal, A.mult, ["VA"], ["PA0"], 192)
+    ts(T.PA1[:], T.VA[:], 32.0, -1024.0, A.is_equal, A.mult, ["VA"], ["PA1"], 192)
     for r, v in ((12, 1024.0), (13, 896.0), (14, 896.0), (15, -128.0)):
-        ms(T.PA[96:97, r:384:16], v, ["PAc"], 24)
+        dv(lambda r=r, v=v: g.vector.memset(T.PA0[32:33, r:384:16], v), ["PA0"], [("PA0", r)], 24)
     ts(T.IB[:], T.V1[:], 0.0, None, A.is_equal, None, ["V1"], ["IB"], 64)
     ts(T.IS[:], T.V1[:], 0.0, 1.0 / 64, A.is_equal, A.mult, ["V1"], ["IS"], 64)
     ts(T.Q0[0:8, :], T.VQ[0:8, :], 0.0, None, A.is_equal, None, ["VQ"], ["Q0"], 72)
     SC = (-1.0, 3.0 / 64, -3.75 / 64)
     for i, v in enumerate(SC):
-        ac(T.ID[:, 128 * i:128 * i + 128], T.IB[:], ["IB"], [("ID", i)], 128, scale=v)
+        ts(T.ID[:, 128 * i:128 * i + 128], T.V1[:], 0.0, v, A.is_equal, A.mult, ["V1"], [("ID", i)], 64)
 
     def ID(v):
         i = SC.index(v)
         return T.ID[:, 128 * i:128 * i + 128]
 
     when("iota")
-    for j, (s1, s2) in enumerate(((0, 15), (0, 112), (0, 1), (1, 7), (3, 1), (0, 7))):
+    for j, (s1, s2) in enumerate(((0, 15), (0, 112), (0, 1), (1, 7), (3, 1), (0, 7), (2, 3), (0, 3))):
         if s1:
             ts(T.PJ[:, j:j + 1], T.PI[:], s1, s2, A.arith_shift_right, A.bitwise_and, ["PI"], [("PJ", j)], 1)
         else:
             ts(T.PJ[:, j:j + 1], T.PI[:], s2, None, A.bitwise_and, None, ["PI"], [("PJ", j)], 1)
-    names = ["row", "g16", "par", "hm", "u8", "r7"]
-    cp(T.PC[:, 0:6], T.PJ[:, 0:6], [("PJ", j) for j in range(6)], [("c", x) for x in names], 6)
+    names = ["row", "g16", "par", "hm", "u8", "r7", "r4", "r3"]
+    cp(T.PC[:, 0:8], T.PJ[:, 0:8], [("PJ", j) for j in range(8)], [("c", x) for x in names], 8)
 
     def col(x):
         return T.PC[:, names.index(x):names.index(x) + 1]
@@ -342,21 +359,25 @@ def build_ops(g, T, topo, core, me):
     tt(T.Q[:, 128:256], T.Q[:, 256:384], T.Q[:, 0:128], A.mult, ["Q1", "Q3", ("Q3", 0), ("Q3", 15)], ["Q2"], 256)
     ts(T.SEL[:], X_(0, 8), col("hm"), col("h5"), A.is_equal, A.add, ["XF", ("c", "hm"), ("c", "h5")], ["SEL"], 8)
     for m in (0, 1, 2, 3, 4, 6):
-        ac(T.PEN[:, 128 * m:128 * m + 128], T.Q[:, 128:256], ["Q2", "SEL"], [("PEN", m)], 128, scale=T.SEL[:, m:m + 1])
+        ts(T.PEN[:, 128 * m:128 * m + 128], T.Q[:, 128:256], T.SEL[:, m:m + 1], None, A.mult, None, ["Q2", "SEL"], [("PEN", m)], 64)
     eq(T.SW[:], 16, 144, "g16", 64.0, ["SW"])
     when("late")
-    if not EARLY:
-        cs("cq", "u8", "g16", None, A.add)
-        cs("mq", "r7", 0.0, None, A.is_equal)
-        eq(T.QW[:], 14, 144, "cq", "mq", ["QW"])
+    cs("cq", "u8", "g16", None, A.add)
+    cs("mq", "r7", 0.0, None, A.is_equal)
+    eq(T.QW[:], 14, 144, "cq", "mq", ["QW"])
     cs("m12", "row", 12.0, None, A.is_ge)
+    cs("hk", "m12", HB, "h5", A.mult, A.add)
+    cs("c4", "r4", "g16", None, A.add)
+    cs("m4", "r3", 0.0, None, A.is_equal)
+    cs("b4", "m4", -585 * HB / 128, None, A.mult)
+    eq(T.Q4[:], 12, 144, "c4", "m4", ["Q4"])
     ts(T.TA[:, 0:4], X_(-12, 4), col("row"), 7.0, A.is_lt, A.mult, ["XF", ("c", "row")], ["TA0"], 4)
     ts(T.TA[:, 4:8], T.TA[:, 0:4], 1.0, None, A.add, None, ["TA0"], ["TA1"], 4)
     names.append("pw")
     dv(lambda: g.vector.tensor_reduce(col("pw"), T.TA[:, 4:8], AxisListType.X, A.mult), ["TA1"], [("c", "pw")], 4)
     cs("p8", "pw", "m12", 1.0 / 128, A.mult, A.mult)
     eq(T.CWL[:], 16, 144, "g16", "p8", ["CWL"])
-    ac(T.KY[:], T.IB[:], ["IB", ("c", "m12")], ["KY"], 128, scale=col("m12"))
+    ts(T.KY[:], T.V1[:], 0.0, col("m12"), A.is_equal, A.mult, ["V1", ("c", "m12")], ["KY"], 64)
     cs("n15", "row", 15.0, None, A.is_lt)
     ts(T.SH[:], T.V1[:], -1.0, col("n15"), A.is_equal, A.mult, ["V1", ("c", "n15")], ["SH"], 64)
     cs("f64", "row", 0.0, 1.0 / 64, A.is_equal, A.mult)
@@ -388,34 +409,31 @@ def build_ops(g, T, topo, core, me):
     when("cf")
     for h in range(2):
         c = slice(512 * h, 512 * h + 512)
-        cp(T.CF[0:24, c], T.CT[0:24, c], CTt, [("CF", h)], 512)
+        lin(("CF", h), T.CF[0:24, c], T.CT[0:24, c], 1.0, 0.0, CTt, [("CF", h)], 512)
         mm([(P(h)[:], T.RE[0:24, :], T.CF[0:24, c], 512)], ["RE", ("CF", h)], [B(h)])
-        ac(T.FF[:, c], P(h)[:], SFt, [B(h), ("FF", h)], 512, scale=T.SF[:, 0:1], bias=128.5 + 1.0 / 1024)
+        ac(T.FF[:, c], P(h)[:], SFt, [B(h), ("FF", h)], 512, scale=T.SF[:, 0:1], bias=T.SF[:, 1:2])
 
     def pieces(o, tb, c):
-        return [(o, T.PA[:, 128 * tb:128 * tb + 128], T.FF[:, c], 512), (o, T.PB[0:24, 128 * tb:128 * tb + 128], T.CF[0:24, c], 512)]
+        return [(o, M[:, 128 * tb:128 * tb + 128], T.FF[:, c], 512) for M in (T.PA0, T.PA1)]
 
     SWC = 9216.0
 
     def swap(o, src, unit, c, tk, j, ident):
         n = c.stop - c.start
         for F, nm, b in ((T.F2, "F2", 2048 + 49152 - 127.5), (T.F1, "F1", 2048 + 196608 - 511.5)):
-            if nm == "F2":
-                ac(F[:, c], src, [tk], [(nm, j)], n, scale=unit, bias=b)
-            else:
-                ts(F[:, c], src, unit, b, A.mult, A.add, [tk], [(nm, j)], n // 2)
+            ts(F[:, c], src, unit, b, A.mult, A.add, [tk], [(nm, j)], n // 2)
         return ([(o, ID(3.0 / 64), T.F2[:, c], n), (o, ID(-3.75 / 64), T.F1[:, c], n), (o, ident, src, n)],
                 [tk, ("F1", j), ("F2", j), ("ID", 1), ("ID", 2)])
 
-    PAt = ["PA", "PAc", "PB"]
+    PAt = ["PA0", "PA1"] + [("PA0", r) for r in range(12, 16)]
     for h in range(2):
         c = slice(512 * h, 512 * h + 512)
         when("env%d" % h)
-        ts(T.N16[:, c], T.LCE[:, c], -2048.0, None, A.add, None, [("LCE", h)], [("N16", h)], 512)
+        lin(("N16", h), T.N16[:, c], T.LCE[:, c], 1.0, -2048.0, [("LCE", h)], [("N16", h)], 512)
         lst, rd = swap(P(6 + h)[:], T.N16[:, c], 1.0, c, ("N16", h), h, T.IS[:])
         mm(pieces(P(6 + h)[:], 0, c) + lst, ["IS", ("FF", h), ("CF", h)] + rd + PAt, [B(6 + h)])
         if ENV == "u16":
-            ts(T.MU[:, c], P(6 + h)[:], 64.0, 2048.0 + 64 * SWC, A.mult, A.add, [], [B(6 + h), ("MU", h)], 512)
+            lin(("MU", h), T.MU[:, c], P(6 + h)[:], 64.0, 2048.0 + 64 * SWC, [], [B(6 + h), ("MU", h)], 512)
             for b in (2 * h, 2 * h + 1):
                 m = T.MU[:, 256 * b:256 * b + 256]
                 if b in OWN:
@@ -438,7 +456,7 @@ def build_ops(g, T, topo, core, me):
         ops[i]["also"] = max(j for j, o in enumerate(ops) if o["kind"] == "send")
     when("e16")
     c = slice(1024, 1280)
-    ts(T.N16[:, c], T.LE[:], -2048.0, None, A.add, None, ["LE"], [("N16", 2)], 256)
+    lin(("N16", 2), T.N16[:, c], T.LE[:], 1.0, -2048.0, ["LE"], [("N16", 2)], 256)
     lst, rd = swap(P(5)[:, 0:256], T.N16[:, c], 1.0, c, ("N16", 2), 2, T.IS[:])
     mm(lst, ["IS"] + rd, [B(5)])
     for X in range(2):
@@ -449,8 +467,8 @@ def build_ops(g, T, topo, core, me):
     when("u")
     for h in range(2):
         c = slice(512 * h, 512 * h + 512)
-        ts(T.U[:, c], T.LCD[:, c], -8.0, None, A.add, None, [("LCD", h)], [("U", h)], 512)
-        ac(T.U2[:, c], T.U[:, c], [("U", h)], [("U2", h)], 512, func=ACT.Square)
+        lin(("U", h), T.U[:, c], T.LCD[:, c], 1.0, -8.0, [("LCD", h)], [("U", h)], 512)
+        ac(T.U2[:, c], T.LCD[:, c], [("LCD", h)], [("U2", h)], 512, bias=-8.0, func=ACT.Square)
     TB = (T.TB0, T.TB1, T.TB2)
     when("tb")
     for i in (1, 0, 2):
@@ -458,15 +476,19 @@ def build_ops(g, T, topo, core, me):
             c, bank = slice(512 * h, 512 * h + 512), 6 + h
             o = P(bank)[:]
             lst = [(o, T.AW[:, 144 * i + 1:144 * i + 129], T.U[:, c], 512), (o, T.AW[:, 144 * i:144 * i + 128], T.U2[:, c], 512)]
-            mm(lst + (pieces(o, i, c) if i else []), [("AW", i), ("U", h), ("U2", h), ("FF", h), ("CF", h)] + PAt, [B(bank)])
-            ac(TB[i][:, c], o, [("c", "h5")], [B(bank), ("TB", i, h)], 512, bias=col("h5"))
+            lst = (pieces(o, i, c) if i else []) + lst
+            for x, one in enumerate(lst):
+                mm([one], [("AW", i), ("FF", h)] + PAt + ([("U", h), ("U2", h)] if x >= len(lst) - 2 else []), [B(bank)],
+                   x == 0, x == len(lst) - 1)
+            x = "hk" if i == 2 else "h5"
+            ac(TB[i][:, c], o, [("c", x)], [B(bank), ("TB", i, h)], 512, bias=col(x))
         dma("sp", TB[i][:, 1024:2048], TB[i][:, 0:1024], [("TB", i, 0), ("TB", i, 1)], [("TB", i, 2), ("TB", i, 3)], 256)
     when("conv")
     for b in range(4 if ENV == "u16" else 0):
         for r in peers:
             e, l = 256 + 1024 * b + 256 * r, 1024 * r + 256 * b
-            ts(T.HE[:, e:e + 256], T.LU[:, l:l + 256], 1.0 / 64, HB - 32, A.mult, A.add, [("LU", b)],
-               [("HE", e // 128), ("HE", e // 128 + 1)], 256)
+            lin(("conv", b), T.HE[:, e:e + 256], T.LU[:, l:l + 256], 1.0 / 64, HB - 32, [("LU", b)],
+                [("HE", e // 128), ("HE", e // 128 + 1)], 256)
     when("g0")
 
     C0 = 64.0 * 67840 + 2048
@@ -486,8 +508,9 @@ def build_ops(g, T, topo, core, me):
         q, qt = (T.Z16[:, 16 * X:16 * X + 8], ("Z16", X)) if t else (T.Q0L[:, 8 * X:8 * X + 8], "Q0L")
         for i in (1, 0, 2) if t else (1, 2):
             ag(tile(i, X), TB[i][:, 0:wide].indirect(q), [("TB", i, h) for h in range(wide // 512)] + [qt], [("G", i, X)], 128)
-        ag(T.GZ[:, 128 * X:128 * X + 128], T.ZT[:, 0:wide].indirect(q), [("ZT", h) for h in range(wide // 1024)] + [qt],
-           [("GZ", X)], 128)
+        if X not in FUSED:
+            ag(T.GZ[:, 128 * X:128 * X + 128], T.ZT[:, 0:wide].indirect(q), [("ZT", h) for h in range(wide // 1024)] + [qt],
+               [("GZ", X)], 128)
 
         def rows(i):
             if t:
@@ -500,14 +523,19 @@ def build_ops(g, T, topo, core, me):
             c, o, tt_ = slice(128 * X, 128 * X + 128), tb[:, 128:256], t % 4
             lst, rd = [(o, T.IH[:], T.E16[:, c], 128)], ["IH", ("E16", X)]
             if tt_:
-                ts(T.WR[:, c], T.E16[:, c], 16.0 * tt_ - 32, 64.0, A.is_lt, A.mult, [("E16", X)], [("WR", X)], 64)
-                lst.append((o, T.IH[:], T.WR[:, c], 128))
-                rd.append(("WR", X))
+                if ("WR", X) in ON_SCALAR:
+                    ac(T.WR[:, c], T.E16[:, c], [("E16", X)], [("WR", X)], 128, bias=32 - 16.0 * tt_ + 1.0 / 128, func=ACT.Sign)
+                    lst.append((o, T.IN[:], T.WR[:, c], 128))
+                    tt_ -= 2
+                else:
+                    ts(T.WR[:, c], T.E16[:, c], 16.0 * tt_ - 32, 64.0, A.is_lt, A.mult, [("E16", X)], [("WR", X)], 64)
+                    lst.append((o, T.IH[:], T.WR[:, c], 128))
+                rd += [("WR", X), "IN"]
             part(("W2", X))
             mm(lst, rd, [B(2 + X)])
             for x in range(REP):
                 e = 128 * (REP * X + x)
-                ac(T.ER[:, e:e + 128], o, [], [B(2 + X), ("ER", X, x)], 128, bias=-16.0 * tt_)
+                lin(("ER", X, x), T.ER[:, e:e + 128], o, 1.0, -16.0 * tt_, [], [B(2 + X), ("ER", X, x)], 128)
         part(("T1", X))
         ERt = [("ER", X, x) for x in range(REP)]
         for i in range(4):
@@ -526,7 +554,11 @@ def build_ops(g, T, topo, core, me):
                     s, y0 = 8 * u + k % 8, 2048 * X + 128 * k
                     lst.append((o, T.SW[:, 16 - s:144 - s], T.Y[:, y0 + u:y0 + 128:2], 64))
             mm(lst, ["SW"] + [("Y", X, i, x) for x in range(4 // REP)], [B(2 + X)], i % 2 == 0, i % 2 == 1)
-        ts(T.TL[:, 128 * X:128 * X + 128], tb[:, 0:128], C0, None, A.add, None, [], [B(2 + X), ("TL", X)], 128)
+            if i % 2:
+                a = 128 * X + side_at(X, i // 2)
+                lin(("TL", X, i // 2), T.TL[:, a:a + 64], o, 1.0, C0, [], [B(2 + X), ("TL", X, i // 2)], 64)
+            if i == 1:
+                ac(T.T16[:, 64 * X:64 * X + 64], o, [], [B(2 + X), ("T16", X)], 64, bias=C0 - 2048)
 
     def record(t, X):
         part(("R", X))
@@ -543,34 +575,42 @@ def build_ops(g, T, topo, core, me):
     def outcomes(t, X):
         part(("O", X))
         o, l = P(6)[:, 0:8], T.T0L[:, 8 * X:8 * X + 8]
-        if EARLY:
-            mm([(o, T.SW[:, 16 - s:144 - s], T.Y[:, 2048 * X + s:2048 * X + 128:16], 8) for s in range(16)], ["SW", ("Y", X, 0, 0)], [B(6)])
-            c0 = C0
+        mm([(o, T.QW[:, 14 - 2 * a:142 - 2 * a], T.T16[:, 64 * X + a:64 * X + 64:8], 8) for a in range(8)], ["QW", ("T16", X)], [B(6)])
+        lin(("T0L", X), l, o, 1.0, 2048.0, [], [B(6), ("T0L", X)], 8)
+        if t < S - 1:
+            ac(T.HI[:, 16 * X + 8:16 * X + 16], o, [], [B(6), ("HIl", X)], 8, bias=2048.0 + 128 + 128 * X)
         else:
-            if AF16:
-                a = side_at(X, 0)
-                ac(T.T16[:, 64 * X:64 * X + 64], P(2 + X)[:, a:a + 64], [], [B(2 + X), ("T16", X)], 64, bias=C0 - 2048)
-            else:
-                ts(T.T16[:, 64 * X:64 * X + 64], T.TL[:, 64 + 64 * X:128 + 64 * X], -2048.0, None, A.add, None, [("TL", X)], [("T16", X)], 32)
-            mm([(o, T.QW[:, 14 - 2 * a:142 - 2 * a], T.T16[:, 64 * X + a:64 * X + 64:8], 8) for a in range(8)], ["QW", ("T16", X)], [B(6)])
-            c0 = 2048.0
-        ts(l, o, c0, None, A.add, None, [], [B(6), ("T0L", X)], 8)
-        ac(T.HI[:, 16 * X + 8:16 * X + 16], o, [], [B(6), ("HIl", X)], 8, bias=c0 + 128 + 128 * X)
+            ac(T.HI[:, 16 * X + 8:16 * X + 16], T.LO[:, 16 * X + 8:16 * X + 16], [("LOc", X)], [("HIl", X)], 8, bias=128.0)
         e = 256 + 1024 * t
         ag(high(X), T.HE[:, e:e + 4096].indirect(l), [("HE", e // 128 + x) for x in range(32)] + [("T0L", X)], [("HA", X)], 128)
-        mm([(P(6)[:, 16:32], T.CWL[:, 16 - s:144 - s], T.HK[:, 256 * X + s:256 * X + 256:16], 16) for s in range(16)],
+        mm([(P(6)[:, 64:128], T.CWL[:, 16 - 4 * u:144 - 4 * u], T.HK[:, 256 * X + u:256 * X + 256:4], 64) for u in range(4)],
            ["CWL", ("HA", X), ("G", 2, X)], [B(6)])
-        ac(T.HI[:, 16 * X:16 * X + 8], P(6)[:, 16:24], [], [B(6), ("HIq", X)], 8, bias=1024.0 - 585 * HB / 128)
+        ac(T.C4[:, 64 * X:64 * X + 64], P(6)[:, 64:128], [("c", "b4")], [B(6), ("C4", X)], 64, bias=col("b4"))
+        mm([(P(6)[:, 16:32], T.Q4[:, 12 - 4 * a:140 - 4 * a], T.C4[:, 64 * X + a:64 * X + 64:4], 16) for a in range(4)],
+           ["Q4", ("C4", X)], [B(6)])
+        ac(T.HI[:, 16 * X:16 * X + 8], P(6)[:, 16:24], [], [B(6), ("HIq", X)], 8, bias=1024.0)
         ac(T.LO[:, 16 * X:16 * X + 8], P(6)[:, 24:32], [], [B(6), ("LOq", X)], 8)
 
     def bound(t, X):
         part(("E", X))
         o = P(7)[:, 256 + 128 * X:384 + 128 * X]
         e = T.E16[:, 128 * X:128 * X + 128]
-        mm([(o, T.SH[:], e, 128), (o, T.IB[:], T.IT[:], 128), (o, T.IB[:], high(X), 128)],
-           ["SH", "IB", "IT", ("E16", X), ("HA", X)], [B(7)])
         c, b = 1024 * t + 128 * (1 - X), 2 * (t % 4) + X
-        ac(T.HE[:, c:c + 128], o, ["BC"], [B(7), ("HE", c // 128)], 128, bias=T.BC[:, b:b + 1])
+        lst, rd = [(o, T.SH[:], e, 128), (o, T.IB[:], T.IT[:], 128)], ["SH", "IB", "IT", ("E16", X)]
+        if t < S - 1:
+            mm(lst + [(o, T.IB[:], high(X), 128)], rd + [("HA", X)], [B(7)])
+            ac(T.HE[:, c:c + 128], o, ["BC"], [B(7), ("HE", c // 128)], 128, bias=T.BC[:, b:b + 1])
+            return
+        part(("L", X))
+        mm(lst, rd, [B(7)])
+        c, e = slice(256 * X, 256 * X + 256), 256 + 1024 * t
+        ac(T.EO[:, 256 * X:256 * X + 128], o, ["BC"], [B(7), ("EOb", X)], 128, bias=T.BC[:, b:b + 1])
+        dg(T.EO[:, 256 * X + 128:256 * X + 256], T.HE[:, e:e + 4096].indirect(T.T0L[:, 8 * X:8 * X + 8]), high(X), A.subtract,
+           [("HE", e // 128 + x) for x in range(32)] + [("T0L", X), ("HA", X), ("EOb", X)], [("EO", X)], 128)
+        o = P(X)[:, 0:256]
+        lst, rd = swap(o, T.EO[:, c], 64.0, c, ("EO", X), 3 + X, T.IH[:])
+        mm(lst, ["IH"] + rd, [B(X)])
+        ac(T.OW[:, c], o, [], [B(X), ("OW", X)], 256, scale=64.0, bias=2048.0 + 64 * SWC)
 
     def values(t, X):
         part(("V", X))
@@ -580,12 +620,12 @@ def build_ops(g, T, topo, core, me):
         for h in range(2):
             j, la, lb = 2 * X + h, 128 * X + 32 * h + side_at(X, 0), 128 * X + 32 * h + side_at(X, 1)
             c = slice(512 * j, 512 * j + 512)
-            ag(T.GA[:, c], win.indirect(T.TL[:, la:la + 32]), wt + [("TL", X)], [("GA", j)], 512)
-            dg(T.GB[:, c], win.indirect(T.TL[:, lb:lb + 32]), T.GA[:, c], A.max, wt + [("TL", X), ("GA", j)], [("GB", j)], 512)
+            ag(T.GA[:, c], win.indirect(T.TL[:, la:la + 32]), wt + [("TL", X, 0)], [("GA", j)], 512)
+            dg(T.GB[:, c], win.indirect(T.TL[:, lb:lb + 32]), T.GA[:, c], A.max, wt + [("TL", X, 1), ("GA", j)], [("GB", j)], 512)
             mm([(sb[:, 64 * h:64 * h + 64], T.IB[:], T.GB[:, 512 * j + p:512 * j + 512:8], 64) for p in range(8)],
                ["IB", ("GB", j)], [B(4 + X)], False, h == 1)
         c, o = slice(128 * X, 128 * X + 128), sb[:, 0:128]
-        ac(T.FB[:, c], o, [], [B(4 + X), ("FB", X)], 128, bias=-127.5)
+        lin(("FB", X), T.FB[:, c], o, 1.0, -127.5, [], [B(4 + X), ("FB", X)], 128)
         if t < S - 1:
             h0 = 4096 + 1024 * t + 256 * me + 128 * X
             w, tk = T.HV[:, h0:h0 + 128], ("HV", h0 // 128)
@@ -595,8 +635,13 @@ def build_ops(g, T, topo, core, me):
         if t < S - 1:
             spread([w], "w%d" % (2 * t + X), [tk], [("HV", (h0 + 256 * (r - me)) // 128) for r in peers], 96)
         o = sb[:, 128:256]
-        mm([(o, ID(-1.0), T.GZ[:, c], 128), (o, T.IB[:], w, 128)], [("ID", 0), "IB", tk, ("GZ", X)], [B(4 + X)])
-        ac(T.YS[:, c], o, [], [B(4 + X), ("YS", X)], 128, bias=0.5, func=ACT.Sign)
+        if X in FUSED:
+            wide = 2048 if t else 1024
+            q, qt = (T.Z16[:, 16 * X:16 * X + 8], ("Z16", X)) if t else (T.Q0L[:, 8 * X:8 * X + 8], "Q0L")
+            dg(T.YS[:, c], T.ZT[:, 0:wide].indirect(q), w, A.is_le, [("ZT", h) for h in range(wide // 1024)] + [qt, tk], [("YS", X)], 128)
+        else:
+            mm([(o, ID(-1.0), T.GZ[:, c], 128), (o, T.IB[:], w, 128)], [("ID", 0), "IB", tk, ("GZ", X)], [B(4 + X)])
+            ac(T.YS[:, c], o, [], [B(4 + X), ("YS", X)], 128, bias=0.5, func=ACT.Sign)
         part(("D", X))
         if t == S - 1:
             dma("sp", T.yx[:, 1280 + 128 * X:1408 + 128 * X], w, [tk], [], 32)
@@ -606,31 +651,23 @@ def build_ops(g, T, topo, core, me):
     def choose(t, X):
         part(("C", X))
         o, c, sb = P(4 + X)[:, 256:272], slice(16 * X, 16 * X + 16), B(4 + X)
-        mm([(o, T.Q[:, 0:128], T.M16[:], 16), (o, T.YS[:, 128 * X:128 * X + 128], T.O16[:], 16)],
+        f = X in FUSED
+        mm([(o, T.Q[:, 0:128], T.M16[:], 16), (o, T.YS[:, 128 * X:128 * X + 128], T.O16[:, 16 * f:16 * f + 16], 16)],
            ["Q1", ("M16", 0), ("M16", 1), "O16", ("YS", X)], [sb])
-        ac(T.VR[:, c], o, [], [sb, ("VR", X)], 16, bias=-16.0, func=ACT.Relu)
+        ac(T.VR[:, c], o, [], [sb, ("VR", X)], 16, bias=-8.0 if f else -16.0, func=ACT.Relu)
         o = P(4 + X)[:, 272:288]
-        if AF16:
-            mm([(o, T.IH[:], T.LO[:, c], 16), (o, T.DG[:], T.VR[:, c], 16)], ["DG", "IH", ("VR", X), ("LOc", X), ("LOq", X)], [sb])
-            tt(T.Z2[:, c], o, T.HI[:, c], A.min, [("HIl", X), ("HIq", X)], [sb, ("Z2", X)], 16)
-        else:
-            mm([(o, T.DG[:], T.VR[:, c], 16)], ["DG", ("VR", X)], [sb])
-            tt(T.Z1[:, c], o, T.LO[:, c], A.max, [("LOc", X), ("LOq", X)], [sb, ("Z1", X)], 16)
-            tt(T.Z2[:, c], T.Z1[:, c], T.HI[:, c], A.min, [("Z1", X), ("HIl", X), ("HIq", X)], [("Z2", X)], 32)
-        cp(T.Z16[:, c], T.Z2[:, c], [("Z2", X)], [("Z16", X)], 16)
-        src = T.HE[:, 1024 * t:1024 * t + 4352].indirect(T.Z16[:, 16 * X + 8:16 * X + 16])
-        a = 1024 * t + 128 * (1 - X)
-        src = T.HE[:, a:1024 * t + 4352].indirect(T.Z16[:, 16 * X + 8:16 * X + 16])
-        rd = [("HE", 8 * t + x) for x in range(1 - X, 34)] + [("Z16", X), ("HA", X)]
-        ha, c = high(X), slice(128 * X, 128 * X + 128)
-        dg(T.E16[:, c], src, ha, A.subtract, rd, [("E16", X)], 128)
+        mm([(o, T.IH[:], T.LO[:, c], 16), (o, T.DG[:], T.VR[:, c], 16)], ["DG", "IH", ("VR", X), ("LOc", X), ("LOq", X)], [sb])
+        tt(T.Z16[:, c], o, T.HI[:, c], A.min, [("HIl", X), ("HIq", X)], [sb, ("Z16", X)], 16)
+        l = T.Z16[:, 16 * X + 8:16 * X + 16]
         if t < S - 1:
+            a = 1024 * t + 128 * (1 - X)
+            dg(T.E16[:, 128 * X:128 * X + 128], T.HE[:, a:1024 * t + 4352].indirect(l), high(X), A.subtract,
+               [("HE", 8 * t + x) for x in range(1 - X, 34)] + [("Z16", X), ("HA", X)], [("E16", X)], 128)
             return
         part(None)
-        o = P(2 + X)[:, 256:384]
-        lst, rd = swap(o, T.E16[:, c], 64.0, c, ("E16", X), 3 + X, T.IH[:])
-        mm(lst, ["IH"] + rd, [B(2 + X)])
-        ac(T.OUT[:, c], o, [], [B(2 + X), ("OUT", X)], 128, scale=64.0, bias=2048.0 + 64 * SWC)
+        c = slice(128 * X, 128 * X + 128)
+        op("dve", lambda: g.vector.tensor_copy(T.OUT[:, c], T.OW[:, 256 * X:256 * X + 256].indirect(l)), [("OW", X), ("Z16", X)],
+           [("OUT", X)], 0.06 + 128 * GAT, cls=0)
         dma("sp", T.ye[:, c], T.OUT[:, c], [("OUT", X)], [], 64)
         ag(T.YC[:, c], T.IDX[:, 0:2048].indirect(T.Z16[:, 16 * X:16 * X + 8]), [("IDX", x) for x in range(4)] + [("Z16", X)],
            [("YC", X)], 128)
@@ -719,35 +756,65 @@ def search(ops):
         return p["dur"] + p["lat"] + HOP
 
     pre = [[(d, gap(i, d)) for d in sorted(ops[i]["dep"])] for i in range(n)]
+    above = [0] * n
+    for i in range(n):
+        far = 0
+        for d, _ in pre[i]:
+            far |= above[d]
+        above[i] = far | sum(1 << d for d, _ in pre[i])
+        pre[i] = [(d, x) for d, x in pre[i] if not far >> d & 1 or ops[d]["lat"]]
     dur = [o["dur"] for o in ops]
     eng = [o["eng"] for o in ops]
-    prio = [o["dur"] + o["lat"] for o in ops]
-    for i in range(n - 1, -1, -1):
+    lat = [o["lat"] for o in ops]
+    post = [[] for _ in range(n)]
+    for i in range(n):
         for d, x in pre[i]:
-            prio[d] = max(prio[d], prio[i] + x)
+            post[d].append((i, x - dur[d] + dur[i]))
     cases = []
     for cs in CASES:
-        du = [o["dur"] * (cs[o.get("cls", 2 if o["eng"] == "pe" else 1)] if o["kind"] == "c" else 1.0) for o in ops]
+        du = [o["dur"] * (cs[o.get("cls", 2 if o["eng"] == "pe" else 1)] if o["kind"] == "c" else cs[4] if o["kind"] == "recv" else 1.0)
+              for o in ops]
         cases.append((du, [[(d, x - dur[d] + du[d] + (cs[3] if ops[d]["kind"] == "recv" else 0.0)) for d, x in pre[i]]
                            for i in range(n)]))
 
-    def place(key):
+    def fill(order, dep, first):
+        busy, t0 = {e: [] for e in eng}, [0.0] * n
+        for i in order:
+            s, du = first[i], dur[i]
+            for d, x in dep[i]:
+                if t0[d] + x > s:
+                    s = t0[d] + x
+            row = busy[eng[i]]
+            k = len(row)
+            while k > 0 and row[k - 1][1] > s:
+                k -= 1
+            while k < len(row) and row[k][0] < s + du - 1e-9:
+                if row[k][1] > s:
+                    s = row[k][1]
+                k += 1
+            row.insert(k, (s, s + du))
+            t0[i] = s
+        return t0
+
+    zero = [0.0] * n
+
+    def forward(key):
         for i in range(n - 1, -1, -1):
             for d, _ in pre[i]:
                 if key[d] > key[i]:
                     key[d] = key[i]
-        busy, t0 = {}, [0.0] * n
-        for i in sorted(range(n), key=lambda j: (key[j], j)):
-            s = max([t0[d] + x for d, x in pre[i]], default=0.0)
-            row = busy.setdefault(eng[i], [])
-            k = len(row)
-            while k > 0 and row[k - 1][1] > s:
-                k -= 1
-            while k < len(row) and row[k][0] < s + dur[i] - 1e-9:
-                s = max(s, row[k][1])
-                k += 1
-            row.insert(k, (s, s + dur[i]))
-            t0[i] = s
+        return fill(sorted(range(n), key=lambda j: (key[j], j)), pre, zero)
+
+    def place(key, turn=False):
+        t0 = forward(key)
+        if turn:
+            key = [-t0[i] - dur[i] for i in range(n)]
+            for i in range(n):
+                for d, _ in post[i]:
+                    if key[d] > key[i]:
+                        key[d] = key[i]
+            u = fill(sorted(range(n), key=lambda j: (key[j], -j)), post, lat)
+            t0 = forward([-u[i] - dur[i] for i in range(n)])
         seq = sorted(range(n), key=lambda j: (t0[j], j))
         total = 0.0
         for du, pr in cases:
@@ -759,7 +826,8 @@ def search(ops):
                         s = t1[d] + x
                 t1[i] = s
                 free[eng[i]] = s + du[i]
-                last = max(last, s + du[i] + ops[i]["lat"])
+                if s + du[i] + lat[i] > last:
+                    last = s + du[i] + lat[i]
             total += last
         return total / len(cases), t0
 
@@ -772,9 +840,8 @@ def search(ops):
     names = sorted(set(o["role"] for o in ops), key=str)
     place_of = {x: i for i, x in enumerate(names)}
     rid = [place_of[o["role"]] for o in ops]
-    pools = ([i for i, x in enumerate(names) if x[0] != "once"], [i for i, x in enumerate(names) if x[0] == "once"])
-    top = max(prio)
-    base = [top - p for p in prio]
+    pool = [i for i, x in enumerate(names) if x[0] != "once"]
+    base = [0.0] * n
     for i, o in enumerate(ops):
         if "aim" in o:
             base[i] = FIRST + PERIOD * o["step"] + o["aim"]
@@ -799,26 +866,26 @@ def search(ops):
 
     end, t0 = place(base)
     links = queue_links(t0)
-    best, off = (end, t0), [0.0] * len(names)
+    best = (end, t0)
     for it in range(ROUNDS):
-        if it % 400 == 399:
-            base, off = list(t0), [0.0] * len(names)
-        o2 = list(off)
-        if links and rnd() < 0.6:
+        off, move, amp = [0.0] * len(names), rnd(), (0.2, 0.6, 1.2)[int(rnd() * 3)]
+        if links and move < 0.35:
             a, b = links[int(rnd() * len(links))]
             x = t0[b] - t0[a] + 0.05 + rnd() * rnd() * 2.0
             if rnd() < 0.5:
-                o2[rid[b]] -= x
+                off[rid[b]] -= x
             else:
-                o2[rid[a]] += x
-        else:
-            pool = pools[0] if rnd() < 0.7 else pools[1]
-            amp = (0.3, 1.0, 3.0)[int(rnd() * 3)]
-            for _ in range(1 + int(rnd() * 3)):
-                o2[pool[int(rnd() * len(pool))]] += amp * (rnd() + rnd() - 1.0)
-        e2, t2 = place([base[i] + o2[rid[i]] for i in range(n)])
+                off[rid[a]] += x
+        elif move < 0.6:
+            for _ in range((2, 6, 20)[int(rnd() * 3)]):
+                off[pool[int(rnd() * len(pool))]] += amp * (rnd() + rnd() - 1.0)
+        key = [t0[i] + off[rid[i]] for i in range(n)]
+        if move >= 0.6:
+            lo, wd = rnd() * rnd() * end - 2.0, (3.0, 6.0, 12.0)[int(rnd() * 3)]
+            key = [x + amp * (rnd() + rnd() - 1.0) if lo < x < lo + wd else x for x in key]
+        e2, t2 = place(key, rnd() < 0.15)
         if e2 <= end + 2.0 * HEAT * (1.0 - it / ROUNDS) * rnd():
-            end, off, t0 = e2, o2, t2
+            end, t0 = e2, t2
             links = queue_links(t0)
             if e2 < best[0]:
                 best = (e2, t2)

@@ -4,16 +4,26 @@ from concourse.mybir import AluOpType, AxisListType, ActivationFunctionType
 N, S = 4, 6
 F32, BF, F16, I32, U16 = "float32", "bfloat16", "float16", "int32", "uint16"
 REP = 2
-HB = 17408.0
-ENV = "u16"
+UN = 4096.0
+HB = 272.0
+W16 = False
+QUART = ()
+NARROW = (0,)
+TBO = (0, 1, 2)
+WIDE = (1,)
+EU = UN if W16 else 1.0
+DIRECT = (0, 1)
+ENV = "f32" if W16 else "u16"
 EARLY = False
-ON_SCALAR = {("TL", 0, 0), ("WR", 1), ("T0L", 0), ("T0L", 1), ("N16", 0), ("N16", 1), ("N16", 2), ("U", 0), ("U", 1), ("CF", 1),
-             ("FB", 0), ("FB", 1)} | {("ER", X, x) for X in range(2) for x in range(REP)}
+ON_SCALAR = {("TL", 0, 0), ("TL", 0, 1), ("TL", 1, 0), ("TL", 1, 1), ("ER2", 0), ("ER2", 1), ("WR", 1), ("T0L", 0), ("T0L", 1), ("N16", 0), ("U", 0), ("U", 1), ("CF", 1), ("GF", 2), ("GF", 0), ("ER0", 1), ("conv", 1),
+             ("FB", 0), ("FB", 1)} | {("ER", X, x) for X in range(2) for x in range(REP)} | {("own", b) for b in range(4)}
 ON_VECTOR = set()
 FUSED = (0,)
 OWN = (0, 2, 3)
 VOWN = (0, 1)
-KT = [(1, m) for m in range(5)] + [(0, m) for m in (0, 1, 2)] + [(2, m) for m in range(5)] + [(0, m) for m in (3, 4, 6)]
+VIA = {"hv2": (1, 0), "hv3": (1, 1), "hu1": (1, 2)}
+STEP2 = 1
+KT = [divmod(k, 7) for k in range(16)]
 
 
 def _sb(cols, dtype):
@@ -21,7 +31,7 @@ def _sb(cols, dtype):
 
 
 SCRATCH = {
-    "HV": _sb(9216, BF), "HE": _sb(9472, F32), "W5": _sb(256, BF),
+    "HV": _sb(9216, BF), "HE": _sb(9472, U16 if W16 else F32), "HH": _sb(256, BF), "W5": _sb(256, BF),
     "LCD": _sb(1024, I32), "LCE": _sb(1024, I32), "LE": _sb(256, I32), "CT": _sb(1024, I32), "C0": _sb(256, I32),
     "U": _sb(1024, BF), "U2": _sb(1024, BF), "CF": _sb(1024, F16), "C16": _sb(256, F16), "FF": _sb(1024, F16),
     "N16": _sb(1280, F16), "MU": _sb(1024, U16), "LU": _sb(4096, U16),
@@ -33,10 +43,10 @@ SCRATCH = {
     "HI": _sb(32, F32), "LO": _sb(32, F16), "Z1": _sb(32, F32), "Z2": _sb(32, F32), "Z16": _sb(32, U16),
     "GA": _sb(2048, BF), "GB": _sb(2048, BF), "FB": _sb(256, BF), "YS": _sb(512, BF),
     "OE": _sb(256, F32), "OUT": _sb(256, F32), "YC": _sb(256, F32),
-    "PI": _sb(1, I32), "PJ": _sb(8, I32), "PC": _sb(64, F32), "XF": _sb(176, BF), "V1": _sb(128, BF), "JP": _sb(128, BF),
-    "BG": _sb(128, BF), "VA": _sb(384, BF), "V2": _sb(128, BF), "VQ": _sb(144, BF), "TA": _sb(8, F32), "SEL": _sb(8, F32),
+    "PI": _sb(1, I32), "PJ": _sb(8, I32), "PC": _sb(96, F32), "XF": _sb(176, BF), "V1": _sb(128, BF), "JP": _sb(128, BF),
+    "BG": _sb(128, BF), "VA": _sb(384, BF), "V2": _sb(128, BF), "VQ": _sb(144, BF), "RQ": _sb(56, F32), "SEL": _sb(8, F32),
     "Q": _sb(384, BF), "PEN": _sb(896, BF), "SW": _sb(144, F16), "CWL": _sb(144, BF), "QW": _sb(144, F16), "VW": _sb(144, BF),
-    "Q0": _sb(144, F16), "AW": _sb(3 * 144, BF), "PA0": _sb(384, F16),
+    "Q0": _sb(144, F16), "AW": _sb(512, BF), "XH": _sb(128, BF), "PK": _sb(256, F16), "PA0": _sb(384, F16),
     "PA1": _sb(384, F16), "RE": _sb(128, F16), "IB": _sb(128, BF), "ID": _sb(640, BF), "IH": _sb(128, F16),
     "IS": _sb(128, F16), "SH": _sb(128, F16), "KY": _sb(128, BF), "IT": _sb(128, BF), "BC": _sb(8, F32), "CK": _sb(256, BF),
     "SF": _sb(2, F32),
@@ -45,15 +55,16 @@ for _b in range(8):
     SCRATCH["P%d" % _b] = ("psum", [128, 512], F32)
 NDMA = 40
 SEMAPHORES = (["pe", "act", "dve", "pool", "sent"] + ["d%d" % i for i in range(NDMA)]
-              + ["%s%d" % (x, i) for x in ("w", "e", "h") for i in range(10)] + ["%s%d" % (x, i) for x in ("u", "hu", "v", "hv") for i in range(4)])
+              + ["%s%d" % (x, i) for x in ("w", "x", "e", "h") for i in range(10)] + ["%s%d" % (x, i) for x in ("u", "hu", "v", "hv") for i in range(4)])
 
-CYC, GAT, PEC, HOP, LAT, RATE, LOCAL = 1.0e-3, 1.45e-3, 0.5e-3, 0.09, 2.7, 80.0, 250.0
-CASES = ((1.0, 1.0, 1.0, 0.0, 1.0), (0.75, 0.9, 0.9, 0.7, 1.4), (1.2, 1.1, 1.1, -0.3, 0.8))
-ROUNDS, HEAT, SEED, PLAN = 20000, 0.04, 1, {}
-PERIOD, FIRST = 10.4, 16.5
-START = {"x01": 0.0, "codes": 0.1, "x23": 0.2, "ce0": 0.3, "ce1": 0.4, "cd": 0.5, "e": 0.6, "z": 6.0, "send": 2.6, "iota": 0.0,
-         "iota2": 2.9, "idx": 12.0, "early": 0.1, "cols": 0.5, "mats": 4.6, "late": 9.5, "q0": 4.5, "cf": 1.0, "env0": 1.5,
-         "env1": 2.0, "fast": 5.0, "e16": 5.5, "u": 11.5, "tb": 13.5, "conv": 16.0, "g0": 15.0, "t0": 4.2}
+CYC, GAT, PEC, HOP, LAT, RATE, LOCAL = 1.0e-3, 1.45e-3, 0.5e-3, 0.09, 1.7, 80.0, 250.0
+CASES = ((1.0, 1.0, 1.0, 0.2, 1.0), (0.75, 0.9, 0.9, 1.7, 1.3), (1.2, 1.1, 1.1, 0.0, 0.9))
+ROUNDS, HEAT, SEED, PLAN = 30000, 0.04, 1, {}
+PERIOD, FIRST = 10.5, 16.0
+START = {"x01": 0.0, "codes": 0.2, "x23": 0.15, "ce0": 0.3, "ce1": 0.5, "cd": 0.4, "e": 0.35, "z": 6.0, "send": 2.6, "iota": 0.0,
+         "iota2": 2.9, "idx": 12.0, "early": 0.1, "cols": 0.5, "mats": 4.0, "late": 12.5, "q0": 3.4, "cf": 1.0, "env0": 0.9,
+         "env1": 8.6, "fast": 7.0, "e16": 5.0, "u": 9.6, "tb": 10.0, "tb0": 11.0, "tb1": 12.0, "tb2": 14.0, "conv": 15.0,
+         "g0": 16.5, "t0": 2.5}
 
 
 def _mins(a):
@@ -61,19 +72,22 @@ def _mins(a):
             for x in [-1.2] + [0.3 * y * REP / 2 for y in range(4 // REP)] + [1.0] + [1.3] * (0, 2, 0, 1)[i]]
 
 
-AIM = {("V", 0): [-0.3, 0.0, 0.9, 1.8, 0.8, 1.7, 2.6, 3.0, 3.3, 3.6, 4.2, 3.5],
-       ("V", 1): [1.0, 1.6, 2.5, 3.5, 2.4, 3.75, 4.6, 5.0, 5.25, 5.5, 6.2, 5.5],
-       ("C", 0): [3.8, 4.0, 4.2, 4.55, 4.7], ("C", 1): [5.8, 6.0, 6.2, 6.4, 6.7],
-       ("T", 0): [4.7, 5.2, 6.0], ("T", 1): [6.6, 6.9, 7.2], ("W", 0): [5.0], ("W", 1): [7.0],
-       ("W2", 0): [5.15, 5.4, 5.6], ("W2", 1): [7.2, 7.5, 7.7], ("T1", 0): _mins(5.9), ("T1", 1): _mins(8.6),
-       ("R", 0): [-2.0, -1.8, -1.6, -1.0], ("R", 1): [-1.2, -1.0, -0.8, 0.0],
-       ("O", 0): [-1.3, -0.9, -0.8, -0.7, -0.4, -0.2, 2.0, 3.4], ("O", 1): [3.6, 3.9, 4.0, 4.1, 4.4, 4.6, 4.9, 5.3],
-       ("E", 0): [1.5, 3.5], ("E", 1): [4.6, 5.9], ("L", 0): [-0.5], ("L", 1): [4.0],
+AIM = {("V", 0): [1.2, 0.0, 1.2, 2.4, 0.8, 2.0, 2.9, 3.5, 3.8, 4.1, 4.7, 4.1],
+       ("V", 1): [1.6, 1.7, 3.0, 4.2, 2.7, 4.3, 5.2, 5.6, 5.9, 6.1, 6.7, 6.1, 6.5],
+       ("C", 0): [4.5, 4.7, 4.9, 5.1, 5.3], ("C", 1): [6.9, 7.1, 7.3, 7.5, 7.7],
+       ("T", 0): [5.3, 5.8, 6.4], ("T", 1): [7.6, 8.0, 8.4, 9.6], ("W", 0): [5.6], ("W", 1): [8.1],
+       ("W2", 0): [5.8, 6.2], ("W2", 1): [8.3, 8.7, 8.9],
+       ("T1", 0): [5.6, 6.2, 6.35, 6.6, 7.4, 6.0, 6.9, 7.2, 8.0, 8.4, 8.5, 6.6, 7.8, 8.4, 9.9, 7.4, 8.7, 9.0, 10.3, 11.0],
+       ("T1", 1): [8.3, 9.3, 9.6, 10.6, 8.9, 9.9, 10.2, 10.9, 11.4, 12.0, 9.5, 10.5, 10.7, 12.2, 10.1, 11.0, 11.3, 12.5, 13.0],
+       ("R", 0): [-3.4, -3.2, -2.9, -2.3], ("R", 1): [-1.0, -0.7, -0.4, 0.2],
+       ("O", 0): [-0.8, -0.4, -0.3, -0.2, 1.0, 2.5, 3.2, 3.6, 3.7], ("O", 1): [3.9, 4.3, 4.3, 4.4, 4.8, 5.0, 5.5, 6.8, 7.1],
+       ("E", 0): [1.3, 3.8], ("E", 1): [6.6, 6.9], ("L", 0): [-0.5], ("L", 1): [3.0],
        ("D", 0): [6.0], ("D", 1): [7.0]}
 
 
-def helper_of(core, topo):
-    return [c for c in topo.cores_of(core) if topo.die(c) != topo.die(core)][0]
+def helper_of(core, topo, sem="h0"):
+    far, i = VIA.get(sem, (1, int(sem[-1]) % 2 * STEP2))
+    return [c for c in topo.cores_of(core) if c != core and (topo.die(c) != topo.die(core)) == bool(far)][i]
 
 
 def dst_id(topo, c):
@@ -194,7 +208,6 @@ def build_ops(g, T, topo, core, me):
     peers = [(me + k) % N for k in (1, 2, 3)]
     out_e = topo.engines(core, T.cores[peers[0]])
     ne = len(out_e)
-    hc = helper_of(core, topo)
     in_e = inner_engines(topo, core, T.cores[peers[0]])
     ids = [dst_id(topo, T.cores[r]) for r in peers]
 
@@ -211,15 +224,16 @@ def build_ops(g, T, topo, core, me):
         sd = op("pool", lambda: g.remote_dma_fused(trs, local_sem=T.sem.sent), rd, [], 0.5, kind="send", inc=ne)
         recv(sd, "link", LAT, kb, sem, 3 * ne, wr)
 
-    last = [None]
+    last = {}
 
     def relay(ap, hsem, sem, rd, wr, kb):
+        hc = helper_of(core, topo, hsem)
         rid, pid, _ = topo.addr(hc)
         sd = op("pool", lambda: g.remote_dma(ap, ap, T.sem[hsem], T.sem.sent, pid, rid, mask(in_e)), rd, [], 0.5,
                 kind="send", inc=len(in_e))
-        i = recv(sd, "link2", 2 * LAT + 0.5 + kb / 450.0, kb, sem, 3 * ne, wr)
-        ops[i]["also"] = last[0]
-        last[0] = i
+        i = recv(sd, "link" if topo.die(hc) == topo.die(core) else "link2", 2 * LAT + 0.5 + kb / 450.0, kb, sem, 3 * ne, wr)
+        ops[i]["also"] = last.get(hc)
+        last[hc] = i
 
     for b in range(4):
         c = 1024 * b + 256 * me
@@ -252,11 +266,12 @@ def build_ops(g, T, topo, core, me):
                   [("HV", 8 * b + 2 * me + x) for x in (0, 1)], [("HV", 8 * b + 2 * r + x) for r in peers for x in (0, 1)], 192)
 
     when("iota")
-    io(T.PI[:], [[0, 1]], 0, 1, ["PI"], 1, flag=False)
-    io(T.VA[:], [[-1, 24], [-1000, 4], [-32, 4]], 2999, 1, ["VA"], 384)
+    io(T.PJ[:, 3:4], [[0, 1]], 0, 1, ["PI"], 1, flag=False)
+    io(T.XF[:], [[1, 176]], -16, 0, ["XF"], 176)
+    io(T.VA[:], [[-1, 24], [-1000, 4], [-32, 4]], 999, 1, ["VA"], 384)
+    io(T.XH[:], [[1, 64], [0, 2]], 0, 0, ["XH"], 128)
     io(T.V2[0:32, :], [[0, 4], [-1, 32]], 1, 1, ["V2"], 128)
     io(T.V1[:], [[-1, 128]], 0, 1, ["V1"], 128)
-    io(T.XF[:], [[1, 176]], -16, 0, ["XF"], 176)
     when("iota2")
     io(T.VQ[0:8, :], [[1, 144]], -16, -16, ["VQ"], 144)
     io(T.JP[:], [[0, 8], [1, 16]], -8, 0, ["JP"], 128)
@@ -271,26 +286,25 @@ def build_ops(g, T, topo, core, me):
     ms(T.SF[:, 1:2], 1535.5 + 1.0 / 1024, [("SF", 4)], 1)
     ms(T.SF[0:32, 1:2], 0.0, [("SF", 4)], 1)
     SFt = [("SF", b) for b in range(5)]
-    when("late")
     ms(T.CK[:, 0:128], 192.0, [("CK", 0)], 64)
     ms(T.CK[:, 128:256], 256.0, [("CK", 1)], 64)
     CKt = [("CK", 0), ("CK", 1)]
     ms(T.O16[:, 0:16], -1.0 / 16, ["O16"], 8)
     ms(T.O16[:, 16:32], -1.0 / 8, ["O16"], 8)
-    io(T.BX[:], [[16, 4], [2, 2]], 4 * me - 32, 0, ["BX"], 8)
+    when("late")
+    io(T.BX[:], [[1024, 4], [128, 2]], 256 * me - 2048, 0, ["BX"], 8)
     ts(T.IH[:], T.V1[:], 0.0, None, A.is_equal, None, ["V1"], ["IH"], 64)
-    if ("WR", 0) in ON_SCALAR or ("WR", 1) in ON_SCALAR:
-        ts(T.IN[:], T.V1[:], 0.0, -32.0, A.is_equal, A.mult, ["V1"], ["IN"], 64)
+    ts(T.IN[:], T.V1[:], 0.0, -0.5 * EU, A.is_equal, A.mult, ["V1"], ["IN"], 64)
     when("early")
     ts(T.RE[0:32, :], T.V2[0:32, :], 0.0, None, A.is_equal, None, ["V2"], ["RE"], 64)
-    ts(T.PA0[:], T.VA[:], 0.0, 128.0, A.is_equal, A.mult, ["VA"], ["PA0"], 192)
-    ts(T.PA1[:], T.VA[:], 32.0, -1024.0, A.is_equal, A.mult, ["VA"], ["PA1"], 192)
-    for r, v in ((12, 1024.0), (13, 896.0), (14, 896.0), (15, -128.0)):
-        dv(lambda r=r, v=v: g.vector.memset(T.PA0[32:33, r:384:16], v), ["PA0"], [("PA0", r)], 24)
+    ts(T.PA0[:], T.VA[:], 0.0, 2.0, A.is_equal, A.mult, ["VA"], ["PA0"], 192)
+    ts(T.PA1[:], T.VA[:], 32.0, -16.0, A.is_equal, A.mult, ["VA"], ["PA1"], 192)
+    for r, v in ((4, 16.0), (5, 14.0), (6, 14.0), (7, -2.0)):
+        ac(T.PA0[32:33, r:384:16], T.XF[32:33, 0:24], ["PA0", "XF"], [("PA0", r)], 24, scale=0.0, bias=v)
     ts(T.IB[:], T.V1[:], 0.0, None, A.is_equal, None, ["V1"], ["IB"], 64)
-    ts(T.IS[:], T.V1[:], 0.0, 1.0 / 64, A.is_equal, A.mult, ["V1"], ["IS"], 64)
+    ts(T.IS[:], T.V1[:], 0.0, 1.0 / UN, A.is_equal, A.mult, ["V1"], ["IS"], 64)
     ts(T.Q0[0:8, :], T.VQ[0:8, :], 0.0, None, A.is_equal, None, ["VQ"], ["Q0"], 72)
-    SC = (-1.0, 3.0 / 64, -3.75 / 64)
+    SC = (-1.0, 3.0 / UN, -3.75 / UN)
     for i, v in enumerate(SC):
         ts(T.ID[:, 128 * i:128 * i + 128], T.V1[:], 0.0, v, A.is_equal, A.mult, ["V1"], [("ID", i)], 64)
 
@@ -299,16 +313,18 @@ def build_ops(g, T, topo, core, me):
         return T.ID[:, 128 * i:128 * i + 128]
 
     when("iota")
-    for j, (s1, s2) in enumerate(((0, 15), (0, 112), (0, 1), (1, 7), (3, 1), (0, 7), (2, 3), (0, 3))):
-        if s1:
-            ts(T.PJ[:, j:j + 1], T.PI[:], s1, s2, A.arith_shift_right, A.bitwise_and, ["PI"], [("PJ", j)], 1)
-        else:
-            ts(T.PJ[:, j:j + 1], T.PI[:], s2, None, A.bitwise_and, None, ["PI"], [("PJ", j)], 1)
-    names = ["row", "g16", "par", "hm", "u8", "r7", "r4", "r3"]
-    cp(T.PC[:, 0:8], T.PJ[:, 0:8], [("PJ", j) for j in range(8)], [("c", x) for x in names], 8)
+    for j, m in enumerate((15, 1, 3)):
+        ts(T.PJ[:, j:j + 1], T.PJ[:, 3:4], m, None, A.bitwise_and, None, ["PI"], [("PJ", j)], 1)
+    names = ["row", "par", "r3", "p"]
+    cp(T.PC[:, 0:4], T.PJ[:, 0:4], ["PI"] + [("PJ", j) for j in range(3)], [("c", x) for x in names], 4)
 
     def col(x):
         return T.PC[:, names.index(x):names.index(x) + 1]
+
+    for x, o in (("is", A.is_equal), ("lt", A.is_gt)):
+        a = len(names)
+        names += ["%s%d" % (x, r) for r in range(16)]
+        ts(T.PC[:, a:a + 16], X_(0, 16), col("row"), None, o, None, ["XF", ("c", "row")], [("c", y) for y in names[a:]], 16)
 
     def cs(x, src, s1, s2, o0, o1=None):
         names.append(x)
@@ -326,68 +342,76 @@ def build_ops(g, T, topo, core, me):
            ["XF", ("c", x)] + ([("c", v)] if isinstance(v, str) else []), wr, n // 2)
 
     when("cols")
-    cs("is10", "row", 10.0, None, A.is_equal)
-    cs("is11", "row", 11.0, None, A.is_equal)
-    cs("h5", "hm", 5.0, None, A.is_equal)
-    cs("gam", "is11", -64.0, None, A.mult)
-    cs("a1", "par", -128.0, 128.0, A.mult, A.add)
-    cs("al", "is10", -128.0, "a1", A.mult, A.add)
-    cs("b1", "is10", 32.0, None, A.mult)
-    cs("b2", "is11", 64.0, "b1", A.mult, A.add)
-    cs("be", "par", -64.0, "b2", A.mult, A.add)
-    for x, (a, b, c10, c11) in (("e0", (224.0, 448.0, 32.0, -26880.0)), ("e15", (672.0, 448.0, 0.0, -26624.0))):
+    cs("g16", "row", -1.0, "p", A.mult, A.add)
+    cs("rh", "row", 0.5, None, A.mult)
+    cs("hm", "par", -0.5, "rh", A.mult, A.add)
+    cs("u8", "lt8", -1.0, 1.0, A.mult, A.add)
+    cs("h7", "is14", "is15", None, A.add)
+    cs("sq", "par", "is14", None, A.add)
+    cs("gam", "is14", -64.0, None, A.mult)
+    cs("a1", "par", 128.0, -64.0, A.mult, A.add)
+    cs("al", "is15", -64.0, "a1", A.mult, A.add)
+    cs("b1", "sq", 64.0, -64.0, A.mult, A.add)
+    cs("be", "is15", 32.0, "b1", A.mult, A.add)
+    for x, (a, b) in (("e0", (336.0, 112.0)), ("e15", (112.0, 336.0))):
         cs(x + "a", "par", b - a, a, A.mult, A.add)
-        cs(x + "b", "is10", c10 - a, x + "a", A.mult, A.add)
-        cs(x, "is11", c11 - b, x + "b", A.mult, A.add)
-    cs("c23", "r7", 2.0, "g16", A.mult, A.add)
-    cs("v5", "r7", 5.0, None, A.is_lt)
-    cs("v2", "row", 5.0, None, A.is_lt)
-    cs("v3", "v5", "u8", None, A.mult)
-    cs("v1", "r7", 5.0, None, A.is_ge)
-    cs("t1", "row", 15.0, 2.0, A.is_equal, A.mult)
-    cs("t2", "u8", 6.0, "t1", A.mult, A.add)
-    cs("c1", "t2", "c23", -10.0, A.add, A.add)
+        cs(x + "b", "is14", -26880.0 - a, x + "a", A.mult, A.add)
+        cs(x, "is15", -80.0 - b, x + "b", A.mult, A.add)
+    cs("k0", "g16", 0.5, "row", A.mult, A.add)
+    cs("k1", "k0", -7.0, None, A.add)
+    cs("k2", "k0", -14.0, None, A.add)
+    cs("v1", "lt7", -1.0, "lt14", A.mult, A.add)
     when("mats")
-    for i, (x, v) in enumerate((("c1", "v1"), ("c23", "v2"), ("c23", "v3"))):
-        eq(T.AW[:, 144 * i:144 * i + 130], 1, 130, x, v, [("AW", i)])
-    ts(T.Q[:, 0:128], T.JP[:], col("gam"), col("al"), A.mult, A.add, ["JP", ("c", "gam"), ("c", "al")], ["Q1"], 64)
-    tt(T.Q[:, 128:256], T.Q[:, 0:128], T.JP[:], A.mult, ["Q1", "JP"], ["Q2"], 256)
-    ts(T.Q[:, 0:128], T.BG[:], col("g16"), None, A.is_equal, None, ["BG", ("c", "g16")], ["Q1"], 64)
-    ts(T.Q[:, 256:384], T.Q[:, 128:256], col("be"), None, A.add, None, ["Q2", ("c", "be")], ["Q3"], 64)
+    for i, (x, v) in enumerate((("k0", "lt7"), ("k1", "v1"), ("k2", "h7"))):
+        ts(T.AW[:, 128 * i:128 * i + 128], T.XH[:], col(x), col(v), A.is_equal, A.mult, ["XH", ("c", x), ("c", v)], [("AW", i)], 64)
+    when("cols")
+    ac(T.RQ[:, 0:16], X_(8, 16), ["XF", ("c", "gam"), ("c", "al")], ["R1"], 16, scale=col("gam"), bias=col("al"))
+    tt(T.RQ[:, 16:32], T.RQ[:, 0:16], X_(8, 16), A.mult, ["R1", "XF"], ["R2"], 32)
+    ac(T.RQ[:, 32:48], T.RQ[:, 16:32], ["R2", ("c", "be")], ["R3"], 16, bias=col("be"))
     for j, x in ((0, "e0"), (15, "e15")):
-        ac(T.Q[:, 256 + j:384:16], X_(0, 8), ["XF", ("c", x), "Q3"], [("Q3", j)], 8, scale=0.0, bias=col(x))
-    tt(T.Q[:, 128:256], T.Q[:, 256:384], T.Q[:, 0:128], A.mult, ["Q1", "Q3", ("Q3", 0), ("Q3", 15)], ["Q2"], 256)
-    ts(T.SEL[:], X_(0, 8), col("hm"), col("h5"), A.is_equal, A.add, ["XF", ("c", "hm"), ("c", "h5")], ["SEL"], 8)
-    for m in (0, 1, 2, 3, 4, 6):
-        ts(T.PEN[:, 128 * m:128 * m + 128], T.Q[:, 128:256], T.SEL[:, m:m + 1], None, A.mult, None, ["Q2", "SEL"], [("PEN", m)], 64)
-    eq(T.SW[:], 16, 144, "g16", 64.0, ["SW"])
+        ac(T.RQ[:, 32 + j:33 + j], col(x), [("c", x), "R3"], [("R3", j)], 1)
+    ts(T.RQ[:, 48:56], X_(0, 8), 16.0, col("g16"), A.mult, A.is_equal, ["XF", ("c", "g16")], ["R4"], 8)
+    for a in range(8):
+        ac(T.Q[:, 128 + 16 * a:144 + 16 * a], T.RQ[:, 32:48], ["R4", ("R3", 0), ("R3", 15)], [("Q2", a)], 16, scale=T.RQ[:, 48 + a:49 + a])
+    ts(T.SEL[:], X_(0, 8), col("hm"), col("h7"), A.is_equal, A.add, ["XF", ("c", "hm"), ("c", "h7")], ["SEL"], 8)
+    when("mats")
+    for m in range(7):
+        ts(T.PEN[:, 128 * m:128 * m + 128], T.Q[:, 128:256], T.SEL[:, m:m + 1], 64 / UN, A.mult, A.mult,
+           [("Q2", a) for a in range(8)] + ["SEL"], [("PEN", m)], 64)
+    eq(T.SW[:], 16, 144, "g16", UN, ["SW"])
     when("late")
+    ts(T.Q[:, 0:128], T.BG[:], col("g16"), None, A.is_equal, None, ["BG", ("c", "g16")], ["Q1"], 64)
     cs("cq", "u8", "g16", None, A.add)
-    cs("mq", "r7", 0.0, None, A.is_equal)
+    cs("mq", "is0", "is8", None, A.add)
     eq(T.QW[:], 14, 144, "cq", "mq", ["QW"])
-    cs("m12", "row", 12.0, None, A.is_ge)
-    cs("hk", "m12", HB, "h5", A.mult, A.add)
-    cs("c4", "r4", "g16", None, A.add)
-    cs("m4", "r3", 0.0, None, A.is_equal)
-    cs("b4", "m4", -585 * HB / 128, None, A.mult)
+    cs("kb", "row", 2.0, "g16", A.mult, A.add)
+    cs("vb", "h7", 2.0, None, A.mult)
+    eq(T.AW[:, 384:512], -27, 128, "kb", "vb", [("AW", 3)])
+    cs("m47", "lt4", -1.0, "lt8", A.mult, A.add)
+    cs("m8a", "lt8", -1.0, "lt12", A.mult, A.add)
+    cs("m8", "m8a", EU, None, A.mult)
+    cs("h1", "is1", "h7", None, A.add)
+    cs("h3", "is3", "h1", None, A.add)
+    cs("hk", "m47", HB, "h3", A.mult, A.add)
+    cs("rq", "row", 0.25, "g16", A.mult, A.add)
+    cs("c4", "r3", -0.25, "rq", A.mult, A.add)
+    cs("m4a", "is4", "mq", None, A.add)
+    cs("m4", "is12", "m4a", None, A.add)
+    cs("b4", "m4", -585 * HB / 2, None, A.mult)
     eq(T.Q4[:], 12, 144, "c4", "m4", ["Q4"])
-    ts(T.TA[:, 0:4], X_(-12, 4), col("row"), 7.0, A.is_lt, A.mult, ["XF", ("c", "row")], ["TA0"], 4)
-    ts(T.TA[:, 4:8], T.TA[:, 0:4], 1.0, None, A.add, None, ["TA0"], ["TA1"], 4)
-    names.append("pw")
-    dv(lambda: g.vector.tensor_reduce(col("pw"), T.TA[:, 4:8], AxisListType.X, A.mult), ["TA1"], [("c", "pw")], 4)
-    cs("p8", "pw", "m12", 1.0 / 128, A.mult, A.mult)
-    eq(T.CWL[:], 16, 144, "g16", "p8", ["CWL"])
-    ts(T.KY[:], T.V1[:], 0.0, col("m12"), A.is_equal, A.mult, ["V1", ("c", "m12")], ["KY"], 64)
-    cs("n15", "row", 15.0, None, A.is_lt)
-    ts(T.SH[:], T.V1[:], -1.0, col("n15"), A.is_equal, A.mult, ["V1", ("c", "n15")], ["SH"], 64)
-    cs("f64", "row", 0.0, 1.0 / 64, A.is_equal, A.mult)
-    cs("is0", "f64", 64.0, None, A.mult)
-    ac(T.IT[:], X_(0, 128), ["XF", ("c", "f64")], ["IT"], 128, scale=col("f64"))
-    ac(T.BC[:], T.BX[:], ["BX", ("c", "is0")], ["BC"], 8, scale=col("is0"))
+    cs("p0", "is4", 0.5, None, A.mult)
+    for m in (1, 2, 3):
+        cs("p%d" % m, "is%d" % (4 + m), 8.0 ** m / 2, "p%d" % (m - 1), A.mult, A.add)
+    eq(T.CWL[:], 16, 144, "g16", "p3", ["CWL"])
+    ts(T.KY[:], T.V1[:], 4.0, col("m8"), A.is_equal, A.mult, ["V1", ("c", "m8")], ["KY"], 64)
+    ts(T.SH[:], T.V1[:], -1.0, col("lt15"), A.is_equal, A.mult, ["V1", ("c", "lt15")], ["SH"], 64)
+    cs("fu", "is0", EU / UN, None, A.mult)
+    ac(T.IT[:], X_(0, 128), ["XF", ("c", "fu")], ["IT"], 128, scale=col("fu"))
+    ac(T.BC[:], T.BX[:], ["BX", ("c", "fu")], ["BC"], 8, scale=col("fu"))
     cs("r8", "row", -8.0, None, A.add)
     ts(T.DG[:], T.JP[:], col("r8"), 65536.0, A.is_equal, A.mult, ["JP", ("c", "r8")], ["DG"], 64)
     for x in range(2):
-        ac(T.M16[:, 8 * x:8 * x + 8], T.Q[:, 0:128:16], ["Q1"], [("M16", x)], 8)
+        ac(T.M16[:, 8 * x:8 * x + 8], T.RQ[:, 48:56], ["R4"], [("M16", x)], 8)
     for X in range(2):
         ac(T.LO[:, 16 * X + 8:16 * X + 16], X_(0, 8), ["XF", ("c", "row")], [("LOc", X)], 8, scale=16.0, bias=col("row"))
 
@@ -399,13 +423,11 @@ def build_ops(g, T, topo, core, me):
     when("fast")
     op("dve", lambda: g.vector.tensor_scalar(T.U0[:, 0:256], T.LCD[:, 0:1024].indirect(T.Q0L[:]), -8.0, None, A.add),
        [("LCD", 0), ("LCD", 1), "Q0L"], ["U0"], 0.06 + 256 * GAT, cls=0)
-    ac(T.U0[:, 256:512], T.U0[:, 0:256], ["U0"], ["U02"], 256, func=ACT.Square)
-    for i in (1, 0, 2):
-        bank = (3, 2, 3)[i]
+    for i in range(3):
+        bank = (2, 3, 2)[i]
         o = P(bank)[:, 0:256]
-        mm([(o, T.AW[:, 144 * i + 1:144 * i + 129], T.U0[:, 0:256], 256), (o, T.AW[:, 144 * i:144 * i + 128], T.U0[:, 256:512], 256)],
-           [("AW", i), "U0", "U02"], [B(bank)])
-        ac(T.GF[:, 256 * i:256 * i + 256], o, [("c", "h5")], [B(bank), ("GF", i)], 256, bias=col("h5"))
+        mm([(o, T.AW[:, 128 * i:128 * i + 128], T.U0[:, 0:256], 256)], [("AW", i), "U0"], [B(bank)])
+        ac(T.GF[:, 256 * i:256 * i + 256], o, [("c", "sq")], [B(bank), ("GF", i)], 256, bias=col("sq"), func=ACT.Square)
     when("cf")
     for h in range(2):
         c = slice(512 * h, 512 * h + 512)
@@ -416,40 +438,39 @@ def build_ops(g, T, topo, core, me):
     def pieces(o, tb, c):
         return [(o, M[:, 128 * tb:128 * tb + 128], T.FF[:, c], 512) for M in (T.PA0, T.PA1)]
 
-    SWC = 9216.0
+    SWC = 589824 / UN
 
     def swap(o, src, unit, c, tk, j, ident):
         n = c.stop - c.start
         for F, nm, b in ((T.F2, "F2", 2048 + 49152 - 127.5), (T.F1, "F1", 2048 + 196608 - 511.5)):
             ts(F[:, c], src, unit, b, A.mult, A.add, [tk], [(nm, j)], n // 2)
-        return ([(o, ID(3.0 / 64), T.F2[:, c], n), (o, ID(-3.75 / 64), T.F1[:, c], n), (o, ident, src, n)],
+        return ([(o, ID(3.0 / UN), T.F2[:, c], n), (o, ID(-3.75 / UN), T.F1[:, c], n), (o, ident, src, n)],
                 [tk, ("F1", j), ("F2", j), ("ID", 1), ("ID", 2)])
 
-    PAt = ["PA0", "PA1"] + [("PA0", r) for r in range(12, 16)]
+    PAt = ["PA0", "PA1"] + [("PA0", r) for r in range(4, 8)]
     for h in range(2):
         c = slice(512 * h, 512 * h + 512)
         when("env%d" % h)
         lin(("N16", h), T.N16[:, c], T.LCE[:, c], 1.0, -2048.0, [("LCE", h)], [("N16", h)], 512)
         lst, rd = swap(P(6 + h)[:], T.N16[:, c], 1.0, c, ("N16", h), h, T.IS[:])
-        mm(pieces(P(6 + h)[:], 0, c) + lst, ["IS", ("FF", h), ("CF", h)] + rd + PAt, [B(6 + h)])
-        if ENV == "u16":
-            lin(("MU", h), T.MU[:, c], P(6 + h)[:], 64.0, 2048.0 + 64 * SWC, [], [B(6 + h), ("MU", h)], 512)
-            for b in (2 * h, 2 * h + 1):
-                m = T.MU[:, 256 * b:256 * b + 256]
-                if b in OWN:
-                    spread([m], "u%d" % b, [("MU", h)], [("LU", b)], 192, [T.LU[:, 1024 * me + 256 * b:1024 * me + 256 * b + 256]])
-                else:
-                    relay(m, "hu%d" % b, "u%d" % b, [("MU", h)], [("LU", b)], 192)
+        for x, one in enumerate(pieces(P(6 + h)[:], 0, c)):
+            mm([one], [("FF", h)] + PAt, [B(6 + h)], x == 0, False)
+        for x, one in enumerate(lst):
+            mm([one], ["IS"] + rd, [B(6 + h)], False, x == 2)
         for b in (2 * h, 2 * h + 1):
-            e = 256 + 1024 * b + 256 * me
+            e, o = 256 + 1024 * b + 256 * me, P(6 + h)[:, 256 * (b % 2):256 * (b % 2) + 256]
             tk = [("HE", e // 128), ("HE", e // 128 + 1)]
-            ac(T.HE[:, e:e + 256], P(6 + h)[:, 256 * (b % 2):256 * (b % 2) + 256], [], [B(6 + h)] + tk, 256, bias=HB + SWC)
-            if ENV == "f32":
-                far = [("HE", 2 + 8 * b + 2 * r + x) for r in peers for x in (0, 1)]
-                if b in OWN:
-                    spread([T.HE[:, e:e + 256]], "u%d" % b, tk, far, 384)
-                else:
-                    relay(T.HE[:, e:e + 256], "hu%d" % b, "u%d" % b, tk, far, 384)
+            if b in WIDE:
+                lin(("own", b), T.HE[:, e:e + 256], o, 1.0, HB + SWC, [], [B(6 + h)] + tk, 256)
+                relay(T.HE[:, e:e + 256], "hu%d" % b, "u%d" % b, tk, [("HE", 2 + 8 * b + 2 * r + x) for r in peers for x in (0, 1)], 384)
+                continue
+            m = T.MU[:, 256 * b:256 * b + 256]
+            lin(("MU", b), m, o, UN, 2048.0 + UN * SWC, [], [B(6 + h), ("MU", b)], 256)
+            if b in OWN:
+                spread([m], "u%d" % b, [("MU", b)], [("LU", b)], 192, [T.LU[:, 1024 * me + 256 * b:1024 * me + 256 * b + 256]])
+            else:
+                relay(m, "hu%d" % b, "u%d" % b, [("MU", b)], [("LU", b)], 192)
+            lin(("own", b), T.HE[:, e:e + 256], m, 1.0 / UN, HB - 0.5, [("MU", b)], tk, 256)
     when("idx")
     for x in range(4):
         i = io(T.IDX[:, 512 * x:512 * x + 512], [[1, 512]], 512 * (x % 2), 0, [("IDX", x)], 512)
@@ -462,8 +483,8 @@ def build_ops(g, T, topo, core, me):
     for X in range(2):
         for x in range(REP):
             e = 128 * (REP * X + x)
-            ac(T.ER[:, e:e + 128], P(5)[:, 128 * X:128 * X + 128], [], [B(5), ("ER", X, x)], 128, bias=SWC)
-    ac(T.E16[:], P(5)[:, 0:256], [], [B(5), ("E16", 0), ("E16", 1)], 256, bias=SWC)
+            lin(("ER0", x), T.ER[:, e:e + 128], P(5)[:, 128 * X:128 * X + 128], 1.0, SWC, [], [B(5), ("ER", X, x)], 128)
+    ac(T.E16[:], P(5)[:, 0:256], [], [B(5), ("E16", 0), ("E16", 1)], 256, scale=EU, bias=SWC * EU)
     when("u")
     for h in range(2):
         c = slice(512 * h, 512 * h + 512)
@@ -471,23 +492,28 @@ def build_ops(g, T, topo, core, me):
         ac(T.U2[:, c], T.LCD[:, c], [("LCD", h)], [("U2", h)], 512, bias=-8.0, func=ACT.Square)
     TB = (T.TB0, T.TB1, T.TB2)
     when("tb")
-    for i in (1, 0, 2):
+    for x, M in enumerate((T.PA0, T.PA1)):
+        tt(T.PK[:, 128 * x:128 * x + 128], M[:, 124:252], M[:, 256:384], A.add, PAt, [("PK", x)], 256)
+    for i in TBO:
+        when("tb%d" % i)
         for h in range(2):
             c, bank = slice(512 * h, 512 * h + 512), 6 + h
-            o = P(bank)[:]
-            lst = [(o, T.AW[:, 144 * i + 1:144 * i + 129], T.U[:, c], 512), (o, T.AW[:, 144 * i:144 * i + 128], T.U2[:, c], 512)]
-            lst = (pieces(o, i, c) if i else []) + lst
-            for x, one in enumerate(lst):
-                mm([one], [("AW", i), ("FF", h)] + PAt + ([("U", h), ("U2", h)] if x >= len(lst) - 2 else []), [B(bank)],
-                   x == 0, x == len(lst) - 1)
-            x = "hk" if i == 2 else "h5"
-            ac(TB[i][:, c], o, [("c", x)], [B(bank), ("TB", i, h)], 512, bias=col(x))
+            o, aw = P(bank)[:], T.AW[:, 128 * i:128 * i + 128]
+            if i < 2:
+                mm([(o, aw, T.U[:, c], 512)], [("AW", i), ("U", h)], [B(bank)])
+                ac(TB[i][:, c], o, [("c", "sq")], [B(bank), ("TB", i, h)], 512, bias=col("sq"), func=ACT.Square)
+                continue
+            lst = [(T.PK[:, 0:128], T.FF, [("PK", 0), ("FF", h)]), (T.PK[:, 128:256], T.FF, [("PK", 1), ("FF", h)]),
+                   (T.AW[:, 384:512], T.U, [("AW", 3), ("U", h)]), (aw, T.U2, [("AW", 2), ("U2", h)])]
+            for x, (M, R, rd) in enumerate(lst):
+                mm([(o, M, R[:, c], 512)], rd, [B(bank)], x == 0, x == 3)
+            ac(TB[i][:, c], o, [("c", "hk")], [B(bank), ("TB", i, h)], 512, bias=col("hk"))
         dma("sp", TB[i][:, 1024:2048], TB[i][:, 0:1024], [("TB", i, 0), ("TB", i, 1)], [("TB", i, 2), ("TB", i, 3)], 256)
     when("conv")
-    for b in range(4 if ENV == "u16" else 0):
-        for r in peers:
+    for b in range(4):
+        for r in peers if b not in WIDE else ():
             e, l = 256 + 1024 * b + 256 * r, 1024 * r + 256 * b
-            lin(("conv", b), T.HE[:, e:e + 256], T.LU[:, l:l + 256], 1.0 / 64, HB - 32, [("LU", b)],
+            lin(("conv", b), T.HE[:, e:e + 256], T.LU[:, l:l + 256], 1.0 / UN, HB - 0.5, [("LU", b)],
                 [("HE", e // 128), ("HE", e // 128 + 1)], 256)
     when("g0")
 
@@ -495,6 +521,9 @@ def build_ops(g, T, topo, core, me):
 
     def side_at(X, side):
         return 64 * (side if X else 1 - side)
+
+    def fused(t, X):
+        return X in FUSED or t == S - 1
 
     G = (T.G0, T.G1, T.HK)
 
@@ -506,9 +535,9 @@ def build_ops(g, T, topo, core, me):
         part(("T", X) if t else None)
         wide = 2048 if t else 1024
         q, qt = (T.Z16[:, 16 * X:16 * X + 8], ("Z16", X)) if t else (T.Q0L[:, 8 * X:8 * X + 8], "Q0L")
-        for i in (1, 0, 2) if t else (1, 2):
+        for i in (0, 1, 2) if t else (2,):
             ag(tile(i, X), TB[i][:, 0:wide].indirect(q), [("TB", i, h) for h in range(wide // 512)] + [qt], [("G", i, X)], 128)
-        if X not in FUSED:
+        if not fused(t, X):
             ag(T.GZ[:, 128 * X:128 * X + 128], T.ZT[:, 0:wide].indirect(q), [("ZT", h) for h in range(wide // 1024)] + [qt],
                [("GZ", X)], 128)
 
@@ -520,22 +549,32 @@ def build_ops(g, T, topo, core, me):
         tb = P(2 + X)
         if t:
             part(("W", X))
-            c, o, tt_ = slice(128 * X, 128 * X + 128), tb[:, 128:256], t % 4
-            lst, rd = [(o, T.IH[:], T.E16[:, c], 128)], ["IH", ("E16", X)]
-            if tt_:
-                if ("WR", X) in ON_SCALAR:
-                    ac(T.WR[:, c], T.E16[:, c], [("E16", X)], [("WR", X)], 128, bias=32 - 16.0 * tt_ + 1.0 / 128, func=ACT.Sign)
-                    lst.append((o, T.IN[:], T.WR[:, c], 128))
-                    tt_ -= 2
+            c, o, off, e = slice(128 * X, 128 * X + 128), tb[:, 128:256], t % 4 / 4, 128 * REP * X
+            if X in DIRECT:
+                if off:
+                    ts(T.WR[:, c], T.E16[:, c], off - 0.5, off, A.is_lt, A.subtract, [("E16", X)], [("WR", X)], 64)
+                part(("W2", X))
+                if off:
+                    tt(T.ER[:, e:e + 128], T.E16[:, c], T.WR[:, c], A.add, [("E16", X), ("WR", X)], [("ER", X, 0)], 256)
                 else:
-                    ts(T.WR[:, c], T.E16[:, c], 16.0 * tt_ - 32, 64.0, A.is_lt, A.mult, [("E16", X)], [("WR", X)], 64)
+                    cp(T.ER[:, e:e + 128], T.E16[:, c], [("E16", X)], [("ER", X, 0)], 64)
+                lin(("ER2", X), T.ER[:, e + 128:e + 256], T.ER[:, e:e + 128], 1.0, 0.0, [("ER", X, 0)], [("ER", X, 1)],
+                    128 if ("ER2", X) in ON_SCALAR else 64)
+            else:
+                lst, rd = [(o, T.IH[:], T.E16[:, c], 128)], ["IH", ("E16", X)]
+                if off and ("WR", X) in ON_SCALAR:
+                    ac(T.WR[:, c], T.E16[:, c], [("E16", X)], [("WR", X)], 128, bias=(0.5 - off + 0.5 / UN) * EU, func=ACT.Sign)
+                    lst.append((o, T.IN[:], T.WR[:, c], 128))
+                    rd += [("WR", X), "IN"]
+                    off -= 0.5
+                elif off:
+                    ts(T.WR[:, c], T.E16[:, c], (off - 0.5) * EU, EU, A.is_lt, A.mult, [("E16", X)], [("WR", X)], 64)
                     lst.append((o, T.IH[:], T.WR[:, c], 128))
-                rd += [("WR", X), "IN"]
-            part(("W2", X))
-            mm(lst, rd, [B(2 + X)])
-            for x in range(REP):
-                e = 128 * (REP * X + x)
-                lin(("ER", X, x), T.ER[:, e:e + 128], o, 1.0, -16.0 * tt_, [], [B(2 + X), ("ER", X, x)], 128)
+                    rd += [("WR", X)]
+                part(("W2", X))
+                mm(lst, rd, [B(2 + X)])
+                for x in range(REP):
+                    lin(("ER", X, x), T.ER[:, e + 128 * x:e + 128 * x + 128], o, 1.0 / EU, -off, [], [B(2 + X), ("ER", X, x)], 128)
         part(("T1", X))
         ERt = [("ER", X, x) for x in range(REP)]
         for i in range(4):
@@ -546,6 +585,11 @@ def build_ops(g, T, topo, core, me):
             wd = 128 * REP
             for x in range(4 // REP):
                 y0 = 2048 * X + 512 * i + wd * x
+                if i == 0 and x == 0 and X in NARROW:
+                    for y in range(REP):
+                        tt(T.Y[:, y0 + 128 * y:y0 + 128 * y + 128], P(bank)[:, 128 * y:128 * y + 128], T.ER[:, wd * X:wd * X + 128], A.min,
+                           [("ER", X, 0)], [B(bank), ("Y", X, 0, 0) if y else ("Y0", X)], 128)
+                    continue
                 tt(T.Y[:, y0:y0 + wd], P(bank)[:, wd * x:wd * x + wd], T.ER[:, wd * X:wd * X + wd], A.min, ERt,
                    [B(bank), ("Y", X, i, x)], wd)
             lst, o = [], tb[:, side_at(X, i // 2):side_at(X, i // 2) + 64]
@@ -553,7 +597,7 @@ def build_ops(g, T, topo, core, me):
                 for u in range(2):
                     s, y0 = 8 * u + k % 8, 2048 * X + 128 * k
                     lst.append((o, T.SW[:, 16 - s:144 - s], T.Y[:, y0 + u:y0 + 128:2], 64))
-            mm(lst, ["SW"] + [("Y", X, i, x) for x in range(4 // REP)], [B(2 + X)], i % 2 == 0, i % 2 == 1)
+            mm(lst, ["SW"] + [("Y0", X)] * (i == 0) + [("Y", X, i, x) for x in range(4 // REP)], [B(2 + X)], i % 2 == 0, i % 2 == 1)
             if i % 2:
                 a = 128 * X + side_at(X, i // 2)
                 lin(("TL", X, i // 2), T.TL[:, a:a + 64], o, 1.0, C0, [], [B(2 + X), ("TL", X, i // 2)], 64)
@@ -564,13 +608,18 @@ def build_ops(g, T, topo, core, me):
         part(("R", X))
         o = P(7)[:, 128 * X:128 * X + 128]
         e = T.E16[:, 128 * X:128 * X + 128]
-        mm([(o, T.IH[:], e, 128), (o, T.KY[:], tile(1, X), 128)], ["IH", "KY", ("E16", X), ("G", 1, X)], [B(7)])
+        mm([(o, T.IH[:], e, 128), (o, T.KY[:], tile(2, X), 128)], ["IH", "KY", ("E16", X), ("G", 2, X)], [B(7)])
         ap, tk = env_at(T, t, me, X)
-        ac(ap, o, [], [B(7), tk], 128, bias=HB)
-        relay(ap, "h%d" % (2 * t + X), "e%d" % (2 * t + X), [tk], [env_at(T, t, r, X)[1] for r in peers], 192)
+        ac(ap, o, [], [B(7), tk], 128, bias=2048.0 if W16 else HB)
+        relay(ap, "h%d" % (2 * t + X), "e%d" % (2 * t + X), [tk], [env_at(T, t, r, X)[1] for r in peers], 96 if W16 else 192)
 
     def high(X):
         return T.HK[:, 256 * X:256 * X + 128]
+
+    HT = "HH" if W16 else "HA"
+
+    def above(X):
+        return T.HH[:, 128 * X:128 * X + 128] if W16 else high(X)
 
     def outcomes(t, X):
         part(("O", X))
@@ -582,7 +631,14 @@ def build_ops(g, T, topo, core, me):
         else:
             ac(T.HI[:, 16 * X + 8:16 * X + 16], T.LO[:, 16 * X + 8:16 * X + 16], [("LOc", X)], [("HIl", X)], 8, bias=128.0)
         e = 256 + 1024 * t
-        ag(high(X), T.HE[:, e:e + 4096].indirect(l), [("HE", e // 128 + x) for x in range(32)] + [("T0L", X)], [("HA", X)], 128)
+        src, rd = T.HE[:, e:e + 4096].indirect(l), [("HE", e // 128 + x) for x in range(32)] + [("T0L", X)]
+        if W16:
+            op("act", lambda: g.scalar.activation(high(X), src, ACT.Identity, bias=HB - 0.5, scale=1 / UN), rd, [("HA", X)],
+               0.06 + 128 * GAT, cls=0)
+            lin(("HH", X), T.HH[:, 128 * X:128 * X + 128], high(X), UN, 2048 - UN * HB, [("HA", X)], [("HH", X)],
+                128 if ("HH", X) in ON_SCALAR else 64)
+        else:
+            ag(high(X), src, rd, [("HA", X)], 128)
         mm([(P(6)[:, 64:128], T.CWL[:, 16 - 4 * u:144 - 4 * u], T.HK[:, 256 * X + u:256 * X + 256:4], 64) for u in range(4)],
            ["CWL", ("HA", X), ("G", 2, X)], [B(6)])
         ac(T.C4[:, 64 * X:64 * X + 64], P(6)[:, 64:128], [("c", "b4")], [B(6), ("C4", X)], 64, bias=col("b4"))
@@ -598,60 +654,69 @@ def build_ops(g, T, topo, core, me):
         c, b = 1024 * t + 128 * (1 - X), 2 * (t % 4) + X
         lst, rd = [(o, T.SH[:], e, 128), (o, T.IB[:], T.IT[:], 128)], ["SH", "IB", "IT", ("E16", X)]
         if t < S - 1:
-            mm(lst + [(o, T.IB[:], high(X), 128)], rd + [("HA", X)], [B(7)])
+            mm(lst + [(o, T.IB[:], above(X), 128)], rd + [(HT, X)], [B(7)])
             ac(T.HE[:, c:c + 128], o, ["BC"], [B(7), ("HE", c // 128)], 128, bias=T.BC[:, b:b + 1])
             return
         part(("L", X))
         mm(lst, rd, [B(7)])
         c, e = slice(256 * X, 256 * X + 256), 256 + 1024 * t
         ac(T.EO[:, 256 * X:256 * X + 128], o, ["BC"], [B(7), ("EOb", X)], 128, bias=T.BC[:, b:b + 1])
-        dg(T.EO[:, 256 * X + 128:256 * X + 256], T.HE[:, e:e + 4096].indirect(T.T0L[:, 8 * X:8 * X + 8]), high(X), A.subtract,
-           [("HE", e // 128 + x) for x in range(32)] + [("T0L", X), ("HA", X), ("EOb", X)], [("EO", X)], 128)
+        dg(T.EO[:, 256 * X + 128:256 * X + 256], T.HE[:, e:e + 4096].indirect(T.T0L[:, 8 * X:8 * X + 8]), above(X), A.subtract,
+           [("HE", e // 128 + x) for x in range(32)] + [("T0L", X), (HT, X), ("EOb", X)], [("EO", X)], 128)
         o = P(X)[:, 0:256]
-        lst, rd = swap(o, T.EO[:, c], 64.0, c, ("EO", X), 3 + X, T.IH[:])
-        mm(lst, ["IH"] + rd, [B(X)])
-        ac(T.OW[:, c], o, [], [B(X), ("OW", X)], 256, scale=64.0, bias=2048.0 + 64 * SWC)
+        lst, rd = swap(o, T.EO[:, c], UN / EU, c, ("EO", X), 3 + X, T.IS[:] if W16 else T.IH[:])
+        mm(lst, ["IH", "IS"] + rd, [B(X)])
+        ac(T.OW[:, c], o, [], [B(X), ("OW", X)], 256, scale=UN, bias=2048.0 + UN * SWC)
 
     def values(t, X):
         part(("V", X))
-        win, wt = T.HV[:, 1024 * t:1024 * t + 4096], [("HV", 8 * t + x) for x in range(32)]
-        sb = P(4 + X)
-        mm([(sb[:, 0:128], T.CK[0:1, 0:128], T.CK[0:1, 128:256], 128)], CKt, [B(4 + X)], True, False)
+        win, wt = T.HV[:, 1024 * t:1024 * t + 4096], [(y, 8 * t + x) for x in range(32) for y in ("HV", "HQ")]
+        sb, c = P(4 + X), slice(128 * X, 128 * X + 128)
+        cut = X in QUART and t < S - 1
+        h0 = 4096 + 1024 * t + 256 * me + 128 * X
+        w, tk = (T.HV[:, h0:h0 + 128], ("HV", h0 // 128)) if t < S - 1 else (T.W5[:, c], ("W5", X))
+
+        def finish(a, n, y):
+            o, f = sb[:, a:a + n], T.FB[:, 128 * X + a:128 * X + a + n]
+            out, k = (T.HV[:, h0 + a:h0 + a + n], (y, h0 // 128)) if t < S - 1 else (w, tk)
+            lin(("FB", X), f, o, 1.0, -127.5, [], [B(4 + X), ("FB", X, a)], n)
+            tt(out, o, f, A.subtract, [("FB", X, a)], [B(4 + X), k], n)
+            if t < S - 1:
+                spread([out], "%s%d" % ({"HV": "w", "HQ": "x"}[y], 2 * t + X), [k], [(y, (h0 + 256 * (r - me)) // 128) for r in peers], 0.75 * n)
+
         for h in range(2):
             j, la, lb = 2 * X + h, 128 * X + 32 * h + side_at(X, 0), 128 * X + 32 * h + side_at(X, 1)
-            c = slice(512 * j, 512 * j + 512)
-            ag(T.GA[:, c], win.indirect(T.TL[:, la:la + 32]), wt + [("TL", X, 0)], [("GA", j)], 512)
-            dg(T.GB[:, c], win.indirect(T.TL[:, lb:lb + 32]), T.GA[:, c], A.max, wt + [("TL", X, 1), ("GA", j)], [("GB", j)], 512)
+            g0 = slice(512 * j, 512 * j + 512)
+            if cut or h == 0:
+                a, n = (64 * h, 64) if cut else (0, 128)
+                mm([(sb[:, a:a + n], T.CK[0:1, 0:128], T.CK[0:1, 128:128 + n], n)], CKt, [B(4 + X)], True, False)
+            ag(T.GA[:, g0], win.indirect(T.TL[:, la:la + 32]), wt + [("TL", X, 0)], [("GA", j)], 512)
+            dg(T.GB[:, g0], win.indirect(T.TL[:, lb:lb + 32]), T.GA[:, g0], A.max, wt + [("TL", X, 1), ("GA", j)], [("GB", j)], 512)
             mm([(sb[:, 64 * h:64 * h + 64], T.IB[:], T.GB[:, 512 * j + p:512 * j + 512:8], 64) for p in range(8)],
-               ["IB", ("GB", j)], [B(4 + X)], False, h == 1)
-        c, o = slice(128 * X, 128 * X + 128), sb[:, 0:128]
-        lin(("FB", X), T.FB[:, c], o, 1.0, -127.5, [], [B(4 + X), ("FB", X)], 128)
-        if t < S - 1:
-            h0 = 4096 + 1024 * t + 256 * me + 128 * X
-            w, tk = T.HV[:, h0:h0 + 128], ("HV", h0 // 128)
-        else:
-            w, tk = T.W5[:, c], ("W5", X)
-        tt(w, o, T.FB[:, c], A.subtract, [("FB", X)], [B(4 + X), tk], 128)
-        if t < S - 1:
-            spread([w], "w%d" % (2 * t + X), [tk], [("HV", (h0 + 256 * (r - me)) // 128) for r in peers], 96)
-        o = sb[:, 128:256]
-        if X in FUSED:
+               ["IB", ("GB", j)], [B(4 + X)], False, cut or h == 1)
+            if cut:
+                finish(64 * h, 64, ("HQ", "HV")[h])
+        if not cut:
+            finish(0, 128, "HV")
+        o, tks = sb[:, 128:256], [tk, ("HQ", h0 // 128)]
+        if fused(t, X):
             wide = 2048 if t else 1024
             q, qt = (T.Z16[:, 16 * X:16 * X + 8], ("Z16", X)) if t else (T.Q0L[:, 8 * X:8 * X + 8], "Q0L")
-            dg(T.YS[:, c], T.ZT[:, 0:wide].indirect(q), w, A.is_le, [("ZT", h) for h in range(wide // 1024)] + [qt, tk], [("YS", X)], 128)
+            dg(T.YS[:, c], T.ZT[:, 0:wide].indirect(q), w, A.is_le, [("ZT", h) for h in range(wide // 1024)] + [qt] + tks, [("YS", X)], 128)
         else:
-            mm([(o, ID(-1.0), T.GZ[:, c], 128), (o, T.IB[:], w, 128)], [("ID", 0), "IB", tk, ("GZ", X)], [B(4 + X)])
+            mm([(o, ID(-1.0), T.GZ[:, c], 128), (o, T.IB[:], w, 128)], [("ID", 0), "IB", ("GZ", X)] + tks, [B(4 + X)])
             ac(T.YS[:, c], o, [], [B(4 + X), ("YS", X)], 128, bias=0.5, func=ACT.Sign)
         part(("D", X))
         if t == S - 1:
             dma("sp", T.yx[:, 1280 + 128 * X:1408 + 128 * X], w, [tk], [], 32)
         elif X == 1:
-            dma("sp", T.yx[:, 256 * t:256 * t + 256], T.HV[:, h0 - 128:h0 + 128], [tk, ("HV", h0 // 128 - 1)], [], 64)
+            dma("sp", T.yx[:, 256 * t:256 * t + 256], T.HV[:, h0 - 128:h0 + 128],
+                tks + [("HV", h0 // 128 - 1), ("HQ", h0 // 128 - 1)], [], 64)
 
     def choose(t, X):
         part(("C", X))
         o, c, sb = P(4 + X)[:, 256:272], slice(16 * X, 16 * X + 16), B(4 + X)
-        f = X in FUSED
+        f = fused(t, X)
         mm([(o, T.Q[:, 0:128], T.M16[:], 16), (o, T.YS[:, 128 * X:128 * X + 128], T.O16[:, 16 * f:16 * f + 16], 16)],
            ["Q1", ("M16", 0), ("M16", 1), "O16", ("YS", X)], [sb])
         ac(T.VR[:, c], o, [], [sb, ("VR", X)], 16, bias=-8.0 if f else -16.0, func=ACT.Relu)
@@ -661,8 +726,8 @@ def build_ops(g, T, topo, core, me):
         l = T.Z16[:, 16 * X + 8:16 * X + 16]
         if t < S - 1:
             a = 1024 * t + 128 * (1 - X)
-            dg(T.E16[:, 128 * X:128 * X + 128], T.HE[:, a:1024 * t + 4352].indirect(l), high(X), A.subtract,
-               [("HE", 8 * t + x) for x in range(1 - X, 34)] + [("Z16", X), ("HA", X)], [("E16", X)], 128)
+            dg(T.E16[:, 128 * X:128 * X + 128], T.HE[:, a:1024 * t + 4352].indirect(l), above(X), A.subtract,
+               [("HE", 8 * t + x) for x in range(1 - X, 34)] + [("Z16", X), (HT, X)], [("E16", X)], 128)
             return
         part(None)
         c = slice(128 * X, 128 * X + 128)
@@ -698,15 +763,16 @@ def helper_program(g, core, T, topo, r):
     n_in = len(inner_engines(topo, T.cores[r], T.cores[peers[0]]))
     ids = [dst_id(topo, T.cores[p]) for p in peers]
     jobs = [("hu%d" % b, "u%d" % b, T.MU[:, 256 * b:256 * b + 256], T.LU[:, 1024 * r + 256 * b:1024 * r + 256 * b + 256])
+            if b not in WIDE else ("hu%d" % b, "u%d" % b) + 2 * (T.HE[:, 256 + 1024 * b + 256 * r:512 + 1024 * b + 256 * r],)
             for b in range(4) if b not in OWN]
-    if ENV == "f32":
-        jobs = [("hu%d" % b, "u%d" % b) + 2 * (T.HE[:, 256 + 1024 * b + 256 * r:512 + 1024 * b + 256 * r],)
-                for b in range(4) if b not in OWN]
     jobs = [("hv%d" % b, "v%d" % b) + 2 * (T.HV[:, 1024 * b + 256 * r:1024 * b + 256 * r + 256],)
             for b in range(4) if b not in VOWN] + jobs
     for i in range(2 * (S - 1)):
         ap = env_at(T, i // 2, r, i % 2)[0]
         jobs.append(("h%d" % i, "e%d" % i, ap, ap))
+    jobs = [j for j in jobs if helper_of(T.cores[r], topo, j[0]) == core]
+    if not jobs:
+        return
     for got, sem, src, dst in jobs:
         g.wait_ge(T.sem[got], n_in)
         g.remote_dma_fused([RemoteDMATransfer(dst_ids=ids, dma_engine_mask=full, remote_sem=T.sem[sem], srcs=[src],
@@ -799,26 +865,32 @@ def search(ops):
     zero = [0.0] * n
 
     def forward(key):
-        for i in range(n - 1, -1, -1):
+        m = len(key)
+        for i in range(m - 1, -1, -1):
             for d, _ in pre[i]:
                 if key[d] > key[i]:
                     key[d] = key[i]
-        return fill(sorted(range(n), key=lambda j: (key[j], j)), pre, zero)
+        return fill(sorted(range(m), key=lambda j: (key[j], j)), pre, zero)[:m]
 
-    def place(key, turn=False):
+    def backward(t0, post, lat):
+        m = len(t0)
+        key = [-t0[i] - dur[i] for i in range(m)]
+        for i in range(m):
+            for d, _ in post[i]:
+                if key[d] > key[i]:
+                    key[d] = key[i]
+        return fill(sorted(range(m), key=lambda j: (key[j], -j)), post, lat)
+
+    def place(key, post, lat, turn=False):
         t0 = forward(key)
+        m = len(key)
         if turn:
-            key = [-t0[i] - dur[i] for i in range(n)]
-            for i in range(n):
-                for d, _ in post[i]:
-                    if key[d] > key[i]:
-                        key[d] = key[i]
-            u = fill(sorted(range(n), key=lambda j: (key[j], -j)), post, lat)
-            t0 = forward([-u[i] - dur[i] for i in range(n)])
-        seq = sorted(range(n), key=lambda j: (t0[j], j))
+            u = backward(t0, post, lat)
+            t0 = forward([-u[i] - dur[i] for i in range(m)])
+        seq = sorted(range(m), key=lambda j: (t0[j], j))
         total = 0.0
         for du, pr in cases:
-            free, t1, last = {}, [0.0] * n, 0.0
+            free, t1, last = {}, [0.0] * m, 0.0
             for i in seq:
                 s = free.get(eng[i], 0.0)
                 for d, x in pr[i]:
@@ -848,12 +920,12 @@ def search(ops):
         else:
             base[i] = FIRST + PERIOD * S if o["step"] > 0 else o["at"]
 
-    def queue_links(t0):
+    def queue_links(t0, lat):
         prev, last = {}, {}
-        for i in sorted(range(n), key=lambda j: (t0[j], j)):
+        for i in sorted(range(len(t0)), key=lambda j: (t0[j], j)):
             prev[i] = last.get(eng[i])
             last[eng[i]] = i
-        i, out = max(range(n), key=lambda j: t0[j] + dur[j] + ops[j]["lat"]), []
+        i, out = max(range(len(t0)), key=lambda j: t0[j] + dur[j] + lat[j]), []
         while True:
             s, d = max([(t0[d] + x, d) for d, x in pre[i]], default=(0.0, None))
             if prev[i] is not None and t0[i] > s + 1e-6:
@@ -864,32 +936,67 @@ def search(ops):
             else:
                 i = d
 
-    end, t0 = place(base)
-    links = queue_links(t0)
-    best = (end, t0)
-    for it in range(ROUNDS):
-        off, move, amp = [0.0] * len(names), rnd(), (0.2, 0.6, 1.2)[int(rnd() * 3)]
-        if links and move < 0.35:
-            a, b = links[int(rnd() * len(links))]
-            x = t0[b] - t0[a] + 0.05 + rnd() * rnd() * 2.0
-            if rnd() < 0.5:
-                off[rid[b]] -= x
-            else:
-                off[rid[a]] += x
-        elif move < 0.6:
-            for _ in range((2, 6, 20)[int(rnd() * 3)]):
-                off[pool[int(rnd() * len(pool))]] += amp * (rnd() + rnd() - 1.0)
-        key = [t0[i] + off[rid[i]] for i in range(n)]
-        if move >= 0.6:
-            lo, wd = rnd() * rnd() * end - 2.0, (3.0, 6.0, 12.0)[int(rnd() * 3)]
-            key = [x + amp * (rnd() + rnd() - 1.0) if lo < x < lo + wd else x for x in key]
-        e2, t2 = place(key, rnd() < 0.15)
-        if e2 <= end + 2.0 * HEAT * (1.0 - it / ROUNDS) * rnd():
-            end, t0 = e2, t2
-            links = queue_links(t0)
-            if e2 < best[0]:
-                best = (e2, t2)
-    return best
+    def anneal(key, post, lat, rounds, heat, zone=None):
+        end, t0 = place(key, post, lat)
+        links = queue_links(t0, lat)
+        best = (end, t0)
+        for it in range(rounds):
+            off, move, amp = [0.0] * len(names), rnd(), (0.2, 0.6, 1.2)[int(rnd() * 3)]
+            if zone:
+                key, near = list(t0), [x for x in links if t0[x[0]] > zone]
+                if near and move < 0.5:
+                    a, b = near[int(rnd() * len(near))]
+                    key[b] = t0[a] - 0.05 - rnd() * rnd()
+                else:
+                    lo = zone + rnd() * 10.0
+                    key = [x + amp * (rnd() + rnd() - 1.0) if lo < x < lo + 4.0 else x for x in key]
+                e2, t2 = place(key, post, lat)
+                if e2 <= end + 2.0 * heat * (1.0 - it / rounds) * rnd():
+                    end, t0 = e2, t2
+                    links = queue_links(t0, lat)
+                    best = min(best, (e2, t2))
+                continue
+            if links and move < 0.35:
+                a, b = links[int(rnd() * len(links))]
+                x = t0[b] - t0[a] + 0.05 + rnd() * rnd() * 2.0
+                if rnd() < 0.5:
+                    off[rid[b]] -= x
+                else:
+                    off[rid[a]] += x
+            elif move < 0.6:
+                for _ in range((2, 6, 20)[int(rnd() * 3)]):
+                    off[pool[int(rnd() * len(pool))]] += amp * (rnd() + rnd() - 1.0)
+            key = [x + off[rid[i]] for i, x in enumerate(t0)]
+            if move >= 0.6:
+                top = max(t0)
+                lo, wd = (rnd() * top, top - 16.0 * rnd())[int(rnd() * 1.5)] - 2.0, (3.0, 6.0, 12.0)[int(rnd() * 3)]
+                key = [x + amp * (rnd() + rnd() - 1.0) if lo < x < lo + wd else x for x in key]
+            e2, t2 = place(key, post, lat, rnd() < 0.15)
+            if e2 <= end + 2.0 * heat * (1.0 - it / rounds) * rnd():
+                end, t0 = e2, t2
+                links = queue_links(t0, lat)
+                if e2 < best[0]:
+                    best = (e2, t2)
+        return best
+
+    end, t0 = anneal(base, post, lat, ROUNDS // 4, HEAT)
+    for step, share in ((1, 2), (2, 4)):
+        m, u = min(i for i in range(n) if ops[i]["step"] == step), backward(t0, post, lat)
+        tail = [max([lat[i]] + [u[j] + x for j, x in post[i] if j >= m]) for i in range(m)]
+        near = [[(j, x) for j, x in post[i] if j < m] for i in range(m)]
+        e1, t1 = anneal(list(t0[:m]), near, tail, ROUNDS // share, 2 * HEAT)
+        gain = max(t0[i] + dur[i] + tail[i] for i in range(m)) - max(t1[i] + dur[i] + tail[i] for i in range(m))
+        end, t0 = min((end, t0), anneal(t1 + [x - gain for x in t0[m:]], post, lat, ROUNDS // 8, HEAT / 2))
+    ga = [t0[i] for i in range(n) if ops[i]["role"] == (("V", 0), 1)]
+    tries = [(end, t0)]
+    for s in (1, 2, 3):
+        rel = {o["role"]: t0[i] - ga[s] for i, o in enumerate(ops) if o["step"] == s}
+        per = ga[s + 1] - ga[s]
+        key = [t0[i] if o["step"] < 1 else ga[1] + per * (o["step"] - 1) + (rel[o["role"]] if o["step"] < S - 1 and o["role"] in rel
+                                                                           else t0[i] - ga[o["step"]]) for i, o in enumerate(ops)]
+        tries.append(place(key, post, lat))
+    end, t0 = min((end, t0), anneal(list(min(tries)[1]), post, lat, ROUNDS // 8, HEAT / 2))
+    return anneal(list(t0), post, lat, ROUNDS // 8, HEAT, max(t0) - 12.0)
 
 
 def emit(g, T, ops, seq):
@@ -949,7 +1056,7 @@ def rank_program(g, core, T, topo):
     me = T.rank_of(core)
     if me is None:
         for r, c in enumerate(T.cores):
-            if helper_of(c, topo) == core:
+            if core in topo.cores_of(c):
                 helper_program(g, core, T, topo, r)
         return
     ops = build_ops(g, T, topo, core, me)

@@ -3,27 +3,28 @@ from concourse.mybir import AluOpType, AxisListType, ActivationFunctionType
 
 N, S = 4, 6
 F32, BF, F16, I32, U16 = "float32", "bfloat16", "float16", "int32", "uint16"
-REP = 2
 UN = 4096.0
 HB = 272.0
 W16 = False
 QUART = ()
 NARROW = (0,)
+KT = [divmod(k, 7) for k in range(16)]
 TBO = (0, 1, 2)
 WIDE = (1,)
 EU = UN if W16 else 1.0
-DIRECT = (0, 1)
-ENV = "f32" if W16 else "u16"
-EARLY = False
-ON_SCALAR = {("TL", 0, 0), ("TL", 0, 1), ("TL", 1, 0), ("TL", 1, 1), ("ER2", 0), ("ER2", 1), ("WR", 1), ("T0L", 0), ("T0L", 1), ("N16", 0), ("U", 0), ("U", 1), ("CF", 1), ("GF", 2), ("GF", 0), ("ER0", 1), ("conv", 1),
-             ("FB", 0), ("FB", 1)} | {("ER", X, x) for X in range(2) for x in range(REP)} | {("own", b) for b in range(4)}
+ON_SCALAR = ({(x, X) for x in ("T0L", "T0C", "LOq", "HIq", "HIl", "C4", "VR", "TB2", "FB", "ER2", "U") for X in range(2)} | {("N16", 0), ("T16", 0), ("E0", 0), ("E0", 1), ("CF", 1), ("FF", 1), ("conv", 0, 0), ("conv", 2, 0), ("conv", 3, 0)}
+             | {("TL", X, 0) for X in range(2)} | {("own", b) for b in range(4)})
 ON_VECTOR = set()
-FUSED = (0,)
+ON_POOL = set()
+AFTER = (0,)
+WFIRST = (1,)
+PIECES = ((32,), (32,), (32,), (32,))
+FUSED = ()
+SIGN = ()
 OWN = (0, 2, 3)
 VOWN = (0, 1)
 VIA = {"hv2": (1, 0), "hv3": (1, 1), "hu1": (1, 2)}
 STEP2 = 1
-KT = [divmod(k, 7) for k in range(16)]
 
 
 def _sb(cols, dtype):
@@ -31,58 +32,55 @@ def _sb(cols, dtype):
 
 
 SCRATCH = {
-    "HV": _sb(9216, BF), "HE": _sb(9472, U16 if W16 else F32), "HH": _sb(256, BF), "W5": _sb(256, BF),
+    "HV": _sb(8192, BF), "HE": _sb(9472, U16 if W16 else F32), "HH": _sb(256, BF), "W5": _sb(256, BF),
     "LCD": _sb(1024, I32), "LCE": _sb(1024, I32), "LE": _sb(256, I32), "CT": _sb(1024, I32), "C0": _sb(256, I32),
-    "U": _sb(1024, BF), "U2": _sb(1024, BF), "CF": _sb(1024, F16), "C16": _sb(256, F16), "FF": _sb(1024, F16),
-    "N16": _sb(1280, F16), "MU": _sb(1024, U16), "LU": _sb(4096, U16),
+    "U": _sb(1024, BF), "CF": _sb(1024, F16), "C16": _sb(256, F16), "FF": _sb(1024, F16),
+    "N16": _sb(1280, F16), "LU": _sb(4096, U16),
     "TB0": _sb(2048, BF), "TB1": _sb(2048, BF), "TB2": _sb(2048, BF), "ZT": _sb(2048, BF), "IDX": _sb(2048, F32),
-    "ER": _sb(256 * REP, F16), "SG": _sb(256, BF), "OW": _sb(512, F32), "EO": _sb(512, F16), "G0": _sb(256, BF), "G1": _sb(256, BF), "HK": _sb(512, BF), "GZ": _sb(256, BF),
-    "E16": _sb(256, F16), "WR": _sb(256, F16), "F1": _sb(1280, BF), "F2": _sb(1280, BF), "VR": _sb(32, BF),
-    "IN": _sb(128, F16), "C4": _sb(128, F16), "Q4": _sb(144, F16), "Q0L": _sb(16, U16), "U0": _sb(512, BF), "GF": _sb(768, BF), "BX": _sb(8, BF), "DG": _sb(128, BF), "M16": _sb(16, BF), "O16": _sb(32, BF),
-    "Y": _sb(4096, F16), "TL": _sb(256, U16), "T16": _sb(128, F16), "T0L": _sb(16, U16),
-    "HI": _sb(32, F32), "LO": _sb(32, F16), "Z1": _sb(32, F32), "Z2": _sb(32, F32), "Z16": _sb(32, U16),
+    "OW": _sb(512, F32), "EO": _sb(512, F16), "G0": _sb(256, BF), "G1": _sb(256, BF), "HK": _sb(512, BF), "GZ": _sb(256, F16),
+    "F1": _sb(1280, BF), "F2": _sb(1280, BF), "VR": _sb(32, BF),
+    "C4": _sb(128, F16), "Q4": _sb(144, F16), "Q0L": _sb(16, U16), "U0": _sb(256, BF), "GF": _sb(768, BF), "BX": _sb(8, BF), "DG": _sb(128, BF), "M16": _sb(16, BF), "O16": _sb(64, BF),
+    "Y": _sb(4096, F16), "ER": _sb(512, F16), "SG": _sb(16, BF), "HI": _sb(32, F32), "T0C": _sb(16, F16), "IN": _sb(128, BF), "U2": _sb(1024, BF),
+    "PEN": _sb(896, BF), "SW": _sb(144, F16), "SEL": _sb(8, F32),
+    "TL": _sb(256, U16), "T16": _sb(128, F16), "T0L": _sb(16, U16),
+    "LO": _sb(32, F16), "Z16": _sb(32, U16),
     "GA": _sb(2048, BF), "GB": _sb(2048, BF), "FB": _sb(256, BF), "YS": _sb(512, BF),
     "OE": _sb(256, F32), "OUT": _sb(256, F32), "YC": _sb(256, F32),
     "PI": _sb(1, I32), "PJ": _sb(8, I32), "PC": _sb(96, F32), "XF": _sb(176, BF), "V1": _sb(128, BF), "JP": _sb(128, BF),
-    "BG": _sb(128, BF), "VA": _sb(384, BF), "V2": _sb(128, BF), "VQ": _sb(144, BF), "RQ": _sb(56, F32), "SEL": _sb(8, F32),
-    "Q": _sb(384, BF), "PEN": _sb(896, BF), "SW": _sb(144, F16), "CWL": _sb(144, BF), "QW": _sb(144, F16), "VW": _sb(144, BF),
-    "Q0": _sb(144, F16), "AW": _sb(512, BF), "XH": _sb(128, BF), "PK": _sb(256, F16), "PA0": _sb(384, F16),
+    "BG": _sb(128, BF), "VA": _sb(384, BF), "V2": _sb(128, BF), "VQ": _sb(144, BF), "RQ": _sb(56, F32),
+    "Q": _sb(256, BF), "CWL": _sb(144, BF), "QW": _sb(144, F16),
+    "Q0": _sb(144, F16), "AW": _sb(512, BF), "XH": _sb(128, BF), "PK": _sb(128, F16), "PA0": _sb(384, F16),
     "PA1": _sb(384, F16), "RE": _sb(128, F16), "IB": _sb(128, BF), "ID": _sb(640, BF), "IH": _sb(128, F16),
     "IS": _sb(128, F16), "SH": _sb(128, F16), "KY": _sb(128, BF), "IT": _sb(128, BF), "BC": _sb(8, F32), "CK": _sb(256, BF),
     "SF": _sb(2, F32),
 }
 for _b in range(8):
     SCRATCH["P%d" % _b] = ("psum", [128, 512], F32)
-NDMA = 40
+NDMA = 52
 SEMAPHORES = (["pe", "act", "dve", "pool", "sent"] + ["d%d" % i for i in range(NDMA)]
               + ["%s%d" % (x, i) for x in ("w", "x", "e", "h") for i in range(10)] + ["%s%d" % (x, i) for x in ("u", "hu", "v", "hv") for i in range(4)])
 
-CYC, GAT, PEC, HOP, LAT, RATE, LOCAL = 1.0e-3, 1.45e-3, 0.5e-3, 0.09, 1.7, 80.0, 250.0
-CASES = ((1.0, 1.0, 1.0, 0.2, 1.0), (0.75, 0.9, 0.9, 1.7, 1.3), (1.2, 1.1, 1.1, 0.0, 0.9))
-ROUNDS, HEAT, SEED, PLAN = 30000, 0.04, 1, {}
-PERIOD, FIRST = 10.5, 16.0
-START = {"x01": 0.0, "codes": 0.2, "x23": 0.15, "ce0": 0.3, "ce1": 0.5, "cd": 0.4, "e": 0.35, "z": 6.0, "send": 2.6, "iota": 0.0,
-         "iota2": 2.9, "idx": 12.0, "early": 0.1, "cols": 0.5, "mats": 4.0, "late": 12.5, "q0": 3.4, "cf": 1.0, "env0": 0.9,
-         "env1": 8.6, "fast": 7.0, "e16": 5.0, "u": 9.6, "tb": 10.0, "tb0": 11.0, "tb1": 12.0, "tb2": 14.0, "conv": 15.0,
-         "g0": 16.5, "t0": 2.5}
-
-
-def _mins(a):
-    return [a + 0.6 * i + x for i in range(4)
-            for x in [-1.2] + [0.3 * y * REP / 2 for y in range(4 // REP)] + [1.0] + [1.3] * (0, 2, 0, 1)[i]]
-
-
-AIM = {("V", 0): [1.2, 0.0, 1.2, 2.4, 0.8, 2.0, 2.9, 3.5, 3.8, 4.1, 4.7, 4.1],
-       ("V", 1): [1.6, 1.7, 3.0, 4.2, 2.7, 4.3, 5.2, 5.6, 5.9, 6.1, 6.7, 6.1, 6.5],
-       ("C", 0): [4.5, 4.7, 4.9, 5.1, 5.3], ("C", 1): [6.9, 7.1, 7.3, 7.5, 7.7],
-       ("T", 0): [5.3, 5.8, 6.4], ("T", 1): [7.6, 8.0, 8.4, 9.6], ("W", 0): [5.6], ("W", 1): [8.1],
-       ("W2", 0): [5.8, 6.2], ("W2", 1): [8.3, 8.7, 8.9],
-       ("T1", 0): [5.6, 6.2, 6.35, 6.6, 7.4, 6.0, 6.9, 7.2, 8.0, 8.4, 8.5, 6.6, 7.8, 8.4, 9.9, 7.4, 8.7, 9.0, 10.3, 11.0],
-       ("T1", 1): [8.3, 9.3, 9.6, 10.6, 8.9, 9.9, 10.2, 10.9, 11.4, 12.0, 9.5, 10.5, 10.7, 12.2, 10.1, 11.0, 11.3, 12.5, 13.0],
-       ("R", 0): [-3.4, -3.2, -2.9, -2.3], ("R", 1): [-1.0, -0.7, -0.4, 0.2],
-       ("O", 0): [-0.8, -0.4, -0.3, -0.2, 1.0, 2.5, 3.2, 3.6, 3.7], ("O", 1): [3.9, 4.3, 4.3, 4.4, 4.8, 5.0, 5.5, 6.8, 7.1],
-       ("E", 0): [1.3, 3.8], ("E", 1): [6.6, 6.9], ("L", 0): [-0.5], ("L", 1): [3.0],
-       ("D", 0): [6.0], ("D", 1): [7.0]}
+CYC, GAT, PEC, HOP, LAT, RATE, LOCAL = 1.0e-3, 1.45e-3, 0.5e-3, 0.115, 1.7, 80.0, 250.0
+CASES = ((0.95, 0.95, 0.95, 0.2, 1.0, 0.0, 1.0), (0.75, 0.9, 0.9, 1.7, 1.3, -0.02, 1.4), (1.2, 1.1, 1.1, 0.0, 0.9, 0.03, 0.8))
+CYCLE, WARM = 1000, 0.005
+ROUNDS, HEAT, SEED, PLAN = 150000, 0.04, 1, {}
+PERIOD, FIRST = 9.74, 16.0
+START = {"x01": 0.0, "codes": 0.2, "x23": 0.02, "ce0": 0.3, "ce1": 0.36, "cd": 0.4, "e": 0.33, "z": 6.0, "send": 2.6, "iota": 0.0,
+         "iota2": 4.5, "idx": 12.0, "early": 0.1, "cols": 0.5, "mats": 4.0, "late": 12.5, "q0": 3.4, "cf": 1.0, "env0": 0.9,
+         "env1": 5.5, "fast": 7.0, "e16": 5.0, "u": 9.6, "tb": 10.0, "tb0": 11.0, "tb1": 12.0, "tb2": 14.0, "conv": 15.0,
+         "g0": 16.5, "t0": 2.5, "carry": 14.0}
+AIM = {("V", 0): [-0.69, 0.0, 1.19, 2.34, 0.76, 1.95, 2.83, 3.28, 3.69, 3.85, 4.12, 4.74],
+       ("V", 1): [1.33, 1.76, 2.93, 3.88, 2.52, 4.01, 4.88, 5.33, 5.62, 5.78, 5.9, 6.51],
+       ("C", 0): [4.17, 4.42, 4.54, 4.61, 4.81, 5.02], ("C", 1): [6.33, 6.59, 5.73, 6.77, 7.11, 7.49],
+       ("T", 0): [5.09, 5.64, 6.05, 6.66], ("T", 1): [7.32, 7.95, 8.37, 13.39], ("W2", 0): [5.87], ("W2", 1): [8.19],
+       ("T1", 0): [5.44, 5.94, 6.1, 6.26, 7.02, 6.04, 6.54, 6.83, 7.31], ("T1", 1): [7.89, 8.57, 8.85, 10.31, 9.15, 9.7, 9.98, 10.61],
+       ("T4", 0): [6.47, 7.21, 7.72, 9.73, 7.6, 8.01, 8.29, 10.02], ("T4", 1): [8.47, 9.13, 9.42, 11.49, 9.44, 10.26, 10.64, 11.78],
+       ("T3", 0, 0): [7.72, 7.84], ("T3", 1, 0): [11.26, 12.55], ("T3", 0, 1): [10.54], ("T3", 1, 1): [12.45],
+       ("R", 0): [-2.89, -2.6, -2.31, -1.69], ("R", 1): [-0.97, -0.69, -0.39, 0.72],
+       ("O", 0): [-1.55], ("O", 1): [3.12], ("O2", 0): [-1.14, -1.07, -0.8], ("O2", 1): [3.52, 3.59, 3.77], ("K",): [0.0, 0.22],
+       ("O3", 0): [-0.51, -0.44, -0.33, 1.16, 1.64, 3.41, 3.89, 4.06], ("O3", 1): [3.99, 4.49, 4.17, 4.69, 4.98, 5.21, 5.51, 5.57],
+       ("E", 0): [4.31, 4.65], ("E", 1): [5.81, 6.28], ("L", 0): [-0.5], ("L", 1): [3.0],
+       ("D", 0): [6.0], ("D", 1): [5.9, 6.11]}
 
 
 def helper_of(core, topo, sem="h0"):
@@ -134,7 +132,7 @@ def build_ops(g, T, topo, core, me):
         return len(ops) - 1
 
     def dv(fn, rd, wr, n):
-        return op("dve", fn, rd, wr, 0.03 + max(64, n) * CYC)
+        return op("dve", fn, rd, wr, 0.04 + max(64, n) * CYC)
 
     def ts(out, in0, s1, s2, o0, o1, rd, wr, n):
         if o1 is None:
@@ -194,6 +192,9 @@ def build_ops(g, T, topo, core, me):
             return op("pool", lambda: g.iota(out, pat, base, cm, allow_small_or_imprecise_dtypes=True), [], wr, 0.13 + 2 * n * CYC)
         return op("pool", lambda: g.iota(out, pat, base, cm), [], wr, 0.13 + 2 * n * CYC)
 
+    def pc(out, in_, rd, wr, n):
+        return op("pool", lambda: g.affine_select(out, in_, [[0, n]], A.is_ge, 0.0, 0, 0), rd, wr, 0.17 + 2 * n * CYC)
+
     def dma(q, out, in_, rd, wr, kb):
         e = g.sync if q == "sp" else g.scalar
         i = op(q, lambda: e.dma_start(out, in_), rd, wr, 0.1, kind="dma")
@@ -204,6 +205,9 @@ def build_ops(g, T, topo, core, me):
 
     def B(b):
         return ("B", b)
+
+    def env(X):
+        return T.ER[:, 256 * X:256 * X + 128]
 
     peers = [(me + k) % N for k in (1, 2, 3)]
     out_e = topo.engines(core, T.cores[peers[0]])
@@ -240,9 +244,9 @@ def build_ops(g, T, topo, core, me):
         when("x01" if b < 2 else "x23")
         dma("sp", T.HV[:, c:c + 256], T.x0[:, 256 * b:256 * b + 256], [], [("HV", c // 128), ("HV", c // 128 + 1)], 64)
     when("codes")
-    for i, src in enumerate((T.cc0, T.ky, T.kid)):
-        dma("act", T.CT[8 * i:8 * i + 8, :], src[:], [], [("CT", i)], 64)
     dma("act", T.C0[0:8, :], T.c0[:], [], ["C0"], 16)
+    for i, src in enumerate((T.cc0, T.ky, T.kid)):
+        dma("act", T.CT[8 * i:8 * i + 8, :], src[:], [], [("CT", i)], 48)
     for h in range(2):
         when("ce%d" % h)
         dma("sp", T.LCE[:, 512 * h:512 * h + 512], T.ce0[:, 512 * h:512 * h + 512], [], [("LCE", h)], 256)
@@ -286,25 +290,26 @@ def build_ops(g, T, topo, core, me):
     ms(T.SF[:, 1:2], 1535.5 + 1.0 / 1024, [("SF", 4)], 1)
     ms(T.SF[0:32, 1:2], 0.0, [("SF", 4)], 1)
     SFt = [("SF", b) for b in range(5)]
-    ms(T.CK[:, 0:128], 192.0, [("CK", 0)], 64)
-    ms(T.CK[:, 128:256], 256.0, [("CK", 1)], 64)
-    CKt = [("CK", 0), ("CK", 1)]
-    ms(T.O16[:, 0:16], -1.0 / 16, ["O16"], 8)
-    ms(T.O16[:, 16:32], -1.0 / 8, ["O16"], 8)
+    ms(T.CK[:, 0:128], 128.0, ["CK"], 64)
+    CKt = ["CK"]
+    for i, v in enumerate((1.0 / 2048, -1.0 / 2048, -1.0 / 8, -1.0 / 16)):
+        if (len(FUSED) < 2, len(FUSED) < 2, FUSED, SIGN)[i]:
+            ms(T.O16[:, 16 * i:16 * i + 16], v, ["O16"], 8)
     when("late")
     io(T.BX[:], [[1024, 4], [128, 2]], 256 * me - 2048, 0, ["BX"], 8)
-    ts(T.IH[:], T.V1[:], 0.0, None, A.is_equal, None, ["V1"], ["IH"], 64)
-    ts(T.IN[:], T.V1[:], 0.0, -0.5 * EU, A.is_equal, A.mult, ["V1"], ["IN"], 64)
     when("early")
+    ts(T.IH[:], T.V1[:], 0.0, None, A.is_equal, None, ["V1"], ["IH"], 64)
     ts(T.RE[0:32, :], T.V2[0:32, :], 0.0, None, A.is_equal, None, ["V2"], ["RE"], 64)
     ts(T.PA0[:], T.VA[:], 0.0, 2.0, A.is_equal, A.mult, ["VA"], ["PA0"], 192)
     ts(T.PA1[:], T.VA[:], 32.0, -16.0, A.is_equal, A.mult, ["VA"], ["PA1"], 192)
     for r, v in ((4, 16.0), (5, 14.0), (6, 14.0), (7, -2.0)):
         ac(T.PA0[32:33, r:384:16], T.XF[32:33, 0:24], ["PA0", "XF"], [("PA0", r)], 24, scale=0.0, bias=v)
+    tt(T.PA1[:], T.PA0[:], T.PA1[:], A.add, ["PA0", "PA1"] + [("PA0", r) for r in range(4, 8)], ["PA1"], 768)
+    tt(T.PK[:], T.PA1[:, 124:252], T.PA1[:, 256:384], A.add, ["PA1"], ["PK"], 256)
     ts(T.IB[:], T.V1[:], 0.0, None, A.is_equal, None, ["V1"], ["IB"], 64)
     ts(T.IS[:], T.V1[:], 0.0, 1.0 / UN, A.is_equal, A.mult, ["V1"], ["IS"], 64)
     ts(T.Q0[0:8, :], T.VQ[0:8, :], 0.0, None, A.is_equal, None, ["VQ"], ["Q0"], 72)
-    SC = (-1.0, 3.0 / UN, -3.75 / UN)
+    SC = (3.0 / UN, -3.75 / UN)
     for i, v in enumerate(SC):
         ts(T.ID[:, 128 * i:128 * i + 128], T.V1[:], 0.0, v, A.is_equal, A.mult, ["V1"], [("ID", i)], 64)
 
@@ -343,15 +348,16 @@ def build_ops(g, T, topo, core, me):
 
     when("cols")
     cs("g16", "row", -1.0, "p", A.mult, A.add)
+    cs("u8", "lt8", -1.0, 1.0, A.mult, A.add)
     cs("rh", "row", 0.5, None, A.mult)
     cs("hm", "par", -0.5, "rh", A.mult, A.add)
-    cs("u8", "lt8", -1.0, 1.0, A.mult, A.add)
     cs("h7", "is14", "is15", None, A.add)
-    cs("sq", "par", "is14", None, A.add)
+    cs("s1", "par", "is14", None, A.add)
+    cs("sq", "lt14", -8.0, "s1", A.mult, A.add)
     cs("gam", "is14", -64.0, None, A.mult)
     cs("a1", "par", 128.0, -64.0, A.mult, A.add)
     cs("al", "is15", -64.0, "a1", A.mult, A.add)
-    cs("b1", "sq", 64.0, -64.0, A.mult, A.add)
+    cs("b1", "s1", 64.0, -64.0, A.mult, A.add)
     cs("be", "is15", 32.0, "b1", A.mult, A.add)
     for x, (a, b) in (("e0", (336.0, 112.0)), ("e15", (112.0, 336.0))):
         cs(x + "a", "par", b - a, a, A.mult, A.add)
@@ -381,6 +387,7 @@ def build_ops(g, T, topo, core, me):
     eq(T.SW[:], 16, 144, "g16", UN, ["SW"])
     when("late")
     ts(T.Q[:, 0:128], T.BG[:], col("g16"), None, A.is_equal, None, ["BG", ("c", "g16")], ["Q1"], 64)
+    ts(T.IN[:], T.V1[:], 0.0, -2048.0, A.is_equal, A.mult, ["V1"], ["IN"], 64)
     cs("cq", "u8", "g16", None, A.add)
     cs("mq", "is0", "is8", None, A.add)
     eq(T.QW[:], 14, 144, "cq", "mq", ["QW"])
@@ -388,10 +395,9 @@ def build_ops(g, T, topo, core, me):
     cs("vb", "h7", 2.0, None, A.mult)
     eq(T.AW[:, 384:512], -27, 128, "kb", "vb", [("AW", 3)])
     cs("m47", "lt4", -1.0, "lt8", A.mult, A.add)
-    cs("m8a", "lt8", -1.0, "lt12", A.mult, A.add)
-    cs("m8", "m8a", EU, None, A.mult)
-    cs("h1", "is1", "h7", None, A.add)
-    cs("h3", "is3", "h1", None, A.add)
+    cs("m8", "lt8", -1.0, "lt12", A.mult, A.add)
+    cs("h1", "is1", "is3", None, A.add)
+    cs("h3", "h1", -15.0, "h7", A.mult, A.add)
     cs("hk", "m47", HB, "h3", A.mult, A.add)
     cs("rq", "row", 0.25, "g16", A.mult, A.add)
     cs("c4", "r3", -0.25, "rq", A.mult, A.add)
@@ -411,9 +417,9 @@ def build_ops(g, T, topo, core, me):
     cs("r8", "row", -8.0, None, A.add)
     ts(T.DG[:], T.JP[:], col("r8"), 65536.0, A.is_equal, A.mult, ["JP", ("c", "r8")], ["DG"], 64)
     for x in range(2):
-        ac(T.M16[:, 8 * x:8 * x + 8], T.RQ[:, 48:56], ["R4"], [("M16", x)], 8)
+        ac(T.M16[:, 8 * x:8 * x + 8], T.Q[:, 0:128:16], ["Q1"], [("M16", x)], 8)
     for X in range(2):
-        ac(T.LO[:, 16 * X + 8:16 * X + 16], X_(0, 8), ["XF", ("c", "row")], [("LOc", X)], 8, scale=16.0, bias=col("row"))
+        ac(T.LO[:, 16 * X:16 * X + 8], X_(0, 8), ["XF", ("c", "row")], [("LOc", X)], 8, scale=16.0, bias=col("row"))
 
     CTt = [("CT", i) for i in range(3)]
     when("q0")
@@ -421,22 +427,20 @@ def build_ops(g, T, topo, core, me):
     mms([[(P(6)[:, 0:16], T.Q0[0:8, 16 - s:144 - s], T.C16[0:8, s:256:16], 16) for s in range(16)]], ["Q0", "C16"], [B(6)])
     cp(T.Q0L[:], P(6)[:, 0:16], [], [B(6), "Q0L"], 16)
     when("fast")
-    op("dve", lambda: g.vector.tensor_scalar(T.U0[:, 0:256], T.LCD[:, 0:1024].indirect(T.Q0L[:]), -8.0, None, A.add),
+    op("dve", lambda: g.vector.tensor_copy(T.U0[:], T.LCD[:, 0:1024].indirect(T.Q0L[:])),
        [("LCD", 0), ("LCD", 1), "Q0L"], ["U0"], 0.06 + 256 * GAT, cls=0)
-    for i in range(3):
-        bank = (2, 3, 2)[i]
-        o = P(bank)[:, 0:256]
-        mm([(o, T.AW[:, 128 * i:128 * i + 128], T.U0[:, 0:256], 256)], [("AW", i), "U0"], [B(bank)])
-        ac(T.GF[:, 256 * i:256 * i + 256], o, [("c", "sq")], [B(bank), ("GF", i)], 256, bias=col("sq"), func=ACT.Square)
+    for bank, ii in ((2, (0, 1)), (3, (2,))):
+        n = 256 * len(ii)
+        mms([[(P(bank)[:, 256 * x:256 * x + 256], T.AW[:, 128 * i:128 * i + 128], T.U0[:], 256)] for x, i in enumerate(ii)],
+            [("AW", i) for i in ii] + ["U0"], [B(bank)])
+        ac(T.GF[:, 256 * ii[0]:256 * ii[0] + n], P(bank)[:, 0:n], [("c", "sq")], [B(bank)] + [("GF", i) for i in ii], n,
+           bias=col("sq"), func=ACT.Square)
     when("cf")
     for h in range(2):
         c = slice(512 * h, 512 * h + 512)
         lin(("CF", h), T.CF[0:24, c], T.CT[0:24, c], 1.0, 0.0, CTt, [("CF", h)], 512)
         mm([(P(h)[:], T.RE[0:24, :], T.CF[0:24, c], 512)], ["RE", ("CF", h)], [B(h)])
-        ac(T.FF[:, c], P(h)[:], SFt, [B(h), ("FF", h)], 512, scale=T.SF[:, 0:1], bias=T.SF[:, 1:2])
-
-    def pieces(o, tb, c):
-        return [(o, M[:, 128 * tb:128 * tb + 128], T.FF[:, c], 512) for M in (T.PA0, T.PA1)]
+        lin(("FF", h), T.FF[:, c], P(h)[:], T.SF[:, 0:1], T.SF[:, 1:2], SFt, [B(h), ("FF", h)], 512)
 
     SWC = 589824 / UN
 
@@ -445,16 +449,14 @@ def build_ops(g, T, topo, core, me):
         for F, nm, b in ((T.F2, "F2", 2048 + 49152 - 127.5), (T.F1, "F1", 2048 + 196608 - 511.5)):
             ts(F[:, c], src, unit, b, A.mult, A.add, [tk], [(nm, j)], n // 2)
         return ([(o, ID(3.0 / UN), T.F2[:, c], n), (o, ID(-3.75 / UN), T.F1[:, c], n), (o, ident, src, n)],
-                [tk, ("F1", j), ("F2", j), ("ID", 1), ("ID", 2)])
+                [tk, ("F1", j), ("F2", j), ("ID", 0), ("ID", 1)])
 
-    PAt = ["PA0", "PA1"] + [("PA0", r) for r in range(4, 8)]
     for h in range(2):
         c = slice(512 * h, 512 * h + 512)
         when("env%d" % h)
         lin(("N16", h), T.N16[:, c], T.LCE[:, c], 1.0, -2048.0, [("LCE", h)], [("N16", h)], 512)
         lst, rd = swap(P(6 + h)[:], T.N16[:, c], 1.0, c, ("N16", h), h, T.IS[:])
-        for x, one in enumerate(pieces(P(6 + h)[:], 0, c)):
-            mm([one], [("FF", h)] + PAt, [B(6 + h)], x == 0, False)
+        mm([(P(6 + h)[:], T.PA1[:, 0:128], T.FF[:, c], 512)], [("FF", h), "PA1"], [B(6 + h)], True, False)
         for x, one in enumerate(lst):
             mm([one], ["IS"] + rd, [B(6 + h)], False, x == 2)
         for b in (2 * h, 2 * h + 1):
@@ -464,13 +466,12 @@ def build_ops(g, T, topo, core, me):
                 lin(("own", b), T.HE[:, e:e + 256], o, 1.0, HB + SWC, [], [B(6 + h)] + tk, 256)
                 relay(T.HE[:, e:e + 256], "hu%d" % b, "u%d" % b, tk, [("HE", 2 + 8 * b + 2 * r + x) for r in peers for x in (0, 1)], 384)
                 continue
-            m = T.MU[:, 256 * b:256 * b + 256]
+            m = T.LU[:, e - 256:e]
             lin(("MU", b), m, o, UN, 2048.0 + UN * SWC, [], [B(6 + h), ("MU", b)], 256)
             if b in OWN:
-                spread([m], "u%d" % b, [("MU", b)], [("LU", b)], 192, [T.LU[:, 1024 * me + 256 * b:1024 * me + 256 * b + 256]])
+                spread([m], "u%d" % b, [("MU", b)], [("LU", b)], 192)
             else:
                 relay(m, "hu%d" % b, "u%d" % b, [("MU", b)], [("LU", b)], 192)
-            lin(("own", b), T.HE[:, e:e + 256], m, 1.0 / UN, HB - 0.5, [("MU", b)], tk, 256)
     when("idx")
     for x in range(4):
         i = io(T.IDX[:, 512 * x:512 * x + 512], [[1, 512]], 512 * (x % 2), 0, [("IDX", x)], 512)
@@ -481,40 +482,37 @@ def build_ops(g, T, topo, core, me):
     lst, rd = swap(P(5)[:, 0:256], T.N16[:, c], 1.0, c, ("N16", 2), 2, T.IS[:])
     mm(lst, ["IS"] + rd, [B(5)])
     for X in range(2):
-        for x in range(REP):
-            e = 128 * (REP * X + x)
-            lin(("ER0", x), T.ER[:, e:e + 128], P(5)[:, 128 * X:128 * X + 128], 1.0, SWC, [], [B(5), ("ER", X, x)], 128)
-    ac(T.E16[:], P(5)[:, 0:256], [], [B(5), ("E16", 0), ("E16", 1)], 256, scale=EU, bias=SWC * EU)
+        lin(("E0", X), env(X), P(5)[:, 128 * X:128 * X + 128], 1.0, SWC, [], [B(5), ("E16", X)], 128)
     when("u")
     for h in range(2):
         c = slice(512 * h, 512 * h + 512)
-        lin(("U", h), T.U[:, c], T.LCD[:, c], 1.0, -8.0, [("LCD", h)], [("U", h)], 512)
+        if ("U", h) in ON_POOL:
+            i = pc(T.U[:, c], T.LCD[:, c], [("LCD", h)], [("U", h)], 512)
+            ops[i]["also"] = max(j for j, o in enumerate(ops) if o["kind"] == "send")
+        else:
+            lin(("U", h), T.U[:, c], T.LCD[:, c], 1.0, 0.0, [("LCD", h)], [("U", h)], 512)
         ac(T.U2[:, c], T.LCD[:, c], [("LCD", h)], [("U2", h)], 512, bias=-8.0, func=ACT.Square)
     TB = (T.TB0, T.TB1, T.TB2)
-    when("tb")
-    for x, M in enumerate((T.PA0, T.PA1)):
-        tt(T.PK[:, 128 * x:128 * x + 128], M[:, 124:252], M[:, 256:384], A.add, PAt, [("PK", x)], 256)
     for i in TBO:
         when("tb%d" % i)
         for h in range(2):
             c, bank = slice(512 * h, 512 * h + 512), 6 + h
-            o, aw = P(bank)[:], T.AW[:, 128 * i:128 * i + 128]
+            o = P(bank)[:]
             if i < 2:
-                mm([(o, aw, T.U[:, c], 512)], [("AW", i), ("U", h)], [B(bank)])
+                mm([(o, T.AW[:, 128 * i:128 * i + 128], T.U[:, c], 512)], [("AW", i), ("U", h)], [B(bank)])
                 ac(TB[i][:, c], o, [("c", "sq")], [B(bank), ("TB", i, h)], 512, bias=col("sq"), func=ACT.Square)
                 continue
-            lst = [(T.PK[:, 0:128], T.FF, [("PK", 0), ("FF", h)]), (T.PK[:, 128:256], T.FF, [("PK", 1), ("FF", h)]),
-                   (T.AW[:, 384:512], T.U, [("AW", 3), ("U", h)]), (aw, T.U2, [("AW", 2), ("U2", h)])]
-            for x, (M, R, rd) in enumerate(lst):
-                mm([(o, M, R[:, c], 512)], rd, [B(bank)], x == 0, x == 3)
-            ac(TB[i][:, c], o, [("c", "hk")], [B(bank), ("TB", i, h)], 512, bias=col("hk"))
+            mm([(o, T.PK[:], T.FF[:, c], 512)], ["PK", ("FF", h)], [B(bank)], True, False)
+            mm([(o, T.AW[:, 384:512], T.U[:, c], 512)], [("AW", 3), ("U", h)], [B(bank)], False, False)
+            mm([(o, T.AW[:, 256:384], T.U2[:, c], 512)], [("AW", 2), ("U2", h)], [B(bank)], False, True)
+            lin(("TB2", h), TB[i][:, c], o, 1.0, col("hk"), [("c", "hk")], [B(bank), ("TB", i, h)], 512)
         dma("sp", TB[i][:, 1024:2048], TB[i][:, 0:1024], [("TB", i, 0), ("TB", i, 1)], [("TB", i, 2), ("TB", i, 3)], 256)
     when("conv")
     for b in range(4):
-        for r in peers if b not in WIDE else ():
-            e, l = 256 + 1024 * b + 256 * r, 1024 * r + 256 * b
-            lin(("conv", b), T.HE[:, e:e + 256], T.LU[:, l:l + 256], 1.0 / UN, HB - 0.5, [("LU", b)],
-                [("HE", e // 128), ("HE", e // 128 + 1)], 256)
+        for h in range(2 if b not in WIDE else 0):
+            l = 1024 * b + 512 * h
+            lin(("conv", b, h), T.HE[:, 256 + l:768 + l], T.LU[:, l:l + 512], 1.0 / UN, HB - 0.5, [("LU", b), ("MU", b)],
+                [("HE", 2 + l // 128 + x) for x in range(4)], 512)
     when("g0")
 
     C0 = 64.0 * 67840 + 2048
@@ -523,7 +521,10 @@ def build_ops(g, T, topo, core, me):
         return 64 * (side if X else 1 - side)
 
     def fused(t, X):
-        return X in FUSED or t == S - 1
+        return X in FUSED
+
+    def signed(t, X):
+        return X in SIGN and t < S - 1
 
     G = (T.G0, T.G1, T.HK)
 
@@ -534,12 +535,13 @@ def build_ops(g, T, topo, core, me):
     def names_of(t, X):
         part(("T", X) if t else None)
         wide = 2048 if t else 1024
-        q, qt = (T.Z16[:, 16 * X:16 * X + 8], ("Z16", X)) if t else (T.Q0L[:, 8 * X:8 * X + 8], "Q0L")
+        q, qt = (T.Z16[:, 16 * X + 8:16 * X + 16], ("Z16", X)) if t else (T.Q0L[:, 8 * X:8 * X + 8], "Q0L")
         for i in (0, 1, 2) if t else (2,):
             ag(tile(i, X), TB[i][:, 0:wide].indirect(q), [("TB", i, h) for h in range(wide // 512)] + [qt], [("G", i, X)], 128)
         if not fused(t, X):
-            ag(T.GZ[:, 128 * X:128 * X + 128], T.ZT[:, 0:wide].indirect(q), [("ZT", h) for h in range(wide // 1024)] + [qt],
-               [("GZ", X)], 128)
+            op("act", lambda: g.scalar.activation(T.GZ[:, 128 * X:128 * X + 128], T.ZT[:, 0:wide].indirect(q), ACT.Identity,
+                                                  bias=-127.5, scale=-1.0),
+               [("ZT", h) for h in range(wide // 1024)] + [qt], [("GZ", X)], 0.06 + 128 * GAT, cls=0)
 
         def rows(i):
             if t:
@@ -547,70 +549,51 @@ def build_ops(g, T, topo, core, me):
             return T.GF[:, 256 * i + 128 * X:256 * i + 128 * X + 128], ("GF", i)
 
         tb = P(2 + X)
-        if t:
-            part(("W", X))
-            c, o, off, e = slice(128 * X, 128 * X + 128), tb[:, 128:256], t % 4 / 4, 128 * REP * X
-            if X in DIRECT:
-                if off:
-                    ts(T.WR[:, c], T.E16[:, c], off - 0.5, off, A.is_lt, A.subtract, [("E16", X)], [("WR", X)], 64)
-                part(("W2", X))
-                if off:
-                    tt(T.ER[:, e:e + 128], T.E16[:, c], T.WR[:, c], A.add, [("E16", X), ("WR", X)], [("ER", X, 0)], 256)
-                else:
-                    cp(T.ER[:, e:e + 128], T.E16[:, c], [("E16", X)], [("ER", X, 0)], 64)
-                lin(("ER2", X), T.ER[:, e + 128:e + 256], T.ER[:, e:e + 128], 1.0, 0.0, [("ER", X, 0)], [("ER", X, 1)],
-                    128 if ("ER2", X) in ON_SCALAR else 64)
-            else:
-                lst, rd = [(o, T.IH[:], T.E16[:, c], 128)], ["IH", ("E16", X)]
-                if off and ("WR", X) in ON_SCALAR:
-                    ac(T.WR[:, c], T.E16[:, c], [("E16", X)], [("WR", X)], 128, bias=(0.5 - off + 0.5 / UN) * EU, func=ACT.Sign)
-                    lst.append((o, T.IN[:], T.WR[:, c], 128))
-                    rd += [("WR", X), "IN"]
-                    off -= 0.5
-                elif off:
-                    ts(T.WR[:, c], T.E16[:, c], (off - 0.5) * EU, EU, A.is_lt, A.mult, [("E16", X)], [("WR", X)], 64)
-                    lst.append((o, T.IH[:], T.WR[:, c], 128))
-                    rd += [("WR", X)]
-                part(("W2", X))
-                mm(lst, rd, [B(2 + X)])
-                for x in range(REP):
-                    lin(("ER", X, x), T.ER[:, e + 128 * x:e + 128 * x + 128], o, 1.0 / EU, -off, [], [B(2 + X), ("ER", X, x)], 128)
+        e, first = 256 * X, ("E16", X)
+        part(("W2", X))
+        if ("ER2", X) in ON_POOL and t:
+            pc(T.ER[:, e + 128:e + 256], T.ER[:, e:e + 128], [first], [("ER", X, 1)], 128)
+        else:
+            lin(("ER2", X), T.ER[:, e + 128:e + 256], T.ER[:, e:e + 128], 1.0, 0.0, [first], [("ER", X, 1)],
+                128 if ("ER2", X) in ON_SCALAR else 64)
         part(("T1", X))
-        ERt = [("ER", X, x) for x in range(REP)]
         for i in range(4):
             ks = range(4 * i, 4 * i + 4)
             bank = (0, 1, 4 + X, 1 - X)[i]
             mms([[(P(bank)[:, 128 * (k % 4):128 * (k % 4) + 128], T.PEN[:, 128 * KT[k][1]:128 * KT[k][1] + 128], rows(KT[k][0])[0], 128)]
                  for k in ks], [("PEN", KT[k][1]) for k in ks] + [rows(KT[k][0])[1] for k in ks], [B(bank)])
-            wd = 128 * REP
-            for x in range(4 // REP):
-                y0 = 2048 * X + 512 * i + wd * x
+            for x in range(2):
+                y0 = 2048 * X + 512 * i + 256 * x
                 if i == 0 and x == 0 and X in NARROW:
-                    for y in range(REP):
-                        tt(T.Y[:, y0 + 128 * y:y0 + 128 * y + 128], P(bank)[:, 128 * y:128 * y + 128], T.ER[:, wd * X:wd * X + 128], A.min,
-                           [("ER", X, 0)], [B(bank), ("Y", X, 0, 0) if y else ("Y0", X)], 128)
+                    for y in range(2):
+                        tt(T.Y[:, y0 + 128 * y:y0 + 128 * y + 128], P(bank)[:, 128 * y:128 * y + 128], T.ER[:, e:e + 128], A.min,
+                           [first], [B(bank), ("Y", X, 0, 0) if y else ("Y0", X)], 128)
                     continue
-                tt(T.Y[:, y0:y0 + wd], P(bank)[:, wd * x:wd * x + wd], T.ER[:, wd * X:wd * X + wd], A.min, ERt,
-                   [B(bank), ("Y", X, i, x)], wd)
+                tt(T.Y[:, y0:y0 + 256], P(bank)[:, 256 * x:256 * x + 256], T.ER[:, e:e + 256], A.min, [first, ("ER", X, 1)],
+                   [B(bank), ("Y", X, i, x)], 256)
             lst, o = [], tb[:, side_at(X, i // 2):side_at(X, i // 2) + 64]
             for k in ks:
                 for u in range(2):
                     s, y0 = 8 * u + k % 8, 2048 * X + 128 * k
                     lst.append((o, T.SW[:, 16 - s:144 - s], T.Y[:, y0 + u:y0 + 128:2], 64))
-            mm(lst, ["SW"] + [("Y0", X)] * (i == 0) + [("Y", X, i, x) for x in range(4 // REP)], [B(2 + X)], i % 2 == 0, i % 2 == 1)
+            mm(lst, ["SW"] + [("Y0", X)] * (i == 0) + [("Y", X, i, x) for x in range(2)], [B(2 + X)], i % 2 == 0, i % 2 == 1)
             if i % 2:
-                a = 128 * X + side_at(X, i // 2)
-                lin(("TL", X, i // 2), T.TL[:, a:a + 64], o, 1.0, C0, [], [B(2 + X), ("TL", X, i // 2)], 64)
-            if i == 1:
-                ac(T.T16[:, 64 * X:64 * X + 64], o, [], [B(2 + X), ("T16", X)], 64, bias=C0 - 2048)
+                a, c0 = 128 * X + side_at(X, i // 2), C0
+                part(("T3", X, i // 2))
+                lin(("TL", X, i // 2), T.TL[:, a:a + 64], o, 1.0, c0, [], [B(2 + X), ("TL", X, i // 2)], 64)
+                if i == 1 and ("T16", X) in ON_SCALAR:
+                    ac(T.T16[:, 64 * X:64 * X + 64], o, [], [B(2 + X), ("T16", X)], 64, bias=c0 - 2048)
+                elif i == 1:
+                    ts(T.T16[:, 64 * X:64 * X + 64], T.TL[:, a:a + 64], -2048.0, None, A.add, None, [("TL", X, 0)], [("T16", X)], 32)
+                part(("T4", X))
 
     def record(t, X):
         part(("R", X))
-        o = P(7)[:, 128 * X:128 * X + 128]
-        e = T.E16[:, 128 * X:128 * X + 128]
-        mm([(o, T.IH[:], e, 128), (o, T.KY[:], tile(2, X), 128)], ["IH", "KY", ("E16", X), ("G", 2, X)], [B(7)])
+        o = P(6 + X)[:, 128:256]
+        e = env(X)
+        mm([(o, T.IH[:], e, 128), (o, T.KY[:], tile(2, X), 128)], ["IH", "KY", ("E16", X), ("G", 2, X)], [B(6 + X)])
         ap, tk = env_at(T, t, me, X)
-        ac(ap, o, [], [B(7), tk], 128, bias=2048.0 if W16 else HB)
+        ac(ap, o, [], [B(6 + X), tk], 128, bias=2048.0 if W16 else HB)
         relay(ap, "h%d" % (2 * t + X), "e%d" % (2 * t + X), [tk], [env_at(T, t, r, X)[1] for r in peers], 96 if W16 else 192)
 
     def high(X):
@@ -623,13 +606,23 @@ def build_ops(g, T, topo, core, me):
 
     def outcomes(t, X):
         part(("O", X))
-        o, l = P(6)[:, 0:8], T.T0L[:, 8 * X:8 * X + 8]
-        mm([(o, T.QW[:, 14 - 2 * a:142 - 2 * a], T.T16[:, 64 * X + a:64 * X + 64:8], 8) for a in range(8)], ["QW", ("T16", X)], [B(6)])
-        lin(("T0L", X), l, o, 1.0, 2048.0, [], [B(6), ("T0L", X)], 8)
-        if t < S - 1:
-            ac(T.HI[:, 16 * X + 8:16 * X + 16], o, [], [B(6), ("HIl", X)], 8, bias=2048.0 + 128 + 128 * X)
+        b, c, l = t % 4, slice(8 * X, 8 * X + 8), T.T0L[:, 8 * X:8 * X + 8]
+        ob, bk = P(6 + X), B(6 + X)
+        o = ob[:, 0:8]
+        mm([(o, T.QW[:, 14 - 2 * a:142 - 2 * a], T.T16[:, 64 * X + a:64 * X + 64:8], 8) for a in range(8)], ["QW", ("T16", X)], [bk])
+        hi, a = T.HI[:, 16 * X:16 * X + 8], 2048.0
+        if b:
+            part(("O2", X))
+            lin(("T0C", X), T.T0C[:, c], o, 1.0, 0.0, [], [bk, ("T0C", X)], 8)
+            ac(T.SG[:, c], o, [], [bk, ("SG", X)], 8, bias=2048.5 - 1024 * b, func=ACT.Sign)
+            o, a = ob[:, 8:16], 4096.0 - 1024 * b
+            mm([(o, T.IH[:], T.T0C[:, c], 8), (o, T.IN[:], T.SG[:, c], 8)], ["IH", "IN", ("T0C", X), ("SG", X)], [bk])
+        part(("O3", X))
+        lin(("T0L", X), l, o, 1.0, a, [], [bk, ("T0L", X)], 8)
+        if t < S - 1 or X in AFTER:
+            lin(("HIl", X), hi, o, 1.0, a + 128 + 128 * X, [], [bk, ("HIl", X)], 8)
         else:
-            ac(T.HI[:, 16 * X + 8:16 * X + 16], T.LO[:, 16 * X + 8:16 * X + 16], [("LOc", X)], [("HIl", X)], 8, bias=128.0)
+            lin(("HIl", X), hi, T.LO[:, 16 * X:16 * X + 8], 1.0, 128.0, [("LOc", X)], [("HIl", X)], 8)
         e = 256 + 1024 * t
         src, rd = T.HE[:, e:e + 4096].indirect(l), [("HE", e // 128 + x) for x in range(32)] + [("T0L", X)]
         if W16:
@@ -639,28 +632,28 @@ def build_ops(g, T, topo, core, me):
                 128 if ("HH", X) in ON_SCALAR else 64)
         else:
             ag(high(X), src, rd, [("HA", X)], 128)
-        mm([(P(6)[:, 64:128], T.CWL[:, 16 - 4 * u:144 - 4 * u], T.HK[:, 256 * X + u:256 * X + 256:4], 64) for u in range(4)],
-           ["CWL", ("HA", X), ("G", 2, X)], [B(6)])
-        ac(T.C4[:, 64 * X:64 * X + 64], P(6)[:, 64:128], [("c", "b4")], [B(6), ("C4", X)], 64, bias=col("b4"))
-        mm([(P(6)[:, 16:32], T.Q4[:, 12 - 4 * a:140 - 4 * a], T.C4[:, 64 * X + a:64 * X + 64:4], 16) for a in range(4)],
-           ["Q4", ("C4", X)], [B(6)])
-        ac(T.HI[:, 16 * X:16 * X + 8], P(6)[:, 16:24], [], [B(6), ("HIq", X)], 8, bias=1024.0)
-        ac(T.LO[:, 16 * X:16 * X + 8], P(6)[:, 24:32], [], [B(6), ("LOq", X)], 8)
+        mm([(ob[:, 64:128], T.CWL[:, 16 - 4 * u:144 - 4 * u], T.HK[:, 256 * X + u:256 * X + 256:4], 64) for u in range(4)],
+           ["CWL", ("HA", X), ("G", 2, X)], [bk])
+        lin(("C4", X), T.C4[:, 64 * X:64 * X + 64], ob[:, 64:128], 1.0, col("b4"), [("c", "b4")], [bk, ("C4", X)], 64)
+        mm([(ob[:, 16:32], T.Q4[:, 12 - 4 * a:140 - 4 * a], T.C4[:, 64 * X + a:64 * X + 64:4], 16) for a in range(4)],
+           ["Q4", ("C4", X)], [bk])
+        lin(("LOq", X), T.LO[:, 16 * X + 8:16 * X + 16], ob[:, 24:32], 1.0, 0.0, [], [bk, ("LOq", X)], 8)
+        lin(("HIq", X), T.HI[:, 16 * X + 8:16 * X + 16], ob[:, 16:24], 1.0, 1024.0, [], [bk, ("HIq", X)], 8)
 
     def bound(t, X):
         part(("E", X))
-        o = P(7)[:, 256 + 128 * X:384 + 128 * X]
-        e = T.E16[:, 128 * X:128 * X + 128]
+        o, bk = P(6 + X)[:, 256:384], B(6 + X)
+        e = env(X)
         c, b = 1024 * t + 128 * (1 - X), 2 * (t % 4) + X
         lst, rd = [(o, T.SH[:], e, 128), (o, T.IB[:], T.IT[:], 128)], ["SH", "IB", "IT", ("E16", X)]
-        if t < S - 1:
-            mm(lst + [(o, T.IB[:], above(X), 128)], rd + [(HT, X)], [B(7)])
-            ac(T.HE[:, c:c + 128], o, ["BC"], [B(7), ("HE", c // 128)], 128, bias=T.BC[:, b:b + 1])
+        if t < S - 1 or X in AFTER:
+            mm(lst + [(o, T.IB[:], above(X), 128)], rd + [(HT, X)], [bk])
+            ac(T.HE[:, c:c + 128], o, ["BC"], [bk, ("HE", c // 128)], 128, bias=T.BC[:, b:b + 1])
             return
         part(("L", X))
-        mm(lst, rd, [B(7)])
+        mm(lst, rd, [bk])
         c, e = slice(256 * X, 256 * X + 256), 256 + 1024 * t
-        ac(T.EO[:, 256 * X:256 * X + 128], o, ["BC"], [B(7), ("EOb", X)], 128, bias=T.BC[:, b:b + 1])
+        ac(T.EO[:, 256 * X:256 * X + 128], o, ["BC"], [bk, ("EOb", X)], 128, bias=T.BC[:, b:b + 1])
         dg(T.EO[:, 256 * X + 128:256 * X + 256], T.HE[:, e:e + 4096].indirect(T.T0L[:, 8 * X:8 * X + 8]), above(X), A.subtract,
            [("HE", e // 128 + x) for x in range(32)] + [("T0L", X), (HT, X), ("EOb", X)], [("EO", X)], 128)
         o = P(X)[:, 0:256]
@@ -670,42 +663,56 @@ def build_ops(g, T, topo, core, me):
 
     def values(t, X):
         part(("V", X))
-        win, wt = T.HV[:, 1024 * t:1024 * t + 4096], [(y, 8 * t + x) for x in range(32) for y in ("HV", "HQ")]
+        a = 4096 * (t % 2)
+        win, wt = T.HV[:, a:a + 4096], [(y, a // 128 + x) for x in range(32) for y in ("HV", "HQ")]
         sb, c = P(4 + X), slice(128 * X, 128 * X + 128)
         cut = X in QUART and t < S - 1
-        h0 = 4096 + 1024 * t + 256 * me + 128 * X
+        h0 = 4096 - a + 1024 * (t % 4) + 256 * me + 128 * X
+        safe = [("HV", 40 + x) for x in range(8)] if (t, X) == (0, 1) else []
         w, tk = (T.HV[:, h0:h0 + 128], ("HV", h0 // 128)) if t < S - 1 else (T.W5[:, c], ("W5", X))
 
         def finish(a, n, y):
             o, f = sb[:, a:a + n], T.FB[:, 128 * X + a:128 * X + a + n]
             out, k = (T.HV[:, h0 + a:h0 + a + n], (y, h0 // 128)) if t < S - 1 else (w, tk)
             lin(("FB", X), f, o, 1.0, -127.5, [], [B(4 + X), ("FB", X, a)], n)
-            tt(out, o, f, A.subtract, [("FB", X, a)], [B(4 + X), k], n)
+            for x in (1, 0) if X in WFIRST and t < S - 1 else (0, 1):
+                if x:
+                    tt(out, o, f, A.subtract, [("FB", X, a)], [B(4 + X), k], n)
+                elif not fused(t, X) and not signed(t, X):
+                    z = slice(128 * X + a, 128 * X + a + n)
+                    tt(T.YS[:, z], o, T.GZ[:, z], A.add, [("GZ", X)], [B(4 + X), ("YS", X, a)], n)
             if t < S - 1:
-                spread([out], "%s%d" % ({"HV": "w", "HQ": "x"}[y], 2 * t + X), [k], [(y, (h0 + 256 * (r - me)) // 128) for r in peers], 0.75 * n)
+                spread([out], "%s%d" % ({"HV": "w", "HQ": "x"}[y], 2 * t + X), [k] + safe, [(y, (h0 + 256 * (r - me)) // 128) for r in peers], 0.75 * n)
 
         for h in range(2):
             j, la, lb = 2 * X + h, 128 * X + 32 * h + side_at(X, 0), 128 * X + 32 * h + side_at(X, 1)
             g0 = slice(512 * j, 512 * j + 512)
             if cut or h == 0:
                 a, n = (64 * h, 64) if cut else (0, 128)
-                mm([(sb[:, a:a + n], T.CK[0:1, 0:128], T.CK[0:1, 128:128 + n], n)], CKt, [B(4 + X)], True, False)
-            ag(T.GA[:, g0], win.indirect(T.TL[:, la:la + 32]), wt + [("TL", X, 0)], [("GA", j)], 512)
-            dg(T.GB[:, g0], win.indirect(T.TL[:, lb:lb + 32]), T.GA[:, g0], A.max, wt + [("TL", X, 1), ("GA", j)], [("GB", j)], 512)
+                mm([(sb[:, a:a + n], T.CK[0:3, 0:128], T.CK[0:3, 0:n], n)], CKt, [B(4 + X)], True, False)
+            a = 0
+            for n in PIECES[j]:
+                g0 = slice(512 * j + 16 * a, 512 * j + 16 * (a + n))
+                ag(T.GA[:, g0], win.indirect(T.TL[:, la + a:la + a + n]), wt + [("TL", X, 0)], [("GA", j, a)], 16 * n)
+                dg(T.GB[:, g0], win.indirect(T.TL[:, lb + a:lb + a + n]), T.GA[:, g0], A.max, wt + [("TL", X, 1), ("GA", j, a)],
+                   [("GB", j, a)], 16 * n)
+                a += n
             mm([(sb[:, 64 * h:64 * h + 64], T.IB[:], T.GB[:, 512 * j + p:512 * j + 512:8], 64) for p in range(8)],
-               ["IB", ("GB", j)], [B(4 + X)], False, cut or h == 1)
+               ["IB"] + [("GB", j, sum(PIECES[j][:x])) for x in range(len(PIECES[j]))], [B(4 + X)], False, cut or h == 1)
             if cut:
                 finish(64 * h, 64, ("HQ", "HV")[h])
         if not cut:
             finish(0, 128, "HV")
-        o, tks = sb[:, 128:256], [tk, ("HQ", h0 // 128)]
+        tks = [tk, ("HQ", h0 // 128)]
         if fused(t, X):
             wide = 2048 if t else 1024
-            q, qt = (T.Z16[:, 16 * X:16 * X + 8], ("Z16", X)) if t else (T.Q0L[:, 8 * X:8 * X + 8], "Q0L")
-            dg(T.YS[:, c], T.ZT[:, 0:wide].indirect(q), w, A.is_le, [("ZT", h) for h in range(wide // 1024)] + [qt] + tks, [("YS", X)], 128)
-        else:
-            mm([(o, ID(-1.0), T.GZ[:, c], 128), (o, T.IB[:], w, 128)], [("ID", 0), "IB", ("GZ", X)] + tks, [B(4 + X)])
-            ac(T.YS[:, c], o, [], [B(4 + X), ("YS", X)], 128, bias=0.5, func=ACT.Sign)
+            q, qt = (T.Z16[:, 16 * X + 8:16 * X + 16], ("Z16", X)) if t else (T.Q0L[:, 8 * X:8 * X + 8], "Q0L")
+            dg(T.YS[:, c], T.ZT[:, 0:wide].indirect(q), w, A.is_le, [("ZT", h) for h in range(wide // 1024)] + [qt] + tks, [("YS", X, 0)], 128)
+        elif signed(t, X):
+            o = sb[:, 128:256]
+            mm([(o, T.IH[:], T.GZ[:, c], 128), (o, T.IB[:], w, 128)], ["IH", "IB", ("GZ", X)] + tks, [B(4 + X)])
+            ac(T.YS[:, c], o, [], [B(4 + X), ("YS", X, 0)], 128, bias=128.0, func=ACT.Sign)
+
         part(("D", X))
         if t == S - 1:
             dma("sp", T.yx[:, 1280 + 128 * X:1408 + 128 * X], w, [tk], [], 32)
@@ -715,34 +722,59 @@ def build_ops(g, T, topo, core, me):
 
     def choose(t, X):
         part(("C", X))
-        o, c, sb = P(4 + X)[:, 256:272], slice(16 * X, 16 * X + 16), B(4 + X)
-        f = fused(t, X)
-        mm([(o, T.Q[:, 0:128], T.M16[:], 16), (o, T.YS[:, 128 * X:128 * X + 128], T.O16[:, 16 * f:16 * f + 16], 16)],
-           ["Q1", ("M16", 0), ("M16", 1), "O16", ("YS", X)], [sb])
-        ac(T.VR[:, c], o, [], [sb, ("VR", X)], 16, bias=-8.0 if f else -16.0, func=ACT.Relu)
-        o = P(4 + X)[:, 272:288]
-        mm([(o, T.IH[:], T.LO[:, c], 16), (o, T.DG[:], T.VR[:, c], 16)], ["DG", "IH", ("VR", X), ("LOc", X), ("LOq", X)], [sb])
-        tt(T.Z16[:, c], o, T.HI[:, c], A.min, [("HIl", X), ("HIq", X)], [sb, ("Z16", X)], 16)
-        l = T.Z16[:, 16 * X + 8:16 * X + 16]
-        if t < S - 1:
+        o, c, sb, z = P(4 + X)[:, 256:272], slice(16 * X, 16 * X + 16), B(4 + X), slice(128 * X, 128 * X + 128)
+        lst, f = [(o, T.FB[:, z], T.O16[:, 0:16], 16), (o, T.YS[:, z], T.O16[:, 16:32], 16)], -24.0
+        if fused(t, X):
+            lst, f = [(o, T.YS[:, z], T.O16[:, 32:48], 16)], -8.0
+        elif signed(t, X):
+            lst, f = [(o, T.YS[:, z], T.O16[:, 48:64], 16)], -16.0
+        mm([(o, T.Q[:, 0:128], T.M16[:], 16)] + lst,
+           ["Q1", ("M16", 0), ("M16", 1), "O16"] + [(y, X, a) for a in (0, 64) for y in ("YS", "FB")], [sb])
+        if ("VR", X) in ON_SCALAR:
+            ac(T.VR[:, c], o, [], [sb, ("VR", X)], 16, bias=f, func=ACT.Relu)
+        else:
+            ts(T.VR[:, c], o, f, 0.0, A.add, A.max, [], [sb, ("VR", X)], 16)
+        o = P(2 + X)[:, 256:272]
+        mm([(o, T.IH[:], T.LO[:, c], 16)], ["IH", ("LOc", X), ("LOq", X)], [B(2 + X)], True, False)
+        mm([(o, T.DG[:], T.VR[:, c], 16)], ["DG", ("VR", X)], [B(2 + X)], False, True)
+        tt(T.Z16[:, c], o, T.HI[:, c], A.min, [("HIl", X), ("HIq", X)], [B(2 + X), ("Z16", X)], 16)
+        l = T.Z16[:, 16 * X:16 * X + 8]
+        if t < S - 1 or X in AFTER:
             a = 1024 * t + 128 * (1 - X)
-            dg(T.E16[:, 128 * X:128 * X + 128], T.HE[:, a:1024 * t + 4352].indirect(l), above(X), A.subtract,
+            dg(env(X), T.HE[:, a:1024 * t + 4352].indirect(l), above(X), A.subtract,
                [("HE", 8 * t + x) for x in range(1 - X, 34)] + [("Z16", X), (HT, X)], [("E16", X)], 128)
-            return
+            if t < S - 1:
+                return
         part(None)
         c = slice(128 * X, 128 * X + 128)
-        op("dve", lambda: g.vector.tensor_copy(T.OUT[:, c], T.OW[:, 256 * X:256 * X + 256].indirect(l)), [("OW", X), ("Z16", X)],
-           [("OUT", X)], 0.06 + 128 * GAT, cls=0)
+        if X in AFTER:
+            o = P(X)[:, 0:128]
+            lst, rd = swap(o, env(X), UN, slice(256 * X, 256 * X + 128), ("E16", X), 3 + X, T.IH[:])
+            mm(lst, ["IH"] + rd, [B(X)])
+            ac(T.OUT[:, c], o, [], [B(X), ("OUT", X)], 128, scale=UN, bias=2048.0 + UN * SWC)
+        else:
+            op("dve", lambda: g.vector.tensor_copy(T.OUT[:, c], T.OW[:, 256 * X:256 * X + 256].indirect(l)), [("OW", X), ("Z16", X)],
+               [("OUT", X)], 0.06 + 128 * GAT, cls=0)
         dma("sp", T.ye[:, c], T.OUT[:, c], [("OUT", X)], [], 64)
-        ag(T.YC[:, c], T.IDX[:, 0:2048].indirect(T.Z16[:, 16 * X:16 * X + 8]), [("IDX", x) for x in range(4)] + [("Z16", X)],
+        ag(T.YC[:, c], T.IDX[:, 0:2048].indirect(T.Z16[:, 16 * X + 8:16 * X + 16]), [("IDX", x) for x in range(4)] + [("Z16", X)],
            [("YC", X)], 128)
         dma("act", T.yc[:, c], T.YC[0:128:16, c], [("YC", X)], [], 4)
 
+    def carry(a, b):
+        tk = [[(y, (x + 1024 * b) // 128 + i) for i in range(8) for y in ("HV", "HQ")] for x in (a, 4096 - a)]
+        dma("sp", T.HV[:, 4096 - a + 1024 * b:4096 - a + 1024 * b + 1024], T.HV[:, a + 1024 * b:a + 1024 * b + 1024], tk[0], tk[1], 256)
+
+    when("carry")
+    for b in (1, 2, 3):
+        carry(0, b)
     role[2] = -1
     names_of(0, 0)
     names_of(0, 1)
     for t in range(S):
         role[2] = t
+        if 0 < t < S - 1:
+            part(("K",))
+            carry(4096 * (t % 2), (t - 1) % 4)
         for X in range(2 if t < S - 1 else 0):
             record(t, X)
         for X in range(2):
@@ -762,7 +794,7 @@ def helper_program(g, core, T, topo, r):
     full = sum(1 << e for e in es)
     n_in = len(inner_engines(topo, T.cores[r], T.cores[peers[0]]))
     ids = [dst_id(topo, T.cores[p]) for p in peers]
-    jobs = [("hu%d" % b, "u%d" % b, T.MU[:, 256 * b:256 * b + 256], T.LU[:, 1024 * r + 256 * b:1024 * r + 256 * b + 256])
+    jobs = [("hu%d" % b, "u%d" % b) + 2 * (T.LU[:, 1024 * b + 256 * r:1024 * b + 256 * r + 256],)
             if b not in WIDE else ("hu%d" % b, "u%d" % b) + 2 * (T.HE[:, 256 + 1024 * b + 256 * r:512 + 1024 * b + 256 * r],)
             for b in range(4) if b not in OWN]
     jobs = [("hv%d" % b, "v%d" % b) + 2 * (T.HV[:, 1024 * b + 256 * r:1024 * b + 256 * r + 256],)
@@ -838,10 +870,10 @@ def search(ops):
             post[d].append((i, x - dur[d] + dur[i]))
     cases = []
     for cs in CASES:
-        du = [o["dur"] * (cs[o.get("cls", 2 if o["eng"] == "pe" else 1)] if o["kind"] == "c" else cs[4] if o["kind"] == "recv" else 1.0)
-              for o in ops]
-        cases.append((du, [[(d, x - dur[d] + du[d] + (cs[3] if ops[d]["kind"] == "recv" else 0.0)) for d, x in pre[i]]
-                           for i in range(n)]))
+        du = [o["dur"] * (cs[o.get("cls", 2 if o["eng"] == "pe" else 1)] if o["kind"] == "c" else
+                          {"recv": cs[4], "land": cs[6]}.get(o["kind"], 1.0)) for o in ops]
+        cases.append((du, [[(d, x - dur[d] + du[d] + (cs[3] if ops[d]["kind"] == "recv" else 0.0) + cs[5] * (x > dur[d] + 0.01))
+                            for d, x in pre[i]] for i in range(n)]))
 
     def fill(order, dep, first):
         busy, t0 = {e: [] for e in eng}, [0.0] * n
@@ -979,24 +1011,225 @@ def search(ops):
                     best = (e2, t2)
         return best
 
-    end, t0 = anneal(base, post, lat, ROUNDS // 4, HEAT)
-    for step, share in ((1, 2), (2, 4)):
-        m, u = min(i for i in range(n) if ops[i]["step"] == step), backward(t0, post, lat)
-        tail = [max([lat[i]] + [u[j] + x for j, x in post[i] if j >= m]) for i in range(m)]
-        near = [[(j, x) for j, x in post[i] if j < m] for i in range(m)]
-        e1, t1 = anneal(list(t0[:m]), near, tail, ROUNDS // share, 2 * HEAT)
-        gain = max(t0[i] + dur[i] + tail[i] for i in range(m)) - max(t1[i] + dur[i] + tail[i] for i in range(m))
-        end, t0 = min((end, t0), anneal(t1 + [x - gain for x in t0[m:]], post, lat, ROUNDS // 8, HEAT / 2))
-    ga = [t0[i] for i in range(n) if ops[i]["role"] == (("V", 0), 1)]
-    tries = [(end, t0)]
-    for s in (1, 2, 3):
-        rel = {o["role"]: t0[i] - ga[s] for i, o in enumerate(ops) if o["step"] == s}
-        per = ga[s + 1] - ga[s]
-        key = [t0[i] if o["step"] < 1 else ga[1] + per * (o["step"] - 1) + (rel[o["role"]] if o["step"] < S - 1 and o["role"] in rel
-                                                                           else t0[i] - ga[o["step"]]) for i, o in enumerate(ops)]
-        tries.append(place(key, post, lat))
-    end, t0 = min((end, t0), anneal(list(min(tries)[1]), post, lat, ROUNDS // 8, HEAT / 2))
-    return anneal(list(t0), post, lat, ROUNDS // 8, HEAT, max(t0) - 12.0)
+    def cyclic(rounds, heat):
+        own = [i for i in range(n) if ops[i]["step"] == 2]
+        at = {ops[i]["role"]: j for j, i in enumerate(own)}
+        m, laps = len(own), 5
+        en = [eng[i] for i in own]
+        dep = [[[(at[ops[d]["role"]], 2 - ops[d]["step"], x) for d, x in pr[i] if ops[d]["step"] > 0 and ops[d]["role"] in at]
+                for i in own] for _, pr in cases]
+        dus = [[du[i] for i in own] for du, _ in cases]
+        after = [[] for _ in own]
+        for j in range(m):
+            for d, dt, _ in dep[0][j]:
+                after[d].append((j, dt))
+        first = at[(("V", 0), 1)]
+
+        def run(key, per, top=1e9):
+            lap = [int(key[j] // per) for j in range(m)]
+            seq = sorted(range(m), key=lambda j: key[j] - per * lap[j])
+            total, out = 0.0, None
+            for du, pr in zip(dus, dep):
+                rows = [(j, en[j], du[j], [(d, dt + lap[j] - lap[d], x) for d, dt, x in pr[j]]) for j in seq]
+                t, free = [], {}
+                for c in range(laps):
+                    row = [0.0] * m
+                    t.append(row)
+                    for j, e, d0, ps in rows:
+                        s = free.get(e, 0.0)
+                        for d, back, x in ps:
+                            if back <= c and t[c - back][d] + x > s:
+                                s = t[c - back][d] + x
+                        row[j] = s
+                        free[e] = s + d0
+                p = (t[-1][first] - t[1][first]) / (laps - 2)
+                total += p
+                if out is None:
+                    z = t[-2][first] + p * lap[first]
+                    if p > top:
+                        return 1e9, None
+                    out = ([t[-2][j] + p * lap[j] - z + 1e-6 * (key[j] - key[first]) for j in range(m)], p)
+            return total / len(dus), out
+
+        def sound(key, per):
+            return all(key[j] > key[d] - dt * per for j in range(m) for d, dt, _ in dep[0][j])
+
+        per, key = PERIOD, [ops[i]["aim"] for i in own]
+        if "seed" in PLAN:
+            per, key = PLAN["seed"]([ops[i] for i in own])
+        for _ in range(20):
+            for j in range(m):
+                key[j] = max([key[j]] + [key[d] - dt * per + 1e-3 for d, dt, _ in dep[0][j]])
+        while not sound(key, per):
+            per += 0.2
+        cost, out = run(key, per)
+        best = (cost, key, per)
+
+        def waits(t, p):
+            seq, prev, last, found, seen, j = sorted(range(m), key=lambda y: t[y] % p), {}, {}, [], set(), first
+            for y in seq + seq:
+                prev[y] = last.get(en[y])
+                last[en[y]] = y
+            while j not in seen:
+                seen.add(j)
+                s, d = max([(t[d] - dt * p + x, d) for d, dt, x in dep[0][j]], default=(-1e9, None))
+                if t[j] > s + 1e-3:
+                    d = prev[j]
+                    found.append((d, j))
+                j = d
+            return found
+
+        links = None
+        for it in range(rounds):
+            if links is None and sound(*out):
+                key, per = out
+                links = waits(key, per)
+            k2 = list(key)
+            move = rnd()
+            if move < 0.7:
+                j, x = int(rnd() * m), (rnd() + rnd() - 1.0) * (0.5, 1.5)[int(rnd() * 2)]
+                if links and move < 0.4:
+                    a, b = links[int(rnd() * len(links))]
+                    x = (key[b] - key[a]) % per + 0.002 + rnd() * rnd() * rnd()
+                    j, x = (a, x) if rnd() < 0.5 else (b, -x)
+                k2[j] += x
+                todo, left = [j], 3 * m
+                while todo and left:
+                    j, left = todo.pop(), left - 1
+                    for d, dt in after[j] if x > 0 else [y[:2] for y in dep[0][j]]:
+                        edge = k2[j] + (-dt * per + 1e-4 if x > 0 else dt * per - 1e-4)
+                        if (k2[d] < edge) if x > 0 else (k2[d] > edge):
+                            k2[d] = edge
+                            todo.append(d)
+                if todo or not sound(k2, per):
+                    continue
+            for _ in range(int(rnd() * 1.5) if move < 0.7 else 1 + int(rnd() * rnd() * 4)):
+                j = int(rnd() * m)
+                lo = max([k2[d] - dt * per for d, dt, _ in dep[0][j]], default=k2[j] - 3.0)
+                hi = min([k2[d] + dt * per for d, dt in after[j]], default=k2[j] + 3.0)
+                k2[j] = lo + (hi - lo) * (0.001 + 0.998 * rnd())
+            c2, o2 = run(k2, per, out[1] + 0.1 + heat)
+            if c2 <= cost + heat * (1.0 - it / rounds) * rnd():
+                cost, out, key, links = c2, o2, k2, None
+                if c2 < best[0]:
+                    best = (c2, k2, per)
+        cost, key, per = best
+        out = run(key, per)[1]
+        if sound(*out):
+            key, per = out
+        PLAN["cycle"] = (cost, per, [(key[j], en[j], ops[i]) for j, i in enumerate(own)])
+        return [FIRST + per * o["step"] + key[at[o["role"]]] if "aim" in o and o["role"] in at else base[i] for i, o in enumerate(ops)]
+
+    def stretch(key, lo, hi, rounds, heat):
+        seq = sorted(range(n), key=lambda j: (key[j], j))
+        head, mid = [j for j in seq if key[j] < lo], [j for j in seq if lo <= key[j] < hi + 14.0]
+        free = [j for j in mid if key[j] < hi]
+        goal = [j for j in mid if key[j] >= hi + 9.0] or mid
+
+        def times(order, du, pr, t, busy):
+            for j in order:
+                s = busy.get(eng[j], 0.0)
+                for d, x in pr[j]:
+                    if t[d] + x > s:
+                        s = t[d] + x
+                t[j] = s
+                busy[eng[j]] = s + du[j]
+
+        fixed = []
+        for du, pr in cases:
+            fixed.append(([0.0] * n, {}))
+            times(head, du, pr, *fixed[-1])
+
+        def run(k, top=1e9):
+            order, total, out = sorted(mid, key=lambda j: k[j]), 0.0, None
+            for (du, pr), (t, busy) in zip(cases, fixed):
+                t = list(t)
+                times(order, du, pr, t, dict(busy))
+                e = max(t[j] + du[j] + lat[j] for j in goal) if goal is mid else sum(t[j] for j in goal) / len(goal)
+                total += e
+                if out is None:
+                    if e > top:
+                        return 1e9, None
+                    out = (t, e, order)
+            return total / len(cases), out
+
+        def waits(t, order):
+            prev, last, found = {}, {}, []
+            for j in order:
+                prev[j] = last.get(eng[j])
+                last[eng[j]] = j
+            j = max(goal, key=lambda y: t[y] + lat[y]) if goal is mid else goal[int(rnd() * len(goal))]
+            while j in prev:
+                s, d = max([(t[d] + x, d) for d, x in cases[0][1][j]], default=(0.0, None))
+                if t[j] > s + 1e-3 and prev[j] is not None:
+                    d = prev[j]
+                    found.append((d, j))
+                j = d
+            return found
+
+        inside = set(free)
+        cost, out = run(key)
+        best, links = (cost, list(key)), None
+        for it in range(rounds):
+            if links is None or it % 64 == 0:
+                links = [x for x in waits(out[0], out[2]) if x[0] in inside and x[1] in inside]
+            k2, move = list(key), rnd()
+            j, x = free[int(rnd() * len(free))], (rnd() + rnd() - 1.0) * (0.4, 1.5, 3.0)[int(rnd() * 3)]
+            if links and move < 0.5:
+                a, b = links[int(rnd() * len(links))]
+                x = key[b] - key[a] + 0.002 + rnd() * rnd() * rnd() * 2.0
+                j, x = (a, x) if rnd() < 0.5 else (b, -x)
+            k2[j] += x
+            todo, ok = [j], lo <= k2[j] < hi
+            while todo and ok:
+                j = todo.pop()
+                for d, _ in post[j] if x > 0 else pre[j]:
+                    if (k2[d] <= k2[j]) if x > 0 else (k2[d] >= k2[j]):
+                        k2[d] = k2[j] + (1e-4 if x > 0 else -1e-4)
+                        ok = ok and d in inside and lo <= k2[d] < hi
+                        todo.append(d)
+            if not ok:
+                continue
+            c2, o2 = run(k2, out[1] + 0.15 + heat)
+            if c2 <= cost + heat * (1.0 - it / rounds) * rnd():
+                cost, out, key, links = c2, o2, k2, None
+                if c2 < best[0]:
+                    best = (c2, list(k2))
+        return best[1]
+
+    def settle(key):
+        du, pr = cases[0]
+        t, busy = [0.0] * n, {}
+        for r, j in enumerate(sorted(range(n), key=lambda y: (key[y], y))):
+            t[j] = max([busy.get(eng[j], 0.0)] + [t[d] + x for d, x in pr[j]])
+            busy[eng[j]] = t[j] + du[j]
+            key[j] = t[j] + 1e-7 * r
+        return key
+
+    base = cyclic(CYCLE, WARM)
+    if not ROUNDS:
+        return 0.0, forward(base)
+    key = forward(list(base))
+    ga = [i for i in range(n) if ops[i]["role"] == (("V", 0), 1)]
+    for i in range(n):
+        if 0 < ops[i]["step"] < S - 1:
+            key[i] = base[i] - base[ga[1]] + key[ga[1]]
+    for i in range(n - 1, -1, -1):
+        for d, _ in pre[i]:
+            key[d] = min(key[d], key[i] - 1e-4)
+    key = settle(key)
+    for share, heat in ((3, 0.3), (3, 0.1), (6, 0.04)):
+        key = settle(stretch(key, 0.0, key[ga[1]] + 6.0, ROUNDS // share, heat))
+    for heat in (0.15, 0.04):
+        key = settle(stretch(key, key[ga[S - 1]] - 6.0, 1e9, ROUNDS // 6, heat))
+    total = 0.0
+    for du, pr in cases:
+        t, busy = [0.0] * n, {}
+        for j in sorted(range(n), key=lambda y: key[y]):
+            t[j] = max([busy.get(eng[j], 0.0)] + [t[d] + x for d, x in pr[j]])
+            busy[eng[j]] = t[j] + du[j]
+        total += max(t[j] + du[j] + lat[j] for j in range(n))
+    return total / len(cases), key
 
 
 def emit(g, T, ops, seq):

@@ -4,26 +4,27 @@ from concourse.mybir import AluOpType, AxisListType, ActivationFunctionType
 N, S = 4, 6
 F32, BF, F16, I32, U16 = "float32", "bfloat16", "float16", "int32", "uint16"
 UN = 4096.0
-HB = 272.0
-W16 = False
+HB = 136.0
 QUART = ()
 NARROW = (0,)
 KT = [divmod(k, 7) for k in range(16)]
-TBO = (0, 1, 2)
-WIDE = (1,)
-EU = UN if W16 else 1.0
-ON_SCALAR = ({(x, X) for x in ("T0L", "T0C", "LOq", "HIq", "HIl", "C4", "VR", "TB2", "FB", "ER2", "U") for X in range(2)} | {("N16", 0), ("T16", 0), ("E0", 0), ("E0", 1), ("CF", 1), ("FF", 1), ("conv", 0, 0), ("conv", 2, 0), ("conv", 3, 0)}
-             | {("TL", X, 0) for X in range(2)} | {("own", b) for b in range(4)})
+WIDE = ()
+ON_SCALAR = ({(x, X) for x in ("T0L", "T0C", "SG", "LOq", "HIq", "HIl", "C4", "VR", "TB2", "FB", "ER2", "U") for X in range(2)}
+             | {("T16", 0), ("FBL", 0), ("E0", 0), ("E0", 1), ("CF", 1), ("FF", 0), ("FF", 1)}
+             | {("conv", b, h) for b, h in ((0, 0), (1, 0), (2, 0), (3, 0), (0, 1), (2, 1))}
+             | {("TL", X, 0) for X in range(2)} | {(x, b) for x in ("own", "N16") for b in range(4)})
 ON_VECTOR = set()
-ON_POOL = set()
-AFTER = (0,)
+ON_POOL = {("U", 0), ("U", 1)}
+AFTER = ()
+FAST = 2
+VOTES = (2, 5)
 WFIRST = (1,)
 PIECES = ((32,), (32,), (32,), (32,))
 FUSED = ()
 SIGN = ()
-OWN = (0, 2, 3)
-VOWN = (0, 1)
-VIA = {"hv2": (1, 0), "hv3": (1, 1), "hu1": (1, 2)}
+OWN = (0, 2)
+VCUT = (0, 512, 768, 1024)
+VIA = {"hv1": (1, 0), "hv2": (1, 1), "hu1": (1, 2), "hu3": (1, 3)}
 STEP2 = 1
 
 
@@ -32,15 +33,15 @@ def _sb(cols, dtype):
 
 
 SCRATCH = {
-    "HV": _sb(8192, BF), "HE": _sb(9472, U16 if W16 else F32), "HH": _sb(256, BF), "W5": _sb(256, BF),
+    "HV": _sb(8192, BF), "HE": _sb(9984, F32), "W5": _sb(256, BF),
     "LCD": _sb(1024, I32), "LCE": _sb(1024, I32), "LE": _sb(256, I32), "CT": _sb(1024, I32), "C0": _sb(256, I32),
     "U": _sb(1024, BF), "CF": _sb(1024, F16), "C16": _sb(256, F16), "FF": _sb(1024, F16),
-    "N16": _sb(1280, F16), "LU": _sb(4096, U16),
+    "N16": _sb(1024, F16), "LU": _sb(4096, U16),
     "TB0": _sb(2048, BF), "TB1": _sb(2048, BF), "TB2": _sb(2048, BF), "ZT": _sb(2048, BF), "IDX": _sb(2048, F32),
-    "OW": _sb(512, F32), "EO": _sb(512, F16), "G0": _sb(256, BF), "G1": _sb(256, BF), "HK": _sb(512, BF), "GZ": _sb(256, F16),
-    "F1": _sb(1280, BF), "F2": _sb(1280, BF), "VR": _sb(32, BF),
-    "C4": _sb(128, F16), "Q4": _sb(144, F16), "Q0L": _sb(16, U16), "U0": _sb(256, BF), "GF": _sb(768, BF), "BX": _sb(8, BF), "DG": _sb(128, BF), "M16": _sb(16, BF), "O16": _sb(64, BF),
-    "Y": _sb(4096, F16), "ER": _sb(512, F16), "SG": _sb(16, BF), "HI": _sb(32, F32), "T0C": _sb(16, F16), "IN": _sb(128, BF), "U2": _sb(1024, BF),
+    "EO": _sb(512, F32), "G0": _sb(256, BF), "G1": _sb(256, BF), "HK": _sb(512, BF), "GZ": _sb(256, F16),
+    "VR": _sb(32, BF),
+    "C4": _sb(128, F16), "Q4": _sb(144, F16), "Q0L": _sb(16, U16), "BX": _sb(8, BF), "DG": _sb(128, BF), "M16": _sb(16, BF), "O16": _sb(32, BF), "VC": _sb(128, BF), "AC": _sb(128, F16),
+    "Y": _sb(4096, F16), "ER": _sb(512, F16), "SG": _sb(32, BF), "HI": _sb(32, U16), "T0C": _sb(16, F16), "I3": _sb(256, BF),
     "PEN": _sb(896, BF), "SW": _sb(144, F16), "SEL": _sb(8, F32),
     "TL": _sb(256, U16), "T16": _sb(128, F16), "T0L": _sb(16, U16),
     "LO": _sb(32, F16), "Z16": _sb(32, U16),
@@ -49,9 +50,9 @@ SCRATCH = {
     "PI": _sb(1, I32), "PJ": _sb(8, I32), "PC": _sb(96, F32), "XF": _sb(176, BF), "V1": _sb(128, BF), "JP": _sb(128, BF),
     "BG": _sb(128, BF), "VA": _sb(384, BF), "V2": _sb(128, BF), "VQ": _sb(144, BF), "RQ": _sb(56, F32),
     "Q": _sb(256, BF), "CWL": _sb(144, BF), "QW": _sb(144, F16),
-    "Q0": _sb(144, F16), "AW": _sb(512, BF), "XH": _sb(128, BF), "PK": _sb(128, F16), "PA0": _sb(384, F16),
-    "PA1": _sb(384, F16), "RE": _sb(128, F16), "IB": _sb(128, BF), "ID": _sb(640, BF), "IH": _sb(128, F16),
-    "IS": _sb(128, F16), "SH": _sb(128, F16), "KY": _sb(128, BF), "IT": _sb(128, BF), "BC": _sb(8, F32), "CK": _sb(256, BF),
+    "Q0": _sb(144, F16), "AW": _sb(512, BF), "U0": _sb(256, BF), "GF": _sb(768, BF), "XH": _sb(128, BF), "PA0": _sb(384, F16),
+    "PA1": _sb(384, F16), "PC0": _sb(128, F16), "RE": _sb(128, F16), "IB": _sb(128, BF), "IH": _sb(128, F16),
+    "SH": _sb(128, F16), "KY": _sb(128, BF), "IT": _sb(128, BF), "BC": _sb(8, F32), "CK": _sb(256, BF),
     "SF": _sb(2, F32),
 }
 for _b in range(8):
@@ -62,23 +63,25 @@ SEMAPHORES = (["pe", "act", "dve", "pool", "sent"] + ["d%d" % i for i in range(N
 
 CYC, GAT, PEC, HOP, LAT, RATE, LOCAL = 1.0e-3, 1.45e-3, 0.5e-3, 0.115, 1.7, 80.0, 250.0
 CASES = ((0.95, 0.95, 0.95, 0.2, 1.0, 0.0, 1.0), (0.75, 0.9, 0.9, 1.7, 1.3, -0.02, 1.4), (1.2, 1.1, 1.1, 0.0, 0.9, 0.03, 0.8))
-CYCLE, WARM = 1000, 0.005
-ROUNDS, HEAT, SEED, PLAN = 150000, 0.04, 1, {}
-PERIOD, FIRST = 9.74, 16.0
-START = {"x01": 0.0, "codes": 0.2, "x23": 0.02, "ce0": 0.3, "ce1": 0.36, "cd": 0.4, "e": 0.33, "z": 6.0, "send": 2.6, "iota": 0.0,
-         "iota2": 4.5, "idx": 12.0, "early": 0.1, "cols": 0.5, "mats": 4.0, "late": 12.5, "q0": 3.4, "cf": 1.0, "env0": 0.9,
-         "env1": 5.5, "fast": 7.0, "e16": 5.0, "u": 9.6, "tb": 10.0, "tb0": 11.0, "tb1": 12.0, "tb2": 14.0, "conv": 15.0,
-         "g0": 16.5, "t0": 2.5, "carry": 14.0}
+CYCLE, WARM, TURNS = 3000, 0.005, 0
+HEATS, EARLY = ((6, 0.08), (6, 0.06), (6, 0.04), (6, 0.03), (6, 0.015)), 0.3
+ROUNDS, HEAT, SEED, PLAN = 200000, 0.04, 3, {}
+PERIOD, FIRST, LATE = 9.74, 12.5, 3.0
+START = {"x01": 0.02, "codes": 0.05, "x23": 0.0, "ce0": 0.1, "ce1": 0.4, "cd": 0.2, "e": 0.3, "z": 6.0, "send": 2.55, "iota": 0.0,
+         "iota2": 4.0, "idx": 12.0, "early": 0.1, "cols": 0.5, "mats": 3.0, "late": 5.5, "q0": 2.6, "cf": 3.4, "env0": 4.9,
+         "env1": 8.5, "fast": 6.9, "e16": 7.4, "u": 7.3, "tb": 13.0, "tb0": 10.0, "tb1": 10.1, "tb2": 9.2, "conv": 12.4, "conv2": 17.5,
+         "g0": 10.5, "t0": 2.8, "carry": 13.0}
 AIM = {("V", 0): [-0.69, 0.0, 1.19, 2.34, 0.76, 1.95, 2.83, 3.28, 3.69, 3.85, 4.12, 4.74],
        ("V", 1): [1.33, 1.76, 2.93, 3.88, 2.52, 4.01, 4.88, 5.33, 5.62, 5.78, 5.9, 6.51],
-       ("C", 0): [4.17, 4.42, 4.54, 4.61, 4.81, 5.02], ("C", 1): [6.33, 6.59, 5.73, 6.77, 7.11, 7.49],
+       ("C", 0): [4.0, 4.3, 4.6, 4.61, 4.81, 5.02], ("C", 1): [6.33, 6.59, 5.73, 6.77, 7.11, 7.49],
        ("T", 0): [5.09, 5.64, 6.05, 6.66], ("T", 1): [7.32, 7.95, 8.37, 13.39], ("W2", 0): [5.87], ("W2", 1): [8.19],
        ("T1", 0): [5.44, 5.94, 6.1, 6.26, 7.02, 6.04, 6.54, 6.83, 7.31], ("T1", 1): [7.89, 8.57, 8.85, 10.31, 9.15, 9.7, 9.98, 10.61],
        ("T4", 0): [6.47, 7.21, 7.72, 9.73, 7.6, 8.01, 8.29, 10.02], ("T4", 1): [8.47, 9.13, 9.42, 11.49, 9.44, 10.26, 10.64, 11.78],
        ("T3", 0, 0): [7.72, 7.84], ("T3", 1, 0): [11.26, 12.55], ("T3", 0, 1): [10.54], ("T3", 1, 1): [12.45],
        ("R", 0): [-2.89, -2.6, -2.31, -1.69], ("R", 1): [-0.97, -0.69, -0.39, 0.72],
-       ("O", 0): [-1.55], ("O", 1): [3.12], ("O2", 0): [-1.14, -1.07, -0.8], ("O2", 1): [3.52, 3.59, 3.77], ("K",): [0.0, 0.22],
-       ("O3", 0): [-0.51, -0.44, -0.33, 1.16, 1.64, 3.41, 3.89, 4.06], ("O3", 1): [3.99, 4.49, 4.17, 4.69, 4.98, 5.21, 5.51, 5.57],
+       ("O", 0): [-1.55], ("O", 1): [3.12], ("O2", 0): [-1.14, -1.07, -1.0, -0.8], ("O2", 1): [3.46, 3.52, 3.59, 3.77], ("K",): [0.0, 0.52], ("I",): [0.5, 1.3, 2.1],
+       ("O3", 0): [-0.51, -0.33], ("O4", 0): [1.16, 1.64, 3.41, 3.89, 4.06], ("O3", 1): [3.99, 4.17], ("O4", 1): [4.69, 4.98, 5.21, 5.51, 5.57],
+       ("L2", 0): [0.0], ("L2", 1): [3.0],
        ("E", 0): [4.31, 4.65], ("E", 1): [5.81, 6.28], ("L", 0): [-0.5], ("L", 1): [3.0],
        ("D", 0): [6.0], ("D", 1): [5.9, 6.11]}
 
@@ -93,8 +96,16 @@ def dst_id(topo, c):
     return DstId(rid=rid, pnc=pid)
 
 
+def slot(k, r):
+    return 1024 * k + 256 * (k // 4 + 1) + 256 * (N - 1 - r)
+
+
+def values_at(T, r, b):
+    return T.HV[:, 1024 * r + VCUT[b]:1024 * r + VCUT[b + 1]]
+
+
 def env_at(T, t, r, X):
-    c = 4352 + 1024 * t + 256 * r + 128 * X
+    c = slot(4 + t, r) + 128 * X
     return T.HE[:, c:c + 128], ("HE", c // 128)
 
 
@@ -167,6 +178,9 @@ def build_ops(g, T, topo, core, me):
             return op("dve", lambda: g.vector.tensor_copy(out, src), rd, wr, 0.06 + n * GAT, cls=0)
         return op("act", lambda: g.scalar.activation(out, src, ACT.Copy), rd, wr, 0.06 + n * GAT, cls=0)
 
+    def gs(out, src, func, bias, scale, rd, wr, n):
+        return op("act", lambda: g.scalar.activation(out, src, func, bias=bias, scale=scale), rd, wr, 0.06 + n * GAT, cls=0)
+
     def dg(out, src, in1, o, rd, wr, n):
         return op("dve", lambda: g.vector.tensor_tensor(out, src, in1, o), rd, wr, 0.06 + n * GAT, cls=0)
 
@@ -197,7 +211,8 @@ def build_ops(g, T, topo, core, me):
 
     def dma(q, out, in_, rd, wr, kb):
         e = g.sync if q == "sp" else g.scalar
-        i = op(q, lambda: e.dma_start(out, in_), rd, wr, 0.1, kind="dma")
+        pairs = list(zip(out, in_)) if isinstance(out, list) else [(out, in_)]
+        i = op(q, lambda: [e.dma_start(a, b) for a, b in pairs], rd, wr, 0.1 * len(pairs), kind="dma")
         return op("ring", None, [], wr, 0.01 + kb / LOCAL, lat=1.9, kind="land", after=i)
 
     def P(b):
@@ -235,18 +250,24 @@ def build_ops(g, T, topo, core, me):
         rid, pid, _ = topo.addr(hc)
         sd = op("pool", lambda: g.remote_dma(ap, ap, T.sem[hsem], T.sem.sent, pid, rid, mask(in_e)), rd, [], 0.5,
                 kind="send", inc=len(in_e))
-        i = recv(sd, "link" if topo.die(hc) == topo.die(core) else "link2", 2 * LAT + 0.5 + kb / 450.0, kb, sem, 3 * ne, wr)
-        ops[i]["also"] = last.get(hc)
-        last[hc] = i
+        role[1] -= 1
+        hop = op(("helper", hc), None, [], [], 0.5, lat=LAT + kb / 450.0, kind="hop", after=sd)
+        ops[hop]["role"] = ops[hop]["role"] + ("hop",) if role[0] is not None else ops[hop]["role"]
+        ops[hop]["also"] = last.get(hc)
+        last[hc] = hop
+        recv(hop, "link" if topo.die(hc) == topo.die(core) else "link2", LAT, kb, sem, 3 * ne, wr)
 
-    for b in range(4):
-        c = 1024 * b + 256 * me
-        when("x01" if b < 2 else "x23")
-        dma("sp", T.HV[:, c:c + 256], T.x0[:, 256 * b:256 * b + 256], [], [("HV", c // 128), ("HV", c // 128 + 1)], 64)
+    def first_values(r, b):
+        return [("HV", 8 * r + x) for x in range(VCUT[b] // 128, VCUT[b + 1] // 128)]
+
+    for b in range(len(VCUT) - 1):
+        when("x23" if b else "x01")
+        dma("sp", values_at(T, me, b), T.x0[:, VCUT[b]:VCUT[b + 1]], [], first_values(me, b), (VCUT[b + 1] - VCUT[b]) / 4)
     when("codes")
     dma("act", T.C0[0:8, :], T.c0[:], [], ["C0"], 16)
     for i, src in enumerate((T.cc0, T.ky, T.kid)):
         dma("act", T.CT[8 * i:8 * i + 8, :], src[:], [], [("CT", i)], 48)
+    dma("sp", [T.CT[24 + 8 * x:32 + 8 * x, :] for x in range(2)], [T.cd[14 + x:128:16, :] for x in range(2)], [], [("CT", 3)], 96)
     for h in range(2):
         when("ce%d" % h)
         dma("sp", T.LCE[:, 512 * h:512 * h + 512], T.ce0[:, 512 * h:512 * h + 512], [], [("LCE", h)], 256)
@@ -259,15 +280,12 @@ def build_ops(g, T, topo, core, me):
     for h in range(2):
         dma("sp", T.ZT[:, 1024 * h:1024 * h + 1024], T.zt[:], [("LCD", 1), ("LCE", 1)], [("ZT", h)], 256)
     when("send")
-    for bs in (VOWN[:2], VOWN[2:]):
-        if bs:
-            spread([T.HV[:, 1024 * b + 256 * me:1024 * b + 256 * me + 256] for b in bs], "v%d" % bs[0],
-                   [("HV", 8 * b + 2 * me + x) for b in bs for x in (0, 1)],
-                   [("HV", 8 * b + 2 * r + x) for b in bs for r in peers for x in (0, 1)], 192 * len(bs))
-    for b in range(4):
-        if b not in VOWN:
-            relay(T.HV[:, 1024 * b + 256 * me:1024 * b + 256 * me + 256], "hv%d" % b, "v%d" % b,
-                  [("HV", 8 * b + 2 * me + x) for x in (0, 1)], [("HV", 8 * b + 2 * r + x) for r in peers for x in (0, 1)], 192)
+    for b in range(len(VCUT) - 1):
+        got, kb = [x for r in peers for x in first_values(r, b)], 0.75 * (VCUT[b + 1] - VCUT[b])
+        if b:
+            relay(values_at(T, me, b), "hv%d" % b, "v%d" % b, first_values(me, b), got, kb)
+        else:
+            spread([values_at(T, me, b)], "v%d" % b, first_values(me, b), got, kb)
 
     when("iota")
     io(T.PJ[:, 3:4], [[0, 1]], 0, 1, ["PI"], 1, flag=False)
@@ -280,6 +298,10 @@ def build_ops(g, T, topo, core, me):
     io(T.VQ[0:8, :], [[1, 144]], -16, -16, ["VQ"], 144)
     io(T.JP[:], [[0, 8], [1, 16]], -8, 0, ["JP"], 128)
     io(T.BG[:], [[16, 8], [0, 16]], 0, 0, ["BG"], 128)
+    io(T.VC[0:40, :], [[-1, 8], [-8, 8], [0, 2]], -24, 1, ["VC"], 128)
+    when("late")
+    io(T.CK[:, 0:128], [[0, 128]], 128, 0, ["CK"], 128)
+    io(T.O16[:], [[-2, 2], [0, 16]], 1, 0, ["O16"], 32)
     when("early")
 
     def X_(d, n):
@@ -290,32 +312,21 @@ def build_ops(g, T, topo, core, me):
     ms(T.SF[:, 1:2], 1535.5 + 1.0 / 1024, [("SF", 4)], 1)
     ms(T.SF[0:32, 1:2], 0.0, [("SF", 4)], 1)
     SFt = [("SF", b) for b in range(5)]
-    ms(T.CK[:, 0:128], 128.0, ["CK"], 64)
     CKt = ["CK"]
-    for i, v in enumerate((1.0 / 2048, -1.0 / 2048, -1.0 / 8, -1.0 / 16)):
-        if (len(FUSED) < 2, len(FUSED) < 2, FUSED, SIGN)[i]:
-            ms(T.O16[:, 16 * i:16 * i + 16], v, ["O16"], 8)
     when("late")
-    io(T.BX[:], [[1024, 4], [128, 2]], 256 * me - 2048, 0, ["BX"], 8)
+    io(T.BX[:], [[256, 4], [128, 2]], 1024 * me - 2048, 0, ["BX"], 8)
     when("early")
     ts(T.IH[:], T.V1[:], 0.0, None, A.is_equal, None, ["V1"], ["IH"], 64)
     ts(T.RE[0:32, :], T.V2[0:32, :], 0.0, None, A.is_equal, None, ["V2"], ["RE"], 64)
-    ts(T.PA0[:], T.VA[:], 0.0, 2.0, A.is_equal, A.mult, ["VA"], ["PA0"], 192)
-    ts(T.PA1[:], T.VA[:], 32.0, -16.0, A.is_equal, A.mult, ["VA"], ["PA1"], 192)
-    for r, v in ((4, 16.0), (5, 14.0), (6, 14.0), (7, -2.0)):
+    ts(T.PA0[:], T.VA[:], 0.0, None, A.is_equal, None, ["VA"], ["PA0"], 192)
+    ts(T.PA1[:], T.VA[:], 32.0, -8.0, A.is_equal, A.mult, ["VA"], ["PA1"], 192)
+    for r, v in ((4, 8.0), (5, 7.0), (6, 7.0), (7, -1.0)):
         ac(T.PA0[32:33, r:384:16], T.XF[32:33, 0:24], ["PA0", "XF"], [("PA0", r)], 24, scale=0.0, bias=v)
-    tt(T.PA1[:], T.PA0[:], T.PA1[:], A.add, ["PA0", "PA1"] + [("PA0", r) for r in range(4, 8)], ["PA1"], 768)
-    tt(T.PK[:], T.PA1[:, 124:252], T.PA1[:, 256:384], A.add, ["PA1"], ["PK"], 256)
+        tt(T.PA0[:, r:384:16], T.PA0[:, r:384:16], T.PA1[:, r:384:16], A.add, ["PA1"], [("PA0", r)], 48)
+    PAt = [("PA0", r) for r in range(4, 8)]
+    ts(T.PC0[:], T.PA0[:, 0:128], UN, None, A.mult, None, PAt, ["PC0"], 64)
     ts(T.IB[:], T.V1[:], 0.0, None, A.is_equal, None, ["V1"], ["IB"], 64)
-    ts(T.IS[:], T.V1[:], 0.0, 1.0 / UN, A.is_equal, A.mult, ["V1"], ["IS"], 64)
     ts(T.Q0[0:8, :], T.VQ[0:8, :], 0.0, None, A.is_equal, None, ["VQ"], ["Q0"], 72)
-    SC = (3.0 / UN, -3.75 / UN)
-    for i, v in enumerate(SC):
-        ts(T.ID[:, 128 * i:128 * i + 128], T.V1[:], 0.0, v, A.is_equal, A.mult, ["V1"], [("ID", i)], 64)
-
-    def ID(v):
-        i = SC.index(v)
-        return T.ID[:, 128 * i:128 * i + 128]
 
     when("iota")
     for j, m in enumerate((15, 1, 3)):
@@ -365,10 +376,10 @@ def build_ops(g, T, topo, core, me):
         cs(x, "is15", -80.0 - b, x + "b", A.mult, A.add)
     cs("k0", "g16", 0.5, "row", A.mult, A.add)
     cs("k1", "k0", -7.0, None, A.add)
-    cs("k2", "k0", -14.0, None, A.add)
     cs("v1", "lt7", -1.0, "lt14", A.mult, A.add)
     when("mats")
-    for i, (x, v) in enumerate((("k0", "lt7"), ("k1", "v1"), ("k2", "h7"))):
+    ts(T.AC[0:40, :], T.VC[0:40, :], 0.0, None, A.is_equal, None, ["VC"], ["AC"], 64)
+    for i, (x, v) in enumerate((("k0", "lt7"), ("k1", "v1"))):
         ts(T.AW[:, 128 * i:128 * i + 128], T.XH[:], col(x), col(v), A.is_equal, A.mult, ["XH", ("c", x), ("c", v)], [("AW", i)], 64)
     when("cols")
     ac(T.RQ[:, 0:16], X_(8, 16), ["XF", ("c", "gam"), ("c", "al")], ["R1"], 16, scale=col("gam"), bias=col("al"))
@@ -387,41 +398,40 @@ def build_ops(g, T, topo, core, me):
     eq(T.SW[:], 16, 144, "g16", UN, ["SW"])
     when("late")
     ts(T.Q[:, 0:128], T.BG[:], col("g16"), None, A.is_equal, None, ["BG", ("c", "g16")], ["Q1"], 64)
-    ts(T.IN[:], T.V1[:], 0.0, -2048.0, A.is_equal, A.mult, ["V1"], ["IN"], 64)
+    for x, v in enumerate((3.0, -4.25)):
+        ts(T.I3[:, 128 * x:128 * x + 128], T.V1[:], 0.0, v, A.is_equal, A.mult, ["V1"], [("I3", x)], 64)
     cs("cq", "u8", "g16", None, A.add)
     cs("mq", "is0", "is8", None, A.add)
     eq(T.QW[:], 14, 144, "cq", "mq", ["QW"])
-    cs("kb", "row", 2.0, "g16", A.mult, A.add)
-    cs("vb", "h7", 2.0, None, A.mult)
-    eq(T.AW[:, 384:512], -27, 128, "kb", "vb", [("AW", 3)])
-    cs("m47", "lt4", -1.0, "lt8", A.mult, A.add)
     cs("m8", "lt8", -1.0, "lt12", A.mult, A.add)
-    cs("h1", "is1", "is3", None, A.add)
-    cs("h3", "h1", -15.0, "h7", A.mult, A.add)
-    cs("hk", "m47", HB, "h3", A.mult, A.add)
+    cs("n47", "lt4", "u8", None, A.add)
+    cs("hb", "n47", HB, None, A.mult)
+    cs("m411", "lt4", -1.0, "lt12", A.mult, A.add)
+    cs("s2", "m411", 0.5 / HB ** 0.5 - 1.0, 1.0, A.mult, A.add)
+    cs("b2a", "par", -1.0, HB ** 0.5 + 8.0, A.mult, A.add)
+    cs("b2", "m411", "b2a", "sq", A.mult, A.add)
     cs("rq", "row", 0.25, "g16", A.mult, A.add)
     cs("c4", "r3", -0.25, "rq", A.mult, A.add)
     cs("m4a", "is4", "mq", None, A.add)
     cs("m4", "is12", "m4a", None, A.add)
-    cs("b4", "m4", -585 * HB / 2, None, A.mult)
+    cs("b4", "m4", -585 * HB, None, A.mult)
     eq(T.Q4[:], 12, 144, "c4", "m4", ["Q4"])
-    cs("p0", "is4", 0.5, None, A.mult)
     for m in (1, 2, 3):
-        cs("p%d" % m, "is%d" % (4 + m), 8.0 ** m / 2, "p%d" % (m - 1), A.mult, A.add)
+        cs("p%d" % m, "is%d" % (4 + m), 8.0 ** m, "p%d" % (m - 1) if m > 1 else "is4", A.mult, A.add)
     eq(T.CWL[:], 16, 144, "g16", "p3", ["CWL"])
     ts(T.KY[:], T.V1[:], 4.0, col("m8"), A.is_equal, A.mult, ["V1", ("c", "m8")], ["KY"], 64)
     ts(T.SH[:], T.V1[:], -1.0, col("lt15"), A.is_equal, A.mult, ["V1", ("c", "lt15")], ["SH"], 64)
-    cs("fu", "is0", EU / UN, None, A.mult)
+    cs("fu", "is0", 1.0 / UN, None, A.mult)
     ac(T.IT[:], X_(0, 128), ["XF", ("c", "fu")], ["IT"], 128, scale=col("fu"))
     ac(T.BC[:], T.BX[:], ["BX", ("c", "fu")], ["BC"], 8, scale=col("fu"))
     cs("r8", "row", -8.0, None, A.add)
     ts(T.DG[:], T.JP[:], col("r8"), 65536.0, A.is_equal, A.mult, ["JP", ("c", "r8")], ["DG"], 64)
     for x in range(2):
-        ac(T.M16[:, 8 * x:8 * x + 8], T.Q[:, 0:128:16], ["Q1"], [("M16", x)], 8)
+        ac(T.M16[:, 8 * x:8 * x + 8], T.Q[:, 0:128:16], ["Q1"], [("M16", x)], 8, scale=2048.0)
     for X in range(2):
         ac(T.LO[:, 16 * X:16 * X + 8], X_(0, 8), ["XF", ("c", "row")], [("LOc", X)], 8, scale=16.0, bias=col("row"))
 
-    CTt = [("CT", i) for i in range(3)]
+    CTt = [("CT", i) for i in range(4)]
     when("q0")
     cp(T.C16[0:8, :], T.C0[0:8, :], ["C0"], ["C16"], 256)
     mms([[(P(6)[:, 0:16], T.Q0[0:8, 16 - s:144 - s], T.C16[0:8, s:256:16], 16) for s in range(16)]], ["Q0", "C16"], [B(6)])
@@ -429,7 +439,7 @@ def build_ops(g, T, topo, core, me):
     when("fast")
     op("dve", lambda: g.vector.tensor_copy(T.U0[:], T.LCD[:, 0:1024].indirect(T.Q0L[:])),
        [("LCD", 0), ("LCD", 1), "Q0L"], ["U0"], 0.06 + 256 * GAT, cls=0)
-    for bank, ii in ((2, (0, 1)), (3, (2,))):
+    for bank, ii in ((2, (0, 1)), (3, (2,)))[:FAST - 1]:
         n = 256 * len(ii)
         mms([[(P(bank)[:, 256 * x:256 * x + 256], T.AW[:, 128 * i:128 * i + 128], T.U0[:], 256)] for x, i in enumerate(ii)],
             [("AW", i) for i in ii] + ["U0"], [B(bank)])
@@ -438,77 +448,68 @@ def build_ops(g, T, topo, core, me):
     when("cf")
     for h in range(2):
         c = slice(512 * h, 512 * h + 512)
-        lin(("CF", h), T.CF[0:24, c], T.CT[0:24, c], 1.0, 0.0, CTt, [("CF", h)], 512)
+        lin(("CF", h), T.CF[0:40, c], T.CT[0:40, c], 1.0, 0.0, CTt, [("CF", h)], 512)
         mm([(P(h)[:], T.RE[0:24, :], T.CF[0:24, c], 512)], ["RE", ("CF", h)], [B(h)])
         lin(("FF", h), T.FF[:, c], P(h)[:], T.SF[:, 0:1], T.SF[:, 1:2], SFt, [B(h), ("FF", h)], 512)
 
-    SWC = 589824 / UN
-
-    def swap(o, src, unit, c, tk, j, ident):
-        n = c.stop - c.start
-        for F, nm, b in ((T.F2, "F2", 2048 + 49152 - 127.5), (T.F1, "F1", 2048 + 196608 - 511.5)):
-            ts(F[:, c], src, unit, b, A.mult, A.add, [tk], [(nm, j)], n // 2)
-        return ([(o, ID(3.0 / UN), T.F2[:, c], n), (o, ID(-3.75 / UN), T.F1[:, c], n), (o, ident, src, n)],
-                [tk, ("F1", j), ("F2", j), ("ID", 0), ("ID", 1)])
-
     for h in range(2):
-        c = slice(512 * h, 512 * h + 512)
         when("env%d" % h)
-        lin(("N16", h), T.N16[:, c], T.LCE[:, c], 1.0, -2048.0, [("LCE", h)], [("N16", h)], 512)
-        lst, rd = swap(P(6 + h)[:], T.N16[:, c], 1.0, c, ("N16", h), h, T.IS[:])
-        mm([(P(6 + h)[:], T.PA1[:, 0:128], T.FF[:, c], 512)], [("FF", h), "PA1"], [B(6 + h)], True, False)
-        for x, one in enumerate(lst):
-            mm([one], ["IS"] + rd, [B(6 + h)], False, x == 2)
         for b in (2 * h, 2 * h + 1):
-            e, o = 256 + 1024 * b + 256 * me, P(6 + h)[:, 256 * (b % 2):256 * (b % 2) + 256]
+            c, bank = slice(256 * b, 256 * b + 256), 4 + b
+            e, o = slot(b, me), P(bank)[:, 0:256]
             tk = [("HE", e // 128), ("HE", e // 128 + 1)]
+            lst = [(o, T.PC0[:], T.FF[:, c], 256)]
             if b in WIDE:
-                lin(("own", b), T.HE[:, e:e + 256], o, 1.0, HB + SWC, [], [B(6 + h)] + tk, 256)
-                relay(T.HE[:, e:e + 256], "hu%d" % b, "u%d" % b, tk, [("HE", 2 + 8 * b + 2 * r + x) for r in peers for x in (0, 1)], 384)
+                lin(("N16", b), T.N16[:, c], T.LCE[:, c], 1.0, -2048.0, [("LCE", h)], [("N16", b)], 256)
+                mm(lst + [(o, T.IH[:], T.N16[:, c], 256)], [("FF", h), "PC0", "IH", ("N16", b)], [B(bank)])
+                lin(("own", b), T.HE[:, e:e + 256], o, 1.0 / UN, HB, [], [B(bank)] + tk, 256)
+                got = [("HE", slot(b, r) // 128 + x) for r in peers for x in (0, 1)]
+                if b in OWN:
+                    spread([T.HE[:, e:e + 256]], "u%d" % b, tk, got, 384)
+                else:
+                    relay(T.HE[:, e:e + 256], "hu%d" % b, "u%d" % b, tk, got, 384)
                 continue
             m = T.LU[:, e - 256:e]
-            lin(("MU", b), m, o, UN, 2048.0 + UN * SWC, [], [B(6 + h), ("MU", b)], 256)
+            mm(lst, [("FF", h), "PC0"], [B(bank)])
+            tt(m, o, T.LCE[:, c], A.add, [("LCE", h)], [B(bank), ("MU", b)], 256)
             if b in OWN:
                 spread([m], "u%d" % b, [("MU", b)], [("LU", b)], 192)
             else:
                 relay(m, "hu%d" % b, "u%d" % b, [("MU", b)], [("LU", b)], 192)
     when("idx")
-    for x in range(4):
-        i = io(T.IDX[:, 512 * x:512 * x + 512], [[1, 512]], 512 * (x % 2), 0, [("IDX", x)], 512)
-        ops[i]["also"] = max(j for j, o in enumerate(ops) if o["kind"] == "send")
+    def gap(k):
+        c = slot(k, N - 1) - 256
+        return io(T.HE[:, c:c + 256], [[0, 256]], 0, 0, [("HE", c // 128), ("HE", c // 128 + 1)], 256)
+
+    for k in (0, 4):
+        ops[gap(k)]["also"] = max(j for j, o in enumerate(ops) if o["kind"] == "send")
     when("e16")
-    c = slice(1024, 1280)
-    lin(("N16", 2), T.N16[:, c], T.LE[:], 1.0, -2048.0, ["LE"], [("N16", 2)], 256)
-    lst, rd = swap(P(5)[:, 0:256], T.N16[:, c], 1.0, c, ("N16", 2), 2, T.IS[:])
-    mm(lst, ["IS"] + rd, [B(5)])
     for X in range(2):
-        lin(("E0", X), env(X), P(5)[:, 128 * X:128 * X + 128], 1.0, SWC, [], [B(5), ("E16", X)], 128)
+        lin(("E0", X), env(X), T.LE[:, 128 * X:128 * X + 128], 1.0 / UN, -0.5, ["LE"], [("E16", X)], 128)
     when("u")
     for h in range(2):
         c = slice(512 * h, 512 * h + 512)
         if ("U", h) in ON_POOL:
-            i = pc(T.U[:, c], T.LCD[:, c], [("LCD", h)], [("U", h)], 512)
-            ops[i]["also"] = max(j for j, o in enumerate(ops) if o["kind"] == "send")
+            pc(T.U[:, c], T.LCD[:, c], [("LCD", h)], [("U", h)], 512)
         else:
             lin(("U", h), T.U[:, c], T.LCD[:, c], 1.0, 0.0, [("LCD", h)], [("U", h)], 512)
-        ac(T.U2[:, c], T.LCD[:, c], [("LCD", h)], [("U2", h)], 512, bias=-8.0, func=ACT.Square)
     TB = (T.TB0, T.TB1, T.TB2)
-    for i in TBO:
+    for i in range(3):
         when("tb%d" % i)
-        for h in range(2):
-            c, bank = slice(512 * h, 512 * h + 512), 6 + h
+        if i < 2:
+            dma("sp", [TB[i][r:128:16, 0:1024] for r in range(16)], [T.U[7 * i + r // 2:128:16, :] for r in range(16)],
+                [("U", 0), ("U", 1)], [("TB", i, 0), ("TB", i, 1)], 256)
+        for h in range(2 if i == 2 else 0):
+            c, bank = slice(512 * h, 512 * h + 512), 2 + h
             o = P(bank)[:]
-            if i < 2:
-                mm([(o, T.AW[:, 128 * i:128 * i + 128], T.U[:, c], 512)], [("AW", i), ("U", h)], [B(bank)])
-                ac(TB[i][:, c], o, [("c", "sq")], [B(bank), ("TB", i, h)], 512, bias=col("sq"), func=ACT.Square)
-                continue
-            mm([(o, T.PK[:], T.FF[:, c], 512)], ["PK", ("FF", h)], [B(bank)], True, False)
-            mm([(o, T.AW[:, 384:512], T.U[:, c], 512)], [("AW", 3), ("U", h)], [B(bank)], False, False)
-            mm([(o, T.AW[:, 256:384], T.U2[:, c], 512)], [("AW", 2), ("U2", h)], [B(bank)], False, True)
-            lin(("TB2", h), TB[i][:, c], o, 1.0, col("hk"), [("c", "hk")], [B(bank), ("TB", i, h)], 512)
+            mm([(o, T.PA0[:, 256:384], T.FF[:, c], 512)], PAt + [("FF", h)], [B(bank)], True, False)
+            mm([(o, T.PA0[:, 124:252], T.FF[:, c], 512)], PAt + [("FF", h)], [B(bank)], False, False)
+            mm([(o, T.AC[0:40, :], T.CF[0:40, c], 512)], ["AC", ("CF", h)], [B(bank)], False, True)
+            ac(TB[i][:, c], o, [("c", "s2"), ("c", "b2")], [B(bank), ("TB", i, h)], 512, bias=col("b2"), scale=col("s2"), func=ACT.Square)
+        when("tb")
         dma("sp", TB[i][:, 1024:2048], TB[i][:, 0:1024], [("TB", i, 0), ("TB", i, 1)], [("TB", i, 2), ("TB", i, 3)], 256)
-    when("conv")
     for b in range(4):
+        when("conv" if b < 2 else "conv2")
         for h in range(2 if b not in WIDE else 0):
             l = 1024 * b + 512 * h
             lin(("conv", b, h), T.HE[:, 256 + l:768 + l], T.LU[:, l:l + 512], 1.0 / UN, HB - 0.5, [("LU", b), ("MU", b)],
@@ -536,15 +537,18 @@ def build_ops(g, T, topo, core, me):
         part(("T", X) if t else None)
         wide = 2048 if t else 1024
         q, qt = (T.Z16[:, 16 * X + 8:16 * X + 16], ("Z16", X)) if t else (T.Q0L[:, 8 * X:8 * X + 8], "Q0L")
-        for i in (0, 1, 2) if t else (2,):
-            ag(tile(i, X), TB[i][:, 0:wide].indirect(q), [("TB", i, h) for h in range(wide // 512)] + [qt], [("G", i, X)], 128)
+        for i in range(3) if t else (2,):
+            src, rd = TB[i][:, 0:wide].indirect(q), [("TB", i, h) for h in range(wide // 512)] + [qt]
+            if i == 2:
+                ag(tile(i, X), src, rd, [("G", i, X)], 128)
+            else:
+                gs(tile(i, X), src, ACT.Square, col("sq"), col("lt14"), rd + [("c", "sq"), ("c", "lt14")], [("G", i, X)], 128)
         if not fused(t, X):
-            op("act", lambda: g.scalar.activation(T.GZ[:, 128 * X:128 * X + 128], T.ZT[:, 0:wide].indirect(q), ACT.Identity,
-                                                  bias=-127.5, scale=-1.0),
-               [("ZT", h) for h in range(wide // 1024)] + [qt], [("GZ", X)], 0.06 + 128 * GAT, cls=0)
+            gs(T.GZ[:, 128 * X:128 * X + 128], T.ZT[:, 0:wide].indirect(q), ACT.Identity, -127.5, -1.0,
+               [("ZT", h) for h in range(wide // 1024)] + [qt], [("GZ", X)], 128)
 
         def rows(i):
-            if t:
+            if t or i >= FAST:
                 return tile(i, X), ("G", i, X)
             return T.GF[:, 256 * i + 128 * X:256 * i + 128 * X + 128], ("GF", i)
 
@@ -593,45 +597,41 @@ def build_ops(g, T, topo, core, me):
         e = env(X)
         mm([(o, T.IH[:], e, 128), (o, T.KY[:], tile(2, X), 128)], ["IH", "KY", ("E16", X), ("G", 2, X)], [B(6 + X)])
         ap, tk = env_at(T, t, me, X)
-        ac(ap, o, [], [B(6 + X), tk], 128, bias=2048.0 if W16 else HB)
-        relay(ap, "h%d" % (2 * t + X), "e%d" % (2 * t + X), [tk], [env_at(T, t, r, X)[1] for r in peers], 96 if W16 else 192)
+        ac(ap, o, [("c", "hb")], [B(6 + X), tk], 128, bias=col("hb"))
+        relay(ap, "h%d" % (2 * t + X), "e%d" % (2 * t + X), [tk], [env_at(T, t, r, X)[1] for r in peers], 192)
 
-    def high(X):
-        return T.HK[:, 256 * X:256 * X + 128]
-
-    HT = "HH" if W16 else "HA"
+    HT = "HA"
 
     def above(X):
-        return T.HH[:, 128 * X:128 * X + 128] if W16 else high(X)
+        return T.HK[:, 256 * X:256 * X + 128]
+
+    def window(t, X):
+        a, b = slot(t, N - 1) - 256 + 128 * X, slot(t + 3, 0) + 256
+        return T.HE[:, a:b], [("HE", x) for x in range(a // 128, b // 128)]
 
     def outcomes(t, X):
         part(("O", X))
-        b, c, l = t % 4, slice(8 * X, 8 * X + 8), T.T0L[:, 8 * X:8 * X + 8]
+        b, final = t % 4, t == S - 1 and X not in AFTER
+        l, lt = (T.T0L[:, 8 * X:8 * X + 8], ("T0L", X)) if final else (T.HI[:, 16 * X:16 * X + 8], ("HIl", X))
         ob, bk = P(6 + X), B(6 + X)
         o = ob[:, 0:8]
         mm([(o, T.QW[:, 14 - 2 * a:142 - 2 * a], T.T16[:, 64 * X + a:64 * X + 64:8], 8) for a in range(8)], ["QW", ("T16", X)], [bk])
-        hi, a = T.HI[:, 16 * X:16 * X + 8], 2048.0
-        if b:
-            part(("O2", X))
-            lin(("T0C", X), T.T0C[:, c], o, 1.0, 0.0, [], [bk, ("T0C", X)], 8)
-            ac(T.SG[:, c], o, [], [bk, ("SG", X)], 8, bias=2048.5 - 1024 * b, func=ACT.Sign)
-            o, a = ob[:, 8:16], 4096.0 - 1024 * b
-            mm([(o, T.IH[:], T.T0C[:, c], 8), (o, T.IN[:], T.SG[:, c], 8)], ["IH", "IN", ("T0C", X), ("SG", X)], [bk])
+        part(("O2", X))
+        fl = [T.SG[:, 16 * X + 8 * x:16 * X + 8 * x + 8] for x in range(2)]
+        for x, v in enumerate((49152 - 127.5, 196608 - 511.5)):
+            lin(("SG", X), fl[x], o, 1.0, 2048 - 256 * b + v, [], [bk, ("SG", X, x)], 8)
+        y = T.T0C[:, 8 * X:8 * X + 8]
+        lin(("T0C", X), y, o, 1.0, 0.0, [], [bk, ("T0C", X)], 8)
+        mm([(o, T.IH[:], y, 8)] + [(o, T.I3[:, 128 * x:128 * x + 128], fl[x], 8) for x in range(2)],
+           ["IH", ("T0C", X), ("I3", 0), ("I3", 1), ("SG", X, 0), ("SG", X, 1)], [bk])
         part(("O3", X))
-        lin(("T0L", X), l, o, 1.0, a, [], [bk, ("T0L", X)], 8)
-        if t < S - 1 or X in AFTER:
-            lin(("HIl", X), hi, o, 1.0, a + 128 + 128 * X, [], [bk, ("HIl", X)], 8)
-        else:
-            lin(("HIl", X), hi, T.LO[:, 16 * X:16 * X + 8], 1.0, 128.0, [("LOc", X)], [("HIl", X)], 8)
-        e = 256 + 1024 * t
-        src, rd = T.HE[:, e:e + 4096].indirect(l), [("HE", e // 128 + x) for x in range(32)] + [("T0L", X)]
-        if W16:
-            op("act", lambda: g.scalar.activation(high(X), src, ACT.Identity, bias=HB - 0.5, scale=1 / UN), rd, [("HA", X)],
-               0.06 + 128 * GAT, cls=0)
-            lin(("HH", X), T.HH[:, 128 * X:128 * X + 128], high(X), UN, 2048 - UN * HB, [("HA", X)], [("HH", X)],
-                128 if ("HH", X) in ON_SCALAR else 64)
-        else:
-            ag(high(X), src, rd, [("HA", X)], 128)
+        lin(("T0L", X), l, o, 1.0, 2048 - 256 * b - 3 * 49152 + 4.25 * 196608 + 768 + 256 - 128 * X, [], [bk, lt], 8)
+        win, rd = window(t, X)
+        gs(above(X), win.indirect(l), ACT.Identity, 0.5 / UN, 1.0, rd + [lt], [("HA", X)], 128)
+        if final:
+            part(("L2", X))
+            lin(("HIl", X), T.HI[:, 16 * X:16 * X + 8], T.LO[:, 16 * X:16 * X + 8], 1.0, 128.0, [("LOc", X)], [("HIl", X)], 8)
+        part(("O4", X))
         mm([(ob[:, 64:128], T.CWL[:, 16 - 4 * u:144 - 4 * u], T.HK[:, 256 * X + u:256 * X + 256:4], 64) for u in range(4)],
            ["CWL", ("HA", X), ("G", 2, X)], [bk])
         lin(("C4", X), T.C4[:, 64 * X:64 * X + 64], ob[:, 64:128], 1.0, col("b4"), [("c", "b4")], [bk, ("C4", X)], 64)
@@ -644,7 +644,7 @@ def build_ops(g, T, topo, core, me):
         part(("E", X))
         o, bk = P(6 + X)[:, 256:384], B(6 + X)
         e = env(X)
-        c, b = 1024 * t + 128 * (1 - X), 2 * (t % 4) + X
+        c, b = slot(t, N - 1) - 256 + 128 * X, 2 * (t % 4) + X
         lst, rd = [(o, T.SH[:], e, 128), (o, T.IB[:], T.IT[:], 128)], ["SH", "IB", "IT", ("E16", X)]
         if t < S - 1 or X in AFTER:
             mm(lst + [(o, T.IB[:], above(X), 128)], rd + [(HT, X)], [bk])
@@ -652,14 +652,10 @@ def build_ops(g, T, topo, core, me):
             return
         part(("L", X))
         mm(lst, rd, [bk])
-        c, e = slice(256 * X, 256 * X + 256), 256 + 1024 * t
+        win, rd = window(t, X)
         ac(T.EO[:, 256 * X:256 * X + 128], o, ["BC"], [bk, ("EOb", X)], 128, bias=T.BC[:, b:b + 1])
-        dg(T.EO[:, 256 * X + 128:256 * X + 256], T.HE[:, e:e + 4096].indirect(T.T0L[:, 8 * X:8 * X + 8]), above(X), A.subtract,
-           [("HE", e // 128 + x) for x in range(32)] + [("T0L", X), (HT, X), ("EOb", X)], [("EO", X)], 128)
-        o = P(X)[:, 0:256]
-        lst, rd = swap(o, T.EO[:, c], UN / EU, c, ("EO", X), 3 + X, T.IS[:] if W16 else T.IH[:])
-        mm(lst, ["IH", "IS"] + rd, [B(X)])
-        ac(T.OW[:, c], o, [], [B(X), ("OW", X)], 256, scale=UN, bias=2048.0 + UN * SWC)
+        dg(T.EO[:, 256 * X + 128:256 * X + 256], win.indirect(T.T0L[:, 8 * X:8 * X + 8]), above(X), A.subtract,
+           rd + [("T0L", X), (HT, X)], [("EO", X)], 128)
 
     def values(t, X):
         part(("V", X))
@@ -667,14 +663,14 @@ def build_ops(g, T, topo, core, me):
         win, wt = T.HV[:, a:a + 4096], [(y, a // 128 + x) for x in range(32) for y in ("HV", "HQ")]
         sb, c = P(4 + X), slice(128 * X, 128 * X + 128)
         cut = X in QUART and t < S - 1
-        h0 = 4096 - a + 1024 * (t % 4) + 256 * me + 128 * X
-        safe = [("HV", 40 + x) for x in range(8)] if (t, X) == (0, 1) else []
+        h0 = 4096 - a + 1024 * me + 256 * (t % 4) + 128 * X
+        safe = [("HV", 34 + 8 * r + x) for r in range(N) for x in range(2)] if (t, X) == (0, 1) else []
         w, tk = (T.HV[:, h0:h0 + 128], ("HV", h0 // 128)) if t < S - 1 else (T.W5[:, c], ("W5", X))
 
         def finish(a, n, y):
             o, f = sb[:, a:a + n], T.FB[:, 128 * X + a:128 * X + a + n]
             out, k = (T.HV[:, h0 + a:h0 + a + n], (y, h0 // 128)) if t < S - 1 else (w, tk)
-            lin(("FB", X), f, o, 1.0, -127.5, [], [B(4 + X), ("FB", X, a)], n)
+            lin(("FB" if t < S - 1 else "FBL", X), f, o, 1.0, -127.5, [], [B(4 + X), ("FB", X, a)], n)
             for x in (1, 0) if X in WFIRST and t < S - 1 else (0, 1):
                 if x:
                     tt(out, o, f, A.subtract, [("FB", X, a)], [B(4 + X), k], n)
@@ -682,7 +678,7 @@ def build_ops(g, T, topo, core, me):
                     z = slice(128 * X + a, 128 * X + a + n)
                     tt(T.YS[:, z], o, T.GZ[:, z], A.add, [("GZ", X)], [B(4 + X), ("YS", X, a)], n)
             if t < S - 1:
-                spread([out], "%s%d" % ({"HV": "w", "HQ": "x"}[y], 2 * t + X), [k] + safe, [(y, (h0 + 256 * (r - me)) // 128) for r in peers], 0.75 * n)
+                spread([out], "%s%d" % ({"HV": "w", "HQ": "x"}[y], 2 * t + X), [k] + safe, [(y, (h0 + 1024 * (r - me)) // 128) for r in peers], 0.75 * n)
 
         for h in range(2):
             j, la, lb = 2 * X + h, 128 * X + 32 * h + side_at(X, 0), 128 * X + 32 * h + side_at(X, 1)
@@ -722,12 +718,9 @@ def build_ops(g, T, topo, core, me):
 
     def choose(t, X):
         part(("C", X))
-        o, c, sb, z = P(4 + X)[:, 256:272], slice(16 * X, 16 * X + 16), B(4 + X), slice(128 * X, 128 * X + 128)
-        lst, f = [(o, T.FB[:, z], T.O16[:, 0:16], 16), (o, T.YS[:, z], T.O16[:, 16:32], 16)], -24.0
-        if fused(t, X):
-            lst, f = [(o, T.YS[:, z], T.O16[:, 32:48], 16)], -8.0
-        elif signed(t, X):
-            lst, f = [(o, T.YS[:, z], T.O16[:, 48:64], 16)], -16.0
+        vb = VOTES[X] if t < S - 1 else 2 + X
+        o, c, sb, z = P(vb)[:, 384:400], slice(16 * X, 16 * X + 16), B(vb), slice(128 * X, 128 * X + 128)
+        lst, f = [(o, T.FB[:, z], T.O16[:, 0:16], 16), (o, T.YS[:, z], T.O16[:, 16:32], 16)], -24.0 * 2048
         mm([(o, T.Q[:, 0:128], T.M16[:], 16)] + lst,
            ["Q1", ("M16", 0), ("M16", 1), "O16"] + [(y, X, a) for a in (0, 64) for y in ("YS", "FB")], [sb])
         if ("VR", X) in ON_SCALAR:
@@ -735,38 +728,39 @@ def build_ops(g, T, topo, core, me):
         else:
             ts(T.VR[:, c], o, f, 0.0, A.add, A.max, [], [sb, ("VR", X)], 16)
         o = P(2 + X)[:, 256:272]
-        mm([(o, T.IH[:], T.LO[:, c], 16)], ["IH", ("LOc", X), ("LOq", X)], [B(2 + X)], True, False)
-        mm([(o, T.DG[:], T.VR[:, c], 16)], ["DG", ("VR", X)], [B(2 + X)], False, True)
+        if vb == 2 + X:
+            mm([(o, T.IH[:], T.LO[:, c], 16), (o, T.DG[:], T.VR[:, c], 16)], ["IH", ("LOc", X), ("LOq", X), "DG", ("VR", X)], [B(2 + X)])
+            role[1] += 1
+        else:
+            mm([(o, T.IH[:], T.LO[:, c], 16)], ["IH", ("LOc", X), ("LOq", X)], [B(2 + X)], True, False)
+            mm([(o, T.DG[:], T.VR[:, c], 16)], ["DG", ("VR", X)], [B(2 + X)], False, True)
         tt(T.Z16[:, c], o, T.HI[:, c], A.min, [("HIl", X), ("HIq", X)], [B(2 + X), ("Z16", X)], 16)
         l = T.Z16[:, 16 * X:16 * X + 8]
         if t < S - 1 or X in AFTER:
-            a = 1024 * t + 128 * (1 - X)
-            dg(env(X), T.HE[:, a:1024 * t + 4352].indirect(l), above(X), A.subtract,
-               [("HE", 8 * t + x) for x in range(1 - X, 34)] + [("Z16", X), (HT, X)], [("E16", X)], 128)
+            win, rd = window(t, X)
+            dg(env(X), win.indirect(l), above(X), A.subtract, rd + [("Z16", X), (HT, X)], [("E16", X)], 128)
             if t < S - 1:
                 return
         part(None)
         c = slice(128 * X, 128 * X + 128)
         if X in AFTER:
-            o = P(X)[:, 0:128]
-            lst, rd = swap(o, env(X), UN, slice(256 * X, 256 * X + 128), ("E16", X), 3 + X, T.IH[:])
-            mm(lst, ["IH"] + rd, [B(X)])
-            ac(T.OUT[:, c], o, [], [B(X), ("OUT", X)], 128, scale=UN, bias=2048.0 + UN * SWC)
+            ac(T.OUT[:, c], env(X), [("E16", X)], [("OUT", X)], 128, scale=UN, bias=2048.0)
         else:
-            op("dve", lambda: g.vector.tensor_copy(T.OUT[:, c], T.OW[:, 256 * X:256 * X + 256].indirect(l)), [("OW", X), ("Z16", X)],
-               [("OUT", X)], 0.06 + 128 * GAT, cls=0)
+            op("dve", lambda: g.vector.tensor_scalar(T.OUT[:, c], T.EO[:, 256 * X:256 * X + 256].indirect(l), UN, 2048.0, A.mult, A.add),
+               [("EO", X), ("EOb", X), ("Z16", X)], [("OUT", X)], 0.06 + 128 * GAT, cls=0)
         dma("sp", T.ye[:, c], T.OUT[:, c], [("OUT", X)], [], 64)
-        ag(T.YC[:, c], T.IDX[:, 0:2048].indirect(T.Z16[:, 16 * X + 8:16 * X + 16]), [("IDX", x) for x in range(4)] + [("Z16", X)],
+        ag(T.YC[:, c], T.IDX[:, 0:2048].indirect(T.Z16[:, 16 * X + 8:16 * X + 16]), [("IDX", x) for x in range(8)] + [("Z16", X)],
            [("YC", X)], 128)
         dma("act", T.yc[:, c], T.YC[0:128:16, c], [("YC", X)], [], 4)
 
-    def carry(a, b):
-        tk = [[(y, (x + 1024 * b) // 128 + i) for i in range(8) for y in ("HV", "HQ")] for x in (a, 4096 - a)]
-        dma("sp", T.HV[:, 4096 - a + 1024 * b:4096 - a + 1024 * b + 1024], T.HV[:, a + 1024 * b:a + 1024 * b + 1024], tk[0], tk[1], 256)
+    def carry(a, b, n=1):
+        at = [[x + 1024 * r + 256 * b for r in range(N)] for x in (a, 4096 - a)]
+        tk = [[(y, c // 128 + i) for c in x for i in range(2 * n) for y in ("HV", "HQ")] for x in at]
+        dma("sp", [T.HV[:, c:c + 256 * n] for c in at[1]], [T.HV[:, c:c + 256 * n] for c in at[0]], tk[0], tk[1], 256 * n)
 
     when("carry")
-    for b in (1, 2, 3):
-        carry(0, b)
+    carry(0, 1)
+    carry(0, 2, 2)
     role[2] = -1
     names_of(0, 0)
     names_of(0, 1)
@@ -775,12 +769,17 @@ def build_ops(g, T, topo, core, me):
         if 0 < t < S - 1:
             part(("K",))
             carry(4096 * (t % 2), (t - 1) % 4)
+            part(("I",))
+            for x in (2 * t - 2, 2 * t - 1):
+                io(T.IDX[:, 256 * x:256 * x + 256], [[1, 256]], 256 * (x % 4), 0, [("IDX", x), "turn"], 256)
+            if t == 2:
+                ops[gap(8)]["wr"].append("turn")
         for X in range(2 if t < S - 1 else 0):
             record(t, X)
         for X in range(2):
             outcomes(t, X)
-            bound(t, X)
         for X in range(2):
+            bound(t, X)
             values(t, X)
             choose(t, X)
             if t < S - 1:
@@ -794,11 +793,10 @@ def helper_program(g, core, T, topo, r):
     full = sum(1 << e for e in es)
     n_in = len(inner_engines(topo, T.cores[r], T.cores[peers[0]]))
     ids = [dst_id(topo, T.cores[p]) for p in peers]
-    jobs = [("hu%d" % b, "u%d" % b) + 2 * (T.LU[:, 1024 * b + 256 * r:1024 * b + 256 * r + 256],)
-            if b not in WIDE else ("hu%d" % b, "u%d" % b) + 2 * (T.HE[:, 256 + 1024 * b + 256 * r:512 + 1024 * b + 256 * r],)
+    jobs = [("hu%d" % b, "u%d" % b) + 2 * (T.LU[:, slot(b, r) - 256:slot(b, r)],)
+            if b not in WIDE else ("hu%d" % b, "u%d" % b) + 2 * (T.HE[:, slot(b, r):slot(b, r) + 256],)
             for b in range(4) if b not in OWN]
-    jobs = [("hv%d" % b, "v%d" % b) + 2 * (T.HV[:, 1024 * b + 256 * r:1024 * b + 256 * r + 256],)
-            for b in range(4) if b not in VOWN] + jobs
+    jobs = [("hv%d" % b, "v%d" % b) + 2 * (values_at(T, r, b),) for b in range(1, len(VCUT) - 1)] + jobs
     for i in range(2 * (S - 1)):
         ap = env_at(T, i // 2, r, i % 2)[0]
         jobs.append(("h%d" % i, "e%d" % i, ap, ap))
@@ -1197,6 +1195,141 @@ def search(ops):
                     best = (c2, list(k2))
         return best[1]
 
+    def shake(key, lo, hi, rounds, heat):
+        order = sorted(range(n), key=lambda j: (key[j], j))
+        seq = [j for j in order if key[j] < hi + 12.0]
+        free = [j for j in seq if lo <= key[j] < hi]
+        inside, m, known = set(free), len(seq), set(seq)
+        goal = [j for j in seq if key[j] >= hi + 8.0]
+        w = [0.0] * n
+        for j in seq:
+            w[j] = EARLY / m
+        for j in goal:
+            w[j] += 1.0 / len(goal)
+        tail = [] if goal else [j for j in seq if lat[j] or not post[j]]
+        nxt = [[d for d, _ in post[j] if d in known] for j in range(n)]
+        key, pos, pv, ts, ends = list(key), [0] * n, [-1] * n, [], []
+
+        def index(a, b):
+            last = {}
+            for p in range(a, b):
+                j = seq[p]
+                pos[j] = p
+                pv[j] = last.get(eng[j], first.get(eng[j], -1))
+                last[eng[j]] = j
+            for p in range(b, m):
+                if not last:
+                    break
+                j = seq[p]
+                if eng[j] in last:
+                    pv[j] = last.pop(eng[j])
+
+        first = {}
+        index(0, m)
+        for du, pr in cases:
+            t = [0.0] * n
+            for j in seq:
+                t[j] = max([t[pv[j]] + du[pv[j]] if pv[j] >= 0 else 0.0] + [t[d] + x for d, x in pr[j]])
+            ts.append(t)
+            ends.append(max([t[j] + du[j] + lat[j] for j in tail], default=0.0))
+
+        def waits():
+            c = int(rnd() * len(cases))
+            (du, pr), t, found = cases[c], ts[c], []
+            j = max(tail, key=lambda y: t[y] + du[y] + lat[y]) if tail else goal[int(rnd() * len(goal))]
+            while j is not None:
+                s, d = max([(t[d] + x, d) for d, x in pr[j]], default=(0.0, None))
+                if t[j] > s + 1e-3 and pv[j] >= 0:
+                    d = pv[j]
+                    if d in inside and j in inside:
+                        found.append((d, j))
+                j = d
+            return found
+
+        cost, best, links = 0.0, (0.0, list(key)), None
+        for it in range(rounds):
+            if links is None or it % 32 == 0:
+                links = waits()
+            j, x = free[int(rnd() * len(free))], (rnd() + rnd() - 1.0) * (0.3, 1.0, 3.0)[int(rnd() * 3)]
+            if links and rnd() < 0.5:
+                a, b = links[int(rnd() * len(links))]
+                x = key[b] - key[a] + 0.002 + rnd() * rnd() * rnd() * 2.0
+                j, x = (a, x) if rnd() < 0.5 else (b, -x)
+            k2 = {j: key[j] + x}
+            todo, ok = [j], lo <= k2[j] < hi
+            while todo and ok:
+                j = todo.pop()
+                kj = k2[j]
+                for d, _ in post[j] if x > 0 else pre[j]:
+                    kd = k2.get(d, key[d])
+                    if (kd <= kj) if x > 0 else (kd >= kj):
+                        k2[d] = kj + (1e-5 if x > 0 else -1e-5)
+                        ok = ok and d in inside and lo <= k2[d] < hi
+                        todo.append(d)
+            if not ok:
+                continue
+            a, b = min(pos[j] for j in k2), max(pos[j] for j in k2) + 1
+            if x > 0:
+                top = max(k2.values())
+                while b < m and key[seq[b]] < top:
+                    b += 1
+            else:
+                top = min(k2.values())
+                while a > 0 and key[seq[a - 1]] > top:
+                    a -= 1
+            seg = sorted(seq[a:b], key=lambda y: k2.get(y, key[y]))
+            first = {}
+            for j in seq[a:b]:
+                if eng[j] not in first:
+                    first[eng[j]] = pv[j]
+            delta, new, room = 0.0, [], heat * (1.0 - it / rounds) * rnd()
+            for c, (du, pr) in enumerate(cases):
+                old = ts[c]
+                t = list(old)
+                busy = {e: (t[d] + du[d] if d >= 0 else 0.0) for e, d in first.items()}
+                moved, reach, p, gain = set(first), b, a, 0.0
+                while p < m and (moved or p <= reach):
+                    j = seg[p - a] if p < b else seq[p]
+                    p += 1
+                    e = eng[j]
+                    s = busy.get(e)
+                    if s is None:
+                        d = pv[j]
+                        s = t[d] + du[d] if d >= 0 else 0.0
+                    for d, y in pr[j]:
+                        y += t[d]
+                        if y > s:
+                            s = y
+                    busy[e] = s + du[j]
+                    y = s - old[j]
+                    if y > 1e-9 or y < -1e-9:
+                        t[j] = s
+                        gain += w[j] * y
+                        moved.add(e)
+                        for d in nxt[j]:
+                            if pos[d] > reach:
+                                reach = pos[d]
+                    elif p > b:
+                        moved.discard(e)
+                end = max([t[j] + du[j] + lat[j] for j in tail], default=0.0)
+                delta += (gain + end - ends[c]) / len(cases)
+                new.append((t, end))
+                if c == 0 and delta > room + 0.06:
+                    break
+            if delta <= room:
+                for j, y in k2.items():
+                    key[j] = y
+                seq[a:b] = seg
+                index(a, b)
+                for c in range(len(cases)):
+                    ts[c], ends[c] = new[c]
+                cost += delta
+                if delta:
+                    links = None
+                if cost < best[0] - 1e-9:
+                    best = (cost, list(key))
+        return best[1]
+
     def settle(key):
         du, pr = cases[0]
         t, busy = [0.0] * n, {}
@@ -1209,8 +1342,16 @@ def search(ops):
     base = cyclic(CYCLE, WARM)
     if not ROUNDS:
         return 0.0, forward(base)
+    for i, o in enumerate(ops):
+        if o["step"] > 0 or o["step"] == 0 and o["role"][0][0] not in ("o", "V", "R", "O", "O2", "D"):
+            base[i] += LATE
     key = forward(list(base))
     ga = [i for i in range(n) if ops[i]["role"] == (("V", 0), 1)]
+    for _ in range(TURNS):
+        u = backward(key, post, lat)
+        late = forward([-u[i] - dur[i] for i in range(n)])
+        if late[ga[1]] < key[ga[1]]:
+            key = late
     for i in range(n):
         if 0 < ops[i]["step"] < S - 1:
             key[i] = base[i] - base[ga[1]] + key[ga[1]]
@@ -1218,10 +1359,10 @@ def search(ops):
         for d, _ in pre[i]:
             key[d] = min(key[d], key[i] - 1e-4)
     key = settle(key)
-    for share, heat in ((3, 0.3), (3, 0.1), (6, 0.04)):
-        key = settle(stretch(key, 0.0, key[ga[1]] + 6.0, ROUNDS // share, heat))
-    for heat in (0.15, 0.04):
-        key = settle(stretch(key, key[ga[S - 1]] - 6.0, 1e9, ROUNDS // 6, heat))
+    for share, heat in HEATS:
+        key = settle(shake(key, -1.0, key[ga[1]] + 5.0, ROUNDS // share, heat))
+    for heat in (0.1, 0.03):
+        key = settle(shake(key, key[ga[S - 1]] - 6.0, 1e9, ROUNDS // 12, heat))
     total = 0.0
     for du, pr in cases:
         t, busy = [0.0] * n, {}
@@ -1241,6 +1382,8 @@ def emit(g, T, ops, seq):
         if o["kind"] == "recv":
             o["mark"], o["clock"] = (o["sem"], o["cnt"]), {}
             total[o["sem"]] = o["cnt"]
+            continue
+        if o["kind"] == "hop":
             continue
         if o["kind"] == "land":
             o["mark"], o["clock"] = ops[o["after"]]["mark"], ops[o["after"]]["clock"]
@@ -1274,9 +1417,10 @@ def emit(g, T, ops, seq):
         elif o["kind"] == "dma":
             s = "d%d" % ndma
             ndma += 1
-            ins.then_inc(T.sem[s], 16)
-            o["mark"] = (s, 16)
-            total[s] = 16
+            for x in ins:
+                x.then_inc(T.sem[s], 16)
+            o["mark"] = (s, 16 * len(ins))
+            total[s] = 16 * len(ins)
         else:
             sent += o["inc"]
     total["sent"] = sent

from concourse.bass import DstId, RemoteDMATransfer
from concourse.mybir import AluOpType, AxisListType, ActivationFunctionType

N, S = 4, 6
F32, BF, F16, I32, U16 = "float32", "bfloat16", "float16", "int32", "uint16"
UN = 4096.0
HB = 136.0
QUART = ()
NARROW = (0,)
KT = [divmod(k, 7) for k in range(16)]
WIDE = ()
ON_SCALAR = ({(x, X) for x in ("T0L", "T0C", "SG", "LOq", "HIq", "HIl", "C4", "VR", "TB2", "FB", "ER2", "U") for X in range(2)}
             | {("T16", 0), ("FBL", 0), ("E0", 0), ("E0", 1), ("CF", 1), ("FF", 0), ("FF", 1)}
             | {("conv", b, h) for b, h in ((0, 0), (1, 0), (2, 0), (3, 0), (0, 1), (2, 1))}
             | {("TL", X, 0) for X in range(2)} | {(x, b) for x in ("own", "N16") for b in range(4)})
ON_VECTOR = set()
ON_POOL = {("U", 0), ("U", 1)}
AFTER = ()
FAST = 2
VOTES = (2, 5)
WFIRST = (1,)
PIECES = ((32,), (32,), (32,), (32,))
FUSED = ()
SIGN = ()
OWN = (0, 2)
VCUT = (0, 512, 768, 1024)
VIA = {"hv1": (1, 0), "hv2": (1, 1), "hu1": (1, 2), "hu3": (1, 3)}
STEP2 = 1


def _sb(cols, dtype):
    return ("sbuf", [128, cols], dtype)


SCRATCH = {
    "HV": _sb(8192, BF), "HE": _sb(9984, F32), "W5": _sb(256, BF),
    "LCD": _sb(1024, I32), "LCE": _sb(1024, I32), "LE": _sb(256, I32), "CT": _sb(1024, I32), "C0": _sb(256, I32),
    "U": _sb(1024, BF), "CF": _sb(1024, F16), "C16": _sb(256, F16), "FF": _sb(1024, F16),
    "N16": _sb(1024, F16), "LU": _sb(4096, U16),
    "TB0": _sb(2048, BF), "TB1": _sb(2048, BF), "TB2": _sb(2048, BF), "ZT": _sb(2048, BF), "IDX": _sb(2048, F32),
    "EO": _sb(512, F32), "G0": _sb(256, BF), "G1": _sb(256, BF), "HK": _sb(512, BF), "GZ": _sb(256, F16),
    "VR": _sb(32, BF),
    "C4": _sb(128, F16), "Q4": _sb(144, F16), "Q0L": _sb(16, U16), "BX": _sb(8, BF), "DG": _sb(128, BF), "M16": _sb(16, BF), "O16": _sb(32, BF), "VC": _sb(128, BF), "AC": _sb(128, F16),
    "Y": _sb(4096, F16), "ER": _sb(512, F16), "SG": _sb(32, BF), "HI": _sb(32, U16), "T0C": _sb(16, F16), "I3": _sb(256, BF),
    "PEN": _sb(896, BF), "SW": _sb(144, F16), "SEL": _sb(8, F32),
    "TL": _sb(256, U16), "T16": _sb(128, F16), "T0L": _sb(16, U16),
    "LO": _sb(32, F16), "Z16": _sb(32, U16),
    "GA": _sb(2048, BF), "GB": _sb(2048, BF), "FB": _sb(256, BF), "YS": _sb(512, BF),
    "OE": _sb(256, F32), "OUT": _sb(256, F32), "YC": _sb(256, F32),
    "PI": _sb(1, I32), "PJ": _sb(8, I32), "PC": _sb(96, F32), "XF": _sb(176, BF), "V1": _sb(128, BF), "JP": _sb(128, BF),
    "BG": _sb(128, BF), "VA": _sb(384, BF), "V2": _sb(128, BF), "VQ": _sb(144, BF), "RQ": _sb(56, F32),
    "Q": _sb(256, BF), "CWL": _sb(144, BF), "QW": _sb(144, F16),
    "Q0": _sb(144, F16), "AW": _sb(512, BF), "U0": _sb(256, BF), "GF": _sb(768, BF), "XH": _sb(128, BF), "PA0": _sb(384, F16),
    "PA1": _sb(384, F16), "PC0": _sb(128, F16), "RE": _sb(128, F16), "IB": _sb(128, BF), "IH": _sb(128, F16),
    "SH": _sb(128, F16), "KY": _sb(128, BF), "IT": _sb(128, BF), "BC": _sb(8, F32), "CK": _sb(256, BF),
    "SF": _sb(2, F32),
}
for _b in range(8):
    SCRATCH["P%d" % _b] = ("psum", [128, 512], F32)
NDMA = 52
SEMAPHORES = (["pe", "act", "dve", "pool", "sent"] + ["d%d" % i for i in range(NDMA)]
              + ["%s%d" % (x, i) for x in ("w", "x", "e", "h") for i in range(10)] + ["%s%d" % (x, i) for x in ("u", "hu", "v", "hv") for i in range(4)])

CYC, GAT, PEC, HOP, LAT, RATE, LOCAL = 1.0e-3, 1.45e-3, 0.5e-3, 0.115, 1.7, 80.0, 250.0
CASES = ((0.95, 0.95, 0.95, 0.2, 1.0, 0.0, 1.0), (0.75, 0.9, 0.9, 1.7, 1.3, -0.02, 1.4), (1.2, 1.1, 1.1, 0.0, 0.9, 0.03, 0.8))
CYCLE, WARM, TURNS = 3000, 0.005, 0
HEATS, EARLY = ((6, 0.08), (6, 0.06), (6, 0.04), (6, 0.03), (6, 0.015)), 0.3
ROUNDS, HEAT, SEED, PLAN = 200000, 0.04, 3, {}
PERIOD, FIRST, LATE = 9.74, 12.5, 3.0
START = {"x01": 0.02, "codes": 0.05, "x23": 0.0, "ce0": 0.1, "ce1": 0.4, "cd": 0.2, "e": 0.3, "z": 6.0, "send": 2.55, "iota": 0.0,
         "iota2": 4.0, "idx": 12.0, "early": 0.1, "cols": 0.5, "mats": 3.0, "late": 5.5, "q0": 2.6, "cf": 3.4, "env0": 4.9,
         "env1": 8.5, "fast": 6.9, "e16": 7.4, "u": 7.3, "tb": 13.0, "tb0": 10.0, "tb1": 10.1, "tb2": 9.2, "conv": 12.4, "conv2": 17.5,
         "g0": 10.5, "t0": 2.8, "carry": 13.0}
AIM = {("V", 0): [-0.69, 0.0, 1.19, 2.34, 0.76, 1.95, 2.83, 3.28, 3.69, 3.85, 4.12, 4.74],
       ("V", 1): [1.33, 1.76, 2.93, 3.88, 2.52, 4.01, 4.88, 5.33, 5.62, 5.78, 5.9, 6.51],
       ("C", 0): [4.0, 4.3, 4.6, 4.61, 4.81, 5.02], ("C", 1): [6.33, 6.59, 5.73, 6.77, 7.11, 7.49],
       ("T", 0): [5.09, 5.64, 6.05, 6.66], ("T", 1): [7.32, 7.95, 8.37, 13.39], ("W2", 0): [5.87], ("W2", 1): [8.19],
       ("T1", 0): [5.44, 5.94, 6.1, 6.26, 7.02, 6.04, 6.54, 6.83, 7.31], ("T1", 1): [7.89, 8.57, 8.85, 10.31, 9.15, 9.7, 9.98, 10.61],
       ("T4", 0): [6.47, 7.21, 7.72, 9.73, 7.6, 8.01, 8.29, 10.02], ("T4", 1): [8.47, 9.13, 9.42, 11.49, 9.44, 10.26, 10.64, 11.78],
       ("T3", 0, 0): [7.72, 7.84], ("T3", 1, 0): [11.26, 12.55], ("T3", 0, 1): [10.54], ("T3", 1, 1): [12.45],
       ("R", 0): [-2.89, -2.6, -2.31, -1.69], ("R", 1): [-0.97, -0.69, -0.39, 0.72],
       ("O", 0): [-1.55], ("O", 1): [3.12], ("O2", 0): [-1.14, -1.07, -1.0, -0.8], ("O2", 1): [3.46, 3.52, 3.59, 3.77], ("K",): [0.0, 0.52], ("I",): [0.5, 1.3, 2.1],
       ("O3", 0): [-0.51, -0.33], ("O4", 0): [1.16, 1.64, 3.41, 3.89, 4.06], ("O3", 1): [3.99, 4.17], ("O4", 1): [4.69, 4.98, 5.21, 5.51, 5.57],
       ("L2", 0): [0.0], ("L2", 1): [3.0],
       ("E", 0): [4.31, 4.65], ("E", 1): [5.81, 6.28], ("L", 0): [-0.5], ("L", 1): [3.0],
       ("D", 0): [6.0], ("D", 1): [5.9, 6.11]}


def helper_of(core, topo, sem="h0"):
    far, i = VIA.get(sem, (1, int(sem[-1]) % 2 * STEP2))
    return [c for c in topo.cores_of(core) if c != core and (topo.die(c) != topo.die(core)) == bool(far)][i]


def dst_id(topo, c):
    rid, pid, _ = topo.addr(c)
    return DstId(rid=rid, pnc=pid)


def slot(k, r):
    return 1024 * k + 256 * (k // 4 + 1) + 256 * (N - 1 - r)


def values_at(T, r, b):
    return T.HV[:, 1024 * r + VCUT[b]:1024 * r + VCUT[b + 1]]


def env_at(T, t, r, X):
    c = slot(4 + t, r) + 128 * X
    return T.HE[:, c:c + 128], ("HE", c // 128)


def inner_engines(topo, core, far):
    out = topo.engines(core, far)
    return [e for e in topo.engines(core, helper_of(core, topo)) if e not in out]


def build_ops(g, T, topo, core, me):
    A, ACT = AluOpType, ActivationFunctionType
    ops = []
    role = [None, 0, 0]

    now = [0.0]

    def when(name):
        now[0] = START[name]

    def part(name):
        role[0], role[1] = name, 0

    def op(eng, fn, rd, wr, dur, lat=0.0, kind="c", **kw):
        kw["role"] = ("once", len(ops)) if role[0] is None else (role[0], role[1])
        kw["step"] = role[2]
        if role[0] is not None:
            a = AIM[role[0]]
            kw["aim"] = a[min(role[1], len(a) - 1)] + 0.001 * role[1]
            if role[2] < 0:
                kw["role"], kw["at"] = ("once", len(ops)), START["t0"] + kw.pop("aim")
        else:
            kw["at"] = now[0]
            now[0] += 0.002
        role[1] += 1
        ops.append(dict(eng=eng, fn=fn, rd=list(rd), wr=list(wr), dur=dur, lat=lat, kind=kind, **kw))
        return len(ops) - 1

    def dv(fn, rd, wr, n):
        return op("dve", fn, rd, wr, 0.04 + max(64, n) * CYC)

    def ts(out, in0, s1, s2, o0, o1, rd, wr, n):
        if o1 is None:
            return dv(lambda: g.vector.tensor_scalar(out, in0, s1, None, o0), rd, wr, n)
        return dv(lambda: g.vector.tensor_scalar(out, in0, s1, s2, o0, o1), rd, wr, n)

    def cp(out, in_, rd, wr, n):
        return dv(lambda: g.vector.tensor_copy(out, in_), rd, wr, n)

    def tt(out, a, b, o, rd, wr, n):
        return dv(lambda: g.vector.tensor_tensor(out, a, b, o), rd, wr, n)

    def ms(ap, v, wr, n):
        return dv(lambda: g.vector.memset(ap, v), [], wr, n)

    def ac(out, in_, rd, wr, n, bias=None, scale=None, func=None):
        kw = {}
        if bias is not None:
            kw["bias"] = bias
        if scale is not None:
            kw["scale"] = scale
        f = func if func is not None else (ACT.Identity if kw else ACT.Copy)
        return op("act", lambda: g.scalar.activation(out, in_, f, **kw), rd, wr, 0.06 + n * CYC)

    def lin(key, out, in_, a, b, rd, wr, n):
        if key in ON_SCALAR:
            return ac(out, in_, rd, wr, n, scale=a, bias=b)
        return ts(out, in_, a, b, A.mult, A.add, rd, wr, n)

    def ag(out, src, rd, wr, n):
        if wr[-1] in ON_VECTOR:
            return op("dve", lambda: g.vector.tensor_copy(out, src), rd, wr, 0.06 + n * GAT, cls=0)
        return op("act", lambda: g.scalar.activation(out, src, ACT.Copy), rd, wr, 0.06 + n * GAT, cls=0)

    def gs(out, src, func, bias, scale, rd, wr, n):
        return op("act", lambda: g.scalar.activation(out, src, func, bias=bias, scale=scale), rd, wr, 0.06 + n * GAT, cls=0)

    def dg(out, src, in1, o, rd, wr, n):
        return op("dve", lambda: g.vector.tensor_tensor(out, src, in1, o), rd, wr, 0.06 + n * GAT, cls=0)

    def mm(lst, rd, wr, start=True, stop=True):
        def fn():
            last = None
            for i, (o, l, r, n) in enumerate(lst):
                last = g.tensor.matmul(o, l, r, start and i == 0, stop and i == len(lst) - 1)
            return last
        return op("pe", fn, rd, wr, 0.05 + sum(max(64, x[3]) for x in lst) * PEC)

    def mms(groups, rd, wr):
        def fn():
            last = None
            for lst in groups:
                for i, (o, l, r, n) in enumerate(lst):
                    last = g.tensor.matmul(o, l, r, i == 0, i == len(lst) - 1)
            return last
        return op("pe", fn, rd, wr, 0.05 + sum(max(64, x[3]) for lst in groups for x in lst) * PEC)

    def io(out, pat, base, cm, wr, n, flag=True):
        if flag:
            return op("pool", lambda: g.iota(out, pat, base, cm, allow_small_or_imprecise_dtypes=True), [], wr, 0.13 + 2 * n * CYC)
        return op("pool", lambda: g.iota(out, pat, base, cm), [], wr, 0.13 + 2 * n * CYC)

    def pc(out, in_, rd, wr, n):
        return op("pool", lambda: g.affine_select(out, in_, [[0, n]], A.is_ge, 0.0, 0, 0), rd, wr, 0.17 + 2 * n * CYC)

    def dma(q, out, in_, rd, wr, kb):
        e = g.sync if q == "sp" else g.scalar
        pairs = list(zip(out, in_)) if isinstance(out, list) else [(out, in_)]
        i = op(q, lambda: [e.dma_start(a, b) for a, b in pairs], rd, wr, 0.1 * len(pairs), kind="dma")
        return op("ring", None, [], wr, 0.01 + kb / LOCAL, lat=1.9, kind="land", after=i)

    def P(b):
        return T["P%d" % b]

    def B(b):
        return ("B", b)

    def env(X):
        return T.ER[:, 256 * X:256 * X + 128]

    peers = [(me + k) % N for k in (1, 2, 3)]
    out_e = topo.engines(core, T.cores[peers[0]])
    ne = len(out_e)
    in_e = inner_engines(topo, core, T.cores[peers[0]])
    ids = [dst_id(topo, T.cores[r]) for r in peers]

    def mask(es):
        return sum(1 << e for e in es)

    def recv(after, link, lat, kb, sem, cnt, wr):
        return op(link, None, [], wr, 0.01 + kb / RATE, lat=lat, kind="recv", after=after, sem=sem, cnt=cnt)

    def spread(aps, sem, rd, wr, kb, to=None):
        per = ne // len(aps)
        trs = [RemoteDMATransfer(dst_ids=ids, dma_engine_mask=mask(out_e[per * i:per * i + per]), remote_sem=T.sem[sem],
                                 srcs=[a], dsts=3 * [to[i] if to else a]) for i, a in enumerate(aps)]
        sd = op("pool", lambda: g.remote_dma_fused(trs, local_sem=T.sem.sent), rd, [], 0.5, kind="send", inc=ne)
        recv(sd, "link", LAT, kb, sem, 3 * ne, wr)

    last = {}

    def relay(ap, hsem, sem, rd, wr, kb):
        hc = helper_of(core, topo, hsem)
        rid, pid, _ = topo.addr(hc)
        sd = op("pool", lambda: g.remote_dma(ap, ap, T.sem[hsem], T.sem.sent, pid, rid, mask(in_e)), rd, [], 0.5,
                kind="send", inc=len(in_e))
        role[1] -= 1
        hop = op(("helper", hc), None, [], [], 0.5, lat=LAT + kb / 450.0, kind="hop", after=sd)
        ops[hop]["role"] = ops[hop]["role"] + ("hop",) if role[0] is not None else ops[hop]["role"]
        ops[hop]["also"] = last.get(hc)
        last[hc] = hop
        recv(hop, "link" if topo.die(hc) == topo.die(core) else "link2", LAT, kb, sem, 3 * ne, wr)

    def first_values(r, b):
        return [("HV", 8 * r + x) for x in range(VCUT[b] // 128, VCUT[b + 1] // 128)]

    for b in range(len(VCUT) - 1):
        when("x23" if b else "x01")
        dma("sp", values_at(T, me, b), T.x0[:, VCUT[b]:VCUT[b + 1]], [], first_values(me, b), (VCUT[b + 1] - VCUT[b]) / 4)
    when("codes")
    dma("act", T.C0[0:8, :], T.c0[:], [], ["C0"], 16)
    for i, src in enumerate((T.cc0, T.ky, T.kid)):
        dma("act", T.CT[8 * i:8 * i + 8, :], src[:], [], [("CT", i)], 48)
    dma("sp", [T.CT[24 + 8 * x:32 + 8 * x, :] for x in range(2)], [T.cd[14 + x:128:16, :] for x in range(2)], [], [("CT", 3)], 96)
    for h in range(2):
        when("ce%d" % h)
        dma("sp", T.LCE[:, 512 * h:512 * h + 512], T.ce0[:, 512 * h:512 * h + 512], [], [("LCE", h)], 256)
    when("cd")
    for h in range(2):
        dma("sp", T.LCD[:, 512 * h:512 * h + 512], T.cd[:, 512 * h:512 * h + 512], [], [("LCD", h)], 256)
    when("e")
    dma("sp", T.LE[:], T.e0[:], [], ["LE"], 128)
    when("z")
    for h in range(2):
        dma("sp", T.ZT[:, 1024 * h:1024 * h + 1024], T.zt[:], [("LCD", 1), ("LCE", 1)], [("ZT", h)], 256)
    when("send")
    for b in range(len(VCUT) - 1):
        got, kb = [x for r in peers for x in first_values(r, b)], 0.75 * (VCUT[b + 1] - VCUT[b])
        if b:
            relay(values_at(T, me, b), "hv%d" % b, "v%d" % b, first_values(me, b), got, kb)
        else:
            spread([values_at(T, me, b)], "v%d" % b, first_values(me, b), got, kb)

    when("iota")
    io(T.PJ[:, 3:4], [[0, 1]], 0, 1, ["PI"], 1, flag=False)
    io(T.XF[:], [[1, 176]], -16, 0, ["XF"], 176)
    io(T.VA[:], [[-1, 24], [-1000, 4], [-32, 4]], 999, 1, ["VA"], 384)
    io(T.XH[:], [[1, 64], [0, 2]], 0, 0, ["XH"], 128)
    io(T.V2[0:32, :], [[0, 4], [-1, 32]], 1, 1, ["V2"], 128)
    io(T.V1[:], [[-1, 128]], 0, 1, ["V1"], 128)
    when("iota2")
    io(T.VQ[0:8, :], [[1, 144]], -16, -16, ["VQ"], 144)
    io(T.JP[:], [[0, 8], [1, 16]], -8, 0, ["JP"], 128)
    io(T.BG[:], [[16, 8], [0, 16]], 0, 0, ["BG"], 128)
    io(T.VC[0:40, :], [[-1, 8], [-8, 8], [0, 2]], -24, 1, ["VC"], 128)
    when("late")
    io(T.CK[:, 0:128], [[0, 128]], 128, 0, ["CK"], 128)
    io(T.O16[:], [[-2, 2], [0, 16]], 1, 0, ["O16"], 32)
    when("early")

    def X_(d, n):
        return T.XF[:, 16 - d:16 - d + n]

    for b in range(4):
        ms(T.SF[32 * b:32 * b + 32, 0:1], 0.125 ** b, [("SF", b)], 1)
    ms(T.SF[:, 1:2], 1535.5 + 1.0 / 1024, [("SF", 4)], 1)
    ms(T.SF[0:32, 1:2], 0.0, [("SF", 4)], 1)
    SFt = [("SF", b) for b in range(5)]
    CKt = ["CK"]
    when("late")
    io(T.BX[:], [[256, 4], [128, 2]], 1024 * me - 2048, 0, ["BX"], 8)
    when("early")
    ts(T.IH[:], T.V1[:], 0.0, None, A.is_equal, None, ["V1"], ["IH"], 64)
    ts(T.RE[0:32, :], T.V2[0:32, :], 0.0, None, A.is_equal, None, ["V2"], ["RE"], 64)
    ts(T.PA0[:], T.VA[:], 0.0, None, A.is_equal, None, ["VA"], ["PA0"], 192)
    ts(T.PA1[:], T.VA[:], 32.0, -8.0, A.is_equal, A.mult, ["VA"], ["PA1"], 192)
    for r, v in ((4, 8.0), (5, 7.0), (6, 7.0), (7, -1.0)):
        ac(T.PA0[32:33, r:384:16], T.XF[32:33, 0:24], ["PA0", "XF"], [("PA0", r)], 24, scale=0.0, bias=v)
        tt(T.PA0[:, r:384:16], T.PA0[:, r:384:16], T.PA1[:, r:384:16], A.add, ["PA1"], [("PA0", r)], 48)
    PAt = [("PA0", r) for r in range(4, 8)]
    ts(T.PC0[:], T.PA0[:, 0:128], UN, None, A.mult, None, PAt, ["PC0"], 64)
    ts(T.IB[:], T.V1[:], 0.0, None, A.is_equal, None, ["V1"], ["IB"], 64)
    ts(T.Q0[0:8, :], T.VQ[0:8, :], 0.0, None, A.is_equal, None, ["VQ"], ["Q0"], 72)

    when("iota")
    for j, m in enumerate((15, 1, 3)):
        ts(T.PJ[:, j:j + 1], T.PJ[:, 3:4], m, None, A.bitwise_and, None, ["PI"], [("PJ", j)], 1)
    names = ["row", "par", "r3", "p"]
    cp(T.PC[:, 0:4], T.PJ[:, 0:4], ["PI"] + [("PJ", j) for j in range(3)], [("c", x) for x in names], 4)

    def col(x):
        return T.PC[:, names.index(x):names.index(x) + 1]

    for x, o in (("is", A.is_equal), ("lt", A.is_gt)):
        a = len(names)
        names += ["%s%d" % (x, r) for r in range(16)]
        ts(T.PC[:, a:a + 16], X_(0, 16), col("row"), None, o, None, ["XF", ("c", "row")], [("c", y) for y in names[a:]], 16)

    def cs(x, src, s1, s2, o0, o1=None):
        names.append(x)
        rd = [("c", y) for y in (src, s1, s2) if isinstance(y, str)]
        s1, s2 = (col(y) if isinstance(y, str) else y for y in (s1, s2))
        if o0 == A.mult and o1 in (None, A.add):
            ac(col(x), col(src), rd, [("c", x)], 1, scale=s1, bias=s2)
        elif o0 == A.add and o1 is None:
            ac(col(x), col(src), rd, [("c", x)], 1, bias=s1)
        else:
            ts(col(x), col(src), s1, s2, o0, o1, rd, [("c", x)], 1)

    def eq(out, d, n, x, v, wr):
        ts(out, X_(d, n), col(x), col(v) if isinstance(v, str) else v, A.is_equal, A.mult,
           ["XF", ("c", x)] + ([("c", v)] if isinstance(v, str) else []), wr, n // 2)

    when("cols")
    cs("g16", "row", -1.0, "p", A.mult, A.add)
    cs("u8", "lt8", -1.0, 1.0, A.mult, A.add)
    cs("rh", "row", 0.5, None, A.mult)
    cs("hm", "par", -0.5, "rh", A.mult, A.add)
    cs("h7", "is14", "is15", None, A.add)
    cs("s1", "par", "is14", None, A.add)
    cs("sq", "lt14", -8.0, "s1", A.mult, A.add)
    cs("gam", "is14", -64.0, None, A.mult)
    cs("a1", "par", 128.0, -64.0, A.mult, A.add)
    cs("al", "is15", -64.0, "a1", A.mult, A.add)
    cs("b1", "s1", 64.0, -64.0, A.mult, A.add)
    cs("be", "is15", 32.0, "b1", A.mult, A.add)
    for x, (a, b) in (("e0", (336.0, 112.0)), ("e15", (112.0, 336.0))):
        cs(x + "a", "par", b - a, a, A.mult, A.add)
        cs(x + "b", "is14", -26880.0 - a, x + "a", A.mult, A.add)
        cs(x, "is15", -80.0 - b, x + "b", A.mult, A.add)
    cs("k0", "g16", 0.5, "row", A.mult, A.add)
    cs("k1", "k0", -7.0, None, A.add)
    cs("v1", "lt7", -1.0, "lt14", A.mult, A.add)
    when("mats")
    ts(T.AC[0:40, :], T.VC[0:40, :], 0.0, None, A.is_equal, None, ["VC"], ["AC"], 64)
    for i, (x, v) in enumerate((("k0", "lt7"), ("k1", "v1"))):
        ts(T.AW[:, 128 * i:128 * i + 128], T.XH[:], col(x), col(v), A.is_equal, A.mult, ["XH", ("c", x), ("c", v)], [("AW", i)], 64)
    when("cols")
    ac(T.RQ[:, 0:16], X_(8, 16), ["XF", ("c", "gam"), ("c", "al")], ["R1"], 16, scale=col("gam"), bias=col("al"))
    tt(T.RQ[:, 16:32], T.RQ[:, 0:16], X_(8, 16), A.mult, ["R1", "XF"], ["R2"], 32)
    ac(T.RQ[:, 32:48], T.RQ[:, 16:32], ["R2", ("c", "be")], ["R3"], 16, bias=col("be"))
    for j, x in ((0, "e0"), (15, "e15")):
        ac(T.RQ[:, 32 + j:33 + j], col(x), [("c", x), "R3"], [("R3", j)], 1)
    ts(T.RQ[:, 48:56], X_(0, 8), 16.0, col("g16"), A.mult, A.is_equal, ["XF", ("c", "g16")], ["R4"], 8)
    for a in range(8):
        ac(T.Q[:, 128 + 16 * a:144 + 16 * a], T.RQ[:, 32:48], ["R4", ("R3", 0), ("R3", 15)], [("Q2", a)], 16, scale=T.RQ[:, 48 + a:49 + a])
    ts(T.SEL[:], X_(0, 8), col("hm"), col("h7"), A.is_equal, A.add, ["XF", ("c", "hm"), ("c", "h7")], ["SEL"], 8)
    when("mats")
    for m in range(7):
        ts(T.PEN[:, 128 * m:128 * m + 128], T.Q[:, 128:256], T.SEL[:, m:m + 1], 64 / UN, A.mult, A.mult,
           [("Q2", a) for a in range(8)] + ["SEL"], [("PEN", m)], 64)
    eq(T.SW[:], 16, 144, "g16", UN, ["SW"])
    when("late")
    ts(T.Q[:, 0:128], T.BG[:], col("g16"), None, A.is_equal, None, ["BG", ("c", "g16")], ["Q1"], 64)
    for x, v in enumerate((3.0, -4.25)):
        ts(T.I3[:, 128 * x:128 * x + 128], T.V1[:], 0.0, v, A.is_equal, A.mult, ["V1"], [("I3", x)], 64)
    cs("cq", "u8", "g16", None, A.add)
    cs("mq", "is0", "is8", None, A.add)
    eq(T.QW[:], 14, 144, "cq", "mq", ["QW"])
    cs("m8", "lt8", -1.0, "lt12", A.mult, A.add)
    cs("n47", "lt4", "u8", None, A.add)
    cs("hb", "n47", HB, None, A.mult)
    cs("m411", "lt4", -1.0, "lt12", A.mult, A.add)
    cs("s2", "m411", 0.5 / HB ** 0.5 - 1.0, 1.0, A.mult, A.add)
    cs("b2a", "par", -1.0, HB ** 0.5 + 8.0, A.mult, A.add)
    cs("b2", "m411", "b2a", "sq", A.mult, A.add)
    cs("rq", "row", 0.25, "g16", A.mult, A.add)
    cs("c4", "r3", -0.25, "rq", A.mult, A.add)
    cs("m4a", "is4", "mq", None, A.add)
    cs("m4", "is12", "m4a", None, A.add)
    cs("b4", "m4", -585 * HB, None, A.mult)
    eq(T.Q4[:], 12, 144, "c4", "m4", ["Q4"])
    for m in (1, 2, 3):
        cs("p%d" % m, "is%d" % (4 + m), 8.0 ** m, "p%d" % (m - 1) if m > 1 else "is4", A.mult, A.add)
    eq(T.CWL[:], 16, 144, "g16", "p3", ["CWL"])
    ts(T.KY[:], T.V1[:], 4.0, col("m8"), A.is_equal, A.mult, ["V1", ("c", "m8")], ["KY"], 64)
    ts(T.SH[:], T.V1[:], -1.0, col("lt15"), A.is_equal, A.mult, ["V1", ("c", "lt15")], ["SH"], 64)
    cs("fu", "is0", 1.0 / UN, None, A.mult)
    ac(T.IT[:], X_(0, 128), ["XF", ("c", "fu")], ["IT"], 128, scale=col("fu"))
    ac(T.BC[:], T.BX[:], ["BX", ("c", "fu")], ["BC"], 8, scale=col("fu"))
    cs("r8", "row", -8.0, None, A.add)
    ts(T.DG[:], T.JP[:], col("r8"), 65536.0, A.is_equal, A.mult, ["JP", ("c", "r8")], ["DG"], 64)
    for x in range(2):
        ac(T.M16[:, 8 * x:8 * x + 8], T.Q[:, 0:128:16], ["Q1"], [("M16", x)], 8, scale=2048.0)
    for X in range(2):
        ac(T.LO[:, 16 * X:16 * X + 8], X_(0, 8), ["XF", ("c", "row")], [("LOc", X)], 8, scale=16.0, bias=col("row"))

    CTt = [("CT", i) for i in range(4)]
    when("q0")
    cp(T.C16[0:8, :], T.C0[0:8, :], ["C0"], ["C16"], 256)
    mms([[(P(6)[:, 0:16], T.Q0[0:8, 16 - s:144 - s], T.C16[0:8, s:256:16], 16) for s in range(16)]], ["Q0", "C16"], [B(6)])
    cp(T.Q0L[:], P(6)[:, 0:16], [], [B(6), "Q0L"], 16)
    when("fast")
    op("dve", lambda: g.vector.tensor_copy(T.U0[:], T.LCD[:, 0:1024].indirect(T.Q0L[:])),
       [("LCD", 0), ("LCD", 1), "Q0L"], ["U0"], 0.06 + 256 * GAT, cls=0)
    for bank, ii in ((2, (0, 1)), (3, (2,)))[:FAST - 1]:
        n = 256 * len(ii)
        mms([[(P(bank)[:, 256 * x:256 * x + 256], T.AW[:, 128 * i:128 * i + 128], T.U0[:], 256)] for x, i in enumerate(ii)],
            [("AW", i) for i in ii] + ["U0"], [B(bank)])
        ac(T.GF[:, 256 * ii[0]:256 * ii[0] + n], P(bank)[:, 0:n], [("c", "sq")], [B(bank)] + [("GF", i) for i in ii], n,
           bias=col("sq"), func=ACT.Square)
    when("cf")
    for h in range(2):
        c = slice(512 * h, 512 * h + 512)
        lin(("CF", h), T.CF[0:40, c], T.CT[0:40, c], 1.0, 0.0, CTt, [("CF", h)], 512)
        mm([(P(h)[:], T.RE[0:24, :], T.CF[0:24, c], 512)], ["RE", ("CF", h)], [B(h)])
        lin(("FF", h), T.FF[:, c], P(h)[:], T.SF[:, 0:1], T.SF[:, 1:2], SFt, [B(h), ("FF", h)], 512)

    for h in range(2):
        when("env%d" % h)
        for b in (2 * h, 2 * h + 1):
            c, bank = slice(256 * b, 256 * b + 256), 4 + b
            e, o = slot(b, me), P(bank)[:, 0:256]
            tk = [("HE", e // 128), ("HE", e // 128 + 1)]
            lst = [(o, T.PC0[:], T.FF[:, c], 256)]
            if b in WIDE:
                lin(("N16", b), T.N16[:, c], T.LCE[:, c], 1.0, -2048.0, [("LCE", h)], [("N16", b)], 256)
                mm(lst + [(o, T.IH[:], T.N16[:, c], 256)], [("FF", h), "PC0", "IH", ("N16", b)], [B(bank)])
                lin(("own", b), T.HE[:, e:e + 256], o, 1.0 / UN, HB, [], [B(bank)] + tk, 256)
                got = [("HE", slot(b, r) // 128 + x) for r in peers for x in (0, 1)]
                if b in OWN:
                    spread([T.HE[:, e:e + 256]], "u%d" % b, tk, got, 384)
                else:
                    relay(T.HE[:, e:e + 256], "hu%d" % b, "u%d" % b, tk, got, 384)
                continue
            m = T.LU[:, e - 256:e]
            mm(lst, [("FF", h), "PC0"], [B(bank)])
            tt(m, o, T.LCE[:, c], A.add, [("LCE", h)], [B(bank), ("MU", b)], 256)
            if b in OWN:
                spread([m], "u%d" % b, [("MU", b)], [("LU", b)], 192)
            else:
                relay(m, "hu%d" % b, "u%d" % b, [("MU", b)], [("LU", b)], 192)
    when("idx")
    def gap(k):
        c = slot(k, N - 1) - 256
        return io(T.HE[:, c:c + 256], [[0, 256]], 0, 0, [("HE", c // 128), ("HE", c // 128 + 1)], 256)

    for k in (0, 4):
        ops[gap(k)]["also"] = max(j for j, o in enumerate(ops) if o["kind"] == "send")
    when("e16")
    for X in range(2):
        lin(("E0", X), env(X), T.LE[:, 128 * X:128 * X + 128], 1.0 / UN, -0.5, ["LE"], [("E16", X)], 128)
    when("u")
    for h in range(2):
        c = slice(512 * h, 512 * h + 512)
        if ("U", h) in ON_POOL:
            pc(T.U[:, c], T.LCD[:, c], [("LCD", h)], [("U", h)], 512)
        else:
            lin(("U", h), T.U[:, c], T.LCD[:, c], 1.0, 0.0, [("LCD", h)], [("U", h)], 512)
    TB = (T.TB0, T.TB1, T.TB2)
    for i in range(3):
        when("tb%d" % i)
        if i < 2:
            dma("sp", [TB[i][r:128:16, 0:1024] for r in range(16)], [T.U[7 * i + r // 2:128:16, :] for r in range(16)],
                [("U", 0), ("U", 1)], [("TB", i, 0), ("TB", i, 1)], 256)
        for h in range(2 if i == 2 else 0):
            c, bank = slice(512 * h, 512 * h + 512), 2 + h
            o = P(bank)[:]
            mm([(o, T.PA0[:, 256:384], T.FF[:, c], 512)], PAt + [("FF", h)], [B(bank)], True, False)
            mm([(o, T.PA0[:, 124:252], T.FF[:, c], 512)], PAt + [("FF", h)], [B(bank)], False, False)
            mm([(o, T.AC[0:40, :], T.CF[0:40, c], 512)], ["AC", ("CF", h)], [B(bank)], False, True)
            ac(TB[i][:, c], o, [("c", "s2"), ("c", "b2")], [B(bank), ("TB", i, h)], 512, bias=col("b2"), scale=col("s2"), func=ACT.Square)
        when("tb")
        dma("sp", TB[i][:, 1024:2048], TB[i][:, 0:1024], [("TB", i, 0), ("TB", i, 1)], [("TB", i, 2), ("TB", i, 3)], 256)
    for b in range(4):
        when("conv" if b < 2 else "conv2")
        for h in range(2 if b not in WIDE else 0):
            l = 1024 * b + 512 * h
            lin(("conv", b, h), T.HE[:, 256 + l:768 + l], T.LU[:, l:l + 512], 1.0 / UN, HB - 0.5, [("LU", b), ("MU", b)],
                [("HE", 2 + l // 128 + x) for x in range(4)], 512)
    when("g0")

    C0 = 64.0 * 67840 + 2048

    def side_at(X, side):
        return 64 * (side if X else 1 - side)

    def fused(t, X):
        return X in FUSED

    def signed(t, X):
        return X in SIGN and t < S - 1

    G = (T.G0, T.G1, T.HK)

    def tile(i, X):
        a = 256 * X + 128 if i == 2 else 128 * X
        return G[i][:, a:a + 128]

    def names_of(t, X):
        part(("T", X) if t else None)
        wide = 2048 if t else 1024
        q, qt = (T.Z16[:, 16 * X + 8:16 * X + 16], ("Z16", X)) if t else (T.Q0L[:, 8 * X:8 * X + 8], "Q0L")
        for i in range(3) if t else (2,):
            src, rd = TB[i][:, 0:wide].indirect(q), [("TB", i, h) for h in range(wide // 512)] + [qt]
            if i == 2:
                ag(tile(i, X), src, rd, [("G", i, X)], 128)
            else:
                gs(tile(i, X), src, ACT.Square, col("sq"), col("lt14"), rd + [("c", "sq"), ("c", "lt14")], [("G", i, X)], 128)
        if not fused(t, X):
            gs(T.GZ[:, 128 * X:128 * X + 128], T.ZT[:, 0:wide].indirect(q), ACT.Identity, -127.5, -1.0,
               [("ZT", h) for h in range(wide // 1024)] + [qt], [("GZ", X)], 128)

        def rows(i):
            if t or i >= FAST:
                return tile(i, X), ("G", i, X)
            return T.GF[:, 256 * i + 128 * X:256 * i + 128 * X + 128], ("GF", i)

        tb = P(2 + X)
        e, first = 256 * X, ("E16", X)
        part(("W2", X))
        if ("ER2", X) in ON_POOL and t:
            pc(T.ER[:, e + 128:e + 256], T.ER[:, e:e + 128], [first], [("ER", X, 1)], 128)
        else:
            lin(("ER2", X), T.ER[:, e + 128:e + 256], T.ER[:, e:e + 128], 1.0, 0.0, [first], [("ER", X, 1)],
                128 if ("ER2", X) in ON_SCALAR else 64)
        part(("T1", X))
        for i in range(4):
            ks = range(4 * i, 4 * i + 4)
            bank = (0, 1, 4 + X, 1 - X)[i]
            mms([[(P(bank)[:, 128 * (k % 4):128 * (k % 4) + 128], T.PEN[:, 128 * KT[k][1]:128 * KT[k][1] + 128], rows(KT[k][0])[0], 128)]
                 for k in ks], [("PEN", KT[k][1]) for k in ks] + [rows(KT[k][0])[1] for k in ks], [B(bank)])
            for x in range(2):
                y0 = 2048 * X + 512 * i + 256 * x
                if i == 0 and x == 0 and X in NARROW:
                    for y in range(2):
                        tt(T.Y[:, y0 + 128 * y:y0 + 128 * y + 128], P(bank)[:, 128 * y:128 * y + 128], T.ER[:, e:e + 128], A.min,
                           [first], [B(bank), ("Y", X, 0, 0) if y else ("Y0", X)], 128)
                    continue
                tt(T.Y[:, y0:y0 + 256], P(bank)[:, 256 * x:256 * x + 256], T.ER[:, e:e + 256], A.min, [first, ("ER", X, 1)],
                   [B(bank), ("Y", X, i, x)], 256)
            lst, o = [], tb[:, side_at(X, i // 2):side_at(X, i // 2) + 64]
            for k in ks:
                for u in range(2):
                    s, y0 = 8 * u + k % 8, 2048 * X + 128 * k
                    lst.append((o, T.SW[:, 16 - s:144 - s], T.Y[:, y0 + u:y0 + 128:2], 64))
            mm(lst, ["SW"] + [("Y0", X)] * (i == 0) + [("Y", X, i, x) for x in range(2)], [B(2 + X)], i % 2 == 0, i % 2 == 1)
            if i % 2:
                a, c0 = 128 * X + side_at(X, i // 2), C0
                part(("T3", X, i // 2))
                lin(("TL", X, i // 2), T.TL[:, a:a + 64], o, 1.0, c0, [], [B(2 + X), ("TL", X, i // 2)], 64)
                if i == 1 and ("T16", X) in ON_SCALAR:
                    ac(T.T16[:, 64 * X:64 * X + 64], o, [], [B(2 + X), ("T16", X)], 64, bias=c0 - 2048)
                elif i == 1:
                    ts(T.T16[:, 64 * X:64 * X + 64], T.TL[:, a:a + 64], -2048.0, None, A.add, None, [("TL", X, 0)], [("T16", X)], 32)
                part(("T4", X))

    def record(t, X):
        part(("R", X))
        o = P(6 + X)[:, 128:256]
        e = env(X)
        mm([(o, T.IH[:], e, 128), (o, T.KY[:], tile(2, X), 128)], ["IH", "KY", ("E16", X), ("G", 2, X)], [B(6 + X)])
        ap, tk = env_at(T, t, me, X)
        ac(ap, o, [("c", "hb")], [B(6 + X), tk], 128, bias=col("hb"))
        relay(ap, "h%d" % (2 * t + X), "e%d" % (2 * t + X), [tk], [env_at(T, t, r, X)[1] for r in peers], 192)

    HT = "HA"

    def above(X):
        return T.HK[:, 256 * X:256 * X + 128]

    def window(t, X):
        a, b = slot(t, N - 1) - 256 + 128 * X, slot(t + 3, 0) + 256
        return T.HE[:, a:b], [("HE", x) for x in range(a // 128, b // 128)]

    def outcomes(t, X):
        part(("O", X))
        b, final = t % 4, t == S - 1 and X not in AFTER
        l, lt = (T.T0L[:, 8 * X:8 * X + 8], ("T0L", X)) if final else (T.HI[:, 16 * X:16 * X + 8], ("HIl", X))
        ob, bk = P(6 + X), B(6 + X)
        o = ob[:, 0:8]
        mm([(o, T.QW[:, 14 - 2 * a:142 - 2 * a], T.T16[:, 64 * X + a:64 * X + 64:8], 8) for a in range(8)], ["QW", ("T16", X)], [bk])
        part(("O2", X))
        fl = [T.SG[:, 16 * X + 8 * x:16 * X + 8 * x + 8] for x in range(2)]
        for x, v in enumerate((49152 - 127.5, 196608 - 511.5)):
            lin(("SG", X), fl[x], o, 1.0, 2048 - 256 * b + v, [], [bk, ("SG", X, x)], 8)
        y = T.T0C[:, 8 * X:8 * X + 8]
        lin(("T0C", X), y, o, 1.0, 0.0, [], [bk, ("T0C", X)], 8)
        mm([(o, T.IH[:], y, 8)] + [(o, T.I3[:, 128 * x:128 * x + 128], fl[x], 8) for x in range(2)],
           ["IH", ("T0C", X), ("I3", 0), ("I3", 1), ("SG", X, 0), ("SG", X, 1)], [bk])
        part(("O3", X))
        lin(("T0L", X), l, o, 1.0, 2048 - 256 * b - 3 * 49152 + 4.25 * 196608 + 768 + 256 - 128 * X, [], [bk, lt], 8)
        win, rd = window(t, X)
        gs(above(X), win.indirect(l), ACT.Identity, 0.5 / UN, 1.0, rd + [lt], [("HA", X)], 128)
        if final:
            part(("L2", X))
            lin(("HIl", X), T.HI[:, 16 * X:16 * X + 8], T.LO[:, 16 * X:16 * X + 8], 1.0, 128.0, [("LOc", X)], [("HIl", X)], 8)
        part(("O4", X))
        mm([(ob[:, 64:128], T.CWL[:, 16 - 4 * u:144 - 4 * u], T.HK[:, 256 * X + u:256 * X + 256:4], 64) for u in range(4)],
           ["CWL", ("HA", X), ("G", 2, X)], [bk])
        lin(("C4", X), T.C4[:, 64 * X:64 * X + 64], ob[:, 64:128], 1.0, col("b4"), [("c", "b4")], [bk, ("C4", X)], 64)
        mm([(ob[:, 16:32], T.Q4[:, 12 - 4 * a:140 - 4 * a], T.C4[:, 64 * X + a:64 * X + 64:4], 16) for a in range(4)],
           ["Q4", ("C4", X)], [bk])
        lin(("LOq", X), T.LO[:, 16 * X + 8:16 * X + 16], ob[:, 24:32], 1.0, 0.0, [], [bk, ("LOq", X)], 8)
        lin(("HIq", X), T.HI[:, 16 * X + 8:16 * X + 16], ob[:, 16:24], 1.0, 1024.0, [], [bk, ("HIq", X)], 8)

    def bound(t, X):
        part(("E", X))
        o, bk = P(6 + X)[:, 256:384], B(6 + X)
        e = env(X)
        c, b = slot(t, N - 1) - 256 + 128 * X, 2 * (t % 4) + X
        lst, rd = [(o, T.SH[:], e, 128), (o, T.IB[:], T.IT[:], 128)], ["SH", "IB", "IT", ("E16", X)]
        if t < S - 1 or X in AFTER:
            mm(lst + [(o, T.IB[:], above(X), 128)], rd + [(HT, X)], [bk])
            ac(T.HE[:, c:c + 128], o, ["BC"], [bk, ("HE", c // 128)], 128, bias=T.BC[:, b:b + 1])
            return
        part(("L", X))
        mm(lst, rd, [bk])
        win, rd = window(t, X)
        ac(T.EO[:, 256 * X:256 * X + 128], o, ["BC"], [bk, ("EOb", X)], 128, bias=T.BC[:, b:b + 1])
        dg(T.EO[:, 256 * X + 128:256 * X + 256], win.indirect(T.T0L[:, 8 * X:8 * X + 8]), above(X), A.subtract,
           rd + [("T0L", X), (HT, X)], [("EO", X)], 128)

    def values(t, X):
        part(("V", X))
        a = 4096 * (t % 2)
        win, wt = T.HV[:, a:a + 4096], [(y, a // 128 + x) for x in range(32) for y in ("HV", "HQ")]
        sb, c = P(4 + X), slice(128 * X, 128 * X + 128)
        cut = X in QUART and t < S - 1
        h0 = 4096 - a + 1024 * me + 256 * (t % 4) + 128 * X
        safe = [("HV", 34 + 8 * r + x) for r in range(N) for x in range(2)] if (t, X) == (0, 1) else []
        w, tk = (T.HV[:, h0:h0 + 128], ("HV", h0 // 128)) if t < S - 1 else (T.W5[:, c], ("W5", X))

        def finish(a, n, y):
            o, f = sb[:, a:a + n], T.FB[:, 128 * X + a:128 * X + a + n]
            out, k = (T.HV[:, h0 + a:h0 + a + n], (y, h0 // 128)) if t < S - 1 else (w, tk)
            lin(("FB" if t < S - 1 else "FBL", X), f, o, 1.0, -127.5, [], [B(4 + X), ("FB", X, a)], n)
            for x in (1, 0) if X in WFIRST and t < S - 1 else (0, 1):
                if x:
                    tt(out, o, f, A.subtract, [("FB", X, a)], [B(4 + X), k], n)
                elif not fused(t, X) and not signed(t, X):
                    z = slice(128 * X + a, 128 * X + a + n)
                    tt(T.YS[:, z], o, T.GZ[:, z], A.add, [("GZ", X)], [B(4 + X), ("YS", X, a)], n)
            if t < S - 1:
                spread([out], "%s%d" % ({"HV": "w", "HQ": "x"}[y], 2 * t + X), [k] + safe, [(y, (h0 + 1024 * (r - me)) // 128) for r in peers], 0.75 * n)

        for h in range(2):
            j, la, lb = 2 * X + h, 128 * X + 32 * h + side_at(X, 0), 128 * X + 32 * h + side_at(X, 1)
            g0 = slice(512 * j, 512 * j + 512)
            if cut or h == 0:
                a, n = (64 * h, 64) if cut else (0, 128)
                mm([(sb[:, a:a + n], T.CK[0:3, 0:128], T.CK[0:3, 0:n], n)], CKt, [B(4 + X)], True, False)
            a = 0
            for n in PIECES[j]:
                g0 = slice(512 * j + 16 * a, 512 * j + 16 * (a + n))
                ag(T.GA[:, g0], win.indirect(T.TL[:, la + a:la + a + n]), wt + [("TL", X, 0)], [("GA", j, a)], 16 * n)
                dg(T.GB[:, g0], win.indirect(T.TL[:, lb + a:lb + a + n]), T.GA[:, g0], A.max, wt + [("TL", X, 1), ("GA", j, a)],
                   [("GB", j, a)], 16 * n)
                a += n
            mm([(sb[:, 64 * h:64 * h + 64], T.IB[:], T.GB[:, 512 * j + p:512 * j + 512:8], 64) for p in range(8)],
               ["IB"] + [("GB", j, sum(PIECES[j][:x])) for x in range(len(PIECES[j]))], [B(4 + X)], False, cut or h == 1)
            if cut:
                finish(64 * h, 64, ("HQ", "HV")[h])
        if not cut:
            finish(0, 128, "HV")
        tks = [tk, ("HQ", h0 // 128)]
        if fused(t, X):
            wide = 2048 if t else 1024
            q, qt = (T.Z16[:, 16 * X + 8:16 * X + 16], ("Z16", X)) if t else (T.Q0L[:, 8 * X:8 * X + 8], "Q0L")
            dg(T.YS[:, c], T.ZT[:, 0:wide].indirect(q), w, A.is_le, [("ZT", h) for h in range(wide // 1024)] + [qt] + tks, [("YS", X, 0)], 128)
        elif signed(t, X):
            o = sb[:, 128:256]
            mm([(o, T.IH[:], T.GZ[:, c], 128), (o, T.IB[:], w, 128)], ["IH", "IB", ("GZ", X)] + tks, [B(4 + X)])
            ac(T.YS[:, c], o, [], [B(4 + X), ("YS", X, 0)], 128, bias=128.0, func=ACT.Sign)

        part(("D", X))
        if t == S - 1:
            dma("sp", T.yx[:, 1280 + 128 * X:1408 + 128 * X], w, [tk], [], 32)
        elif X == 1:
            dma("sp", T.yx[:, 256 * t:256 * t + 256], T.HV[:, h0 - 128:h0 + 128],
                tks + [("HV", h0 // 128 - 1), ("HQ", h0 // 128 - 1)], [], 64)

    def choose(t, X):
        part(("C", X))
        vb = VOTES[X] if t < S - 1 else 2 + X
        o, c, sb, z = P(vb)[:, 384:400], slice(16 * X, 16 * X + 16), B(vb), slice(128 * X, 128 * X + 128)
        lst, f = [(o, T.FB[:, z], T.O16[:, 0:16], 16), (o, T.YS[:, z], T.O16[:, 16:32], 16)], -24.0 * 2048
        mm([(o, T.Q[:, 0:128], T.M16[:], 16)] + lst,
           ["Q1", ("M16", 0), ("M16", 1), "O16"] + [(y, X, a) for a in (0, 64) for y in ("YS", "FB")], [sb])
        if ("VR", X) in ON_SCALAR:
            ac(T.VR[:, c], o, [], [sb, ("VR", X)], 16, bias=f, func=ACT.Relu)
        else:
            ts(T.VR[:, c], o, f, 0.0, A.add, A.max, [], [sb, ("VR", X)], 16)
        o = P(2 + X)[:, 256:272]
        if vb == 2 + X:
            mm([(o, T.IH[:], T.LO[:, c], 16), (o, T.DG[:], T.VR[:, c], 16)], ["IH", ("LOc", X), ("LOq", X), "DG", ("VR", X)], [B(2 + X)])
            role[1] += 1
        else:
            mm([(o, T.IH[:], T.LO[:, c], 16)], ["IH", ("LOc", X), ("LOq", X)], [B(2 + X)], True, False)
            mm([(o, T.DG[:], T.VR[:, c], 16)], ["DG", ("VR", X)], [B(2 + X)], False, True)
        tt(T.Z16[:, c], o, T.HI[:, c], A.min, [("HIl", X), ("HIq", X)], [B(2 + X), ("Z16", X)], 16)
        l = T.Z16[:, 16 * X:16 * X + 8]
        if t < S - 1 or X in AFTER:
            win, rd = window(t, X)
            dg(env(X), win.indirect(l), above(X), A.subtract, rd + [("Z16", X), (HT, X)], [("E16", X)], 128)
            if t < S - 1:
                return
        part(None)
        c = slice(128 * X, 128 * X + 128)
        if X in AFTER:
            ac(T.OUT[:, c], env(X), [("E16", X)], [("OUT", X)], 128, scale=UN, bias=2048.0)
        else:
            op("dve", lambda: g.vector.tensor_scalar(T.OUT[:, c], T.EO[:, 256 * X:256 * X + 256].indirect(l), UN, 2048.0, A.mult, A.add),
               [("EO", X), ("EOb", X), ("Z16", X)], [("OUT", X)], 0.06 + 128 * GAT, cls=0)
        dma("sp", T.ye[:, c], T.OUT[:, c], [("OUT", X)], [], 64)
        ag(T.YC[:, c], T.IDX[:, 0:2048].indirect(T.Z16[:, 16 * X + 8:16 * X + 16]), [("IDX", x) for x in range(8)] + [("Z16", X)],
           [("YC", X)], 128)
        dma("act", T.yc[:, c], T.YC[0:128:16, c], [("YC", X)], [], 4)

    def carry(a, b, n=1):
        at = [[x + 1024 * r + 256 * b for r in range(N)] for x in (a, 4096 - a)]
        tk = [[(y, c // 128 + i) for c in x for i in range(2 * n) for y in ("HV", "HQ")] for x in at]
        dma("sp", [T.HV[:, c:c + 256 * n] for c in at[1]], [T.HV[:, c:c + 256 * n] for c in at[0]], tk[0], tk[1], 256 * n)

    when("carry")
    carry(0, 1)
    carry(0, 2, 2)
    role[2] = -1
    names_of(0, 0)
    names_of(0, 1)
    for t in range(S):
        role[2] = t
        if 0 < t < S - 1:
            part(("K",))
            carry(4096 * (t % 2), (t - 1) % 4)
            part(("I",))
            for x in (2 * t - 2, 2 * t - 1):
                io(T.IDX[:, 256 * x:256 * x + 256], [[1, 256]], 256 * (x % 4), 0, [("IDX", x), "turn"], 256)
            if t == 2:
                ops[gap(8)]["wr"].append("turn")
        for X in range(2 if t < S - 1 else 0):
            record(t, X)
        for X in range(2):
            outcomes(t, X)
        for X in range(2):
            bound(t, X)
            values(t, X)
            choose(t, X)
            if t < S - 1:
                names_of(t + 1, X)
    return ops


def helper_program(g, core, T, topo, r):
    peers = [(r + k) % N for k in (1, 2, 3)]
    es = topo.engines(core, T.cores[peers[0]])
    full = sum(1 << e for e in es)
    n_in = len(inner_engines(topo, T.cores[r], T.cores[peers[0]]))
    ids = [dst_id(topo, T.cores[p]) for p in peers]
    jobs = [("hu%d" % b, "u%d" % b) + 2 * (T.LU[:, slot(b, r) - 256:slot(b, r)],)
            if b not in WIDE else ("hu%d" % b, "u%d" % b) + 2 * (T.HE[:, slot(b, r):slot(b, r) + 256],)
            for b in range(4) if b not in OWN]
    jobs = [("hv%d" % b, "v%d" % b) + 2 * (values_at(T, r, b),) for b in range(1, len(VCUT) - 1)] + jobs
    for i in range(2 * (S - 1)):
        ap = env_at(T, i // 2, r, i % 2)[0]
        jobs.append(("h%d" % i, "e%d" % i, ap, ap))
    jobs = [j for j in jobs if helper_of(T.cores[r], topo, j[0]) == core]
    if not jobs:
        return
    for got, sem, src, dst in jobs:
        g.wait_ge(T.sem[got], n_in)
        g.remote_dma_fused([RemoteDMATransfer(dst_ids=ids, dma_engine_mask=full, remote_sem=T.sem[sem], srcs=[src],
                                              dsts=[dst, dst, dst])], local_sem=T.sem.sent)
    g.wait_ge(T.sem.sent, len(jobs) * len(es))


def arrange(ops):
    lastw, readers = {}, {}
    n = len(ops)
    for i, o in enumerate(ops):
        raw, other = set(), set()
        for k in o["rd"]:
            if k in lastw:
                raw.add(lastw[k])
        for k in o["wr"]:
            into = other if isinstance(k, tuple) and k[0] == "B" else raw
            if k in lastw:
                into.add(lastw[k])
            into.update(readers.get(k, ()))
        for k in o["rd"]:
            readers.setdefault(k, []).append(i)
        for k in o["wr"]:
            lastw[k] = i
            readers[k] = []
        o["raw"], o["dep"] = raw - {i}, (raw | other) - {i}
        if "after" in o:
            o["dep"] = o["dep"] | {o["after"]}
        if o.get("also") is not None:
            o["dep"] = o["dep"] | {o["also"]}
    if "t0" not in PLAN:
        PLAN["end"], PLAN["t0"] = search(ops)
    for i in range(n):
        ops[i]["t0"] = PLAN["t0"][i]
    return sorted(range(n), key=lambda i: (ops[i]["t0"], i)), PLAN["end"]


def search(ops):
    n = len(ops)

    def gap(i, d):
        p = ops[d]
        if ops[i].get("also") == d:
            return p["dur"]
        if p["eng"] == ops[i]["eng"] and p["kind"] == "c" and ops[i]["kind"] == "c" and d not in ops[i]["raw"]:
            return p["dur"] + 0.001
        return p["dur"] + p["lat"] + HOP

    pre = [[(d, gap(i, d)) for d in sorted(ops[i]["dep"])] for i in range(n)]
    above = [0] * n
    for i in range(n):
        far = 0
        for d, _ in pre[i]:
            far |= above[d]
        above[i] = far | sum(1 << d for d, _ in pre[i])
        pre[i] = [(d, x) for d, x in pre[i] if not far >> d & 1 or ops[d]["lat"]]
    dur = [o["dur"] for o in ops]
    eng = [o["eng"] for o in ops]
    lat = [o["lat"] for o in ops]
    post = [[] for _ in range(n)]
    for i in range(n):
        for d, x in pre[i]:
            post[d].append((i, x - dur[d] + dur[i]))
    cases = []
    for cs in CASES:
        du = [o["dur"] * (cs[o.get("cls", 2 if o["eng"] == "pe" else 1)] if o["kind"] == "c" else
                          {"recv": cs[4], "land": cs[6]}.get(o["kind"], 1.0)) for o in ops]
        cases.append((du, [[(d, x - dur[d] + du[d] + (cs[3] if ops[d]["kind"] == "recv" else 0.0) + cs[5] * (x > dur[d] + 0.01))
                            for d, x in pre[i]] for i in range(n)]))

    def fill(order, dep, first):
        busy, t0 = {e: [] for e in eng}, [0.0] * n
        for i in order:
            s, du = first[i], dur[i]
            for d, x in dep[i]:
                if t0[d] + x > s:
                    s = t0[d] + x
            row = busy[eng[i]]
            k = len(row)
            while k > 0 and row[k - 1][1] > s:
                k -= 1
            while k < len(row) and row[k][0] < s + du - 1e-9:
                if row[k][1] > s:
                    s = row[k][1]
                k += 1
            row.insert(k, (s, s + du))
            t0[i] = s
        return t0

    zero = [0.0] * n

    def forward(key):
        m = len(key)
        for i in range(m - 1, -1, -1):
            for d, _ in pre[i]:
                if key[d] > key[i]:
                    key[d] = key[i]
        return fill(sorted(range(m), key=lambda j: (key[j], j)), pre, zero)[:m]

    def backward(t0, post, lat):
        m = len(t0)
        key = [-t0[i] - dur[i] for i in range(m)]
        for i in range(m):
            for d, _ in post[i]:
                if key[d] > key[i]:
                    key[d] = key[i]
        return fill(sorted(range(m), key=lambda j: (key[j], -j)), post, lat)

    def place(key, post, lat, turn=False):
        t0 = forward(key)
        m = len(key)
        if turn:
            u = backward(t0, post, lat)
            t0 = forward([-u[i] - dur[i] for i in range(m)])
        seq = sorted(range(m), key=lambda j: (t0[j], j))
        total = 0.0
        for du, pr in cases:
            free, t1, last = {}, [0.0] * m, 0.0
            for i in seq:
                s = free.get(eng[i], 0.0)
                for d, x in pr[i]:
                    if t1[d] + x > s:
                        s = t1[d] + x
                t1[i] = s
                free[eng[i]] = s + du[i]
                if s + du[i] + lat[i] > last:
                    last = s + du[i] + lat[i]
            total += last
        return total / len(cases), t0

    state = [SEED]

    def rnd():
        state[0] = (state[0] * 6364136223846793005 + 1442695040888963407) % 2 ** 64
        return (state[0] >> 11) / 2.0 ** 53

    names = sorted(set(o["role"] for o in ops), key=str)
    place_of = {x: i for i, x in enumerate(names)}
    rid = [place_of[o["role"]] for o in ops]
    pool = [i for i, x in enumerate(names) if x[0] != "once"]
    base = [0.0] * n
    for i, o in enumerate(ops):
        if "aim" in o:
            base[i] = FIRST + PERIOD * o["step"] + o["aim"]
        else:
            base[i] = FIRST + PERIOD * S if o["step"] > 0 else o["at"]

    def queue_links(t0, lat):
        prev, last = {}, {}
        for i in sorted(range(len(t0)), key=lambda j: (t0[j], j)):
            prev[i] = last.get(eng[i])
            last[eng[i]] = i
        i, out = max(range(len(t0)), key=lambda j: t0[j] + dur[j] + lat[j]), []
        while True:
            s, d = max([(t0[d] + x, d) for d, x in pre[i]], default=(0.0, None))
            if prev[i] is not None and t0[i] > s + 1e-6:
                out.append((prev[i], i))
                i = prev[i]
            elif d is None:
                return out
            else:
                i = d

    def anneal(key, post, lat, rounds, heat, zone=None):
        end, t0 = place(key, post, lat)
        links = queue_links(t0, lat)
        best = (end, t0)
        for it in range(rounds):
            off, move, amp = [0.0] * len(names), rnd(), (0.2, 0.6, 1.2)[int(rnd() * 3)]
            if zone:
                key, near = list(t0), [x for x in links if t0[x[0]] > zone]
                if near and move < 0.5:
                    a, b = near[int(rnd() * len(near))]
                    key[b] = t0[a] - 0.05 - rnd() * rnd()
                else:
                    lo = zone + rnd() * 10.0
                    key = [x + amp * (rnd() + rnd() - 1.0) if lo < x < lo + 4.0 else x for x in key]
                e2, t2 = place(key, post, lat)
                if e2 <= end + 2.0 * heat * (1.0 - it / rounds) * rnd():
                    end, t0 = e2, t2
                    links = queue_links(t0, lat)
                    best = min(best, (e2, t2))
                continue
            if links and move < 0.35:
                a, b = links[int(rnd() * len(links))]
                x = t0[b] - t0[a] + 0.05 + rnd() * rnd() * 2.0
                if rnd() < 0.5:
                    off[rid[b]] -= x
                else:
                    off[rid[a]] += x
            elif move < 0.6:
                for _ in range((2, 6, 20)[int(rnd() * 3)]):
                    off[pool[int(rnd() * len(pool))]] += amp * (rnd() + rnd() - 1.0)
            key = [x + off[rid[i]] for i, x in enumerate(t0)]
            if move >= 0.6:
                top = max(t0)
                lo, wd = (rnd() * top, top - 16.0 * rnd())[int(rnd() * 1.5)] - 2.0, (3.0, 6.0, 12.0)[int(rnd() * 3)]
                key = [x + amp * (rnd() + rnd() - 1.0) if lo < x < lo + wd else x for x in key]
            e2, t2 = place(key, post, lat, rnd() < 0.15)
            if e2 <= end + 2.0 * heat * (1.0 - it / rounds) * rnd():
                end, t0 = e2, t2
                links = queue_links(t0, lat)
                if e2 < best[0]:
                    best = (e2, t2)
        return best

    def cyclic(rounds, heat):
        own = [i for i in range(n) if ops[i]["step"] == 2]
        at = {ops[i]["role"]: j for j, i in enumerate(own)}
        m, laps = len(own), 5
        en = [eng[i] for i in own]
        dep = [[[(at[ops[d]["role"]], 2 - ops[d]["step"], x) for d, x in pr[i] if ops[d]["step"] > 0 and ops[d]["role"] in at]
                for i in own] for _, pr in cases]
        dus = [[du[i] for i in own] for du, _ in cases]
        after = [[] for _ in own]
        for j in range(m):
            for d, dt, _ in dep[0][j]:
                after[d].append((j, dt))
        first = at[(("V", 0), 1)]

        def run(key, per, top=1e9):
            lap = [int(key[j] // per) for j in range(m)]
            seq = sorted(range(m), key=lambda j: key[j] - per * lap[j])
            total, out = 0.0, None
            for du, pr in zip(dus, dep):
                rows = [(j, en[j], du[j], [(d, dt + lap[j] - lap[d], x) for d, dt, x in pr[j]]) for j in seq]
                t, free = [], {}
                for c in range(laps):
                    row = [0.0] * m
                    t.append(row)
                    for j, e, d0, ps in rows:
                        s = free.get(e, 0.0)
                        for d, back, x in ps:
                            if back <= c and t[c - back][d] + x > s:
                                s = t[c - back][d] + x
                        row[j] = s
                        free[e] = s + d0
                p = (t[-1][first] - t[1][first]) / (laps - 2)
                total += p
                if out is None:
                    z = t[-2][first] + p * lap[first]
                    if p > top:
                        return 1e9, None
                    out = ([t[-2][j] + p * lap[j] - z + 1e-6 * (key[j] - key[first]) for j in range(m)], p)
            return total / len(dus), out

        def sound(key, per):
            return all(key[j] > key[d] - dt * per for j in range(m) for d, dt, _ in dep[0][j])

        per, key = PERIOD, [ops[i]["aim"] for i in own]
        if "seed" in PLAN:
            per, key = PLAN["seed"]([ops[i] for i in own])
        for _ in range(20):
            for j in range(m):
                key[j] = max([key[j]] + [key[d] - dt * per + 1e-3 for d, dt, _ in dep[0][j]])
        while not sound(key, per):
            per += 0.2
        cost, out = run(key, per)
        best = (cost, key, per)

        def waits(t, p):
            seq, prev, last, found, seen, j = sorted(range(m), key=lambda y: t[y] % p), {}, {}, [], set(), first
            for y in seq + seq:
                prev[y] = last.get(en[y])
                last[en[y]] = y
            while j not in seen:
                seen.add(j)
                s, d = max([(t[d] - dt * p + x, d) for d, dt, x in dep[0][j]], default=(-1e9, None))
                if t[j] > s + 1e-3:
                    d = prev[j]
                    found.append((d, j))
                j = d
            return found

        links = None
        for it in range(rounds):
            if links is None and sound(*out):
                key, per = out
                links = waits(key, per)
            k2 = list(key)
            move = rnd()
            if move < 0.7:
                j, x = int(rnd() * m), (rnd() + rnd() - 1.0) * (0.5, 1.5)[int(rnd() * 2)]
                if links and move < 0.4:
                    a, b = links[int(rnd() * len(links))]
                    x = (key[b] - key[a]) % per + 0.002 + rnd() * rnd() * rnd()
                    j, x = (a, x) if rnd() < 0.5 else (b, -x)
                k2[j] += x
                todo, left = [j], 3 * m
                while todo and left:
                    j, left = todo.pop(), left - 1
                    for d, dt in after[j] if x > 0 else [y[:2] for y in dep[0][j]]:
                        edge = k2[j] + (-dt * per + 1e-4 if x > 0 else dt * per - 1e-4)
                        if (k2[d] < edge) if x > 0 else (k2[d] > edge):
                            k2[d] = edge
                            todo.append(d)
                if todo or not sound(k2, per):
                    continue
            for _ in range(int(rnd() * 1.5) if move < 0.7 else 1 + int(rnd() * rnd() * 4)):
                j = int(rnd() * m)
                lo = max([k2[d] - dt * per for d, dt, _ in dep[0][j]], default=k2[j] - 3.0)
                hi = min([k2[d] + dt * per for d, dt in after[j]], default=k2[j] + 3.0)
                k2[j] = lo + (hi - lo) * (0.001 + 0.998 * rnd())
            c2, o2 = run(k2, per, out[1] + 0.1 + heat)
            if c2 <= cost + heat * (1.0 - it / rounds) * rnd():
                cost, out, key, links = c2, o2, k2, None
                if c2 < best[0]:
                    best = (c2, k2, per)
        cost, key, per = best
        out = run(key, per)[1]
        if sound(*out):
            key, per = out
        PLAN["cycle"] = (cost, per, [(key[j], en[j], ops[i]) for j, i in enumerate(own)])
        return [FIRST + per * o["step"] + key[at[o["role"]]] if "aim" in o and o["role"] in at else base[i] for i, o in enumerate(ops)]

    def stretch(key, lo, hi, rounds, heat):
        seq = sorted(range(n), key=lambda j: (key[j], j))
        head, mid = [j for j in seq if key[j] < lo], [j for j in seq if lo <= key[j] < hi + 14.0]
        free = [j for j in mid if key[j] < hi]
        goal = [j for j in mid if key[j] >= hi + 9.0] or mid

        def times(order, du, pr, t, busy):
            for j in order:
                s = busy.get(eng[j], 0.0)
                for d, x in pr[j]:
                    if t[d] + x > s:
                        s = t[d] + x
                t[j] = s
                busy[eng[j]] = s + du[j]

        fixed = []
        for du, pr in cases:
            fixed.append(([0.0] * n, {}))
            times(head, du, pr, *fixed[-1])

        def run(k, top=1e9):
            order, total, out = sorted(mid, key=lambda j: k[j]), 0.0, None
            for (du, pr), (t, busy) in zip(cases, fixed):
                t = list(t)
                times(order, du, pr, t, dict(busy))
                e = max(t[j] + du[j] + lat[j] for j in goal) if goal is mid else sum(t[j] for j in goal) / len(goal)
                total += e
                if out is None:
                    if e > top:
                        return 1e9, None
                    out = (t, e, order)
            return total / len(cases), out

        def waits(t, order):
            prev, last, found = {}, {}, []
            for j in order:
                prev[j] = last.get(eng[j])
                last[eng[j]] = j
            j = max(goal, key=lambda y: t[y] + lat[y]) if goal is mid else goal[int(rnd() * len(goal))]
            while j in prev:
                s, d = max([(t[d] + x, d) for d, x in cases[0][1][j]], default=(0.0, None))
                if t[j] > s + 1e-3 and prev[j] is not None:
                    d = prev[j]
                    found.append((d, j))
                j = d
            return found

        inside = set(free)
        cost, out = run(key)
        best, links = (cost, list(key)), None
        for it in range(rounds):
            if links is None or it % 64 == 0:
                links = [x for x in waits(out[0], out[2]) if x[0] in inside and x[1] in inside]
            k2, move = list(key), rnd()
            j, x = free[int(rnd() * len(free))], (rnd() + rnd() - 1.0) * (0.4, 1.5, 3.0)[int(rnd() * 3)]
            if links and move < 0.5:
                a, b = links[int(rnd() * len(links))]
                x = key[b] - key[a] + 0.002 + rnd() * rnd() * rnd() * 2.0
                j, x = (a, x) if rnd() < 0.5 else (b, -x)
            k2[j] += x
            todo, ok = [j], lo <= k2[j] < hi
            while todo and ok:
                j = todo.pop()
                for d, _ in post[j] if x > 0 else pre[j]:
                    if (k2[d] <= k2[j]) if x > 0 else (k2[d] >= k2[j]):
                        k2[d] = k2[j] + (1e-4 if x > 0 else -1e-4)
                        ok = ok and d in inside and lo <= k2[d] < hi
                        todo.append(d)
            if not ok:
                continue
            c2, o2 = run(k2, out[1] + 0.15 + heat)
            if c2 <= cost + heat * (1.0 - it / rounds) * rnd():
                cost, out, key, links = c2, o2, k2, None
                if c2 < best[0]:
                    best = (c2, list(k2))
        return best[1]

    def shake(key, lo, hi, rounds, heat):
        order = sorted(range(n), key=lambda j: (key[j], j))
        seq = [j for j in order if key[j] < hi + 12.0]
        free = [j for j in seq if lo <= key[j] < hi]
        inside, m, known = set(free), len(seq), set(seq)
        goal = [j for j in seq if key[j] >= hi + 8.0]
        w = [0.0] * n
        for j in seq:
            w[j] = EARLY / m
        for j in goal:
            w[j] += 1.0 / len(goal)
        tail = [] if goal else [j for j in seq if lat[j] or not post[j]]
        nxt = [[d for d, _ in post[j] if d in known] for j in range(n)]
        key, pos, pv, ts, ends = list(key), [0] * n, [-1] * n, [], []

        def index(a, b):
            last = {}
            for p in range(a, b):
                j = seq[p]
                pos[j] = p
                pv[j] = last.get(eng[j], first.get(eng[j], -1))
                last[eng[j]] = j
            for p in range(b, m):
                if not last:
                    break
                j = seq[p]
                if eng[j] in last:
                    pv[j] = last.pop(eng[j])

        first = {}
        index(0, m)
        for du, pr in cases:
            t = [0.0] * n
            for j in seq:
                t[j] = max([t[pv[j]] + du[pv[j]] if pv[j] >= 0 else 0.0] + [t[d] + x for d, x in pr[j]])
            ts.append(t)
            ends.append(max([t[j] + du[j] + lat[j] for j in tail], default=0.0))

        def waits():
            c = int(rnd() * len(cases))
            (du, pr), t, found = cases[c], ts[c], []
            j = max(tail, key=lambda y: t[y] + du[y] + lat[y]) if tail else goal[int(rnd() * len(goal))]
            while j is not None:
                s, d = max([(t[d] + x, d) for d, x in pr[j]], default=(0.0, None))
                if t[j] > s + 1e-3 and pv[j] >= 0:
                    d = pv[j]
                    if d in inside and j in inside:
                        found.append((d, j))
                j = d
            return found

        cost, best, links = 0.0, (0.0, list(key)), None
        for it in range(rounds):
            if links is None or it % 32 == 0:
                links = waits()
            j, x = free[int(rnd() * len(free))], (rnd() + rnd() - 1.0) * (0.3, 1.0, 3.0)[int(rnd() * 3)]
            if links and rnd() < 0.5:
                a, b = links[int(rnd() * len(links))]
                x = key[b] - key[a] + 0.002 + rnd() * rnd() * rnd() * 2.0
                j, x = (a, x) if rnd() < 0.5 else (b, -x)
            k2 = {j: key[j] + x}
            todo, ok = [j], lo <= k2[j] < hi
            while todo and ok:
                j = todo.pop()
                kj = k2[j]
                for d, _ in post[j] if x > 0 else pre[j]:
                    kd = k2.get(d, key[d])
                    if (kd <= kj) if x > 0 else (kd >= kj):
                        k2[d] = kj + (1e-5 if x > 0 else -1e-5)
                        ok = ok and d in inside and lo <= k2[d] < hi
                        todo.append(d)
            if not ok:
                continue
            a, b = min(pos[j] for j in k2), max(pos[j] for j in k2) + 1
            if x > 0:
                top = max(k2.values())
                while b < m and key[seq[b]] < top:
                    b += 1
            else:
                top = min(k2.values())
                while a > 0 and key[seq[a - 1]] > top:
                    a -= 1
            seg = sorted(seq[a:b], key=lambda y: k2.get(y, key[y]))
            first = {}
            for j in seq[a:b]:
                if eng[j] not in first:
                    first[eng[j]] = pv[j]
            delta, new, room = 0.0, [], heat * (1.0 - it / rounds) * rnd()
            for c, (du, pr) in enumerate(cases):
                old = ts[c]
                t = list(old)
                busy = {e: (t[d] + du[d] if d >= 0 else 0.0) for e, d in first.items()}
                moved, reach, p, gain = set(first), b, a, 0.0
                while p < m and (moved or p <= reach):
                    j = seg[p - a] if p < b else seq[p]
                    p += 1
                    e = eng[j]
                    s = busy.get(e)
                    if s is None:
                        d = pv[j]
                        s = t[d] + du[d] if d >= 0 else 0.0
                    for d, y in pr[j]:
                        y += t[d]
                        if y > s:
                            s = y
                    busy[e] = s + du[j]
                    y = s - old[j]
                    if y > 1e-9 or y < -1e-9:
                        t[j] = s
                        gain += w[j] * y
                        moved.add(e)
                        for d in nxt[j]:
                            if pos[d] > reach:
                                reach = pos[d]
                    elif p > b:
                        moved.discard(e)
                end = max([t[j] + du[j] + lat[j] for j in tail], default=0.0)
                delta += (gain + end - ends[c]) / len(cases)
                new.append((t, end))
                if c == 0 and delta > room + 0.06:
                    break
            if delta <= room:
                for j, y in k2.items():
                    key[j] = y
                seq[a:b] = seg
                index(a, b)
                for c in range(len(cases)):
                    ts[c], ends[c] = new[c]
                cost += delta
                if delta:
                    links = None
                if cost < best[0] - 1e-9:
                    best = (cost, list(key))
        return best[1]

    def settle(key):
        du, pr = cases[0]
        t, busy = [0.0] * n, {}
        for r, j in enumerate(sorted(range(n), key=lambda y: (key[y], y))):
            t[j] = max([busy.get(eng[j], 0.0)] + [t[d] + x for d, x in pr[j]])
            busy[eng[j]] = t[j] + du[j]
            key[j] = t[j] + 1e-7 * r
        return key

    base = cyclic(CYCLE, WARM)
    if not ROUNDS:
        return 0.0, forward(base)
    for i, o in enumerate(ops):
        if o["step"] > 0 or o["step"] == 0 and o["role"][0][0] not in ("o", "V", "R", "O", "O2", "D"):
            base[i] += LATE
    key = forward(list(base))
    ga = [i for i in range(n) if ops[i]["role"] == (("V", 0), 1)]
    for _ in range(TURNS):
        u = backward(key, post, lat)
        late = forward([-u[i] - dur[i] for i in range(n)])
        if late[ga[1]] < key[ga[1]]:
            key = late
    for i in range(n):
        if 0 < ops[i]["step"] < S - 1:
            key[i] = base[i] - base[ga[1]] + key[ga[1]]
    for i in range(n - 1, -1, -1):
        for d, _ in pre[i]:
            key[d] = min(key[d], key[i] - 1e-4)
    key = settle(key)
    for share, heat in HEATS:
        key = settle(shake(key, -1.0, key[ga[1]] + 5.0, ROUNDS // share, heat))
    for heat in (0.1, 0.03):
        key = settle(shake(key, key[ga[S - 1]] - 6.0, 1e9, ROUNDS // 12, heat))
    total = 0.0
    for du, pr in cases:
        t, busy = [0.0] * n, {}
        for j in sorted(range(n), key=lambda y: key[y]):
            t[j] = max([busy.get(eng[j], 0.0)] + [t[d] + x for d, x in pr[j]])
            busy[eng[j]] = t[j] + du[j]
        total += max(t[j] + du[j] + lat[j] for j in range(n))
    return total / len(cases), key


def emit(g, T, ops, seq):
    queue = {"pe": g.tensor, "act": g.scalar, "dve": g.vector, "pool": g, "sp": g.sync}
    count, known, total, waited = {}, {e: {} for e in queue}, {}, {}
    ndma, sent = 0, 0
    for i in seq:
        o = ops[i]
        if o["kind"] == "recv":
            o["mark"], o["clock"] = (o["sem"], o["cnt"]), {}
            total[o["sem"]] = o["cnt"]
            continue
        if o["kind"] == "hop":
            continue
        if o["kind"] == "land":
            o["mark"], o["clock"] = ops[o["after"]]["mark"], ops[o["after"]]["clock"]
            continue
        e, kn = o["eng"], known[o["eng"]]
        need = {}
        for d in o["dep"]:
            p = ops[d]
            if p["kind"] == "c" and o["kind"] == "c" and p["eng"] == e and d not in o["raw"]:
                continue
            if p["kind"] == "send":
                continue
            s, n = p["mark"]
            if need.get(s, (0, None))[0] < n:
                need[s] = (n, p)
        for s, (n, p) in sorted(need.items(), key=lambda x: -x[1][1]["t0"]):
            if kn.get(s, 0) >= n:
                continue
            queue[e].wait_ge(T.sem[s], n)
            waited[s] = max(waited.get(s, 0), n)
            kn[s] = n
            for s2, n2 in p["clock"].items():
                kn[s2] = max(kn.get(s2, 0), n2)
        ins = o["fn"]()
        o["clock"] = dict(kn)
        if o["kind"] == "c":
            count[e] = count.get(e, 0) + 1
            ins.then_inc(T.sem[e], 1)
            o["mark"] = (e, count[e])
            total[e] = count[e]
        elif o["kind"] == "dma":
            s = "d%d" % ndma
            ndma += 1
            for x in ins:
                x.then_inc(T.sem[s], 16)
            o["mark"] = (s, 16 * len(ins))
            total[s] = 16 * len(ins)
        else:
            sent += o["inc"]
    total["sent"] = sent
    for s, n in total.items():
        if waited.get(s, 0) < n:
            g.wait_ge(T.sem[s], n)


def rank_program(g, core, T, topo):
    me = T.rank_of(core)
    if me is None:
        for r, c in enumerate(T.cores):
            if core in topo.cores_of(c):
                helper_program(g, core, T, topo, r)
        return
    ops = build_ops(g, T, topo, core, me)
    seq, _ = arrange(ops)
    emit(g, T, ops, seq)
